import numpy as np, ml_dtypes
CORES = [13,21,141,149]
N = 4
BF = ml_dtypes.bfloat16
V, P, L, RO, Q, CAP = 1280, 2048, 256, 3, 3, 96
H, ST = 1024, 5
MS, PO = (4, 4, 5, 5, 6, 6, 7, 8), 14
def rings(rng, hole):
    pool = 1 + np.argsort(rng.random((8, 16, 255)), axis=-1)[..., :PO]
    ms = np.stack([rng.permutation(np.array(MS)) for r in range(N)])
    pal = np.take_along_axis(np.broadcast_to(pool, (N, 8, 16, PO)), np.argsort(rng.random((N, 8, 16, PO)), axis=-1), 3)
    k = np.take_along_axis(pal, (rng.random((N, 8, 16, V)) * ms[:, :, None, None]).astype(np.int64), 3)
    u = rng.random((N, 8, 16, V))
    return np.where(u < hole, 0, np.where(u < hole + 0.05, rng.integers(1, 256, (N, 8, 16, V)), k))
def parts(rng, hole=0.12):
    t = rng.choice(np.array([0, 300, 500, 700, 850]), (N, 8, 16, 1)) + rng.integers(0, 100, (N, 8, 16, 1))
    return rings(rng, hole), rng.integers(0, V, (N, 8, 16, V)), rng.integers(0, 256, (N, 8, 16, P)), rng.integers(0, 256, (N, 8, 16, L)), t
def pack(k, b, x, z, t):
    def bf(a): return np.ascontiguousarray(a.reshape(N, 128, -1)).astype(np.float32).astype(BF)
    return {"ring": bf(k), "nbr": np.ascontiguousarray(b.reshape(N, 128, V)).astype(np.int32), "mat": bf(x), "z0": bf(z), "thr": np.ascontiguousarray(t.reshape(N, 128, 1)).astype(np.int32)}
def setup_inputs(rng):
    return pack(*parts(rng))
def setup_inputs_spread(rng):
    k, b, x, z, t = parts(rng)
    e = rng.integers(5, 13, (N, 8, 1, 1)); ix = np.minimum((255 * rng.random((N, 8, 16, V)) ** e).astype(np.int64), 254)
    keys = 1 + np.argsort(rng.random((8, 16, 255)), axis=-1)
    k = np.take_along_axis(np.broadcast_to(keys, (N, 8, 16, 255)), ix, 3)
    k = np.where(rng.random((N, 8, 16, V)) < rng.random((N, 8, 1, V)) ** 3, 0, k)
    b[:, ::2] = np.minimum((V * rng.random((N, 4, 16, V)) ** 2).astype(np.int64), V - 1)
    x = np.minimum((np.exp2(8 * rng.random((N, 8, 1, P))) * rng.random((N, 8, 16, P))).astype(np.int64), 255)
    z = np.minimum((np.exp2(8 * rng.random((N, 8, 1, L))) * rng.random((N, 8, 16, L))).astype(np.int64), 255)
    t = np.minimum(np.exp2(12 * rng.random((N, 8, 16, 1))).astype(np.int64), 4095)
    return pack(k, b, x, z, t)
def setup_inputs_ends(rng):
    k, b, x, z, t = parts(rng)
    c = rng.random((N, 8, 1, V)); dens = rng.choice(np.array([0.25, 0.25, 0.5]), (N, 8, 1, V))
    k = np.where(c < 0.25, 255, np.where(c < 0.4, 0, np.where(c < 0.85, 255 * (rng.random((N, 8, 16, V)) < dens), k)))
    k[:, 6, :, 2 * ST:ST * (L - 4):ST] = 255
    b = np.where(rng.random((N, 8, 16, V)) < 0.7, (V - 1) * rng.integers(0, 2, (N, 8, 16, V)), b)
    share = np.array([0.5, 0, 0.5, 0, 0, 0, 0, 0]).reshape(8, 1, 1)
    x = np.where(rng.random((N, 8, 1, P)) < share + 0.05, 255 * rng.integers(0, 2, (N, 8, 1, P)), 255 * rng.integers(0, 2, (N, 8, 16, P)))
    z = np.where(rng.random((N, 8, 1, L)) < share, 255 * rng.integers(0, 2, (N, 8, 1, L)), 255 * rng.integers(0, 2, (N, 8, 16, L)))
    t = np.broadcast_to(4095 * (rng.random((1, 8, 16, 1)) < 0.25), (N, 8, 16, 1)); t = np.where(rng.random((N, 8, 16, 1)) < 0.05, 4095 - t, t)
    t[:, 0, 0] = 4095; t[:, 7, 14] = 0; t[:, 7, 15] = 4095
    k[..., V - 1] = 255; k[..., 0] = 255 * (np.argsort(np.argsort(rng.random((N, 8, 16)), axis=-1), axis=-1) < 5)
    x[..., 0] = 0; x[..., P - 1] = 255
    p = np.arange(16)
    for lane in (1, L - 1):
        v = ST * lane; z[..., lane] = 255; k[..., v] = 0; b[:, :, 0, v] = V - 1
        x[..., ((255 * (2 * v + 1) >> 2) + 811 * p) & (P - 1)] = 0 if lane == 1 else 255 * ((p + 1) & 1)
    z[..., 0] = 0; z[..., L - 2] = 0; k[..., ST * (L - 2)] = 0
    a = (15 + Q) >> 1; v = ST * (L - 4); z[..., L - 4] = 0
    k[..., v] = 255 * (p < a); k[..., V - 2] = 255 * (p >= 16 - a); b[:, :, 0, v] = V - 2
    k[..., V - 3] = 255; k[..., V - 4] = 255; b[:, :, 0, V - 2] = V - 2
    for i, u in ((1, V - 1), (14, V - 3), (15, V - 4)): b[:, :, i, V - 2] = u
    return pack(k, b, x, z, t)
def setup_inputs_corners(rng):
    k, b, x, z, t = parts(rng)
    code = rng.integers(1, 256, (N, 8, 16, 1)); code[:, ::2] = code[:1, ::2]; row = np.arange(16)[:, None]
    u = rng.random((N, 8, 1, V))
    k = np.where((row < Q) | (u < 0.33), code, np.where(u < 0.66, rng.integers(1, 256, (N, 8, 16, V)), 0))
    own = np.broadcast_to(np.arange(V), (16, V)); many = (0, 1, CAP - 1, CAP, CAP + 1, L, CAP, L >> 1)
    for r in range(N):
        for g in range(8):
            n = many[(g + r) & 7]; lanes = rng.permutation(L)[:n]; vf = ST * lanes
            if g & 3 == 1: b[r, g] = np.where(rng.random((16, V)) < 0.5, own, b[r, g])
            if g & 3 == 2: b[r, g] = np.where(rng.random((16, V)) < 0.3, (V - 1) * rng.integers(0, 2, (16, V)), b[r, g])
            if g & 3 == 3: b[r, g] = np.where(rng.random((16, V)) < 0.5, rng.integers(0, V, (1, V)), b[r, g])
            gone = np.zeros(V, bool); gone[vf] = True
            b[r, g] = b[r, g] + gone[b[r, g]]
            if g & 3 == 1: b[r, g][:, vf[::2]] = vf[::2]
            k[r, g][:, vf] = np.where((row < Q - 1) & (rng.random(n) < 0.5), code[r, g], 0)
    t = np.where(rng.random((N, 8, 16, 1)) < 0.5, rng.choice(np.array([0, 1, 15, 600, 1000, 4095]), (N, 8, 16, 1)), t); t[:, ::2, :Q] = 0; t[:, 1, 15] = 4095
    x = np.where(rng.random((N, 8, 1, P)) < 0.2, rng.choice(np.array([0, 128, 255]), (N, 8, 1, P)), x)
    z = np.where(rng.random((N, 8, 1, L)) < 0.3, rng.choice(np.array([0, 1, 254, 255]), (N, 8, 1, L)), z)
    return pack(k, b, x, z, t)
def setup_inputs_crowd(rng):
    k, b, x, z, t = parts(rng, 0.22)
    k = np.where(rng.random((N, 8, 1, V)) < 0.03, 0, k)
    hubs = np.argsort(rng.random((N, 8, V)), axis=-1)[..., :12]
    h = np.take_along_axis(hubs, rng.integers(0, 12, (N, 8, 16 * V)), 2).reshape(N, 8, 16, V)
    b = np.where(rng.random((N, 8, 16, V)) < 0.6, h, b)
    x[:, 1::2] = np.take_along_axis(x[:, 1::2], np.broadcast_to(rng.integers(0, 8, (N, 4, 1, P)), (N, 4, 16, P)), 3)
    z[..., 1::2] = z[..., ::2]
    return pack(k, b, x, z, t)
def setup_inputs_far(rng):
    k, b, x, z, t = parts(rng); a = (15 + Q) >> 1; kk = np.arange(16)[:, None]
    up = rng.integers(0, 2, (N, 8, 1, 1)); up[0, 0] = 0; up[N - 1, 7] = 1
    x = rng.integers(0, 48, (N, 8, 16, P)) + 208 * up; z = rng.integers(0, 48, (N, 8, 16, L)) + 208 * (1 - up)
    t = np.where(rng.random((N, 8, 16, 1)) < 0.4, rng.integers(3000, 3500, (N, 8, 16, 1)), t)
    first = ST * np.arange(L); rest = np.setdiff1d(np.arange(V), first)
    for r in range(N):
        for g in range(8):
            if (g + r) & 1: continue
            code = rng.integers(1, 256, (16, 1)); o = rng.permutation(16)[:, None]
            rare = 1 + (code - 1 + rng.integers(1, 255, (16, V))) % 255
            other = np.where(rng.random((16, V)) < 0.7, 0, rare)
            u = rng.permutation(rest); q = len(u) >> 2; near = u[:q]; full = u[q:2 * q]; right = u[2 * q:3 * q]
            kr = k[r, g]; br = b[r, g]
            kr[:, first] = np.where(o < a, code, other[:, first])
            kr[:, right] = np.where(o >= 16 - a, code, other[:, right])
            kr[:, full] = code
            kr[:, near] = np.where(o == rng.integers(a, 16, q), rare[:, near], code)
            e = ST * rng.permutation(L)[:L >> 4]
            kr[:, e[::2]] = 0; kr[:, e[1::2]] = code
            br[:, first] = rng.choice(right, (16, L))
            i = rng.integers(0, 15, q); m = i + 1 + (rng.random(q) * (15 - i)).astype(np.int64)
            pick = rng.random((16, q)); low = rng.choice(near, (16, q)); top = rng.choice(full, (16, q)); poor = rng.choice(np.concatenate([first, u[2 * q:]]), (16, q))
            late = np.where((kk == m) | (pick < 0.4), top, np.where(pick < 0.7, low, poor))
            early = np.where((kk == i) | ((kk > i) & (pick < 0.5)), low, poor)
            br[:, right] = np.where(kk < m, early, late)
    return pack(k, b, x, z, t)
def check_inputs(d):
    bad = []
    for k, lo, hi in (("ring", 0, 255), ("nbr", 0, V - 1), ("mat", 0, 255), ("z0", 0, 255), ("thr", 0, 4095)):
        a = np.asarray(d[k]).astype(np.float64)
        if not (np.min(a) >= lo and np.max(a) <= hi): bad.append("range of " + k)
        elif np.any(a != np.floor(a)): bad.append("whole numbers in " + k)
    return bad
def columns(a, ix):
    return np.take_along_axis(a, ix[:, :, None, :], 3)
def by_lane(a):
    return np.ascontiguousarray(a.transpose(0, 1, 3, 2)).reshape(N, 8, L * 16)
def reference(ring, nbr, mat, z0, thr):
    K = ring.astype(np.float32).astype(np.int64).reshape(N, 8, 16, V); B = nbr.astype(np.int64).reshape(N, 8, 16, V)
    X = mat.astype(np.float32).astype(np.int64).reshape(N, 8, 16, P); z = z0.astype(np.float32).astype(np.int64).reshape(N, 8, 16, L)
    th = thr.astype(np.int64).reshape(N, 8, 16, 1); v = np.array(np.broadcast_to(ST * np.arange(L), (N, 8, L)))
    failures = np.zeros(N, np.int64); rv_old = np.zeros((N, 8, 16), np.int64); row = np.arange(16)[:, None]
    for t in range(RO):
        j = (np.sum(z, axis=2) + t) & 15
        n = np.take_along_axis(columns(B, v), j[:, :, None, :], 2)[:, :, 0]
        Kv = columns(K, v); Kn = columns(K, n)
        direct = np.sum((Kv == Kn) & (Kv > 0), axis=2) >= Q
        cand = by_lane(columns(B, n)); Kc = columns(K, cand).reshape(N, 8, 16, L, 16)
        score = np.minimum(np.sum((Kc == Kv[..., None]) & (Kc > 0), axis=2), np.sum((Kc == Kn[..., None]) & (Kc > 0), axis=2))
        k = np.argmax(score, axis=3)
        bridged = ~direct & (np.max(score, axis=3) >= Q); failed = ~direct & ~bridged
        w = np.where(bridged, np.take_along_axis(cand.reshape(N, 8, L, 16), k[..., None], 3)[..., 0], n)
        Kw = columns(K, w)
        place = (((Kw * (2 * v + 1)[:, :, None, :]) >> 2) + 811 * row + t) & (P - 1)
        Xc = columns(X, by_lane(place)).reshape(N, 8, 16, L, 16)
        d = np.sum(np.abs(Xc - z[..., None]), axis=2)
        p = np.argmin(d, axis=3)
        x = np.take_along_axis(Xc, p[:, :, None, :, None], 4)[..., 0]
        caught = (d.transpose(0, 1, 3, 2) < th + (failures & 15)[:, None, None, None]) & (Kw > 0)
        low = np.argmax(caught, axis=3)
        rv = np.where(np.any(caught, axis=3), np.take_along_axis(Kw, low[..., None], 3)[..., 0], 0)
        fi = failed.astype(np.int64); served = failed & (np.add.accumulate(fi, axis=2) - fi < CAP)
        h = np.sum(Kw * z, axis=2) & (H - 1)
        given = columns(np.roll(K, -1, axis=0), h)
        filled = np.where(Kv > 0, Kv, np.where(bridged[:, :, None, :], Kw, given))
        K2 = np.array(K); B2 = np.array(B); active = bridged | served
        for a in range(N):
            for g in range(8):
                i = np.nonzero(active[a, g])[0]
                u, first = np.unique(v[a, g, i], return_index=True); i = i[first]
                K2[a, g][:, u] = filled[a, g][:, i]
                i = i[bridged[a, g, i]]; B2[a, g, j[a, g, i], v[a, g, i]] = w[a, g, i]
        come = np.roll(rv_old, 1, axis=0)
        K = np.where((K2 == rv[..., None]) | (K2 == come[..., None]), 0, K2); B = B2
        z = (z + x) >> 1; v = w; rv_old = rv; failures = np.sum(fi, axis=(1, 2))
    return {"yk": K.reshape(N, 128, V).astype(np.float32).astype(BF), "yz": z.reshape(N, 128, L).astype(np.float32)}

@@ -1,0 +1,769 @@
+from concourse.bass import DstId, RemoteDMATransfer
+from concourse.mybir import dt, AluOpType, AxisListType, ActivationFunctionType
+import comms_topo
+
+A = AluOpType
+AF = ActivationFunctionType
+RO, SB, CAP = 3, 2048, 96
+BIG = 1.0e9
+PEQ = (0, 2)
+REM = 1536
+WS = 17 * SB
+DIR = 239 * SB
+
+F32 = dict(If=128, G16f=128, G8f=8, DM=256, RN=256, RP=128, T1=1280, B=1536, Bv=256, mB=256, Bk=256, dg=256, sc=256, BnC=256,
+           dr=16, kn=16, cV=256, mn=256, sc2=256, W=16, Aw=256, kp=256, Vn=256, V2=256, pr=256, zx=256, sd=256,
+           Ap=256, dk=256, cd=256, rr=256, ohw=256, zF=256, pcol=1, p2=1, p2b=1, dcol=1, odd=1, even=1, kcol=1, thr=1, thrc=1,
+           nrv=1, rvE1=1, rvE2=1, ncome=1, fs=1, fj=16, d04=16, vmd4=16, x96=16, av=16, hd=16,
+           wr=16, hb=16, hc=16, src=16, w2=16, word=16, t1=16, Aq=256, pm0=1, pm1=1, pm2=1, pl0=1, pl1=1, pl2=1,
+           p5=1, fb=1)
+BF = dict(Ib=128, G16b=128, G8b=8, G8s=8, G8k=8, TriO=128, On=128, LPh=128, LPl=128, UC=256, z=256, Kv=256, Kn=256,
+          Kw=256, evn=256, m0=256, m1=256, Kvr=256, zT=256, hz=256, sgn=256, hole=256, fm=256, code=256, cdE=256, cdO=256, F=16, NF=16, Lb=16,
+          act=16, NM1=1280, NM2=1280)
+I32 = dict(PI=1, pi15=1, pb=1, D1=256, D15=256, D2=128, D3=256, ic=16, iv=16, y1=256, y2=256, pl=256, plm=256,
+           pi=16, pi2=16, dz=256, Wi=16, wT=16, hi=16, h2=16, qi=16, q1=16, q2=16, rvi=1, rva=1, fi=1, fa=1, ci=256, cb=256)
+U16 = dict(bl=16, bl2=16, vO=32, nO=32, wO=32, scO=16, srO=16, dO=32, BnL=256, PL=256)
+
+
+def _layout(d):
+    pos, at = {}, 0
+    for n in d:
+        pos[n] = at
+        at += (d[n] + 15) // 16 * 16
+    return pos, at
+
+
+_PF, _NF = _layout(F32)
+_PB, _NB = _layout(BF)
+_PI, _NI = _layout(I32)
+_PU, _NU = _layout(U16)
+WHERE = {}
+for _d, _p, _n in ((F32, _PF, "SF"), (BF, _PB, "SBF"), (I32, _PI, "SI"), (U16, _PU, "SU")):
+    for _k in _d:
+        WHERE[_k] = (_n, _p[_k], _d[_k])
+_BIGB = dict(KK0=(REM + 1024 * RO, "bfloat16"), KK1=(REM + 1024 * RO, "bfloat16"), RS=(2048, "bfloat16"), X=(2048, "bfloat16"),
+             Kc=(4096, "bfloat16"), eqV=(4096, "bfloat16"), eqN=(4096, "bfloat16"), Xc=(4096, "bfloat16"), df=(4096, "bfloat16"),
+             ab=(4096, "bfloat16"), EA=(2048, "bfloat16"), EB=(1024, "bfloat16"), E0=(2048, "bfloat16"), E1=(1024, "bfloat16"),
+             NBi=(1280, "int32"), Yk=(1280, "bfloat16"), thI=(8, "int32"), rS0=(8, "float32"), rS1=(8, "float32"),
+             rS2=(8, "float32"), cI0=(8, "float32"), cI1=(8, "float32"))
+SCRATCH = {"SF": ("sbuf", [128, _NF], "float32"), "SBF": ("sbuf", [128, _NB], "bfloat16"), "SI": ("sbuf", [128, _NI], "int32"),
+           "SU": ("sbuf", [128, _NU], "uint16")}
+for _k in _BIGB:
+    SCRATCH[_k] = ("sbuf", [128, _BIGB[_k][0]], _BIGB[_k][1])
+    WHERE[_k] = (_k, 0, _BIGB[_k][0])
+for _k in range(8):
+    SCRATCH["b%d" % _k] = ("psum", [128, 512], "float32")
+    WHERE["b%d" % _k] = ("b%d" % _k, 0, 512)
+for _k in range(RO):
+    SCRATCH["hand%d" % _k] = ("sbuf", [128, 512], "bfloat16")
+for _k in range(RO - 1):
+    SCRATCH["hrv%d" % _k] = ("sbuf", [128, 8], "float32")
+SEMAPHORES = ["qv", "qs", "qt", "qg"]
+SEMAPHORES += ["ld%d" % i for i in range(8)] + ["st%d" % i for i in range(5)]
+for _t in range(RO):
+    SEMAPHORES += ["ks%d0" % _t, "ks%d1" % _t, "ki%d0" % _t, "ki%d1" % _t, "ha%d" % _t, "hs%d" % _t]
+for _t in range(RO - 1):
+    SEMAPHORES += ["rs%d" % _t, "ri%d" % _t, "ra%d" % _t, "rl%d" % _t]
+
+CY = 0.00083
+SEQ = []
+TAIL = 0.16
+SIG, SEED, WIN = 0.02, 1080, 0.0
+
+
+def noise(i, seed):
+    return ((i * 2654435761 + seed * 1013904223 + (i ^ seed) * 69069) % 65521) / 65521.0 - 0.5
+
+
+def relays(core, T, topo, dst):
+    out = []
+    for d in (topo.die(core), 1 - topo.die(core)):
+        for c in topo.cores_of(core):
+            if c != core and topo.die(c) == d and T.rank_of(c) is None and topo.may_write(c, dst):
+                out.append(c)
+                break
+    return out
+
+
+def engines_mask(topo, src, dst, n):
+    m = 0
+    for e in topo.engines(src, dst)[:n]:
+        m |= 1 << e
+    return m
+
+
+def remote(g, topo, src, dst, out, in_, rsem, lsem, n):
+    rid, pid = topo.addr(dst, src)
+    return g.remote_dma(out, in_, rsem, lsem, pid, rid, engines_mask(topo, src, dst, n))
+
+
+def view(name, lo=0, hi=None, step=1, plo=0, phi=128):
+    return ("@", name, lo, WHERE[name][2] if hi is None else hi, step, plo, phi)
+
+
+def ind(win, off):
+    return ("#", win, off)
+
+
+def is_view(x):
+    return isinstance(x, tuple) and len(x) > 0 and (x[0] == "@" or x[0] == "#")
+
+
+def count(x):
+    if x[0] == "#":
+        return 16 * (x[2][3] - x[2][2])
+    return (x[3] - x[2] + x[4] - 1) // x[4]
+
+
+def psum(x):
+    return x[0] == "@" and x[1][0] == "b" and len(x[1]) == 2 and x[1][1].isdigit()
+
+
+def two(x):
+    return x[0] == "@" and WHERE[x[1]][0] not in ("SF", "SI", "NBi", "thI") and not psum(x)
+
+
+def clash(a, b):
+    if a[3] <= b[2] or b[3] <= a[2] or a[6] <= b[5] or b[6] <= a[5]:
+        return False
+    if a[4] > 1 and a[4] == b[4] and (a[2] - b[2]) % a[4]:
+        return False
+    return True
+
+
+def covers(a, b):
+    return a[4] == 1 and a[2] <= b[2] and a[3] >= b[3] and a[5] <= b[5] and a[6] >= b[6]
+
+
+def cost(q, m, kw):
+    o = kw.get("out")
+    if q == "t":
+        n, mm = count(kw["rhs"]), count(kw["lhsT"])
+        f = 4 if WHERE[kw["lhsT"][1]][0] == "SF" else 1
+        return max(min(64, mm), n) * f * CY
+    if q == "g":
+        return 0.15 + 2 * count(o) * CY
+    ins = [kw[k] for k in kw if k not in ("out", "accum_out") and is_view(kw[k])]
+    full = [i for i in ins if count(i) > 1]
+    n = max([count(o)] + [count(i) for i in full])
+    if o[0] == "#":
+        return 0.05 + n * 3.8 * CY
+    for i in full:
+        if i[0] == "#":
+            return 0.06 + n * 1.56 * CY
+    c = 1.0
+    if q == "v" and m == "tensor_tensor" and not psum(o) and not [i for i in full if psum(i)]:
+        c = 2.0
+    if q == "v" and m in ("tensor_copy", "tensor_scalar", "memset") and two(o) and not [i for i in full if not two(i)]:
+        c = 0.5
+    return max(64, n * c) * CY
+
+
+def noter(T):
+    ops, hist, opened = [], {}, {}
+
+    def res(x):
+        if x[0] == "#":
+            return res(x[1]).indirect(res(x[2]))
+        b, off, _ = WHERE[x[1]]
+        lo, hi = off + x[2], off + x[3]
+        if x[4] > 1:
+            return T[b][x[5]:x[6], lo:range(lo, hi, x[4])[-1] + 1:x[4]]
+        return T[b][x[5]:x[6], lo:hi]
+
+    def touch(i, q, v, wr, deps):
+        ps = psum(v)
+        keep = []
+        for e in hist.setdefault(v[1], []):
+            ev, ew, eq, ei = e
+            if ei == i:
+                keep.append(e)
+                continue
+            if ps and eq != q:
+                deps.add((ei, True))
+                if wr and covers(v, ev):
+                    continue
+            elif (wr or ew) and clash(v, ev):
+                if not (ps and q == "t"):
+                    deps.add((ei, True))
+                if wr and covers(v, ev):
+                    continue
+            keep.append(e)
+        keep.append((v, wr, q, i))
+        hist[v[1]] = keep
+
+    def rec(q, c, tail, reads, writes, emit, sem=None, inc=1):
+        i = len(ops)
+        deps = set()
+        for v in reads:
+            touch(i, q, v, False, deps)
+        for v in writes:
+            touch(i, q, v, True, deps)
+        ops.append([q, c, tail, deps, emit, sem or "q" + q, inc])
+        return i
+
+    def op(q, m, **kw):
+        reads, writes = [], []
+        for k in kw:
+            x = kw[k]
+            if not is_view(x):
+                continue
+            w = k in ("out", "accum_out")
+            if x[0] == "#":
+                (writes if w else reads).append(x[1])
+                reads.append(x[2])
+            else:
+                (writes if w else reads).append(x)
+
+        def emit(e):
+            a = {}
+            for k in kw:
+                a[k] = res(kw[k]) if is_view(kw[k]) else kw[k]
+            if m == "memset":
+                return e.memset(a["out"], a["constant"])
+            if m == "tensor_copy":
+                return e.tensor_copy(a["out"], a["in_"])
+            if m == "tensor_tensor":
+                return e.tensor_tensor(**a)
+            if m == "tensor_scalar":
+                return e.tensor_scalar(**a)
+            if m == "tensor_reduce":
+                return e.tensor_reduce(**a)
+            if m == "tensor_tensor_scan":
+                return e.tensor_tensor_scan(**a)
+            if m == "matmul":
+                return e.matmul(**a)
+            if m == "activation":
+                return e.activation(**a)
+            if m == "affine_select":
+                return e.affine_select(**a)
+            return e.iota(**a)
+        i = rec(q, cost(q, m, kw), TAIL, reads, writes, emit)
+        if m == "matmul":
+            b = kw["out"][1]
+            if b in opened:
+                for j in (opened[b] if kw["start"] or kw["stop"] else opened[b][:1]):
+                    ops[i][3].add((j, False))
+            if kw["start"] or kw["stop"]:
+                opened[b] = [i]
+            else:
+                opened[b].append(i)
+        return i
+
+    def land(v, sem, inc, i):
+        j = rec("x", 0.0, 8.0, [], [v], None, sem, inc)
+        ops[j][3].add((i, True))
+
+    return ops, op, rec, land, res
+
+
+def order(ops):
+    n = len(ops)
+    users = [[] for _ in range(n)]
+    left = [0] * n
+    for i in range(n):
+        for j, w in ops[i][3]:
+            users[j].append((i, w))
+            left[i] += 1
+    prio = [0.0] * n
+    for i in range(n - 1, -1, -1):
+        b = 0.0
+        for u, w in users[i]:
+            b = max(b, prio[u] + (ops[i][2] if w else 0.0))
+        prio[i] = b + ops[i][1]
+    prio = [p * (1 + SIG * noise(i, SEED)) for i, p in enumerate(prio)]
+    ready = [0.0] * n
+    avail = {}
+    free = {}
+    for i in range(n):
+        if left[i] == 0:
+            avail.setdefault(ops[i][0], []).append(i)
+    out = []
+    while len(out) < n:
+        best = None
+        for q in avail:
+            if not avail[q]:
+                continue
+            f = free.get(q, 0.0)
+            s0 = min(max(f, ready[i]) for i in avail[q])
+            i = max((i for i in avail[q] if max(f, ready[i]) <= s0 + WIN), key=lambda k: (prio[k], -k))
+            s = max(f, ready[i])
+            if best is None or s < best[0]:
+                best = (s, q, i)
+        s, q, i = best
+        avail[q].remove(i)
+        free[q] = s + ops[i][1] if q != "x" else 0.0
+        out.append(i)
+        for u, w in users[i]:
+            ready[u] = max(ready[u], s + (ops[i][1] + ops[i][2] if w else 0.0))
+            left[u] -= 1
+            if left[u] == 0:
+                avail.setdefault(ops[u][0], []).append(u)
+    return out
+
+
+def issue(g, T, ops, seq):
+    Q = {"v": g.vector, "s": g.scalar, "t": g.tensor, "g": g, "y": g.sync, "S": g.scalar}
+    total, tok, know = {}, {}, {}
+    for q in Q:
+        know[q] = {}
+    know["S"] = know["s"]
+    for i in seq:
+        q, c, tail, deps, emit, sem, inc = ops[i]
+        if emit is None:
+            total[sem] = total.get(sem, 0) + inc
+            tok[i] = (sem, total[sem], {})
+            continue
+        k = know[q]
+        need = {}
+        for j, w in deps:
+            if w:
+                s, v, sn = tok[j]
+                if k.get(s, 0) < v and (s not in need or need[s][0] < v):
+                    need[s] = (v, sn)
+        for s in sorted(need):
+            v, sn = need[s]
+            if [o for o in need if o != s and need[o][1].get(s, 0) >= v]:
+                continue
+            Q[q].wait_ge(T.sem[s], v)
+        for s in need:
+            v, sn = need[s]
+            k[s] = max(k.get(s, 0), v)
+            for o in sn:
+                k[o] = max(k.get(o, 0), sn[o])
+        total[sem] = total.get(sem, 0) + inc
+        r = emit(Q[q])
+        if r is not None:
+            r.then_inc(T.sem[sem], inc)
+        tok[i] = (sem, total[sem], dict(k))
+    for s in sorted(total):
+        if know["g"].get(s, 0) < total[s]:
+            g.wait_ge(T.sem[s], total[s])
+
+
+def rank_program(g, core, T, topo):
+    rank = T.rank_of(core)
+    n = len(T.cores)
+    if rank is None:
+        hand_on(g, core, T, topo)
+        return
+    ops, op, rec, land, res = noter(T)
+    below, above = T.cores[(rank - 1) % n], T.cores[(rank + 1) % n]
+    rl = relays(core, T, topo, below)
+    rv_relay = relays(core, T, topo, above)[0]
+    v = view
+
+    def tt(out, a, b, o):
+        return op("v", "tensor_tensor", out=out, in0=a, in1=b, op=o)
+
+    def ts(out, a, s1, o1, s2=None, o2=None):
+        if o2 is None:
+            return op("v", "tensor_scalar", out=out, in0=a, scalar1=s1, scalar2=None, op0=o1)
+        return op("v", "tensor_scalar", out=out, in0=a, scalar1=s1, scalar2=s2, op0=o1, op1=o2)
+
+    def cp(out, a):
+        return op("v", "tensor_copy", out=out, in_=a)
+
+    def act(out, a, f=AF.Copy, **kw):
+        return op("s", "activation", out=out, in_=a, func=f, **kw)
+
+    def mm(out, l, r, start=True, stop=True):
+        return op("t", "matmul", out=out, lhsT=l, rhs=r, start=start, stop=stop)
+
+    def iota(out, pattern, base, cm):
+        kw = dict(out=out, pattern=pattern, base=base, channel_multiplier=cm)
+        if WHERE[out[1]][0] != "SI":
+            kw["allow_small_or_imprecise_dtypes"] = True
+        return op("g", "iota", **kw)
+
+    def scan(out, a, b, o1):
+        return op("v", "tensor_tensor_scan", out=out, data0=a, data1=b, initial=0.0, op0=A.add, op1=o1)
+
+    def load(q, dst, src, k):
+        return rec(q, 0.1, 4.0, [], [dst], lambda e: e.dma_start(res(dst), src), "ld%d" % k, 16)
+
+    def store(dst, srcv, k):
+        return rec("y", 0.1, 2.0, [srcv], [], lambda e: e.dma_start(dst, res(srcv)), "st%d" % k, 16)
+
+    def hv(name, c, w=128):
+        return v(name, w * c, w * c + w)
+
+    def turn(c):
+        if [q for q in PEQ if q // 2 == c]:
+            mm(v("b7", 0, 128), hv("z", c), v("Ib"))
+            act(hv("zT", c), v("b7", 0, 128), scale=-1.0)
+
+    load("y", v("NBi", 0, 640), T.nbr[:, 0:640], 0)
+    load("S", v("z"), T.z0[:], 1)
+    load("S", v("NBi", 640, 1280), T.nbr[:, 640:1280], 2)
+    load("y", v("KK0", 0, 1280), T.ring[:], 3)
+    load("S", v("thI", 0, 1), T.thr[:], 4)
+    load("y", v("X"), T.mat[:], 5)
+
+    iota(v("PI"), [[1, 1]], 0, 1)
+    iota(v("D2"), [[-16, 8], [0, 16]], 128, 1)
+    iota(v("D1"), [[-1, 256]], 256, 1)
+    iota(v("iv"), [[80, 16]], 0, 0)
+    iota(v("D3"), [[0, 16], [1, 16]], 0, 0)
+    iota(v("ic"), [[1, 16]], 0, 0)
+    iota(v("V2"), [[10, 256]], 1, 0)
+    iota(v("LPh"), [[0, 128]], 0, 16)
+    iota(v("LPl"), [[0, 8], [1, 16]], 0, 0)
+    iota(v("UC"), [[-256, 256]], 65536, 0)
+    iota(v("t1"), [[128, 2], [0, 8]], 1280, 1)
+    iota(v("w2"), [[512, 2], [0, 8]], -1280, 4)
+    iota(v("T1"), [[1, 1280]], 0, 0)
+    ts(v("pi15"), v("PI"), 15, A.bitwise_and)
+    cp(v("pcol"), v("pi15"))
+    ts(v("p5"), v("pcol"), 5.0, A.mult)
+    ts(v("vO", 0, 16), v("iv"), v("p5"), A.add)
+    ts(v("pm0"), v("pcol"), -1.0, A.mult, 16.0, A.add)
+    ts(v("D2"), v("D2"), 4, A.arith_shift_right)
+    ts(v("G16f"), v("D2"), 8.0, A.is_equal)
+    ts(v("G16b"), v("D2"), 8.0, A.is_equal)
+    cp(v("G8f"), v("G16f", 0, 128, 16))
+    cp(v("G8b"), v("G16f", 0, 128, 16))
+    ts(v("G8s"), v("G16f", 0, 128, 16), float(WS), A.mult)
+    ts(v("G8k"), v("G16f", 0, 128, 16), 4096.0, A.mult)
+    ts(v("D15"), v("D1"), 15, A.bitwise_and)
+    ts(v("DM"), v("D15"), 0.0, A.is_equal)
+    ts(v("RN"), v("D3"), 0.0, A.is_equal, -BIG, A.mult)
+    ts(v("RP"), v("RN", 0, 128), -1.0, A.mult)
+    ts(v("If"), v("D1", 0, 128), 256.0, A.is_equal)
+    ts(v("Ib"), v("D1", 0, 128), 256.0, A.is_equal)
+    ts(v("kcol"), v("pcol"), -float(SB), A.mult, -35.0 * SB, A.add)
+    cp(v("bl"), v("ic"))
+    ts(v("bl2"), v("ic"), 16.0, A.mult, 15.0, A.add)
+    for t in range(RO):
+        ts(v("pl%d" % t), v("pcol"), 811.0, A.mult, t - 0.375, A.add)
+        if t:
+            ts(v("pm%d" % t), v("pcol"), -1.0, A.mult, 16.0 + t, A.add)
+    ts(v("TriO"), v("D1", 0, 128), 256.0, A.is_lt)
+    op("v", "memset", out=v("On"), constant=1.0)
+    op("v", "memset", out=v("fb"), constant=-15.0)
+    for i in range(2):
+        op("v", "memset", out=v("KK%d" % i, 1280, REM), constant=0.0)
+    if PEQ:
+        for k in range(16):
+            cp(v("RS", k, 2048, 16), v("Ib"))
+    ts(v("d04"), v("t1"), 8192.0, A.mult)
+    ts(v("vmd4"), v("w2"), 8192.0, A.mult)
+    ts(v("pb"), v("PI"), 4, A.arith_shift_right, 1, A.bitwise_and)
+    cp(v("odd"), v("pb"))
+    ts(v("even"), v("odd"), -1.0, A.mult, 1.0, A.add)
+    for i in range(4):
+        ts(v("pb"), v("PI"), i, A.arith_shift_right, 1, A.bitwise_and)
+        f = 2.0 ** -(2 ** i) - 1.0
+        if i == 0:
+            ts(v("p2"), v("pb"), f, A.mult, 1.0, A.add)
+        else:
+            ts(v("p2b"), v("pb"), f, A.mult, 1.0, A.add)
+            ts(v("p2"), v("p2"), v("p2b"), A.mult)
+    ts(v("dcol"), v("p2"), 0.5, A.mult, -0.5, A.add)
+    cp(v("thr"), v("thI", 0, 1))
+    ts(v("thrc"), v("thr"), float(2 ** 30), A.mult)
+    cp(v("B", 0, 640), v("NBi", 0, 640))
+    cp(v("B", 640, 1280), v("NBi", 640, 1280))
+    for c in range(2):
+        cp(v("b1", 128 * c, 128 * c + 128), hv("z", c))
+        turn(c)
+
+    def send_rings(t):
+        kk = "KK%d" % (t % 2)
+        for h in range(2):
+            src = v(kk, 512 * h, 512 * h + 512)
+
+            def emit(e, h=h, src=src):
+                remote(g, topo, core, rl[h], T["hand%d" % t][:], res(src), T.sem["ha%d" % t], T.sem["ks%d%d" % (t, h)], 8)
+            i = rec("g", 0.3, 4.0, [src], [], emit, "ks%d%d" % (t, h), 8)
+            lo = REM + 1024 * t + 512 * h
+            land(v(kk, lo, lo + 512), "ki%d%d" % (t, h), 8, i)
+
+    def send_revoked(t):
+        src = v("rS%d" % t, 0, 1)
+
+        def emit(e):
+            remote(g, topo, core, rv_relay, T["hrv%d" % t][:, 0:1], res(src), T.sem["ra%d" % t], T.sem["rs%d" % t], 8)
+        i = rec("g", 0.3, 4.0, [src], [], emit, "rs%d" % t, 8)
+        land(v("cI%d" % t, 0, 1), "ri%d" % t, 8, i)
+
+    def K(t):
+        return v("KK%d" % (t % 2), 0, 1280)
+
+    def vo(t, c):
+        b = 16 * (t % 2)
+        return v("vO", b + 8 * c, b + 8 * c + 8)
+
+    def first(t, c):
+        tab = v("B", 0, 1280) if t else v("NBi")
+        bv = hv("Bv", c) if t else v("NBi", 640 * c, 640 * c + 640, 5)
+        if t:
+            act(bv, ind(tab, vo(t, c)))
+        mm(v("b6", 0, 128), v("G16b"), hv("z", c))
+        ts(hv("y1", c), v("b6", 0, 128), v("pm%d" % t), A.add)
+        ts(hv("y2", c), hv("y1", c), 15, A.bitwise_and)
+        oh = v("b1", 256 + 128 * c, 384 + 128 * c)
+        ts(oh, hv("y2", c), 0.0, A.is_equal)
+        tt(hv("mB", c), oh, bv, A.mult)
+        nr = v("b6", 128 + 128 * c, 256 + 128 * c)
+        mm(nr, v("G16f"), hv("mB", c))
+        mm(v("b6", 384 + 8 * c, 392 + 8 * c), hv("mB", c), v("G8f"))
+        tt(hv("dg", c), nr, hv("DM", c), A.mult)
+        scan(hv("sc", c), hv("RN", c), hv("dg", c), A.max)
+        cp(v("nO", 16 * c, 16 * c + 8), v("sc", 128 * c + 15, 128 * c + 128, 16))
+        cp(hv("BnL", c), ind(tab, v("nO", 16 * c, 16 * c + 8)))
+        ts(hv("BnC", c), hv("BnL", c), v("kcol"), A.add)
+        if t < RO - 1:
+            tt(hv("Bk", c), bv, hv("mB", c), A.subtract)
+
+    def second(t, c):
+        kv, kn = v("b0", 128 * c, 128 * c + 128), v("b0", 256 + 128 * c, 384 + 128 * c)
+        old = K(max(t - 1, 0))
+        act(hv("Kv", c), ind(old, vo(t, c)))
+        act(hv("Kn", c), ind(old, v("nO", 16 * c, 16 * c + 8)))
+        for raw, dst in (("Kv", kv), ("Kn", kn)):
+            if raw == "Kv":
+                ts(dst, hv(raw, c), 0.0, A.is_equal, -1.0, A.mult)
+                tt(dst, dst, hv(raw, c), A.add)
+            else:
+                ts(dst, hv(raw, c), 0.25, A.max)
+            for i, col in ((0, "cI%d" % (t - 2)), (1, "rS%d" % (t - 1))):
+                if t - 2 + i >= 0:
+                    ts(hv("m%d" % i, c), hv(raw, c), v(col, 0, 1), A.is_equal, -1024.0, A.mult)
+                    tt(dst, dst, hv("m%d" % i, c), A.add)
+        tt(hv("evn", c), kv, hv("Kn", c), A.is_equal)
+        mm(v("b6", 400 + 8 * c, 408 + 8 * c), hv("evn", c), v("G8b"))
+        ts(hv("dr", c, 8), v("b6", 400 + 8 * c, 408 + 8 * c), 3.0, A.is_ge, float(DIR), A.mult)
+        tt(hv("kn", c, 8), v("b6", 384 + 8 * c, 392 + 8 * c), hv("dr", c, 8), A.add)
+        for b in range(128 * c, 128 * c + 128, 32):
+            act(v("Kc", 16 * b, 16 * b + 512), ind(old, v("BnL", b, b + 32)))
+        for q in (2 * c, 2 * c + 1):
+            for eq, b in (("eqV", 0), ("eqN", 256)):
+                for k in range(16):
+                    s = (1024 * q + k, 1024 * q + 1024, 16)
+                    tt(v(eq, *s), v("b0", b + 64 * q, b + 64 * q + 64), v("Kc", *s), A.is_equal)
+
+    def third(t, c):
+        for eq, b in (("eqV", "b2"), ("eqN", "b3")):
+            mm(v(b, 128 * c, 128 * c + 128), hv("BnC", c), v("If"), True, False)
+            for k in range(16):
+                mm(v(b, 128 * c + k, 128 * c + 128, 16), v(eq, 2048 * c + k, 2048 * c + 2048, 16), v("G8s"), False, k == 15)
+        act(hv("cV", c), v("b2", 128 * c, 128 * c + 128))
+        tt(hv("mn", c), v("b3", 128 * c, 128 * c + 128), hv("cV", c), A.min)
+        scan(hv("sc2", c), v("RN", 0, 128), hv("mn", c), A.max)
+        tt(hv("W", c, 8), v("sc2", 128 * c + 15, 128 * c + 128, 16), hv("kn", c, 8), A.max)
+        cp(hv("Wi", c, 8), hv("W", c, 8))
+        ts(hv("wT", c, 8), hv("Wi", c, 8), SB - 1, A.bitwise_and)
+        tt(hv("Aw", c), ind(hv("wT", c, 8), v("bl", 0, 8)), v("DM", 0, 128), A.mult)
+        o = v("b6", 416 + 8 * c, 424 + 8 * c)
+        mm(o, hv("Aw", c), v("G8f"))
+        w = vo(t + 1, c)
+        cp(w, o)
+        tt(hv("kp", c), ind(K(t), w), hv("V2", c), A.mult)
+        ts(hv("pl", c), hv("kp", c), 0.25, A.mult, v("pl%d" % t), A.add)
+        ts(hv("plm", c), hv("pl", c), 2047, A.bitwise_and)
+        cp(hv("PL", c), hv("plm", c))
+        for q in (2 * c, 2 * c + 1):
+            for b in (64 * q, 64 * q + 32):
+                act(v("Xc", 16 * b, 16 * b + 512), ind(v("X"), v("PL", b, b + 32)))
+            if q in PEQ:
+                for b in range(1024 * q, 1024 * q + 1024, 512):
+                    mm(v("b7"), v("Ib"), v("Xc", b, b + 512), True, False)
+                    mm(v("b7"), hv("zT", c), v("RS", b - 2048 * c, b - 2048 * c + 512), False, True)
+                    act(v("ab", b, b + 512), v("b7"), AF.Abs)
+                continue
+            for k in range(16):
+                s = (1024 * q + k, 1024 * q + 1024, 16)
+                tt(v("df", *s), v("b1", 64 * q, 64 * q + 64), v("Xc", *s), A.subtract)
+            act(v("ab", 1024 * q, 1024 * q + 1024), v("df", 1024 * q, 1024 * q + 1024), AF.Abs)
+        act(hv("Kw", c), ind(K(t), w))
+        ts(hv("hz", c), hv("Kw", c), 0.0, A.is_equal, float(2 ** 25), A.mult)
+        if t < RO - 1:
+            act(hv("Vn", c), ind(v("T1"), w))
+            act(hv("V2", c), hv("Vn", c), scale=2.0, bias=1.0)
+        tt(hv("pr", c), v("b1", 128 * c, 128 * c + 128), hv("Kw", c), A.mult)
+        mm(v("b6", 448 + 8 * c, 456 + 8 * c), hv("pr", c), v("G8f"))
+        pa = v("b5", 256 + 128 * c, 384 + 128 * c)
+        mm(pa, v("Ib"), hv("Kw", c), True, False)
+        mm(pa, v("Ib"), hv("UC", c), False, True)
+
+    def fourth(t, c):
+        dT = v("b4", 128 * c, 128 * c + 128)
+        mm(dT, v("Ib"), v("LPh"), True, False)
+        mm(dT, v("Ib"), v("LPl"), False, False)
+        for p in range(16):
+            mm(v("b4", 128 * c + p, 128 * c + 128, 16), v("ab", 2048 * c + p, 2048 * c + 2048, 16), v("G8k"), False, p == 15)
+        act(hv("dk", c), dT)
+        scan(hv("sd", c), v("RP"), dT, A.min)
+        mm(v("b5", 128 * c, 128 * c + 128), v("Ib"), hv("hz", c), True, False)
+        mm(v("b5", 128 * c, 128 * c + 128), hv("dk", c), v("If"), False, True)
+        tt(hv("Ap", c), ind(hv("sd", c), v("bl2", 0, 8)), v("DM", 0, 128), A.mult)
+        o = v("b6", 432 + 8 * c, 440 + 8 * c)
+        mm(o, hv("Ap", c), v("G8f"))
+        cp(hv("pi", c, 8), o)
+        ts(hv("pi2", c, 8), hv("pi", c, 8), 2047, A.bitwise_and)
+        do = v("dO", 16 * c, 16 * c + 8)
+        cp(do, hv("pi2", c, 8))
+        tt(hv("zx", c), ind(v("Xc", 2048 * c, 2048 * c + 2048), do), hv("z", c), A.add)
+        ts(hv("dz", c), hv("zx", c), 0.5, A.mult, -0.25, A.add)
+        zp = v("b1", 128 * c, 128 * c + 128)
+        if t == RO - 1:
+            cp(hv("zF", c), hv("dz", c))
+            store(T.yz[:, 128 * c:128 * c + 128], hv("zF", c), c)
+        else:
+            cp(hv("z", c), hv("dz", c))
+            cp(zp, hv("z", c))
+            turn(c)
+        act(hv("cd", c), v("b5", 128 * c, 128 * c + 128), AF.Relu, scale=-float(2 ** 18), bias=v("thrc"))
+        tt(hv("rr", c), v("b5", 256 + 128 * c, 384 + 128 * c), hv("cd", c), A.min)
+
+    def writers(t):
+        ts(v("F"), v("W"), float(SB), A.is_lt)
+        ts(v("NF"), v("W"), float(SB), A.is_ge, -512.0, A.mult)
+        ts(v("Lb"), v("W"), float(DIR), A.is_lt)
+        mm(v("b2", 400, 408), v("TriO"), v("F", 0, 8), True, False)
+        mm(v("b2", 400, 408), v("Ib"), v("NF", 0, 8), False, True)
+        mm(v("b2", 408, 416), v("TriO"), v("F", 8, 16), True, False)
+        mm(v("b2", 408, 416), v("Ib"), v("NF", 8, 16), False, False)
+        mm(v("b2", 408, 416), v("On"), v("F", 0, 8), False, True)
+        ts(v("x96"), v("b2", 400, 416), float(CAP), A.is_lt)
+        tt(v("act"), v("x96"), v("Lb"), A.mult)
+        tt(v("av"), v("act"), v("vmd4"), A.mult)
+        cp(v("hi"), v("b6", 448, 464))
+        ts(v("h2"), v("hi"), 1023, A.bitwise_and)
+        ts(v("hb"), v("h2"), float(REM + 1024 * t), A.add)
+        tt(v("hc"), v("hb"), v("F"), A.mult)
+        tt(v("src"), v("hc"), v("wT"), A.max)
+        tt(v("hd"), v("src"), v("d04"), A.add)
+        w2 = v("av")
+        if t:
+            for gr in range(8):
+                e, f = 256 * gr, 128 * gr
+                mm(v("b2", 416 + gr, 417 + gr), v("EA", e, e + 128), v("act", gr, gr + 1))
+                mm(v("b2", 424 + gr, 425 + gr), v("EA", e + 128, e + 256), v("act", gr, gr + 1), True, False)
+                mm(v("b2", 424 + gr, 425 + gr), v("EB", f, f + 128), v("act", 8 + gr, 9 + gr), False, True)
+            ts(v("wr"), v("b2", 416, 432), 0.0, A.is_equal)
+            tt(v("w2"), v("wr"), v("av"), A.mult)
+            w2 = v("w2")
+        tt(v("word"), w2, v("hd"), A.add)
+        tt(v("Aq"), ind(v("word"), v("bl")), v("DM"), A.mult)
+        for c in range(2):
+            mm(v("b2", 448 + 8 * c, 456 + 8 * c), hv("Aq", c), v("G8f"))
+        cp(v("qi"), v("b2", 448, 464))
+        ts(v("q1"), v("qi"), 13, A.arith_shift_right)
+        cp(v("scO"), v("q1"))
+        ts(v("q2"), v("qi"), 8191, A.bitwise_and)
+        cp(v("srO"), v("q2"))
+        act(v("sgn"), v("b0", 0, 256), AF.Sign)
+        act(v("hole"), v("sgn"), AF.Relu, scale=-1.0)
+        act(v("Kvr"), v("b0", 0, 256), AF.Relu)
+        kk = "KK%d" % (t % 2)
+        tt(v("fm"), ind(v(kk, 0, REM + 1024 * (t + 1)), v("srO")), v("hole"), A.mult)
+        tt(ind(v(kk, 0, REM), v("scO")), v("fm"), v("Kvr"), A.add)
+        if t < RO - 1:
+            tt(v("ohw"), v("b1", 256, 512), v("Vn"), A.mult)
+            tt(ind(v("B"), v("scO")), v("Bk"), v("ohw"), A.add)
+            mm(v("b2", 432, 448), v("On"), v("F"))
+            act(v("fj"), v("b2", 432, 448), accum_out=v("fs"))
+            cp(v("fi"), v("fs"))
+            ts(v("fa"), v("fi"), 15, A.bitwise_and)
+            ts(v("t1"), v("wT"), 8192.0, A.mult)
+            tt(v("vmd4"), v("t1"), v("d04"), A.subtract)
+
+    def same_node():
+        ts(v("ci"), v("Vn"), v("p2"), A.mult, v("dcol"), A.add)
+        ts(v("cb"), v("ci"), 1, A.bitwise_and)
+        ts(v("code"), v("cb"), -2.0, A.mult, 1.0, A.add)
+        act(v("cdE"), v("code"), scale=v("even"))
+        act(v("cdO"), v("code"), scale=v("odd"))
+        for gr in range(8):
+            lo = 32 * (gr // 2)
+            m = "cdO" if gr % 2 else "cdE"
+            b = "b3" if gr % 2 else "b7"
+            mm(v(b, 0, 256), v(m, 0, 128, 1, lo, lo + 32), v("code", 0, 256, 1, lo, lo + 32))
+            mm(v(b, 256, 384), v(m, 128, 256, 1, lo, lo + 32), v("code", 128, 256, 1, lo, lo + 32))
+            act(v("E0", 256 * gr, 256 * gr + 256), v(b, 0, 256), AF.Relu, bias=v("fb"))
+            act(v("E1", 128 * gr, 128 * gr + 128), v(b, 256, 384), AF.Relu, bias=v("fb"))
+        for e, o, w in (("E0", "EA", 256), ("E1", "EB", 128)):
+            op("g", "affine_select", out=v(o), in_=v(e), pattern=[[0, 8], [1, w]], compare_op=A.is_gt, fill=0.0, base=0,
+               channel_multiplier=-1)
+
+    def revoke(t):
+        if t:
+            come = v("cI%d" % (t - 1), 0, 1)
+            ts(v("ncome"), come, -1.0, A.mult)
+            ts(v("NM2"), K(t), come, A.is_equal, v("ncome"), A.mult)
+        op("v", "tensor_reduce", out=v("rvi"), in_=v("rr"), axis=AxisListType.X, op=A.max)
+        ts(v("rva"), v("rvi"), 255, A.bitwise_and)
+        rv = v("rS%d" % t, 0, 1)
+        cp(rv, v("rva"))
+        if t:
+            ts(v("rvE%d" % t), rv, v("cI%d" % (t - 1), 0, 1), A.not_equal, rv, A.mult)
+            rv = v("rvE%d" % t)
+        ts(v("nrv"), rv, -1.0, A.mult)
+        kk = "KK%d" % (t % 2)
+        blocks = ((0, 512, "b4"), (512, 1024, "b7"), (1024, 1280, "b4"))
+        for lo, hi, b in blocks:
+            ts(v("NM1", lo, hi), v(kk, lo, hi), rv, A.is_equal, v("nrv"), A.mult)
+        for lo, hi, b in blocks:
+            o = v(b, 0, hi - lo)
+            mm(o, v("Ib"), v(kk, lo, hi), True, False)
+            if t:
+                mm(o, v("Ib"), v("NM2", lo, hi), False, False)
+            mm(o, v("Ib"), v("NM1", lo, hi), False, True)
+            if t == RO - 1:
+                act(v("Yk", lo, hi), o)
+                store(T.yk[:, lo:hi], v("Yk", lo, hi), 2 + lo // 512)
+            else:
+                act(v("KK%d" % ((t + 1) % 2), lo, hi), o)
+        if t < RO - 1:
+            send_revoked(t)
+            send_rings(t + 1)
+            ts(v("thrc"), v("fa"), v("thr"), A.add, float(2 ** 30), A.mult)
+
+    send_rings(0)
+    for c in range(2):
+        first(0, c)
+    for t in range(RO):
+        for c in range(2):
+            second(t, c)
+        for c in range(2):
+            third(t, c)
+        writers(t)
+        fourth(t, 0)
+        if t < RO - 1:
+            first(t + 1, 0)
+        fourth(t, 1)
+        revoke(t)
+        if t < RO - 1:
+            first(t + 1, 1)
+            same_node()
+    if not SEQ:
+        SEQ.append(order(ops))
+    issue(g, T, ops, SEQ[0])
+
+
+def hand_on(g, core, T, topo):
+    n = len(T.cores)
+    for r in range(n):
+        src, below, above = T.cores[r], T.cores[(r - 1) % n], T.cores[(r + 1) % n]
+        rl = relays(src, T, topo, below)
+        rv_relay = relays(src, T, topo, above)[0]
+        if core not in rl and core != rv_relay:
+            continue
+        for t in range(RO):
+            if t and core == rv_relay:
+                g.wait_ge(T.sem["ra%d" % (t - 1)], 8)
+                remote(g, topo, core, above, T["cI%d" % (t - 1)][:, 0:1], T["hrv%d" % (t - 1)][:, 0:1],
+                       T.sem["ri%d" % (t - 1)], T.sem["rl%d" % (t - 1)], 8)
+            if core in rl:
+                h = rl.index(core)
+                g.wait_ge(T.sem["ha%d" % t], 8)
+                lo = REM + 1024 * t + 512 * h
+                remote(g, topo, core, below, T["KK%d" % (t % 2)][:, lo:lo + 512], T["hand%d" % t][:],
+                       T.sem["ki%d%d" % (t, h)], T.sem["hs%d" % t], 8)
+        for t in range(RO):
+            if core in rl:
+                g.wait_ge(T.sem["hs%d" % t], 8)
+            if t and core == rv_relay:
+                g.wait_ge(T.sem["rl%d" % (t - 1)], 8)

@@ -6,23 +6,27 @@ A = AluOpType
 AF = ActivationFunctionType
 RO, SB, CAP = 3, 2048, 96
 BIG = 1.0e9
-PEQ = (0, 2)
+R16, R1 = 1.5 * 2 ** 27, 1.5 * 2 ** 23
+HALF = 0.5 - 2.0 ** -11
+PS = [[2, 2], [2, 2], [2, 2]]
+GW = 64
+OPT = dict(za="v", hz="v", cd="s", wr="b5")
 REM = 1536
 WS = 17 * SB
-DIR = 239 * SB
+FAIL, DIR = 51 * SB, 290 * SB
 
-F32 = dict(If=128, G16f=128, G8f=8, DM=256, RN=256, RP=128, T1=1280, B=1536, Bv=256, mB=256, Bk=256, dg=256, sc=256, BnC=256,
-           dr=16, kn=16, cV=256, mn=256, sc2=256, W=16, Aw=256, kp=256, Vn=256, V2=256, pr=256, zx=256, sd=256,
-           Ap=256, dk=256, cd=256, rr=256, ohw=256, zF=256, pcol=1, p2=1, p2b=1, dcol=1, odd=1, even=1, kcol=1, thr=1, thrc=1,
-           nrv=1, rvE1=1, rvE2=1, ncome=1, fs=1, fj=16, d04=16, vmd4=16, x96=16, av=16, hd=16,
-           wr=16, hb=16, hc=16, src=16, w2=16, word=16, t1=16, Aq=256, pm0=1, pm1=1, pm2=1, pl0=1, pl1=1, pl2=1,
-           p5=1, fb=1)
-BF = dict(Ib=128, G16b=128, G8b=8, G8s=8, G8k=8, TriO=128, On=128, LPh=128, LPl=128, UC=256, z=256, Kv=256, Kn=256,
-          Kw=256, evn=256, m0=256, m1=256, Kvr=256, zT=256, hz=256, sgn=256, hole=256, fm=256, code=256, cdE=256, cdO=256, F=16, NF=16, Lb=16,
-          act=16, NM1=1280, NM2=1280)
-I32 = dict(PI=1, pi15=1, pb=1, D1=256, D15=256, D2=128, D3=256, ic=16, iv=16, y1=256, y2=256, pl=256, plm=256,
-           pi=16, pi2=16, dz=256, Wi=16, wT=16, hi=16, h2=16, qi=16, q1=16, q2=16, rvi=1, rva=1, fi=1, fa=1, ci=256, cb=256)
-U16 = dict(bl=16, bl2=16, vO=32, nO=32, wO=32, scO=16, srO=16, dO=32, BnL=256, PL=256)
+F32 = dict(G8f=8, RN=128, RS=128, RD=128, TH=128, T1=1280, r16=256, sc=256, dr=16, kn=16, cV=256, mn=256, sc2=256, Vn=256, V2=128,
+           pr=256, zx=256, za=256, sd=256, cs=256, dl=256, ohd=256, zF=256, row=128, rw=128, pcol=1, p2=1, dcol=1, odd=1, even=1,
+           neven=1, nodd=1, c0=1, wcol=1, w25=1, nrv=1, rvE=1, ncome=1, fs=1, fj=16, d04=16, d00=1, d01=1, vmd=16, av=16, hd=16,
+           wf=16, hb=16, hc=16, src=16, w2=16, word=16, t1=16, Aq=256, p5=1, fb=1, nR1=1, pR1=1, nfb=1, rb=1, lcol=1, h18=1)
+BF = dict(Ib=128, nIb=128, G16b=128, G8b=8, G8s=8, G8m=8, G8x=8, G8a=8, cK=8, Tri=128, On=128, DM=256, DMB=128, C0=128, C1=128,
+          C2=128, NG0=128, NG2=128, NG4=128, Q=16, LR=256, C256=128, z=256, KN=512, Kw=256, evn=256, mh=512, m0=512, m1=512,
+          Kvr=256, hz=256, hole=256, fm=256, code=256, cdE=256, cdO=256, oh=256, nf=256, F=16, D=16, act=16, aw=16, aB=16,
+          NM1=1280, NM2=1280)
+H16 = dict(mB=256, BnH=256, Aw=256, Ap=256, Aqh=256)
+I32 = dict(PI=1, pi15=1, pb=1, pc=1, D1=256, D15=256, D2=128, D3=128, ic=16, iv=16, kp=256, k2=256, pi=16, pi2=16, Wi=16, wT=16,
+           hi=16, h2=16, qi=16, q1=16, q2=16, rvi=1, rva=1, fi=1, fa=1, ci=256, cb=256, nb=256, th=1, tl=1)
+U16 = dict(bl=16, vO=32, nO=32, scO=16, srO=16, dO=32, BnL=256, PL=256)
 
 
 def _layout(d):
@@ -33,21 +37,17 @@ def _layout(d):
     return pos, at
 
 
-_PF, _NF = _layout(F32)
-_PB, _NB = _layout(BF)
-_PI, _NI = _layout(I32)
-_PU, _NU = _layout(U16)
-WHERE = {}
-for _d, _p, _n in ((F32, _PF, "SF"), (BF, _PB, "SBF"), (I32, _PI, "SI"), (U16, _PU, "SU")):
+WHERE, SCRATCH = {}, {}
+for _d, _n, _t in ((F32, "SF", "float32"), (BF, "SBF", "bfloat16"), (H16, "SH", "float16"), (I32, "SI", "int32"),
+                   (U16, "SU", "uint16")):
+    _p, _w = _layout(_d)
+    SCRATCH[_n] = ("sbuf", [128, _w], _t)
     for _k in _d:
         WHERE[_k] = (_n, _p[_k], _d[_k])
-_BIGB = dict(KK0=(REM + 1024 * RO, "bfloat16"), KK1=(REM + 1024 * RO, "bfloat16"), RS=(2048, "bfloat16"), X=(2048, "bfloat16"),
-             Kc=(4096, "bfloat16"), eqV=(4096, "bfloat16"), eqN=(4096, "bfloat16"), Xc=(4096, "bfloat16"), df=(4096, "bfloat16"),
-             ab=(4096, "bfloat16"), EA=(2048, "bfloat16"), EB=(1024, "bfloat16"), E0=(2048, "bfloat16"), E1=(1024, "bfloat16"),
-             NBi=(1280, "int32"), Yk=(1280, "bfloat16"), thI=(8, "int32"), rS0=(8, "float32"), rS1=(8, "float32"),
-             rS2=(8, "float32"), cI0=(8, "float32"), cI1=(8, "float32"))
-SCRATCH = {"SF": ("sbuf", [128, _NF], "float32"), "SBF": ("sbuf", [128, _NB], "bfloat16"), "SI": ("sbuf", [128, _NI], "int32"),
-           "SU": ("sbuf", [128, _NU], "uint16")}
+_BIGB = dict(KK0=(REM + 1024 * RO, "bfloat16"), KK1=(REM + 1024 * RO, "bfloat16"), X=(4096, "bfloat16"),
+             Kc=(4096, "bfloat16"), eqV=(4096, "bfloat16"), eqN=(4096, "bfloat16"), Xc=(4096, "bfloat16"), mx=(4096, "bfloat16"),
+             ab=(2048, "bfloat16"), E=(3072, "bfloat16"), NBi=(REM, "int32"), Yk=(1280, "bfloat16"), thI=(8, "int32"),
+             rS0=(8, "float32"), rS1=(8, "float32"), rS2=(8, "float32"), cI0=(8, "float32"), cI1=(8, "float32"))
 for _k in _BIGB:
     SCRATCH[_k] = ("sbuf", [128, _BIGB[_k][0]], _BIGB[_k][1])
     WHERE[_k] = (_k, 0, _BIGB[_k][0])
@@ -59,7 +59,7 @@ for _k in range(RO):
 for _k in range(RO - 1):
     SCRATCH["hrv%d" % _k] = ("sbuf", [128, 8], "float32")
 SEMAPHORES = ["qv", "qs", "qt", "qg"]
-SEMAPHORES += ["ld%d" % i for i in range(8)] + ["st%d" % i for i in range(5)]
+SEMAPHORES += ["ld%d" % i for i in range(8)] + ["st%d" % i for i in range(6)] + ["ad%d" % i for i in range(4)]
 for _t in range(RO):
     SEMAPHORES += ["ks%d0" % _t, "ks%d1" % _t, "ki%d0" % _t, "ki%d1" % _t, "ha%d" % _t, "hs%d" % _t]
 for _t in range(RO - 1):
@@ -67,8 +67,7 @@ for _t in range(RO - 1):
 
 CY = 0.00083
 SEQ = []
-TAIL = 0.16
-SIG, SEED, WIN = 0.02, 1080, 0.0
+ORD = dict(tail=0.16, f=1.1, ga=1.56, sc=3.8, sig=0.02, seed=1, win=0.0)
 
 
 def noise(i, seed):
@@ -116,11 +115,11 @@ def count(x):
 
 
 def psum(x):
-    return x[0] == "@" and x[1][0] == "b" and len(x[1]) == 2 and x[1][1].isdigit()
+    return x[0] == "@" and SCRATCH[WHERE[x[1]][0]][0] == "psum"
 
 
 def two(x):
-    return x[0] == "@" and WHERE[x[1]][0] not in ("SF", "SI", "NBi", "thI") and not psum(x)
+    return x[0] == "@" and SCRATCH[WHERE[x[1]][0]][2] in ("bfloat16", "float16", "uint16")
 
 
 def clash(a, b):
@@ -137,26 +136,26 @@ def covers(a, b):
 
 def cost(q, m, kw):
     o = kw.get("out")
+    f = ORD["f"] * CY
     if q == "t":
         n, mm = count(kw["rhs"]), count(kw["lhsT"])
-        f = 4 if WHERE[kw["lhsT"][1]][0] == "SF" else 1
-        return max(min(64, mm), n) * f * CY
+        return max(min(64, mm), n) * (1 if two(kw["lhsT"]) else 4) * f
     if q == "g":
-        return 0.15 + 2 * count(o) * CY
+        return 0.15 + 2 * count(o) * f
     ins = [kw[k] for k in kw if k not in ("out", "accum_out") and is_view(kw[k])]
     full = [i for i in ins if count(i) > 1]
     n = max([count(o)] + [count(i) for i in full])
     if o[0] == "#":
-        return 0.05 + n * 3.8 * CY
+        return 0.05 + n * ORD["sc"] * CY
     for i in full:
         if i[0] == "#":
-            return 0.06 + n * 1.56 * CY
+            return 0.06 + n * ORD["ga"] * CY
     c = 1.0
-    if q == "v" and m == "tensor_tensor" and not psum(o) and not [i for i in full if psum(i)]:
+    if q == "v" and m == "tensor_tensor" and not [i for i in full if psum(i)]:
         c = 2.0
     if q == "v" and m in ("tensor_copy", "tensor_scalar", "memset") and two(o) and not [i for i in full if not two(i)]:
         c = 0.5
-    return max(64, n * c) * CY
+    return max(64, n * c) * f
 
 
 def noter(T):
@@ -235,23 +234,17 @@ def noter(T):
                 return e.matmul(**a)
             if m == "activation":
                 return e.activation(**a)
-            if m == "affine_select":
-                return e.affine_select(**a)
             return e.iota(**a)
-        i = rec(q, cost(q, m, kw), TAIL, reads, writes, emit)
+        i = rec(q, cost(q, m, kw), ORD["tail"], reads, writes, emit)
         if m == "matmul":
             b = kw["out"][1]
             if b in opened:
-                for j in (opened[b] if kw["start"] or kw["stop"] else opened[b][:1]):
-                    ops[i][3].add((j, False))
-            if kw["start"] or kw["stop"]:
-                opened[b] = [i]
-            else:
-                opened[b].append(i)
+                ops[i][3].add((opened[b], False))
+            opened[b] = i
         return i
 
-    def land(v, sem, inc, i):
-        j = rec("x", 0.0, 8.0, [], [v], None, sem, inc)
+    def land(v, sem, inc, i, late):
+        j = rec("x", 0.0, late, [], [v], None, sem, inc)
         ops[j][3].add((i, True))
 
     return ops, op, rec, land, res
@@ -271,7 +264,7 @@ def order(ops):
         for u, w in users[i]:
             b = max(b, prio[u] + (ops[i][2] if w else 0.0))
         prio[i] = b + ops[i][1]
-    prio = [p * (1 + SIG * noise(i, SEED)) for i, p in enumerate(prio)]
+    prio = [p * (1 + ORD["sig"] * noise(i, ORD["seed"])) for i, p in enumerate(prio)]
     ready = [0.0] * n
     avail = {}
     free = {}
@@ -286,7 +279,7 @@ def order(ops):
                 continue
             f = free.get(q, 0.0)
             s0 = min(max(f, ready[i]) for i in avail[q])
-            i = max((i for i in avail[q] if max(f, ready[i]) <= s0 + WIN), key=lambda k: (prio[k], -k))
+            i = max((i for i in avail[q] if max(f, ready[i]) <= s0 + ORD["win"]), key=lambda k: (prio[k], -k))
             s = max(f, ready[i])
             if best is None or s < best[0]:
                 best = (s, q, i)
@@ -364,11 +357,18 @@ def rank_program(g, core, T, topo):
     def cp(out, a):
         return op("v", "tensor_copy", out=out, in_=a)
 
+    def fill(out, x):
+        return op("v", "memset", out=out, constant=x)
+
     def act(out, a, f=AF.Copy, **kw):
         return op("s", "activation", out=out, in_=a, func=f, **kw)
 
     def mm(out, l, r, start=True, stop=True):
         return op("t", "matmul", out=out, lhsT=l, rhs=r, start=start, stop=stop)
+
+    def group(out, pairs):
+        for i, (l, r) in enumerate(pairs):
+            mm(out, l, r, i == 0, i == len(pairs) - 1)
 
     def iota(out, pattern, base, cm):
         kw = dict(out=out, pattern=pattern, base=base, channel_multiplier=cm)
@@ -376,97 +376,130 @@ def rank_program(g, core, T, topo):
             kw["allow_small_or_imprecise_dtypes"] = True
         return op("g", "iota", **kw)
 
-    def scan(out, a, b, o1):
-        return op("v", "tensor_tensor_scan", out=out, data0=a, data1=b, initial=0.0, op0=A.add, op1=o1)
+    def scan(out, a, b, o1, first=0.0, o0=A.add):
+        return op("v", "tensor_tensor_scan", out=out, data0=a, data1=b, initial=first, op0=o0, op1=o1)
 
     def load(q, dst, src, k):
-        return rec(q, 0.1, 4.0, [], [dst], lambda e: e.dma_start(res(dst), src), "ld%d" % k, 16)
+        return rec(q, 0.1, 3.5, [], [dst], lambda e: e.dma_start(res(dst), src), "ld%d" % k, 16)
 
     def store(dst, srcv, k):
         return rec("y", 0.1, 2.0, [srcv], [], lambda e: e.dma_start(dst, res(srcv)), "st%d" % k, 16)
 
+    def add_into(dst, src, k):
+        return rec("g", 1.0, 3.0, [src], [dst], lambda e: e.dma_start(res(dst), res(src), accum_op=A.add), "ad%d" % k, 16)
+
+    last = {}
+
+    def chain(name, i):
+        if name in last:
+            ops[i][3].add((last[name], False))
+        last[name] = i
+
     def hv(name, c, w=128):
         return v(name, w * c, w * c + w)
 
-    def turn(c):
-        if [q for q in PEQ if q // 2 == c]:
-            mm(v("b7", 0, 128), hv("z", c), v("Ib"))
-            act(hv("zT", c), v("b7", 0, 128), scale=-1.0)
+    def KV(c, k, w=128):
+        return v("b%d" % c, 128 * k, 128 * k + w)
+
+    def SC(c, k, w=128):
+        return v("b%d" % (2 + c), 128 * k, 128 * k + w)
+
+    def SM(c, k):
+        return v("b%d" % (2 + c), 384 + 8 * k, 392 + 8 * k)
+
+    def MI(c, k):
+        return v("b%d" % (4 + c), 128 * k, 128 * k + 128)
+
+    def WR(k, w=16):
+        return v(OPT["wr"], 384 + k, 384 + k + w)
 
     load("y", v("NBi", 0, 640), T.nbr[:, 0:640], 0)
     load("S", v("z"), T.z0[:], 1)
     load("S", v("NBi", 640, 1280), T.nbr[:, 640:1280], 2)
     load("y", v("KK0", 0, 1280), T.ring[:], 3)
     load("S", v("thI", 0, 1), T.thr[:], 4)
-    load("y", v("X"), T.mat[:], 5)
+    load("y", v("X", 0, 2048), T.mat[:], 5)
+    load("y", v("X", 2048, 4096), T.mat[:], 6)
 
     iota(v("PI"), [[1, 1]], 0, 1)
     iota(v("D2"), [[-16, 8], [0, 16]], 128, 1)
     iota(v("D1"), [[-1, 256]], 256, 1)
-    iota(v("iv"), [[80, 16]], 0, 0)
-    iota(v("D3"), [[0, 16], [1, 16]], 0, 0)
+    iota(v("D3"), [[0, 8], [1, 16]], 0, 0)
     iota(v("ic"), [[1, 16]], 0, 0)
-    iota(v("V2"), [[10, 256]], 1, 0)
-    iota(v("LPh"), [[0, 128]], 0, 16)
-    iota(v("LPl"), [[0, 8], [1, 16]], 0, 0)
-    iota(v("UC"), [[-256, 256]], 65536, 0)
     iota(v("t1"), [[128, 2], [0, 8]], 1280, 1)
-    iota(v("w2"), [[512, 2], [0, 8]], -1280, 4)
     iota(v("T1"), [[1, 1280]], 0, 0)
     ts(v("pi15"), v("PI"), 15, A.bitwise_and)
     cp(v("pcol"), v("pi15"))
-    ts(v("p5"), v("pcol"), 5.0, A.mult)
-    ts(v("vO", 0, 16), v("iv"), v("p5"), A.add)
-    ts(v("pm0"), v("pcol"), -1.0, A.mult, 16.0, A.add)
+    cp(v("lcol"), v("PI"))
+    fill(v("On"), 1.0)
+    for t in range(RO):
+        ts(v("C%d" % t), v("On"), float(t), A.mult, v("pcol"), A.subtract)
     ts(v("D2"), v("D2"), 4, A.arith_shift_right)
-    ts(v("G16f"), v("D2"), 8.0, A.is_equal)
     ts(v("G16b"), v("D2"), 8.0, A.is_equal)
-    cp(v("G8f"), v("G16f", 0, 128, 16))
-    cp(v("G8b"), v("G16f", 0, 128, 16))
-    ts(v("G8s"), v("G16f", 0, 128, 16), float(WS), A.mult)
-    ts(v("G8k"), v("G16f", 0, 128, 16), 4096.0, A.mult)
+    g8 = v("G16b", 0, 128, 16)
+    for name, x in (("G8f", 1), ("G8b", 1), ("G8s", WS), ("G8m", 2 * SB), ("G8x", -SB), ("G8a", SB)):
+        ts(v(name), g8, float(x), A.mult)
+    fill(v("cK"), (FAIL - SB) / 128.0)
     ts(v("D15"), v("D1"), 15, A.bitwise_and)
     ts(v("DM"), v("D15"), 0.0, A.is_equal)
+    ts(v("DMB"), v("DM", 0, 128), 4096.0, A.mult)
     ts(v("RN"), v("D3"), 0.0, A.is_equal, -BIG, A.mult)
-    ts(v("RP"), v("RN", 0, 128), -1.0, A.mult)
-    ts(v("If"), v("D1", 0, 128), 256.0, A.is_equal)
+    ts(v("RS"), v("RN"), float(SB), A.add)
     ts(v("Ib"), v("D1", 0, 128), 256.0, A.is_equal)
-    ts(v("kcol"), v("pcol"), -float(SB), A.mult, -35.0 * SB, A.add)
+    ts(v("nIb"), v("Ib"), -1.0, A.mult)
     cp(v("bl"), v("ic"))
-    ts(v("bl2"), v("ic"), 16.0, A.mult, 15.0, A.add)
-    for t in range(RO):
-        ts(v("pl%d" % t), v("pcol"), 811.0, A.mult, t - 0.375, A.add)
-        if t:
-            ts(v("pm%d" % t), v("pcol"), -1.0, A.mult, 16.0 + t, A.add)
-    ts(v("TriO"), v("D1", 0, 128), 256.0, A.is_lt)
-    op("v", "memset", out=v("On"), constant=1.0)
-    op("v", "memset", out=v("fb"), constant=-15.0)
+    ts(v("pb"), v("pcol"), 811.0, A.mult)
+    ts(v("pc"), v("pb"), SB - 1, A.bitwise_and)
+    cp(v("c0"), v("pc"))
+    ts(v("Tri"), v("D1", 0, 128), 256.0, A.is_lt)
+    ts(v("row"), v("Ib"), 512.0, A.mult)
+    tt(v("Tri"), v("Tri"), v("row"), A.add)
+    for name, x in (("fb", -15.0), ("nR1", -R1), ("pR1", R1), ("nfb", 2.0 ** 18), ("h18", -2.0 ** 18), ("C256", 256.0)):
+        fill(v(name), x)
     for i in range(2):
-        op("v", "memset", out=v("KK%d" % i, 1280, REM), constant=0.0)
-    if PEQ:
-        for k in range(16):
-            cp(v("RS", k, 2048, 16), v("Ib"))
+        fill(v("KK%d" % i, 1280, REM), 0.0)
+    fill(v("NBi", 1280, REM), 0)
     ts(v("d04"), v("t1"), 8192.0, A.mult)
-    ts(v("vmd4"), v("w2"), 8192.0, A.mult)
+    for c in range(2):
+        ts(v("d0%d" % c), v("lcol"), 1280.0 + 128 * c, A.add)
     ts(v("pb"), v("PI"), 4, A.arith_shift_right, 1, A.bitwise_and)
     cp(v("odd"), v("pb"))
     ts(v("even"), v("odd"), -1.0, A.mult, 1.0, A.add)
-    for i in range(4):
-        ts(v("pb"), v("PI"), i, A.arith_shift_right, 1, A.bitwise_and)
-        f = 2.0 ** -(2 ** i) - 1.0
-        if i == 0:
-            ts(v("p2"), v("pb"), f, A.mult, 1.0, A.add)
-        else:
-            ts(v("p2b"), v("pb"), f, A.mult, 1.0, A.add)
-            ts(v("p2"), v("p2"), v("p2b"), A.mult)
+    if OPT["cd"] == "v":
+        ts(v("neven"), v("even"), -2.0, A.mult)
+        ts(v("nodd"), v("odd"), -2.0, A.mult)
+    fill(v("rw"), 0.5)
+    scan(v("row"), v("rw"), v("On"), A.mult, 2.0 ** 64, A.mult)
+    tt(v("rw"), v("row"), v("Ib"), A.mult)
+    op("v", "tensor_reduce", out=v("wcol"), in_=v("rw"), axis=AxisListType.X, op=A.add)
+    ts(v("w25"), v("wcol"), 2.5, A.mult)
+    tt(v("rw", 0, 16), v("row", 0, 16), v("DM", 0, 16), A.mult)
+    op("v", "tensor_reduce", out=v("p2"), in_=v("rw", 0, 16), axis=AxisListType.X, op=A.add)
+    ts(v("p2"), v("p2"), 2.0 ** -63, A.mult)
     ts(v("dcol"), v("p2"), 0.5, A.mult, -0.5, A.add)
-    cp(v("thr"), v("thI", 0, 1))
-    ts(v("thrc"), v("thr"), float(2 ** 30), A.mult)
-    cp(v("B", 0, 640), v("NBi", 0, 640))
-    cp(v("B", 640, 1280), v("NBi", 640, 1280))
+    for s in sorted(set(x for r in PS for x in r)):
+        ts(v("NG%d" % s), v("G16b"), -float(SB), A.mult)
+        if s:
+            fill(v("NG%d" % s, s - 1, 128, s), 0.0)
+    ts(v("th"), v("thI", 0, 1), 6, A.arith_shift_right)
+    ts(v("tl"), v("thI", 0, 1), 63, A.bitwise_and)
+    ts(v("Q", 0, 1), v("th"), -64.0 * SB, A.mult)
+    ts(v("Q", 1, 2), v("tl"), -float(SB), A.mult)
+    cp(v("Q", 2, 3), v("pcol"))
+    fill(v("Q", 3, 4), 16.0)
+    fill(v("Q", 4, 7), 1.0)
+    cp(v("Q", 7, 8), v("lcol"))
+    mm(v("b6", 0, 128, 1, 0, 4), v("Q", 0, 4), v("Ib"))
+    mm(v("b6", 128, 256, 1, 0, 4), v("Q", 4, 8), v("Ib"))
+    act(v("LR", 0, 256, 1, 0, 4), v("b6", 0, 256, 1, 0, 4))
+    mm(v("b6", 256, 384), v("LR", 128, 256, 1, 0, 2), v("LR", 0, 128, 1, 0, 2))
+    act(v("TH"), v("b6", 256, 384))
+    tt(v("RD", 1, 128), v("b6", 257, 384), v("TH", 0, 127), A.subtract)
+    fill(v("RD", 0, 128, 16), BIG)
     for c in range(2):
-        cp(v("b1", 128 * c, 128 * c + 128), hv("z", c))
-        turn(c)
+        iota(v("V2"), [[10, 128]], 1 + 1280 * c, 0)
+        act(MI(c, 2), v("V2"))
+        act(KV(c, 2), hv("z", c))
 
     def send_rings(t):
         kk = "KK%d" % (t % 2)
@@ -477,7 +510,7 @@ def rank_program(g, core, T, topo):
                 remote(g, topo, core, rl[h], T["hand%d" % t][:], res(src), T.sem["ha%d" % t], T.sem["ks%d%d" % (t, h)], 8)
             i = rec("g", 0.3, 4.0, [src], [], emit, "ks%d%d" % (t, h), 8)
             lo = REM + 1024 * t + 512 * h
-            land(v(kk, lo, lo + 512), "ki%d%d" % (t, h), 8, i)
+            land(v(kk, lo, lo + 512), "ki%d%d" % (t, h), 8, i, 8.0)
 
     def send_revoked(t):
         src = v("rS%d" % t, 0, 1)
@@ -485,7 +518,7 @@ def rank_program(g, core, T, topo):
         def emit(e):
             remote(g, topo, core, rv_relay, T["hrv%d" % t][:, 0:1], res(src), T.sem["ra%d" % t], T.sem["rs%d" % t], 8)
         i = rec("g", 0.3, 4.0, [src], [], emit, "rs%d" % t, 8)
-        land(v("cI%d" % t, 0, 1), "ri%d" % t, 8, i)
+        land(v("cI%d" % t, 0, 1), "ri%d" % t, 8, i, 5.0)
 
     def K(t):
         return v("KK%d" % (t % 2), 0, 1280)
@@ -494,232 +527,261 @@ def rank_program(g, core, T, topo):
         b = 16 * (t % 2)
         return v("vO", b + 8 * c, b + 8 * c + 8)
 
+    def fifth(name, c):
+        return v(name, 640 * c, 640 * c + 640, 5)
+
+    tab = v("NBi", 0, 1280)
+
     def first(t, c):
-        tab = v("B", 0, 1280) if t else v("NBi")
-        bv = hv("Bv", c) if t else v("NBi", 640 * c, 640 * c + 640, 5)
+        u = MI(c, 0)
+        group(u, [(v("Ib"), v("C%d" % t)), (v("G16b"), hv("z", c))])
+        ts(hv("r16", c), u, R16, A.add, -R16, A.add)
         if t:
-            act(bv, ind(tab, vo(t, c)))
-        mm(v("b6", 0, 128), v("G16b"), hv("z", c))
-        ts(hv("y1", c), v("b6", 0, 128), v("pm%d" % t), A.add)
-        ts(hv("y2", c), hv("y1", c), 15, A.bitwise_and)
-        oh = v("b1", 256 + 128 * c, 384 + 128 * c)
-        ts(oh, hv("y2", c), 0.0, A.is_equal)
-        tt(hv("mB", c), oh, bv, A.mult)
-        nr = v("b6", 128 + 128 * c, 256 + 128 * c)
-        mm(nr, v("G16f"), hv("mB", c))
-        mm(v("b6", 384 + 8 * c, 392 + 8 * c), hv("mB", c), v("G8f"))
-        tt(hv("dg", c), nr, hv("DM", c), A.mult)
-        scan(hv("sc", c), hv("RN", c), hv("dg", c), A.max)
-        cp(v("nO", 16 * c, 16 * c + 8), v("sc", 128 * c + 15, 128 * c + 128, 16))
-        cp(hv("BnL", c), ind(tab, v("nO", 16 * c, 16 * c + 8)))
-        ts(hv("BnC", c), hv("BnL", c), v("kcol"), A.add)
+            tt(hv("oh", c), u, hv("r16", c), A.is_equal)
+            tt(hv("mB", c), ind(tab, vo(t, c)), hv("oh", c), A.mult)
+        else:
+            tt(KV(c, 3), u, hv("r16", c), A.is_equal)
+            tt(hv("mB", c), KV(c, 3), fifth("NBi", c), A.mult)
+        group(u, [(v("Ib"), v("DMB")), (v("G16b"), hv("mB", c))])
+        scan(hv("sc", c), v("RN"), u, A.max)
+        no = v("nO", 16 * c, 16 * c + 8)
+        ts(no, v("sc", 128 * c + 15, 128 * c + 128, 16), -4096.0, A.add)
+        cp(hv("BnL", c), ind(tab, no))
+        cp(hv("BnH", c), hv("BnL", c))
+        group(SM(c, 0), [(v("On"), v("cK")), (hv("mB", c), v("G8b"))])
         if t < RO - 1:
-            tt(hv("Bk", c), bv, hv("mB", c), A.subtract)
+            mm(MI(c, 1), v("G16b"), hv("mB", c))
 
     def second(t, c):
-        kv, kn = v("b0", 128 * c, 128 * c + 128), v("b0", 256 + 128 * c, 384 + 128 * c)
         old = K(max(t - 1, 0))
-        act(hv("Kv", c), ind(old, vo(t, c)))
-        act(hv("Kn", c), ind(old, v("nO", 16 * c, 16 * c + 8)))
-        for raw, dst in (("Kv", kv), ("Kn", kn)):
-            if raw == "Kv":
-                ts(dst, hv(raw, c), 0.0, A.is_equal, -1.0, A.mult)
-                tt(dst, dst, hv(raw, c), A.add)
-            else:
-                ts(dst, hv(raw, c), 0.25, A.max)
+        both, rawv, rawn = hv("KN", c, 256), v("KN", 256 * c, 256 * c + 128), v("KN", 256 * c + 128, 256 * c + 256)
+        act(rawn, ind(old, v("nO", 16 * c, 16 * c + 8)))
+        if t:
+            act(rawv, ind(old, vo(t, c)))
+            ts(hv("mh", c, 256), both, 0.0, A.is_equal, -1024.0, A.mult)
+            parts = [both, hv("mh", c, 256)]
             for i, col in ((0, "cI%d" % (t - 2)), (1, "rS%d" % (t - 1))):
                 if t - 2 + i >= 0:
-                    ts(hv("m%d" % i, c), hv(raw, c), v(col, 0, 1), A.is_equal, -1024.0, A.mult)
-                    tt(dst, dst, hv("m%d" % i, c), A.add)
-        tt(hv("evn", c), kv, hv("Kn", c), A.is_equal)
-        mm(v("b6", 400 + 8 * c, 408 + 8 * c), hv("evn", c), v("G8b"))
-        ts(hv("dr", c, 8), v("b6", 400 + 8 * c, 408 + 8 * c), 3.0, A.is_ge, float(DIR), A.mult)
-        tt(hv("kn", c, 8), v("b6", 384 + 8 * c, 392 + 8 * c), hv("dr", c, 8), A.add)
-        for b in range(128 * c, 128 * c + 128, 32):
-            act(v("Kc", 16 * b, 16 * b + 512), ind(old, v("BnL", b, b + 32)))
-        for q in (2 * c, 2 * c + 1):
-            for eq, b in (("eqV", 0), ("eqN", 256)):
+                    ts(hv("m%d" % i, c, 256), both, v(col, 0, 1), A.is_equal, -1024.0, A.mult)
+                    parts.append(hv("m%d" % i, c, 256))
+            group(KV(c, 0, 256), [(v("Ib"), x) for x in parts])
+        else:
+            ts(v("mh", 256 * c, 256 * c + 128), fifth("KK0", c), 0.0, A.is_equal, -1024.0, A.mult)
+            ts(v("mh", 256 * c + 128, 256 * c + 256), rawn, 0.0, A.is_equal, -1024.0, A.mult)
+            mm(KV(c, 0, 256), v("Ib"), hv("mh", c, 256), True, False)
+            mm(KV(c, 0), v("Ib"), fifth("KK0", c), False, False)
+            mm(KV(c, 1), v("Ib"), rawn, False, True)
+        for b in range(128 * c, 128 * c + 128, GW):
+            chain("s", act(v("Kc", 16 * b, 16 * (b + GW)), ind(old, v("BnL", b, b + GW))))
+        tt(hv("evn", c), KV(c, 0), rawn, A.is_equal)
+        mm(SM(c, 1), hv("evn", c), v("G8b"))
+        ts(hv("dr", c, 8), SM(c, 1), 3.0, A.is_ge, float(DIR - FAIL + SB), A.mult)
+        tt(hv("kn", c, 8), SM(c, 0), hv("dr", c, 8), A.add)
+        for q in range(2):
+            for eq, b in (("eqV", 0), ("eqN", 128)):
                 for k in range(16):
-                    s = (1024 * q + k, 1024 * q + 1024, 16)
-                    tt(v(eq, *s), v("b0", b + 64 * q, b + 64 * q + 64), v("Kc", *s), A.is_equal)
+                    s = (2048 * c + 1024 * q + k, 2048 * c + 1024 * q + 1024, 16)
+                    chain("v", tt(v(eq, *s), v("b%d" % c, b + 64 * q, b + 64 * q + 64), v("Kc", *s), A.is_equal))
 
     def third(t, c):
-        for eq, b in (("eqV", "b2"), ("eqN", "b3")):
-            mm(v(b, 128 * c, 128 * c + 128), hv("BnC", c), v("If"), True, False)
+        act(hv("hole", c), KV(c, 0), AF.Relu, scale=-1.0)
+        if t:
+            act(hv("Kvr", c), KV(c, 0), AF.Relu)
+        for k0, eq in enumerate(("eqV", "eqN")):
+            mm(SC(c, k0), hv("BnH", c), v("Ib"), True, False)
             for k in range(16):
-                mm(v(b, 128 * c + k, 128 * c + 128, 16), v(eq, 2048 * c + k, 2048 * c + 2048, 16), v("G8s"), False, k == 15)
-        act(hv("cV", c), v("b2", 128 * c, 128 * c + 128))
-        tt(hv("mn", c), v("b3", 128 * c, 128 * c + 128), hv("cV", c), A.min)
-        scan(hv("sc2", c), v("RN", 0, 128), hv("mn", c), A.max)
-        tt(hv("W", c, 8), v("sc2", 128 * c + 15, 128 * c + 128, 16), hv("kn", c, 8), A.max)
-        cp(hv("Wi", c, 8), hv("W", c, 8))
+                mm(v("b%d" % (2 + c), 128 * k0 + k, 128 * k0 + 128, 16), v(eq, 2048 * c + k, 2048 * c + 2048, 16), v("G8s"),
+                   False, k == 15)
+            if not k0:
+                act(hv("cV", c), SC(c, 0))
+        tt(hv("mn", c), SC(c, 1), hv("cV", c), A.min)
+        scan(hv("sc2", c), v("RS"), hv("mn", c), A.max)
+        tt(hv("Wi", c, 8), v("sc2", 128 * c + 15, 128 * c + 128, 16), hv("kn", c, 8), A.max)
         ts(hv("wT", c, 8), hv("Wi", c, 8), SB - 1, A.bitwise_and)
         tt(hv("Aw", c), ind(hv("wT", c, 8), v("bl", 0, 8)), v("DM", 0, 128), A.mult)
-        o = v("b6", 416 + 8 * c, 424 + 8 * c)
-        mm(o, hv("Aw", c), v("G8f"))
+        mm(SM(c, 2), hv("Aw", c), v("G8b"))
         w = vo(t + 1, c)
-        cp(w, o)
-        tt(hv("kp", c), ind(K(t), w), hv("V2", c), A.mult)
-        ts(hv("pl", c), hv("kp", c), 0.25, A.mult, v("pl%d" % t), A.add)
-        ts(hv("plm", c), hv("pl", c), 2047, A.bitwise_and)
-        cp(hv("PL", c), hv("plm", c))
-        for q in (2 * c, 2 * c + 1):
-            for b in (64 * q, 64 * q + 32):
-                act(v("Xc", 16 * b, 16 * b + 512), ind(v("X"), v("PL", b, b + 32)))
-            if q in PEQ:
-                for b in range(1024 * q, 1024 * q + 1024, 512):
-                    mm(v("b7"), v("Ib"), v("Xc", b, b + 512), True, False)
-                    mm(v("b7"), hv("zT", c), v("RS", b - 2048 * c, b - 2048 * c + 512), False, True)
-                    act(v("ab", b, b + 512), v("b7"), AF.Abs)
-                continue
-            for k in range(16):
-                s = (1024 * q + k, 1024 * q + 1024, 16)
-                tt(v("df", *s), v("b1", 64 * q, 64 * q + 64), v("Xc", *s), A.subtract)
-            act(v("ab", 1024 * q, 1024 * q + 1024), v("df", 1024 * q, 1024 * q + 1024), AF.Abs)
+        cp(w, SM(c, 2))
         act(hv("Kw", c), ind(K(t), w))
-        ts(hv("hz", c), hv("Kw", c), 0.0, A.is_equal, float(2 ** 25), A.mult)
+        tt(hv("kp", c), MI(c, 2), hv("Kw", c), A.mult)
+        ts(hv("k2", c), hv("kp", c), 2, A.arith_shift_right, SB - 1, A.bitwise_and)
+        ts(hv("PL", c), hv("k2", c), v("c0"), A.add, float(t), A.add)
+        s = PS[t][c]
+        for q in range(2):
+            lo = 2048 * c + 1024 * q
+            for b in range(lo // 16, lo // 16 + 64, GW):
+                chain("s", act(v("Xc", 16 * b, 16 * (b + GW)), ind(v("X"), v("PL", b, b + GW))))
+            if s:
+                m, bank = 16 // s, "b%d" % (6 + q)
+                mm(v(bank, 0, 64 * m), v("Ib"), v("Xc", lo + s - 1, lo + 1024, s), True, False)
+                for i in range(m):
+                    mm(v(bank, i, 64 * m, m), v("nIb"), v("z", lo // 16, lo // 16 + 64), False, i == m - 1)
+                act(v("ab", 1024 * c + 64 * m * q, 1024 * c + 64 * m * (q + 1)), v(bank, 0, 64 * m), AF.Abs)
+            for p in range(16):
+                if not s or p % s != s - 1:
+                    chain("v", tt(v("mx", lo + p, lo + 1024, 16), v("b%d" % c, 256 + 64 * q, 320 + 64 * q),
+                                  v("Xc", lo + p, lo + 1024, 16), A.max))
+        if OPT["hz"] == "v":
+            ts(hv("hz", c), hv("Kw", c), 0.0, A.is_equal, -2.0 ** 18, A.mult)
+        tt(hv("pr", c), KV(c, 2), hv("Kw", c), A.mult)
+        mm(WR(8 * c, 8), hv("pr", c), v("G8f"))
         if t < RO - 1:
             act(hv("Vn", c), ind(v("T1"), w))
-            act(hv("V2", c), hv("Vn", c), scale=2.0, bias=1.0)
-        tt(hv("pr", c), v("b1", 128 * c, 128 * c + 128), hv("Kw", c), A.mult)
-        mm(v("b6", 448 + 8 * c, 456 + 8 * c), hv("pr", c), v("G8f"))
-        pa = v("b5", 256 + 128 * c, 384 + 128 * c)
-        mm(pa, v("Ib"), hv("Kw", c), True, False)
-        mm(pa, v("Ib"), hv("UC", c), False, True)
+            act(MI(c, 2), hv("Vn", c), scale=2.0, bias=1.0)
+            if t:
+                tt(KV(c, 3), MI(c, 1), hv("Vn", c), A.subtract)
+                tt(hv("ohd", c), KV(c, 3), hv("oh", c), A.mult)
+            else:
+                tt(hv("dl", c), MI(c, 1), hv("Vn", c), A.subtract)
+                tt(KV(c, 3), KV(c, 3), hv("dl", c), A.mult)
 
     def fourth(t, c):
-        dT = v("b4", 128 * c, 128 * c + 128)
-        mm(dT, v("Ib"), v("LPh"), True, False)
-        mm(dT, v("Ib"), v("LPl"), False, False)
+        dT, s, lo = SC(c, 2), PS[t][c], 2048 * c
+        mm(dT, v("LR", 128, 256, 1, 0, 4), v("LR", 0, 128, 1, 0, 4), True, False)
         for p in range(16):
-            mm(v("b4", 128 * c + p, 128 * c + 128, 16), v("ab", 2048 * c + p, 2048 * c + 2048, 16), v("G8k"), False, p == 15)
-        act(hv("dk", c), dT)
-        scan(hv("sd", c), v("RP"), dT, A.min)
-        mm(v("b5", 128 * c, 128 * c + 128), v("Ib"), hv("hz", c), True, False)
-        mm(v("b5", 128 * c, 128 * c + 128), hv("dk", c), v("If"), False, True)
-        tt(hv("Ap", c), ind(hv("sd", c), v("bl2", 0, 8)), v("DM", 0, 128), A.mult)
-        o = v("b6", 432 + 8 * c, 440 + 8 * c)
-        mm(o, hv("Ap", c), v("G8f"))
-        cp(hv("pi", c, 8), o)
-        ts(hv("pi2", c, 8), hv("pi", c, 8), 2047, A.bitwise_and)
+            o = v("b%d" % (2 + c), 256 + p, 384, 16)
+            if s and p % s == s - 1:
+                m = 16 // s
+                mm(o, v("ab", 1024 * c + p // s, 1024 * c + 128 * m, m), v("G8a"), False, False)
+            else:
+                mm(o, v("mx", lo + p, lo + 2048, 16), v("G8m"), False, False)
+                mm(o, v("Xc", lo + p, lo + 2048, 16), v("G8x"), False, False)
+        mm(dT, hv("z", c), v("NG%d" % s), False, True)
+        scan(hv("sd", c), v("RD"), dT, A.min)
+        act(hv("nf", c), dT, AF.Relu, scale=2.0 ** 19, bias=v("nfb"))
+        cp(hv("pi", c, 8), v("sd", 128 * c + 15, 128 * c + 128, 16))
+        ts(hv("pi2", c, 8), hv("pi", c, 8), SB - 1, A.bitwise_and)
+        tt(hv("Ap", c), ind(hv("pi2", c, 8), v("bl", 0, 8)), v("DM", 0, 128), A.mult)
+        mm(SM(c, 3), hv("Ap", c), v("G8b"))
         do = v("dO", 16 * c, 16 * c + 8)
-        cp(do, hv("pi2", c, 8))
-        tt(hv("zx", c), ind(v("Xc", 2048 * c, 2048 * c + 2048), do), hv("z", c), A.add)
-        ts(hv("dz", c), hv("zx", c), 0.5, A.mult, -0.25, A.add)
-        zp = v("b1", 128 * c, 128 * c + 128)
+        cp(do, SM(c, 3))
+        tt(hv("zx", c), ind(v("Xc", lo, lo + 2048), do), hv("z", c), A.add)
+        if OPT["za"] == "v":
+            ts(hv("za", c), hv("zx", c), HALF, A.mult, R1, A.add)
+        else:
+            act(hv("za", c), hv("zx", c), AF.Identity, scale=HALF, bias=v("pR1"))
         if t == RO - 1:
-            cp(hv("zF", c), hv("dz", c))
+            act(hv("zF", c), hv("za", c), AF.Identity, bias=v("nR1"))
             store(T.yz[:, 128 * c:128 * c + 128], hv("zF", c), c)
         else:
-            cp(hv("z", c), hv("dz", c))
-            cp(zp, hv("z", c))
-            turn(c)
-        act(hv("cd", c), v("b5", 128 * c, 128 * c + 128), AF.Relu, scale=-float(2 ** 18), bias=v("thrc"))
-        tt(hv("rr", c), v("b5", 256 + 128 * c, 384 + 128 * c), hv("cd", c), A.min)
+            act(hv("z", c), hv("za", c), AF.Identity, bias=v("nR1"))
+            act(KV(c, 2), hv("za", c), AF.Identity, bias=v("nR1"))
+        group(MI(c, 1), [(v("Ib"), hv("Kw", c)), (v("Ib"), hv("hz", c)), (hv("nf", c), v("nIb"))])
+        scan(hv("cs", c), v("C256"), MI(c, 1), A.max, v("cs", 127, 128) if c else -2.0 ** 20)
 
     def writers(t):
-        ts(v("F"), v("W"), float(SB), A.is_lt)
-        ts(v("NF"), v("W"), float(SB), A.is_ge, -512.0, A.mult)
-        ts(v("Lb"), v("W"), float(DIR), A.is_lt)
-        mm(v("b2", 400, 408), v("TriO"), v("F", 0, 8), True, False)
-        mm(v("b2", 400, 408), v("Ib"), v("NF", 0, 8), False, True)
-        mm(v("b2", 408, 416), v("TriO"), v("F", 8, 16), True, False)
-        mm(v("b2", 408, 416), v("Ib"), v("NF", 8, 16), False, False)
-        mm(v("b2", 408, 416), v("On"), v("F", 0, 8), False, True)
-        ts(v("x96"), v("b2", 400, 416), float(CAP), A.is_lt)
-        tt(v("act"), v("x96"), v("Lb"), A.mult)
-        tt(v("av"), v("act"), v("vmd4"), A.mult)
-        cp(v("hi"), v("b6", 448, 464))
+        kk = "KK%d" % (t % 2)
+        ts(v("F"), v("Wi"), float(FAIL), A.is_lt)
+        ts(v("D"), v("Wi"), float(DIR), A.is_ge, 1024.0, A.mult)
+        y = WR(16)
+        mm(y, v("Tri"), v("F"), True, False)
+        mm(WR(24, 8), v("On"), v("F", 0, 8), False, False)
+        mm(y, v("Ib"), v("D"), False, True)
+        cp(v("hi"), WR(0))
         ts(v("h2"), v("hi"), 1023, A.bitwise_and)
         ts(v("hb"), v("h2"), float(REM + 1024 * t), A.add)
         tt(v("hc"), v("hb"), v("F"), A.mult)
         tt(v("src"), v("hc"), v("wT"), A.max)
-        tt(v("hd"), v("src"), v("d04"), A.add)
-        w2 = v("av")
         if t:
+            ts(v("aw"), y, 512.0 + CAP, A.is_lt, v("wcol"), A.mult)
+            ts(v("aB"), y, 512.0 + CAP, A.is_lt, 2.0 ** 70, A.mult)
+            tt(v("av"), v("aB"), v("vmd"), A.mult)
+            tt(v("hd"), v("src"), v("d04"), A.add)
             for gr in range(8):
-                e, f = 256 * gr, 128 * gr
-                mm(v("b2", 416 + gr, 417 + gr), v("EA", e, e + 128), v("act", gr, gr + 1))
-                mm(v("b2", 424 + gr, 425 + gr), v("EA", e + 128, e + 256), v("act", gr, gr + 1), True, False)
-                mm(v("b2", 424 + gr, 425 + gr), v("EB", f, f + 128), v("act", 8 + gr, 9 + gr), False, True)
-            ts(v("wr"), v("b2", 416, 432), 0.0, A.is_equal)
-            tt(v("w2"), v("wr"), v("av"), A.mult)
-            w2 = v("w2")
-        tt(v("word"), w2, v("hd"), A.add)
-        tt(v("Aq"), ind(v("word"), v("bl")), v("DM"), A.mult)
-        for c in range(2):
-            mm(v("b2", 448 + 8 * c, 456 + 8 * c), hv("Aq", c), v("G8f"))
-        cp(v("qi"), v("b2", 448, 464))
-        ts(v("q1"), v("qi"), 13, A.arith_shift_right)
-        cp(v("scO"), v("q1"))
-        ts(v("q2"), v("qi"), 8191, A.bitwise_and)
-        cp(v("srO"), v("q2"))
-        act(v("sgn"), v("b0", 0, 256), AF.Sign)
-        act(v("hole"), v("sgn"), AF.Relu, scale=-1.0)
-        act(v("Kvr"), v("b0", 0, 256), AF.Relu)
-        kk = "KK%d" % (t % 2)
-        tt(v("fm"), ind(v(kk, 0, REM + 1024 * (t + 1)), v("srO")), v("hole"), A.mult)
-        tt(ind(v(kk, 0, REM), v("scO")), v("fm"), v("Kvr"), A.add)
+                e = 384 * gr
+                mm(WR(32 + gr, 1), v("E", e, e + 128), v("aw", gr, gr + 1))
+                group(WR(40 + gr, 1), [(v("E", e + 128, e + 256), v("aB", gr, gr + 1)),
+                                       (v("E", e + 256, e + 384), v("aw", 8 + gr, 9 + gr))])
+            ts(v("wf"), WR(32), v("w25"), A.is_lt)
+            tt(v("w2"), v("wf"), v("av"), A.mult)
+            tt(v("word"), v("w2"), v("hd"), A.add)
+            tt(v("Aq"), ind(v("word"), v("bl")), v("DM"), A.mult)
+            for c in range(2):
+                mm(WR(48 + 8 * c, 8), hv("Aq", c), v("G8f"))
+            cp(v("qi"), WR(48))
+            ts(v("q1"), v("qi"), 13, A.arith_shift_right)
+            cp(v("scO"), v("q1"))
+            ts(v("q2"), v("qi"), 8191, A.bitwise_and)
+            cp(v("srO"), v("q2"))
+        else:
+            ts(v("act"), y, 512.0 + CAP, A.is_lt)
+            ts(v("hd"), v("src"), -1280.0, A.add)
+            tt(v("word"), v("hd"), v("act"), A.mult)
+            tt(v("Aqh"), ind(v("word"), v("bl")), v("DM"), A.mult)
+            for c in range(2):
+                mm(WR(48 + 8 * c, 8), hv("Aqh", c), v("G8b"))
+            ts(v("srO"), WR(48), 1280.0, A.add)
+        tt(v("fm"), ind(v(kk, 0, REM + 1024 * (t + 1)), v("srO")), v("hole"), A.min)
+        if t:
+            tt(ind(v(kk, 0, REM), v("scO")), v("fm"), v("Kvr"), A.add)
+        else:
+            for c in range(2):
+                tt(fifth(kk, c), KV(c, 0), hv("fm", c), A.max)
+                tt(fifth("NBi", c), fifth("NBi", c), KV(c, 3), A.subtract)
+        if t == 1:
+            tt(v("nb"), ind(tab, v("vO", 16, 32)), v("ohd"), A.subtract)
+            cp(ind(v("NBi"), v("scO")), v("nb"))
         if t < RO - 1:
-            tt(v("ohw"), v("b1", 256, 512), v("Vn"), A.mult)
-            tt(ind(v("B"), v("scO")), v("Bk"), v("ohw"), A.add)
-            mm(v("b2", 432, 448), v("On"), v("F"))
-            act(v("fj"), v("b2", 432, 448), accum_out=v("fs"))
+            mm(WR(64), v("On"), v("F"))
+            act(v("fj"), WR(64), accum_out=v("fs"))
             cp(v("fi"), v("fs"))
             ts(v("fa"), v("fi"), 15, A.bitwise_and)
-            ts(v("t1"), v("wT"), 8192.0, A.mult)
-            tt(v("vmd4"), v("t1"), v("d04"), A.subtract)
+            for c in range(2):
+                ts(hv("vmd", c, 8), hv("wT", c, 8), v("d0%d" % c), A.subtract, 2.0 ** -57, A.mult)
+        if t:
+            come = v("cI%d" % (t - 1), 0, 1)
+            ts(v("ncome"), come, -1.0, A.mult)
+            if t < RO - 1:
+                ts(K(t + 1), K(t), come, A.is_equal, v("ncome"), A.mult)
+                add_into(K(t + 1), K(t), 1)
+            else:
+                ts(v("NM2"), K(t), come, A.is_equal, v("ncome"), A.mult)
+                add_into(K(t), v("NM2"), 3)
 
     def same_node():
         ts(v("ci"), v("Vn"), v("p2"), A.mult, v("dcol"), A.add)
         ts(v("cb"), v("ci"), 1, A.bitwise_and)
-        ts(v("code"), v("cb"), -2.0, A.mult, 1.0, A.add)
-        act(v("cdE"), v("code"), scale=v("even"))
-        act(v("cdO"), v("code"), scale=v("odd"))
+        if OPT["cd"] == "v":
+            ts(v("cdE"), v("cb"), v("neven"), A.mult, v("even"), A.add)
+            ts(v("cdO"), v("cb"), v("nodd"), A.mult, v("odd"), A.add)
+        else:
+            ts(v("code"), v("cb"), -2.0, A.mult, 1.0, A.add)
+            act(v("cdE"), v("code"), scale=v("even"))
+            act(v("cdO"), v("code"), scale=v("odd"))
         for gr in range(8):
             lo = 32 * (gr // 2)
             m = "cdO" if gr % 2 else "cdE"
-            b = "b3" if gr % 2 else "b7"
-            mm(v(b, 0, 256), v(m, 0, 128, 1, lo, lo + 32), v("code", 0, 256, 1, lo, lo + 32))
-            mm(v(b, 256, 384), v(m, 128, 256, 1, lo, lo + 32), v("code", 128, 256, 1, lo, lo + 32))
-            act(v("E0", 256 * gr, 256 * gr + 256), v(b, 0, 256), AF.Relu, bias=v("fb"))
-            act(v("E1", 128 * gr, 128 * gr + 128), v(b, 256, 384), AF.Relu, bias=v("fb"))
-        for e, o, w in (("E0", "EA", 256), ("E1", "EB", 128)):
-            op("g", "affine_select", out=v(o), in_=v(e), pattern=[[0, 8], [1, w]], compare_op=A.is_gt, fill=0.0, base=0,
-               channel_multiplier=-1)
+            b = "b%d" % (6 + gr % 2)
+            mm(v(b, 0, 256), v(m, 0, 128, 1, lo, lo + 32), v(m, 0, 256, 1, lo, lo + 32))
+            mm(v(b, 256, 384), v(m, 128, 256, 1, lo, lo + 32), v(m, 128, 256, 1, lo, lo + 32))
+            act(v("E", 384 * gr, 384 * gr + 384), v(b, 0, 384), AF.Relu, bias=v("fb"))
 
     def revoke(t):
-        if t:
-            come = v("cI%d" % (t - 1), 0, 1)
-            ts(v("ncome"), come, -1.0, A.mult)
-            ts(v("NM2"), K(t), come, A.is_equal, v("ncome"), A.mult)
-        op("v", "tensor_reduce", out=v("rvi"), in_=v("rr"), axis=AxisListType.X, op=A.max)
+        ts(v("rvi"), v("cs", 255, 256), 0.0, A.max)
         ts(v("rva"), v("rvi"), 255, A.bitwise_and)
+        if t == RO - 1:
+            ts(v("rb"), v("rva"), -256.0, A.mult)
+            for i in range(4):
+                lo, o = 320 * i, v("b%d" % (6 + i % 2), 0, 320)
+                act(o, v("KK0", lo, lo + 320), AF.Abs, scale=256.0, bias=v("rb"))
+                tt(v("Yk", lo, lo + 320), o, v("KK0", lo, lo + 320), A.min)
+                store(T.yk[:, lo:lo + 320], v("Yk", lo, lo + 320), 2 + i)
+            return
         rv = v("rS%d" % t, 0, 1)
         cp(rv, v("rva"))
+        send_revoked(t)
         if t:
-            ts(v("rvE%d" % t), rv, v("cI%d" % (t - 1), 0, 1), A.not_equal, rv, A.mult)
-            rv = v("rvE%d" % t)
+            ts(v("rvE"), rv, v("cI%d" % (t - 1), 0, 1), A.not_equal, rv, A.mult)
+            rv = v("rvE")
         ts(v("nrv"), rv, -1.0, A.mult)
-        kk = "KK%d" % (t % 2)
-        blocks = ((0, 512, "b4"), (512, 1024, "b7"), (1024, 1280, "b4"))
-        for lo, hi, b in blocks:
-            ts(v("NM1", lo, hi), v(kk, lo, hi), rv, A.is_equal, v("nrv"), A.mult)
-        for lo, hi, b in blocks:
-            o = v(b, 0, hi - lo)
-            mm(o, v("Ib"), v(kk, lo, hi), True, False)
-            if t:
-                mm(o, v("Ib"), v("NM2", lo, hi), False, False)
-            mm(o, v("Ib"), v("NM1", lo, hi), False, True)
-            if t == RO - 1:
-                act(v("Yk", lo, hi), o)
-                store(T.yk[:, lo:hi], v("Yk", lo, hi), 2 + lo // 512)
-            else:
-                act(v("KK%d" % ((t + 1) % 2), lo, hi), o)
-        if t < RO - 1:
-            send_revoked(t)
-            send_rings(t + 1)
-            ts(v("thrc"), v("fa"), v("thr"), A.add, float(2 ** 30), A.mult)
+        if t:
+            ts(v("NM1"), K(t), rv, A.is_equal, v("nrv"), A.mult)
+            add_into(K(t + 1), v("NM1"), 2)
+        else:
+            ts(K(t + 1), K(t), rv, A.is_equal, v("nrv"), A.mult)
+            add_into(K(t + 1), K(t), 0)
+        send_rings(t + 1)
+        ts(v("nfb"), v("fa"), -2.0 ** 30, A.mult, 2.0 ** 18, A.add)
 
     send_rings(0)
     for c in range(2):

@@ -1,3 +1,4 @@
+import numpy as np
 from concourse.bass import DstId, RemoteDMATransfer
 from concourse.mybir import dt, AluOpType, AxisListType, ActivationFunctionType
 import comms_topo
@@ -8,22 +9,27 @@ RO, SB, CAP = 3, 2048, 96
 BIG = 1.0e9
 R16, R1 = 1.5 * 2 ** 27, 1.5 * 2 ** 23
 HALF = 0.5 - 2.0 ** -11
-PS = [[2, 2], [2, 2], [2, 2]]
+PS = [[8, 4], [8, 4], [8, 0]]
+ROWS = {0: [], 4: [(4, 3)], 8: [(2, 1)], 12: [(2, 1), (4, 0)], 16: [(2, 1), (2, 0)]}
+EQ = [[0, 0], [0, 0], [0, 0]]
+KP = [[0, 0], [0, 0], [0, 0]]
+ONV = []
 GW = 64
-OPT = dict(za="v", hz="v", cd="s", wr="b5")
+OPT = dict(za="s", hz="s", r16="v", mh="v", zx="v", wr="b4")
 REM = 1536
 WS = 17 * SB
 FAIL, DIR = 51 * SB, 290 * SB
 
-F32 = dict(G8f=8, RN=128, RS=128, RD=128, TH=128, T1=1280, r16=256, sc=256, dr=16, kn=16, cV=256, mn=256, sc2=256, Vn=256, V2=128,
+F32 = dict(G8f=8, RN=128, RS=128, RD=128, TH=128, T1=1280, r16=256, sc=256, dr=16, kn=16, cV=256, mn=256, sc2=256, Vn=256, V2=256,
            pr=256, zx=256, za=256, sd=256, cs=256, dl=256, ohd=256, zF=256, row=128, rw=128, pcol=1, p2=1, dcol=1, odd=1, even=1,
            neven=1, nodd=1, c0=1, wcol=1, w25=1, nrv=1, rvE=1, ncome=1, fs=1, fj=16, d04=16, d00=1, d01=1, vmd=16, av=16, hd=16,
-           wf=16, hb=16, hc=16, src=16, w2=16, word=16, t1=16, Aq=256, p5=1, fb=1, nR1=1, pR1=1, nfb=1, rb=1, lcol=1, h18=1)
+           wf=16, hb=16, hc=16, src=16, w2=16, word=16, t1=16, Aq=256, p5=1, fb=1, nR1=1, pR1=1, nfb=1, rb=1, lcol=1, h18=1, sgn=16,
+           r17=256, pR16=1, nR16=1, h10=1, xb=256)
 BF = dict(Ib=128, nIb=128, G16b=128, G8b=8, G8s=8, G8m=8, G8x=8, G8a=8, cK=8, Tri=128, On=128, DM=256, DMB=128, C0=128, C1=128,
-          C2=128, NG0=128, NG2=128, NG4=128, Q=16, LR=256, C256=128, z=256, KN=512, Kw=256, evn=256, mh=512, m0=512, m1=512,
+          C2=128, NG0=128, NG4=128, NG8=128, NG12=128, CT=1280, Q=16, LR=256, C256=128, z=256, KN=512, Kw=256, evn=256, mh=512, m0=512, m1=512,
           Kvr=256, hz=256, hole=256, fm=256, code=256, cdE=256, cdO=256, oh=256, nf=256, F=16, D=16, act=16, aw=16, aB=16,
-          NM1=1280, NM2=1280)
-H16 = dict(mB=256, BnH=256, Aw=256, Ap=256, Aqh=256)
+          val=256, vm=256)
+H16 = dict(mB=256, BnH=256, Aw=256, Ap=256, Aqh=256, dOh=16)
 I32 = dict(PI=1, pi15=1, pb=1, pc=1, D1=256, D15=256, D2=128, D3=128, ic=16, iv=16, kp=256, k2=256, pi=16, pi2=16, Wi=16, wT=16,
            hi=16, h2=16, qi=16, q1=16, q2=16, rvi=1, rva=1, fi=1, fa=1, ci=256, cb=256, nb=256, th=1, tl=1)
 U16 = dict(bl=16, vO=32, nO=32, scO=16, srO=16, dO=32, BnL=256, PL=256)
@@ -44,9 +50,9 @@ for _d, _n, _t in ((F32, "SF", "float32"), (BF, "SBF", "bfloat16"), (H16, "SH", 
     SCRATCH[_n] = ("sbuf", [128, _w], _t)
     for _k in _d:
         WHERE[_k] = (_n, _p[_k], _d[_k])
-_BIGB = dict(KK0=(REM + 1024 * RO, "bfloat16"), KK1=(REM + 1024 * RO, "bfloat16"), X=(4096, "bfloat16"),
+_BIGB = dict(KK0=(REM + 1024, "bfloat16"), KK1=(REM + 2048, "bfloat16"), X=(4096, "bfloat16"),
              Kc=(4096, "bfloat16"), eqV=(4096, "bfloat16"), eqN=(4096, "bfloat16"), Xc=(4096, "bfloat16"), mx=(4096, "bfloat16"),
-             ab=(2048, "bfloat16"), E=(3072, "bfloat16"), NBi=(REM, "int32"), Yk=(1280, "bfloat16"), thI=(8, "int32"),
+             ab=(4096, "bfloat16"), E=(3072, "bfloat16"), NBi=(REM, "int32"), Yk=(1280, "bfloat16"), thI=(8, "int32"),
              rS0=(8, "float32"), rS1=(8, "float32"), rS2=(8, "float32"), cI0=(8, "float32"), cI1=(8, "float32"))
 for _k in _BIGB:
     SCRATCH[_k] = ("sbuf", [128, _BIGB[_k][0]], _BIGB[_k][1])
@@ -66,12 +72,15 @@ for _t in range(RO - 1):
     SEMAPHORES += ["rs%d" % _t, "ri%d" % _t, "ra%d" % _t, "rl%d" % _t]
 
 CY = 0.00083
+STEP = [""]
 SEQ = []
-ORD = dict(tail=0.16, f=1.1, ga=1.56, sc=3.8, sig=0.02, seed=1, win=0.0)
+INFO = []
+ORD = dict(tail=0.16, hop=5.0, tries=6000, seed=1, slack=0.28, share=0.05, move=3.0, shake=0.15)
+PACE = [(1.2, 1.56, 3.8), (1.0, 1.56, 3.8), (1.45, 1.3, 3.0), (1.1, 2.0, 5.0)]
 
 
-def noise(i, seed):
-    return ((i * 2654435761 + seed * 1013904223 + (i ^ seed) * 69069) % 65521) / 65521.0 - 0.5
+def rem(t):
+    return REM + 1024 * max(t - 1, 0)
 
 
 def relays(core, T, topo, dst):
@@ -136,26 +145,26 @@ def covers(a, b):
 
 def cost(q, m, kw):
     o = kw.get("out")
-    f = ORD["f"] * CY
     if q == "t":
         n, mm = count(kw["rhs"]), count(kw["lhsT"])
-        return max(min(64, mm), n) * (1 if two(kw["lhsT"]) else 4) * f
+        return (0.0, max(min(64, mm), n) * (1 if two(kw["lhsT"]) else 4), 0, 0)
     if q == "g":
-        return 0.15 + 2 * count(o) * f
+        return (0.0, 160 + 2 * count(o), 0, 0)
     ins = [kw[k] for k in kw if k not in ("out", "accum_out") and is_view(kw[k])]
     full = [i for i in ins if count(i) > 1]
     n = max([count(o)] + [count(i) for i in full])
     if o[0] == "#":
-        return 0.05 + n * ORD["sc"] * CY
+        return (0.05, 0, 0, n)
     for i in full:
         if i[0] == "#":
-            return 0.06 + n * ORD["ga"] * CY
+            return (0.065 if q == "s" else 0.05, 0, n, 0)
     c = 1.0
     if q == "v" and m == "tensor_tensor" and not [i for i in full if psum(i)]:
         c = 2.0
-    if q == "v" and m in ("tensor_copy", "tensor_scalar", "memset") and two(o) and not [i for i in full if not two(i)]:
+    if q == "v" and m in ("tensor_copy", "tensor_scalar", "memset", "tensor_tensor_scan") and two(o) and not [
+            i for i in full if not two(i)]:
         c = 0.5
-    return max(64, n * c) * f
+    return (0.0, max(64, n * c), 0, 0)
 
 
 def noter(T):
@@ -198,7 +207,10 @@ def noter(T):
             touch(i, q, v, False, deps)
         for v in writes:
             touch(i, q, v, True, deps)
-        ops.append([q, c, tail, deps, emit, sem or "q" + q, inc])
+        if not isinstance(c, tuple):
+            c = (c, 0, 0, 0)
+        name = writes[0][1] if writes else "out"
+        ops.append([q, c, tail, deps, emit, sem or "q" + q, inc, STEP[0] + (name[:2] if q == "v" and name[:2] in ("eq", "mx") else q)])
         return i
 
     def op(q, m, **kw):
@@ -252,47 +264,97 @@ def noter(T):
 
 def order(ops):
     n = len(ops)
-    users = [[] for _ in range(n)]
-    left = [0] * n
+    q = ["s" if o[0] == "S" else o[0] for o in ops]
+    tail = [o[2] for o in ops]
+    deps, before = [], [0] * n
     for i in range(n):
-        for j, w in ops[i][3]:
-            users[j].append((i, w))
-            left[i] += 1
-    prio = [0.0] * n
-    for i in range(n - 1, -1, -1):
-        b = 0.0
-        for u, w in users[i]:
-            b = max(b, prio[u] + (ops[i][2] if w else 0.0))
-        prio[i] = b + ops[i][1]
-    prio = [p * (1 + ORD["sig"] * noise(i, ORD["seed"])) for i, p in enumerate(prio)]
-    ready = [0.0] * n
-    avail = {}
-    free = {}
+        keep, seen = [], 0
+        for j, w in sorted(ops[i][3], reverse=True):
+            if not (w and seen >> j & 1):
+                keep.append((j, w))
+            if w:
+                seen |= before[j]
+                before[i] |= before[j] | 1 << j
+        deps.append(keep)
+    durs = [[o[1][0] + (o[1][1] * f + o[1][2] * ga + o[1][3] * sc) * CY for o in ops] for f, ga, sc in PACE]
+    fwds = [[[(j, d[j] + (tail[j] if w else 0.0)) for j, w in deps[i]] for i in range(n)] for d in durs]
+    dur, fwd, bwd = durs[0], fwds[0], [[] for _ in range(n)]
     for i in range(n):
-        if left[i] == 0:
-            avail.setdefault(ops[i][0], []).append(i)
-    out = []
-    while len(out) < n:
-        best = None
-        for q in avail:
-            if not avail[q]:
-                continue
-            f = free.get(q, 0.0)
-            s0 = min(max(f, ready[i]) for i in avail[q])
-            i = max((i for i in avail[q] if max(f, ready[i]) <= s0 + ORD["win"]), key=lambda k: (prio[k], -k))
-            s = max(f, ready[i])
-            if best is None or s < best[0]:
-                best = (s, q, i)
-        s, q, i = best
-        avail[q].remove(i)
-        free[q] = s + ops[i][1] if q != "x" else 0.0
-        out.append(i)
-        for u, w in users[i]:
-            ready[u] = max(ready[u], s + (ops[i][1] + ops[i][2] if w else 0.0))
-            left[u] -= 1
-            if left[u] == 0:
-                avail.setdefault(ops[u][0], []).append(u)
-    return out
+        for j, w in deps[i]:
+            bwd[j].append((i, dur[i] + (tail[j] if w else 0.0)))
+    ends = [i for i in range(n) if not bwd[i] and q[i] != "x"]
+    span = np.array([dur[i] + (0.0 if bwd[i] else tail[i]) for i in range(n)])
+    names = sorted(set(o[7] for o in ops))
+    step = np.array([names.index(o[7]) for o in ops])
+    state = [ORD["seed"]]
+
+    def draw(k):
+        state[0] = (state[0] * 6364136223846793005 + 1442695040888963407) % 2 ** 64
+        x = (np.arange(1, k + 1) * (state[0] >> 44 | 1) + (state[0] >> 20 & 65535)) % 1048573
+        return (x * x % 1048573) / 1048573.0
+
+    def place(pre, key, turn):
+        key = list(key)
+        for i in turn:
+            for j, _ in pre[i]:
+                if key[j] >= key[i]:
+                    key[i] = key[j] + 1e-7
+        st = [0.0] * n
+        busy = {x: ([], []) for x in set(q)}
+        for i in sorted(turn, key=lambda k: key[k]):
+            s = 0.0
+            for j, lag in pre[i]:
+                if st[j] + lag > s:
+                    s = st[j] + lag
+            if q[i] != "x":
+                lo, hi = busy[q[i]]
+                k = m = len(lo)
+                while k and hi[k - 1] > s:
+                    k -= 1
+                while k < m and lo[k] < s + dur[i] - 1e-9:
+                    s = max(s, hi[k])
+                    k += 1
+                lo.insert(k, s)
+                hi.insert(k, s + dur[i])
+            st[i] = s
+        return st
+
+    def replay(seq, d, pre):
+        free, st = {x: 0.0 for x in set(q)}, [0.0] * n
+        for i in seq:
+            s = free[q[i]]
+            for j, lag in pre[i]:
+                if st[j] + lag > s:
+                    s = st[j] + lag
+            st[i] = s
+            if q[i] != "x":
+                free[q[i]] = s + d[i]
+        return max(st[i] + d[i] + tail[i] for i in ends)
+
+    up, down = list(range(n)), list(range(n - 1, -1, -1))
+    key = up
+    best = cur = None
+    for _ in range(ORD["tries"]):
+        st = place(fwd, key, up)
+        end = max(st[i] + dur[i] + tail[i] for i in ends)
+        r = draw(4)
+        if cur is None or end <= cur[2][0] * 1.01:
+            seq = sorted(up, key=lambda k: st[k])
+            e = [end] + [replay(seq, durs[k], fwds[k]) for k in range(1, len(PACE))]
+            val = sum(x / p[0] ** 0.85 for x, p in zip(e, PACE)) / len(e)
+            if best is None or val < best[0]:
+                best = (val, st, e, seq)
+            if cur is None or val <= cur[0] + ORD["slack"] * r[0]:
+                cur = (val, st, e, seq)
+            if cur[0] > best[0] + 3 * ORD["slack"]:
+                cur = best
+        move = (draw(len(names)) < ORD["share"]) * (draw(len(names)) - 0.5) * 2 * ORD["move"]
+        key = np.array(cur[1])
+        if r[1] < 0.7:
+            key = -(np.array(place(bwd, -(key + span) + ORD["shake"] * r[2] * draw(n), down)) + np.array(dur))
+        key = key + move[step] + ORD["shake"] * r[2] * draw(n)
+    INFO[:] = [best[0], best[2], {x: sum(durs[1][i] for i in up if q[i] == x) for x in "vst"}]
+    return best[3]
 
 
 def issue(g, T, ops, seq):
@@ -302,7 +364,7 @@ def issue(g, T, ops, seq):
         know[q] = {}
     know["S"] = know["s"]
     for i in seq:
-        q, c, tail, deps, emit, sem, inc = ops[i]
+        q, c, tail, deps, emit, sem, inc = ops[i][:7]
         if emit is None:
             total[sem] = total.get(sem, 0) + inc
             tok[i] = (sem, total[sem], {})
@@ -380,7 +442,8 @@ def rank_program(g, core, T, topo):
         return op("v", "tensor_tensor_scan", out=out, data0=a, data1=b, initial=first, op0=o0, op1=o1)
 
     def load(q, dst, src, k):
-        return rec(q, 0.1, 3.5, [], [dst], lambda e: e.dma_start(res(dst), src), "ld%d" % k, 16)
+        chain("load" + q, rec(q, 0.05, (2.7, 2.5, 4.0, 5.3, 2.7, 7.3, 9.4)[k], [], [dst], lambda e: e.dma_start(res(dst), src),
+                              "ld%d" % k, 16))
 
     def store(dst, srcv, k):
         return rec("y", 0.1, 2.0, [srcv], [], lambda e: e.dma_start(dst, res(srcv)), "st%d" % k, 16)
@@ -388,12 +451,18 @@ def rank_program(g, core, T, topo):
     def add_into(dst, src, k):
         return rec("g", 1.0, 3.0, [src], [dst], lambda e: e.dma_start(res(dst), res(src), accum_op=A.add), "ad%d" % k, 16)
 
-    last = {}
+    last, turn = {}, [0]
 
     def chain(name, i):
         if name in last:
             ops[i][3].add((last[name], False))
         last[name] = i
+
+    def gather(which, out, src):
+        if which in ONV:
+            cp(out, src)
+        else:
+            chain("s", act(out, src))
 
     def hv(name, c, w=128):
         return v(name, w * c, w * c + w)
@@ -415,7 +484,7 @@ def rank_program(g, core, T, topo):
 
     load("y", v("NBi", 0, 640), T.nbr[:, 0:640], 0)
     load("S", v("z"), T.z0[:], 1)
-    load("S", v("NBi", 640, 1280), T.nbr[:, 640:1280], 2)
+    load("y", v("NBi", 640, 1280), T.nbr[:, 640:1280], 2)
     load("y", v("KK0", 0, 1280), T.ring[:], 3)
     load("S", v("thI", 0, 1), T.thr[:], 4)
     load("y", v("X", 0, 2048), T.mat[:], 5)
@@ -426,7 +495,7 @@ def rank_program(g, core, T, topo):
     iota(v("D1"), [[-1, 256]], 256, 1)
     iota(v("D3"), [[0, 8], [1, 16]], 0, 0)
     iota(v("ic"), [[1, 16]], 0, 0)
-    iota(v("t1"), [[128, 2], [0, 8]], 1280, 1)
+    iota(v("t1"), [[16, 16]], 1280, 0)
     iota(v("T1"), [[1, 1280]], 0, 0)
     ts(v("pi15"), v("PI"), 15, A.bitwise_and)
     cp(v("pcol"), v("pi15"))
@@ -438,15 +507,15 @@ def rank_program(g, core, T, topo):
     ts(v("G16b"), v("D2"), 8.0, A.is_equal)
     g8 = v("G16b", 0, 128, 16)
     for name, x in (("G8f", 1), ("G8b", 1), ("G8s", WS), ("G8m", 2 * SB), ("G8x", -SB), ("G8a", SB)):
-        ts(v(name), g8, float(x), A.mult)
-    fill(v("cK"), (FAIL - SB) / 128.0)
+        act(v(name), g8, scale=float(x))
+    act(v("cK"), v("On", 0, 8), scale=(FAIL - SB) / 128.0)
     ts(v("D15"), v("D1"), 15, A.bitwise_and)
     ts(v("DM"), v("D15"), 0.0, A.is_equal)
-    ts(v("DMB"), v("DM", 0, 128), 4096.0, A.mult)
+    act(v("DMB"), v("DM", 0, 128), scale=4096.0)
     ts(v("RN"), v("D3"), 0.0, A.is_equal, -BIG, A.mult)
     ts(v("RS"), v("RN"), float(SB), A.add)
     ts(v("Ib"), v("D1", 0, 128), 256.0, A.is_equal)
-    ts(v("nIb"), v("Ib"), -1.0, A.mult)
+    act(v("nIb"), v("Ib"), scale=-1.0)
     cp(v("bl"), v("ic"))
     ts(v("pb"), v("pcol"), 811.0, A.mult)
     ts(v("pc"), v("pb"), SB - 1, A.bitwise_and)
@@ -454,33 +523,32 @@ def rank_program(g, core, T, topo):
     ts(v("Tri"), v("D1", 0, 128), 256.0, A.is_lt)
     ts(v("row"), v("Ib"), 512.0, A.mult)
     tt(v("Tri"), v("Tri"), v("row"), A.add)
-    for name, x in (("fb", -15.0), ("nR1", -R1), ("pR1", R1), ("nfb", 2.0 ** 18), ("h18", -2.0 ** 18), ("C256", 256.0)):
-        fill(v(name), x)
+    for name, x in (("fb", -15.0), ("nR1", -R1), ("pR1", R1), ("nfb", 2.0 ** 18), ("h18", 2.0 ** 18), ("C256", 256.0),
+                    ("pR16", R16), ("nR16", -R16), ("h10", 1024.0)):
+        act(v(name), v("On", 0, count(v(name))), scale=x)
     for i in range(2):
         fill(v("KK%d" % i, 1280, REM), 0.0)
     fill(v("NBi", 1280, REM), 0)
-    ts(v("d04"), v("t1"), 8192.0, A.mult)
+    ts(v("dOh"), v("t1"), v("pcol"), A.add)
     for c in range(2):
         ts(v("d0%d" % c), v("lcol"), 1280.0 + 128 * c, A.add)
     ts(v("pb"), v("PI"), 4, A.arith_shift_right, 1, A.bitwise_and)
     cp(v("odd"), v("pb"))
-    ts(v("even"), v("odd"), -1.0, A.mult, 1.0, A.add)
-    if OPT["cd"] == "v":
-        ts(v("neven"), v("even"), -2.0, A.mult)
-        ts(v("nodd"), v("odd"), -2.0, A.mult)
     fill(v("rw"), 0.5)
     scan(v("row"), v("rw"), v("On"), A.mult, 2.0 ** 64, A.mult)
     tt(v("rw"), v("row"), v("Ib"), A.mult)
     op("v", "tensor_reduce", out=v("wcol"), in_=v("rw"), axis=AxisListType.X, op=A.add)
-    ts(v("w25"), v("wcol"), 2.5, A.mult)
-    tt(v("rw", 0, 16), v("row", 0, 16), v("DM", 0, 16), A.mult)
-    op("v", "tensor_reduce", out=v("p2"), in_=v("rw", 0, 16), axis=AxisListType.X, op=A.add)
-    ts(v("p2"), v("p2"), 2.0 ** -63, A.mult)
-    ts(v("dcol"), v("p2"), 0.5, A.mult, -0.5, A.add)
+    act(v("w25"), v("wcol"), scale=2.5)
+    act(v("sgn"), v("DM", 0, 16), scale=-2.0, bias=1.0)
+    act(v("CT", 0, 1), v("On", 0, 1))
+    for r in range(11):
+        w = min(2 ** r, 1280 - 2 ** r)
+        act(v("CT", 2 ** r, 2 ** r + w), v("CT", 0, w), scale=v("sgn", r, r + 1))
     for s in sorted(set(x for r in PS for x in r)):
-        ts(v("NG%d" % s), v("G16b"), -float(SB), A.mult)
-        if s:
-            fill(v("NG%d" % s, s - 1, 128, s), 0.0)
+        if s < 16:
+            act(v("NG%d" % s), v("G16b"), scale=-float(SB))
+            for x, o in ROWS[s]:
+                fill(v("NG%d" % s, o, 128, x), 0.0)
     ts(v("th"), v("thI", 0, 1), 6, A.arith_shift_right)
     ts(v("tl"), v("thI", 0, 1), 63, A.bitwise_and)
     ts(v("Q", 0, 1), v("th"), -64.0 * SB, A.mult)
@@ -497,20 +565,22 @@ def rank_program(g, core, T, topo):
     tt(v("RD", 1, 128), v("b6", 257, 384), v("TH", 0, 127), A.subtract)
     fill(v("RD", 0, 128, 16), BIG)
     for c in range(2):
-        iota(v("V2"), [[10, 128]], 1 + 1280 * c, 0)
-        act(MI(c, 2), v("V2"))
+        iota(hv("V2", c), [[10, 128]], 1 + 1280 * c, 0)
+        if not KP[0][c]:
+            act(MI(c, 2), hv("V2", c))
         act(KV(c, 2), hv("z", c))
 
     def send_rings(t):
-        kk = "KK%d" % (t % 2)
+        kk = "KK%d" % min(t, 1)
         for h in range(2):
             src = v(kk, 512 * h, 512 * h + 512)
 
             def emit(e, h=h, src=src):
                 remote(g, topo, core, rl[h], T["hand%d" % t][:], res(src), T.sem["ha%d" % t], T.sem["ks%d%d" % (t, h)], 8)
-            i = rec("g", 0.3, 4.0, [src], [], emit, "ks%d%d" % (t, h), 8)
-            lo = REM + 1024 * t + 512 * h
-            land(v(kk, lo, lo + 512), "ki%d%d" % (t, h), 8, i, 8.0)
+            i = rec("g", 0.3 if t or h else 2.5, 4.0, [src], [], emit, "ks%d%d" % (t, h), 8)
+            chain("send", i)
+            lo = rem(t) + 512 * h
+            land(v(kk, lo, lo + 512), "ki%d%d" % (t, h), 8, i, ORD["hop"])
 
     def send_revoked(t):
         src = v("rS%d" % t, 0, 1)
@@ -521,7 +591,7 @@ def rank_program(g, core, T, topo):
         land(v("cI%d" % t, 0, 1), "ri%d" % t, 8, i, 5.0)
 
     def K(t):
-        return v("KK%d" % (t % 2), 0, 1280)
+        return v("KK%d" % min(t, 1), 0, 1280)
 
     def vo(t, c):
         b = 16 * (t % 2)
@@ -535,7 +605,11 @@ def rank_program(g, core, T, topo):
     def first(t, c):
         u = MI(c, 0)
         group(u, [(v("Ib"), v("C%d" % t)), (v("G16b"), hv("z", c))])
-        ts(hv("r16", c), u, R16, A.add, -R16, A.add)
+        if OPT["r16"] == "v":
+            ts(hv("r16", c), u, R16, A.add, -R16, A.add)
+        else:
+            act(hv("r17", c), u, AF.Identity, bias=v("pR16"))
+            act(hv("r16", c), hv("r17", c), AF.Identity, bias=v("nR16"))
         if t:
             tt(hv("oh", c), u, hv("r16", c), A.is_equal)
             tt(hv("mB", c), ind(tab, vo(t, c)), hv("oh", c), A.mult)
@@ -552,49 +626,49 @@ def rank_program(g, core, T, topo):
         if t < RO - 1:
             mm(MI(c, 1), v("G16b"), hv("mB", c))
 
+    def holes(out, keys):
+        if OPT["mh"] == "v":
+            ts(out, keys, 0.0, A.is_equal, 1024.0, A.mult)
+        else:
+            act(out, keys, AF.Relu, scale=-1024.0, bias=v("h10"))
+
     def second(t, c):
-        old = K(max(t - 1, 0))
+        old = K(0)
         both, rawv, rawn = hv("KN", c, 256), v("KN", 256 * c, 256 * c + 128), v("KN", 256 * c + 128, 256 * c + 256)
         act(rawn, ind(old, v("nO", 16 * c, 16 * c + 8)))
         if t:
             act(rawv, ind(old, vo(t, c)))
-            ts(hv("mh", c, 256), both, 0.0, A.is_equal, -1024.0, A.mult)
-            parts = [both, hv("mh", c, 256)]
-            for i, col in ((0, "cI%d" % (t - 2)), (1, "rS%d" % (t - 1))):
-                if t - 2 + i >= 0:
-                    ts(hv("m%d" % i, c, 256), both, v(col, 0, 1), A.is_equal, -1024.0, A.mult)
-                    parts.append(hv("m%d" % i, c, 256))
-            group(KV(c, 0, 256), [(v("Ib"), x) for x in parts])
+            holes(hv("mh", c, 256), both)
+            ts(hv("m1", c, 256), both, v("rS%d" % (t - 1), 0, 1), A.is_equal, 1024.0, A.mult)
+            group(KV(c, 0, 256), [(v("Ib"), both), (v("nIb"), hv("mh", c, 256)), (v("nIb"), hv("m1", c, 256))])
         else:
-            ts(v("mh", 256 * c, 256 * c + 128), fifth("KK0", c), 0.0, A.is_equal, -1024.0, A.mult)
-            ts(v("mh", 256 * c + 128, 256 * c + 256), rawn, 0.0, A.is_equal, -1024.0, A.mult)
-            mm(KV(c, 0, 256), v("Ib"), hv("mh", c, 256), True, False)
+            holes(v("mh", 256 * c, 256 * c + 128), fifth("KK0", c))
+            holes(v("mh", 256 * c + 128, 256 * c + 256), rawn)
+            mm(KV(c, 0, 256), v("nIb"), hv("mh", c, 256), True, False)
             mm(KV(c, 0), v("Ib"), fifth("KK0", c), False, False)
             mm(KV(c, 1), v("Ib"), rawn, False, True)
         for b in range(128 * c, 128 * c + 128, GW):
-            chain("s", act(v("Kc", 16 * b, 16 * (b + GW)), ind(old, v("BnL", b, b + GW))))
+            gather(("K", t, b // 64), v("Kc", 16 * b, 16 * (b + GW)), ind(old, v("BnL", b, b + GW)))
         tt(hv("evn", c), KV(c, 0), rawn, A.is_equal)
         mm(SM(c, 1), hv("evn", c), v("G8b"))
         ts(hv("dr", c, 8), SM(c, 1), 3.0, A.is_ge, float(DIR - FAIL + SB), A.mult)
         tt(hv("kn", c, 8), SM(c, 0), hv("dr", c, 8), A.add)
-        for q in range(2):
-            for eq, b in (("eqV", 0), ("eqN", 128)):
-                for k in range(16):
-                    s = (2048 * c + 1024 * q + k, 2048 * c + 1024 * q + 1024, 16)
-                    chain("v", tt(v(eq, *s), v("b%d" % c, b + 64 * q, b + 64 * q + 64), v("Kc", *s), A.is_equal))
+        steps = [(q, e) for q in range(2) for e in range(2)]
+        if EQ[t][c]:
+            steps = [(q, e) for e in range(2) for q in range(2)]
+        for q, e in steps:
+            for k in range(16):
+                s = (2048 * c + 1024 * q + k, 2048 * c + 1024 * q + 1024, 16)
+                b = 128 * e + 64 * q
+                chain("v", tt(v(("eqV", "eqN")[e], *s), v("b%d" % c, b, b + 64), v("Kc", *s), A.is_equal))
 
     def third(t, c):
-        act(hv("hole", c), KV(c, 0), AF.Relu, scale=-1.0)
-        if t:
-            act(hv("Kvr", c), KV(c, 0), AF.Relu)
-        for k0, eq in enumerate(("eqV", "eqN")):
-            mm(SC(c, k0), hv("BnH", c), v("Ib"), True, False)
+        for o, eq in ((SC(c, 0), "eqV"), (MI(c, 0), "eqN")):
+            mm(o, hv("BnH", c), v("Ib"), True, False)
             for k in range(16):
-                mm(v("b%d" % (2 + c), 128 * k0 + k, 128 * k0 + 128, 16), v(eq, 2048 * c + k, 2048 * c + 2048, 16), v("G8s"),
-                   False, k == 15)
-            if not k0:
-                act(hv("cV", c), SC(c, 0))
-        tt(hv("mn", c), SC(c, 1), hv("cV", c), A.min)
+                mm(v(o[1], k, 128, 16), v(eq, 2048 * c + k, 2048 * c + 2048, 16), v("G8s"), False, k == 15)
+        act(hv("cV", c), SC(c, 0))
+        tt(hv("mn", c), MI(c, 0), hv("cV", c), A.min)
         scan(hv("sc2", c), v("RS"), hv("mn", c), A.max)
         tt(hv("Wi", c, 8), v("sc2", 128 * c + 15, 128 * c + 128, 16), hv("kn", c, 8), A.max)
         ts(hv("wT", c, 8), hv("Wi", c, 8), SB - 1, A.bitwise_and)
@@ -603,117 +677,162 @@ def rank_program(g, core, T, topo):
         w = vo(t + 1, c)
         cp(w, SM(c, 2))
         act(hv("Kw", c), ind(K(t), w))
-        tt(hv("kp", c), MI(c, 2), hv("Kw", c), A.mult)
+        if KP[t][c]:
+            tt(hv("kp", c), ind(K(t), w), hv("V2", c), A.mult)
+        else:
+            tt(hv("kp", c), MI(c, 2), hv("Kw", c), A.mult)
         ts(hv("k2", c), hv("kp", c), 2, A.arith_shift_right, SB - 1, A.bitwise_and)
         ts(hv("PL", c), hv("k2", c), v("c0"), A.add, float(t), A.add)
-        s = PS[t][c]
+        act(hv("hole", c), KV(c, 0), AF.Relu, scale=-1.0)
+        if OPT["hz"] == "v":
+            ts(hv("hz", c), hv("Kw", c), 0.0, A.is_equal, 2.0 ** 18, A.mult)
+        else:
+            act(hv("hz", c), hv("Kw", c), AF.Relu, scale=-2.0 ** 18, bias=v("h18"))
+        tt(hv("pr", c), KV(c, 2), hv("Kw", c), A.mult)
+        if not c:
+            mm(WR(0, 8), hv("pr", c), v("G8f"))
+
+    def next_nodes(t, c):
+        w = vo(t + 1, c)
+        act(hv("Vn", c), ind(v("T1"), w))
+        act(hv("V2", c) if KP[t + 1][c] else MI(c, 2), hv("Vn", c), scale=2.0, bias=1.0)
+        if t:
+            tt(KV(c, 3), MI(c, 1), hv("Vn", c), A.subtract)
+            tt(hv("ohd", c), KV(c, 3), hv("oh", c), A.mult)
+        else:
+            tt(hv("dl", c), MI(c, 1), hv("Vn", c), A.subtract)
+            tt(KV(c, 3), KV(c, 3), hv("dl", c), A.mult)
+
+    def material(t, c):
         for q in range(2):
             lo = 2048 * c + 1024 * q
             for b in range(lo // 16, lo // 16 + 64, GW):
-                chain("s", act(v("Xc", 16 * b, 16 * (b + GW)), ind(v("X"), v("PL", b, b + GW))))
-            if s:
-                m, bank = 16 // s, "b%d" % (6 + q)
-                mm(v(bank, 0, 64 * m), v("Ib"), v("Xc", lo + s - 1, lo + 1024, s), True, False)
+                gather(("X", t, b // 64), v("Xc", 16 * b, 16 * (b + GW)), ind(v("X"), v("PL", b, b + GW)))
+            for k, (s, o) in enumerate(ROWS[PS[t][c]]):
+                turn[0] += 1
+                m, bank, at = 16 // s, "b%d" % (6 + turn[0] % 2), 2048 * c + 1024 * k
+                mm(v(bank, 0, 64 * m), v("Ib"), v("Xc", lo + o, lo + 1024, s), True, False)
                 for i in range(m):
                     mm(v(bank, i, 64 * m, m), v("nIb"), v("z", lo // 16, lo // 16 + 64), False, i == m - 1)
-                act(v("ab", 1024 * c + 64 * m * q, 1024 * c + 64 * m * (q + 1)), v(bank, 0, 64 * m), AF.Abs)
+                act(v("ab", at + 64 * m * q, at + 64 * m * (q + 1)), v(bank, 0, 64 * m), AF.Abs)
             for p in range(16):
-                if not s or p % s != s - 1:
+                if not [s for s, o in ROWS[PS[t][c]] if p % s == o]:
                     chain("v", tt(v("mx", lo + p, lo + 1024, 16), v("b%d" % c, 256 + 64 * q, 320 + 64 * q),
                                   v("Xc", lo + p, lo + 1024, 16), A.max))
-        if OPT["hz"] == "v":
-            ts(hv("hz", c), hv("Kw", c), 0.0, A.is_equal, -2.0 ** 18, A.mult)
-        tt(hv("pr", c), KV(c, 2), hv("Kw", c), A.mult)
-        mm(WR(8 * c, 8), hv("pr", c), v("G8f"))
-        if t < RO - 1:
-            act(hv("Vn", c), ind(v("T1"), w))
-            act(MI(c, 2), hv("Vn", c), scale=2.0, bias=1.0)
-            if t:
-                tt(KV(c, 3), MI(c, 1), hv("Vn", c), A.subtract)
-                tt(hv("ohd", c), KV(c, 3), hv("oh", c), A.mult)
-            else:
-                tt(hv("dl", c), MI(c, 1), hv("Vn", c), A.subtract)
-                tt(KV(c, 3), KV(c, 3), hv("dl", c), A.mult)
 
     def fourth(t, c):
         dT, s, lo = SC(c, 2), PS[t][c], 2048 * c
         mm(dT, v("LR", 128, 256, 1, 0, 4), v("LR", 0, 128, 1, 0, 4), True, False)
-        for p in range(16):
+        for p in sorted(range(16), key=lambda r: len([x for x, y in ROWS[s] if r % x == y])):
             o = v("b%d" % (2 + c), 256 + p, 384, 16)
-            if s and p % s == s - 1:
-                m = 16 // s
-                mm(o, v("ab", 1024 * c + p // s, 1024 * c + 128 * m, m), v("G8a"), False, False)
+            part = [(k, x) for k, (x, y) in enumerate(ROWS[s]) if p % x == y]
+            if part:
+                at, m = lo + 1024 * part[0][0], 16 // part[0][1]
+                mm(o, v("ab", at + p // part[0][1], at + 128 * m, m), v("G8a"), False, p == 15 and s == 16)
             else:
                 mm(o, v("mx", lo + p, lo + 2048, 16), v("G8m"), False, False)
                 mm(o, v("Xc", lo + p, lo + 2048, 16), v("G8x"), False, False)
-        mm(dT, hv("z", c), v("NG%d" % s), False, True)
-        scan(hv("sd", c), v("RD"), dT, A.min)
-        act(hv("nf", c), dT, AF.Relu, scale=2.0 ** 19, bias=v("nfb"))
+        if s < 16:
+            mm(dT, hv("z", c), v("NG%d" % s), False, True)
+        for step in ((0, 1), (1, 0))[c]:
+            if step:
+                act(hv("nf", c), dT, AF.Relu, scale=2.0 ** 19, bias=v("nfb"))
+            else:
+                scan(hv("sd", c), v("RD"), dT, A.min)
         cp(hv("pi", c, 8), v("sd", 128 * c + 15, 128 * c + 128, 16))
         ts(hv("pi2", c, 8), hv("pi", c, 8), SB - 1, A.bitwise_and)
         tt(hv("Ap", c), ind(hv("pi2", c, 8), v("bl", 0, 8)), v("DM", 0, 128), A.mult)
         mm(SM(c, 3), hv("Ap", c), v("G8b"))
         do = v("dO", 16 * c, 16 * c + 8)
         cp(do, SM(c, 3))
-        tt(hv("zx", c), ind(v("Xc", lo, lo + 2048), do), hv("z", c), A.add)
-        if OPT["za"] == "v":
-            ts(hv("za", c), hv("zx", c), HALF, A.mult, R1, A.add)
+        zx = hv("zx", c)
+        if OPT["zx"] == "v":
+            tt(zx, ind(v("Xc", lo, lo + 2048), do), hv("z", c), A.add)
         else:
-            act(hv("za", c), hv("zx", c), AF.Identity, scale=HALF, bias=v("pR1"))
+            zx = SC(c, 1)
+            act(hv("evn", c), ind(v("Xc", lo, lo + 2048), do))
+            group(zx, [(v("Ib"), hv("z", c)), (v("Ib"), hv("evn", c))])
+        if OPT["za"] == "v":
+            ts(hv("za", c), zx, HALF, A.mult, R1, A.add)
+        else:
+            act(hv("za", c), zx, AF.Identity, scale=HALF, bias=v("pR1"))
         if t == RO - 1:
             act(hv("zF", c), hv("za", c), AF.Identity, bias=v("nR1"))
             store(T.yz[:, 128 * c:128 * c + 128], hv("zF", c), c)
         else:
             act(hv("z", c), hv("za", c), AF.Identity, bias=v("nR1"))
             act(KV(c, 2), hv("za", c), AF.Identity, bias=v("nR1"))
-        group(MI(c, 1), [(v("Ib"), hv("Kw", c)), (v("Ib"), hv("hz", c)), (hv("nf", c), v("nIb"))])
+        group(MI(c, 1), [(v("Ib"), hv("Kw", c)), (v("nIb"), hv("hz", c)), (hv("nf", c), v("nIb"))])
         scan(hv("cs", c), v("C256"), MI(c, 1), A.max, v("cs", 127, 128) if c else -2.0 ** 20)
 
+    def active(t, c):
+        f, y = hv("F", c, 8), WR(16 + 8 * c, 8)
+        ts(f, hv("Wi", c, 8), float(FAIL), A.is_lt)
+        ts(hv("D", c, 8), hv("Wi", c, 8), float(DIR), A.is_ge, 1024.0, A.mult)
+        mm(y, v("Tri"), f, not c, False)
+        mm(y, v("Ib"), hv("D", c, 8), False, True)
+        ts(hv("aw", c, 8), y, 512.0 + CAP, A.is_lt, v("wcol"), A.mult)
+        ts(hv("aB", c, 8), y, 512.0 + CAP, A.is_lt, 2.0 ** 70, A.mult)
+        for gr in range(8):
+            e = 384 * gr + 256 * c
+            mm(WR(32 + 8 * c + gr, 1), v("E", e, e + 128), v("aw", 8 * c + gr, 8 * c + gr + 1))
+        if not c:
+            mm(WR(24, 8), v("On"), f, True, False)
+            for gr in range(8):
+                mm(WR(24 + gr, 1), v("E", 384 * gr + 128, 384 * gr + 256), v("aB", gr, gr + 1), False, False)
+
     def writers(t):
-        kk = "KK%d" % (t % 2)
-        ts(v("F"), v("Wi"), float(FAIL), A.is_lt)
-        ts(v("D"), v("Wi"), float(DIR), A.is_ge, 1024.0, A.mult)
-        y = WR(16)
-        mm(y, v("Tri"), v("F"), True, False)
-        mm(WR(24, 8), v("On"), v("F", 0, 8), False, False)
-        mm(y, v("Ib"), v("D"), False, True)
+        kk = "KK%d" % min(t, 1)
+        if t:
+            come = v("cI%d" % (t - 1), 0, 1)
+            ts(v("ncome"), come, -1.0, A.mult)
+            ts(K(0), K(t), come, A.is_equal, v("ncome"), A.mult)
+            add_into(K(0), K(t), 1 + t)
+        if t:
+            active(t, 1)
+            ts(v("wf"), WR(32), v("w25"), A.is_lt)
+            tt(v("av"), v("aB"), v("vmd"), A.mult)
+        else:
+            ts(v("F"), v("Wi"), float(FAIL), A.is_lt)
+            ts(v("D"), v("Wi"), float(DIR), A.is_ge, 1024.0, A.mult)
+            mm(WR(16), v("Tri"), v("F"), True, False)
+            mm(WR(24, 8), v("On"), v("F", 0, 8), False, False)
+            mm(WR(16), v("Ib"), v("D"), False, True)
+            ts(v("act"), WR(16), 512.0 + CAP, A.is_lt)
+        mm(WR(8, 8), hv("pr", 1), v("G8f"))
         cp(v("hi"), WR(0))
         ts(v("h2"), v("hi"), 1023, A.bitwise_and)
-        ts(v("hb"), v("h2"), float(REM + 1024 * t), A.add)
+        ts(v("hb"), v("h2"), float(rem(t)), A.add)
         tt(v("hc"), v("hb"), v("F"), A.mult)
         tt(v("src"), v("hc"), v("wT"), A.max)
         if t:
-            ts(v("aw"), y, 512.0 + CAP, A.is_lt, v("wcol"), A.mult)
-            ts(v("aB"), y, 512.0 + CAP, A.is_lt, 2.0 ** 70, A.mult)
-            tt(v("av"), v("aB"), v("vmd"), A.mult)
-            tt(v("hd"), v("src"), v("d04"), A.add)
-            for gr in range(8):
-                e = 384 * gr
-                mm(WR(32 + gr, 1), v("E", e, e + 128), v("aw", gr, gr + 1))
-                group(WR(40 + gr, 1), [(v("E", e + 128, e + 256), v("aB", gr, gr + 1)),
-                                       (v("E", e + 256, e + 384), v("aw", 8 + gr, 9 + gr))])
-            ts(v("wf"), WR(32), v("w25"), A.is_lt)
             tt(v("w2"), v("wf"), v("av"), A.mult)
-            tt(v("word"), v("w2"), v("hd"), A.add)
-            tt(v("Aq"), ind(v("word"), v("bl")), v("DM"), A.mult)
+            tt(v("Aqh"), ind(v("w2"), v("bl")), v("DM"), A.mult)
+            mm(WR(80), v("Ib"), v("dOh"), True, False)
+            for c in range(2):
+                mm(WR(80 + 8 * c, 8), hv("Aqh", c), v("G8b"), False, c == 1)
+            cp(v("scO"), WR(80))
+            tt(v("Aq"), ind(v("src"), v("bl")), v("DM"), A.mult)
             for c in range(2):
                 mm(WR(48 + 8 * c, 8), hv("Aq", c), v("G8f"))
-            cp(v("qi"), WR(48))
-            ts(v("q1"), v("qi"), 13, A.arith_shift_right)
-            cp(v("scO"), v("q1"))
-            ts(v("q2"), v("qi"), 8191, A.bitwise_and)
-            cp(v("srO"), v("q2"))
+            cp(v("srO"), WR(48))
         else:
-            ts(v("act"), y, 512.0 + CAP, A.is_lt)
             ts(v("hd"), v("src"), -1280.0, A.add)
             tt(v("word"), v("hd"), v("act"), A.mult)
             tt(v("Aqh"), ind(v("word"), v("bl")), v("DM"), A.mult)
             for c in range(2):
                 mm(WR(48 + 8 * c, 8), hv("Aqh", c), v("G8b"))
             ts(v("srO"), WR(48), 1280.0, A.add)
-        tt(v("fm"), ind(v(kk, 0, REM + 1024 * (t + 1)), v("srO")), v("hole"), A.min)
+        if t < RO - 1:
+            mm(WR(64), v("On"), v("F"))
+            act(v("fj"), WR(64), accum_out=v("fs"))
+            next_nodes(t, 1)
+        tt(v("fm"), ind(v(kk, 0, rem(t) + 1024), v("srO")), v("hole"), A.min)
         if t:
-            tt(ind(v(kk, 0, REM), v("scO")), v("fm"), v("Kvr"), A.add)
+            for c in range(2):
+                tt(hv("val", c), KV(c, 0), hv("fm", c), A.max)
+            ts(v("vm"), v("val"), come, A.not_equal)
+            tt(ind(v("KK0", 0, REM), v("scO")), v("val"), v("vm"), A.mult)
         else:
             for c in range(2):
                 tt(fifth(kk, c), KV(c, 0), hv("fm", c), A.max)
@@ -722,38 +841,20 @@ def rank_program(g, core, T, topo):
             tt(v("nb"), ind(tab, v("vO", 16, 32)), v("ohd"), A.subtract)
             cp(ind(v("NBi"), v("scO")), v("nb"))
         if t < RO - 1:
-            mm(WR(64), v("On"), v("F"))
-            act(v("fj"), WR(64), accum_out=v("fs"))
             cp(v("fi"), v("fs"))
             ts(v("fa"), v("fi"), 15, A.bitwise_and)
             for c in range(2):
-                ts(hv("vmd", c, 8), hv("wT", c, 8), v("d0%d" % c), A.subtract, 2.0 ** -57, A.mult)
-        if t:
-            come = v("cI%d" % (t - 1), 0, 1)
-            ts(v("ncome"), come, -1.0, A.mult)
-            if t < RO - 1:
-                ts(K(t + 1), K(t), come, A.is_equal, v("ncome"), A.mult)
-                add_into(K(t + 1), K(t), 1)
-            else:
-                ts(v("NM2"), K(t), come, A.is_equal, v("ncome"), A.mult)
-                add_into(K(t), v("NM2"), 3)
+                ts(hv("vmd", c, 8), hv("wT", c, 8), v("d0%d" % c), A.subtract, 2.0 ** -70, A.mult)
 
-    def same_node():
-        ts(v("ci"), v("Vn"), v("p2"), A.mult, v("dcol"), A.add)
-        ts(v("cb"), v("ci"), 1, A.bitwise_and)
-        if OPT["cd"] == "v":
-            ts(v("cdE"), v("cb"), v("neven"), A.mult, v("even"), A.add)
-            ts(v("cdO"), v("cb"), v("nodd"), A.mult, v("odd"), A.add)
-        else:
-            ts(v("code"), v("cb"), -2.0, A.mult, 1.0, A.add)
-            act(v("cdE"), v("code"), scale=v("even"))
-            act(v("cdO"), v("code"), scale=v("odd"))
+    def same_node(t):
+        act(v("code"), ind(v("CT"), v("vO", 16 * (t % 2), 16 * (t % 2) + 16)))
+        act(v("cdO"), v("code"), scale=v("odd"))
         for gr in range(8):
             lo = 32 * (gr // 2)
-            m = "cdO" if gr % 2 else "cdE"
+            m, hi = ("cdO", lo + 32) if gr % 2 else ("code", lo + 16)
             b = "b%d" % (6 + gr % 2)
-            mm(v(b, 0, 256), v(m, 0, 128, 1, lo, lo + 32), v(m, 0, 256, 1, lo, lo + 32))
-            mm(v(b, 256, 384), v(m, 128, 256, 1, lo, lo + 32), v(m, 128, 256, 1, lo, lo + 32))
+            mm(v(b, 0, 256), v(m, 0, 128, 1, lo, hi), v(m, 0, 256, 1, lo, hi))
+            mm(v(b, 256, 384), v(m, 128, 256, 1, lo, hi), v(m, 128, 256, 1, lo, hi))
             act(v("E", 384 * gr, 384 * gr + 384), v(b, 0, 384), AF.Relu, bias=v("fb"))
 
     def revoke(t):
@@ -770,36 +871,29 @@ def rank_program(g, core, T, topo):
         rv = v("rS%d" % t, 0, 1)
         cp(rv, v("rva"))
         send_revoked(t)
-        if t:
-            ts(v("rvE"), rv, v("cI%d" % (t - 1), 0, 1), A.not_equal, rv, A.mult)
-            rv = v("rvE")
-        ts(v("nrv"), rv, -1.0, A.mult)
-        if t:
-            ts(v("NM1"), K(t), rv, A.is_equal, v("nrv"), A.mult)
-            add_into(K(t + 1), v("NM1"), 2)
-        else:
-            ts(K(t + 1), K(t), rv, A.is_equal, v("nrv"), A.mult)
-            add_into(K(t + 1), K(t), 0)
+        ts(v("nrv"), v("rva"), -1.0, A.mult)
+        ts(K(t + 1), K(0), rv, A.is_equal, v("nrv"), A.mult)
+        add_into(K(t + 1), K(0), t)
         send_rings(t + 1)
         ts(v("nfb"), v("fa"), -2.0 ** 30, A.mult, 2.0 ** 18, A.add)
 
     send_rings(0)
-    for c in range(2):
-        first(0, c)
+    steps = [("first", first, 0, 0), ("first", first, 0, 1)]
     for t in range(RO):
-        for c in range(2):
-            second(t, c)
-        for c in range(2):
-            third(t, c)
-        writers(t)
-        fourth(t, 0)
-        if t < RO - 1:
-            first(t + 1, 0)
-        fourth(t, 1)
-        revoke(t)
-        if t < RO - 1:
-            first(t + 1, 1)
-            same_node()
+        more = t < RO - 1
+        steps += [("second", second, t, 0), ("third", third, t, 0), ("second", second, t, 1)]
+        steps += [("same", same_node, t)] * (t > 0)
+        steps += [("third", third, t, 1), ("material", material, t, 0)]
+        steps += [("next", next_nodes, t, 0)] * more
+        steps += [("active", active, t, 0)] * (t > 0)
+        steps += [("writers", writers, t), ("fourth", fourth, t, 0), ("material", material, t, 1)]
+        steps += [("first", first, t + 1, 0)] * more
+        steps += [("fourth", fourth, t, 1), ("revoke", revoke, t)]
+        steps += [("first", first, t + 1, 1)] * more
+    for s in steps:
+        STEP[0] = "%s%s" % (s[0], s[2:])
+        s[1](*s[2:])
+    STEP[0] = ""
     if not SEQ:
         SEQ.append(order(ops))
     issue(g, T, ops, SEQ[0])
@@ -821,8 +915,8 @@ def hand_on(g, core, T, topo):
             if core in rl:
                 h = rl.index(core)
                 g.wait_ge(T.sem["ha%d" % t], 8)
-                lo = REM + 1024 * t + 512 * h
-                remote(g, topo, core, below, T["KK%d" % (t % 2)][:, lo:lo + 512], T["hand%d" % t][:],
+                lo = rem(t) + 512 * h
+                remote(g, topo, core, below, T["KK%d" % min(t, 1)][:, lo:lo + 512], T["hand%d" % t][:],
                        T.sem["ki%d%d" % (t, h)], T.sem["hs%d" % t], 8)
         for t in range(RO):
             if core in rl:

@@ -22,13 +22,13 @@ FAIL, DIR = 51 * SB, 290 * SB
 
 F32 = dict(G8f=8, RN=128, RS=128, RD=128, TH=128, T1=1280, r16=256, sc=256, dr=16, kn=16, cV=256, mn=256, sc2=256, Vn=256, V2=256,
            pr=256, zx=256, za=256, sd=256, cs=256, dl=256, ohd=256, zF=256, row=128, rw=128, pcol=1, p2=1, dcol=1, odd=1, even=1,
-           neven=1, nodd=1, c0=1, wcol=1, w25=1, nrv=1, rvE=1, ncome=1, fs=1, fj=16, d04=16, d00=1, d01=1, vmd=16, av=16, hd=16,
+           neven=1, nodd=1, c0=1, wcol=1, w25=1, fs=1, fj=16, d04=16, d00=1, d01=1, vmd=16, av=16, hd=16,
            wf=16, hb=16, hc=16, src=16, w2=16, word=16, t1=16, Aq=256, p5=1, fb=1, nR1=1, pR1=1, nfb=1, rb=1, lcol=1, h18=1, sgn=16,
            r17=256, pR16=1, nR16=1, h10=1, xb=256)
 BF = dict(Ib=128, nIb=128, G16b=128, G8b=8, G8s=8, G8m=8, G8x=8, G8a=8, cK=8, Tri=128, On=128, DM=256, DMB=128, C0=128, C1=128,
           C2=128, NG0=128, NG4=128, NG8=128, NG12=128, CT=1280, Q=16, LR=256, C256=128, z=256, KN=512, Kw=256, evn=256, mh=512, m0=512, m1=512,
           Kvr=256, hz=256, hole=256, fm=256, code=256, cdE=256, cdO=256, oh=256, nf=256, F=16, D=16, act=16, aw=16, aB=16,
-          val=256, vm=256)
+          val=256, vm=256, NM=1280, nrv=1, ncome=1)
 H16 = dict(mB=256, BnH=256, Aw=256, Ap=256, Aqh=256, dOh=16)
 I32 = dict(PI=1, pi15=1, pb=1, pc=1, D1=256, D15=256, D2=128, D3=128, ic=16, iv=16, kp=256, k2=256, pi=16, pi2=16, Wi=16, wT=16,
            hi=16, h2=16, qi=16, q1=16, q2=16, rvi=1, rva=1, fi=1, fa=1, ci=256, cb=256, nb=256, th=1, tl=1)
@@ -53,7 +53,7 @@ for _d, _n, _t in ((F32, "SF", "float32"), (BF, "SBF", "bfloat16"), (H16, "SH", 
 _BIGB = dict(KK0=(REM + 1024, "bfloat16"), KK1=(REM + 2048, "bfloat16"), X=(4096, "bfloat16"),
              Kc=(4096, "bfloat16"), eqV=(4096, "bfloat16"), eqN=(4096, "bfloat16"), Xc=(4096, "bfloat16"), mx=(4096, "bfloat16"),
              ab=(4096, "bfloat16"), E=(3072, "bfloat16"), NBi=(REM, "int32"), Yk=(1280, "bfloat16"), thI=(8, "int32"),
-             rS0=(8, "float32"), rS1=(8, "float32"), rS2=(8, "float32"), cI0=(8, "float32"), cI1=(8, "float32"))
+             rS0=(8, "bfloat16"), rS1=(8, "bfloat16"), cI0=(8, "bfloat16"), cI1=(8, "bfloat16"))
 for _k in _BIGB:
     SCRATCH[_k] = ("sbuf", [128, _BIGB[_k][0]], _BIGB[_k][1])
     WHERE[_k] = (_k, 0, _BIGB[_k][0])
@@ -63,11 +63,11 @@ for _k in range(8):
 for _k in range(RO):
     SCRATCH["hand%d" % _k] = ("sbuf", [128, 512], "bfloat16")
 for _k in range(RO - 1):
-    SCRATCH["hrv%d" % _k] = ("sbuf", [128, 8], "float32")
+    SCRATCH["hrv%d" % _k] = ("sbuf", [128, 8], "bfloat16")
 SEMAPHORES = ["qv", "qs", "qt", "qg"]
-SEMAPHORES += ["ld%d" % i for i in range(8)] + ["st%d" % i for i in range(6)] + ["ad%d" % i for i in range(4)]
+SEMAPHORES += ["ld%d" % i for i in range(8)] + ["st%d" % i for i in range(6)] + ["ad%d" % i for i in range(4)] + ["cp0", "cp1"]
 for _t in range(RO):
-    SEMAPHORES += ["ks%d0" % _t, "ks%d1" % _t, "ki%d0" % _t, "ki%d1" % _t, "ha%d" % _t, "hs%d" % _t]
+    SEMAPHORES += ["ks%d0" % _t, "ki%d0" % _t, "ki%d1" % _t, "ha%d" % _t, "hs%d" % _t]
 for _t in range(RO - 1):
     SEMAPHORES += ["rs%d" % _t, "ri%d" % _t, "ra%d" % _t, "rl%d" % _t]
 
@@ -75,8 +75,8 @@ CY = 0.00083
 STEP = [""]
 SEQ = []
 INFO = []
-ORD = dict(tail=0.16, hop=5.0, tries=6000, seed=1, slack=0.28, share=0.05, move=3.0, shake=0.15)
-PACE = [(1.2, 1.56, 3.8), (1.0, 1.56, 3.8), (1.45, 1.3, 3.0), (1.1, 2.0, 5.0)]
+ORD = dict(tail=0.16, hop=7.0, tries=6000, seed=1, slack=0.28, share=0.05, move=3.0, shake=0.15, own=0.25, other=1.0)
+PACE = [(1.2, 1.56, 3.8, 0.25), (1.0, 1.56, 3.8, 0.2), (1.45, 1.3, 3.0, 0.22), (1.1, 2.0, 5.0, 0.2)]
 
 
 def rem(t):
@@ -247,7 +247,7 @@ def noter(T):
             if m == "activation":
                 return e.activation(**a)
             return e.iota(**a)
-        i = rec(q, cost(q, m, kw), ORD["tail"], reads, writes, emit)
+        i = rec(q, cost(q, m, kw), 0.0, reads, writes, emit)
         if m == "matmul":
             b = kw["out"][1]
             if b in opened:
@@ -265,7 +265,6 @@ def noter(T):
 def order(ops):
     n = len(ops)
     q = ["s" if o[0] == "S" else o[0] for o in ops]
-    tail = [o[2] for o in ops]
     deps, before = [], [0] * n
     for i in range(n):
         keep, seen = [], 0
@@ -276,8 +275,10 @@ def order(ops):
                 seen |= before[j]
                 before[i] |= before[j] | 1 << j
         deps.append(keep)
-    durs = [[o[1][0] + (o[1][1] * f + o[1][2] * ga + o[1][3] * sc) * CY for o in ops] for f, ga, sc in PACE]
-    fwds = [[[(j, d[j] + (tail[j] if w else 0.0)) for j, w in deps[i]] for i in range(n)] for d in durs]
+    durs = [[o[1][0] + (o[1][1] * p[0] + o[1][2] * p[1] + o[1][3] * p[2]) * CY for o in ops] for p in PACE]
+    tails = [[o[2] or p[3] for o in ops] for p in PACE]
+    tail = tails[0]
+    fwds = [[[(j, d[j] + (x[j] if w else 0.0)) for j, w in deps[i]] for i in range(n)] for d, x in zip(durs, tails)]
     dur, fwd, bwd = durs[0], fwds[0], [[] for _ in range(n)]
     for i in range(n):
         for j, w in deps[i]:
@@ -354,12 +355,12 @@ def order(ops):
             key = -(np.array(place(bwd, -(key + span) + ORD["shake"] * r[2] * draw(n), down)) + np.array(dur))
         key = key + move[step] + ORD["shake"] * r[2] * draw(n)
     INFO[:] = [best[0], best[2], {x: sum(durs[1][i] for i in up if q[i] == x) for x in "vst"}]
-    return best[3]
+    return best[3], [(best[1][i], best[1][i] + durs[1][i]) for i in up]
 
 
-def issue(g, T, ops, seq):
+def issue(g, T, ops, seq, when):
     Q = {"v": g.vector, "s": g.scalar, "t": g.tensor, "g": g, "y": g.sync, "S": g.scalar}
-    total, tok, know = {}, {}, {}
+    total, tok, know, done = {}, {}, {}, {}
     for q in Q:
         know[q] = {}
     know["S"] = know["s"]
@@ -376,6 +377,14 @@ def issue(g, T, ops, seq):
                 s, v, sn = tok[j]
                 if k.get(s, 0) < v and (s not in need or need[s][0] < v):
                     need[s] = (v, sn)
+        for s in need:
+            ahead = ORD["own"] if s == sem else ORD["other"]
+            for j in reversed(done.get(s, [])):
+                if tok[j][1] <= need[s][0]:
+                    break
+                if when[j][1] + ahead <= when[i][0]:
+                    need[s] = tok[j][1:]
+                    break
         for s in sorted(need):
             v, sn = need[s]
             if [o for o in need if o != s and need[o][1].get(s, 0) >= v]:
@@ -391,6 +400,8 @@ def issue(g, T, ops, seq):
         if r is not None:
             r.then_inc(T.sem[sem], inc)
         tok[i] = (sem, total[sem], dict(k))
+        if inc == 1:
+            done.setdefault(sem, []).append(i)
     for s in sorted(total):
         if know["g"].get(s, 0) < total[s]:
             g.wait_ge(T.sem[s], total[s])
@@ -442,14 +453,14 @@ def rank_program(g, core, T, topo):
         return op("v", "tensor_tensor_scan", out=out, data0=a, data1=b, initial=first, op0=o0, op1=o1)
 
     def load(q, dst, src, k):
-        chain("load" + q, rec(q, 0.05, (2.7, 2.5, 4.0, 5.3, 2.7, 7.3, 9.4)[k], [], [dst], lambda e: e.dma_start(res(dst), src),
+        chain("load" + q, rec(q, 0.05, (2.7, 2.5, 5.2, 5.3, 5.4, 7.5, 9.6)[k], [], [dst], lambda e: e.dma_start(res(dst), src),
                               "ld%d" % k, 16))
 
-    def store(dst, srcv, k):
-        return rec("y", 0.1, 2.0, [srcv], [], lambda e: e.dma_start(dst, res(srcv)), "st%d" % k, 16)
+    def store(q, dst, srcv, k):
+        return rec(q, 0.1, 2.0, [srcv], [], lambda e: e.dma_start(dst, res(srcv)), "st%d" % k, 16)
 
     def add_into(dst, src, k):
-        return rec("g", 1.0, 3.0, [src], [dst], lambda e: e.dma_start(res(dst), res(src), accum_op=A.add), "ad%d" % k, 16)
+        return rec("g", 1.0, 4.5, [src], [dst], lambda e: e.dma_start(res(dst), res(src), accum_op=A.add), "ad%d" % k, 16)
 
     last, turn = {}, [0]
 
@@ -484,7 +495,7 @@ def rank_program(g, core, T, topo):
 
     load("y", v("NBi", 0, 640), T.nbr[:, 0:640], 0)
     load("S", v("z"), T.z0[:], 1)
-    load("y", v("NBi", 640, 1280), T.nbr[:, 640:1280], 2)
+    load("S", v("NBi", 640, 1280), T.nbr[:, 640:1280], 2)
     load("y", v("KK0", 0, 1280), T.ring[:], 3)
     load("S", v("thI", 0, 1), T.thr[:], 4)
     load("y", v("X", 0, 2048), T.mat[:], 5)
@@ -571,16 +582,22 @@ def rank_program(g, core, T, topo):
         act(KV(c, 2), hv("z", c))
 
     def send_rings(t):
-        kk = "KK%d" % min(t, 1)
-        for h in range(2):
-            src = v(kk, 512 * h, 512 * h + 512)
+        names = ("KK0", "NM") if t else ("KK0",)
 
-            def emit(e, h=h, src=src):
-                remote(g, topo, core, rl[h], T["hand%d" % t][:], res(src), T.sem["ha%d" % t], T.sem["ks%d%d" % (t, h)], 8)
-            i = rec("g", 0.3 if t or h else 2.5, 4.0, [src], [], emit, "ks%d%d" % (t, h), 8)
-            chain("send", i)
+        def emit(e):
+            parts = []
+            for h in range(2):
+                rid, pid = topo.addr(rl[h], core)
+                eng = topo.engines(core, rl[h])
+                mask = sum(1 << x for x in eng[8 * h:8 * h + 8])
+                parts.append(RemoteDMATransfer(dst_ids=[DstId(rid=rid, pnc=pid)], dma_engine_mask=mask, remote_sem=T.sem["ha%d" % t],
+                                               srcs=[res(v(x, 512 * h, 512 * h + 512)) for x in names],
+                                               dsts=[T["hand%d" % t][:]], alu_op=len(names) - 1))
+            g.remote_dma_fused(parts, local_sem=T.sem["ks%d0" % t])
+        i = rec("g", 0.4 if t else 3.0, 4.0, [v(x, 0, 1024) for x in names], [], emit, "ks%d0" % t, 16)
+        for h in range(2):
             lo = rem(t) + 512 * h
-            land(v(kk, lo, lo + 512), "ki%d%d" % (t, h), 8, i, ORD["hop"])
+            land(v("KK%d" % min(t, 1), lo, lo + 512), "ki%d%d" % (t, h), 8, i, ORD["hop"] + (0 if t else 3))
 
     def send_revoked(t):
         src = v("rS%d" % t, 0, 1)
@@ -758,7 +775,7 @@ def rank_program(g, core, T, topo):
             act(hv("za", c), zx, AF.Identity, scale=HALF, bias=v("pR1"))
         if t == RO - 1:
             act(hv("zF", c), hv("za", c), AF.Identity, bias=v("nR1"))
-            store(T.yz[:, 128 * c:128 * c + 128], hv("zF", c), c)
+            store("Sy"[c], T.yz[:, 128 * c:128 * c + 128], hv("zF", c), c)
         else:
             act(hv("z", c), hv("za", c), AF.Identity, bias=v("nR1"))
             act(KV(c, 2), hv("za", c), AF.Identity, bias=v("nR1"))
@@ -866,15 +883,17 @@ def rank_program(g, core, T, topo):
                 lo, o = 320 * i, v("b%d" % (6 + i % 2), 0, 320)
                 act(o, v("KK0", lo, lo + 320), AF.Abs, scale=256.0, bias=v("rb"))
                 tt(v("Yk", lo, lo + 320), o, v("KK0", lo, lo + 320), A.min)
-                store(T.yk[:, lo:lo + 320], v("Yk", lo, lo + 320), 2 + i)
+                if i % 2:
+                    store("yS"[i // 2], T.yk[:, lo - 320:lo + 320], v("Yk", lo - 320, lo + 320), 2 + i)
             return
         rv = v("rS%d" % t, 0, 1)
         cp(rv, v("rva"))
         send_revoked(t)
         ts(v("nrv"), v("rva"), -1.0, A.mult)
-        ts(K(t + 1), K(0), rv, A.is_equal, v("nrv"), A.mult)
-        add_into(K(t + 1), K(0), t)
+        rec("y", 0.05, 3.5, [K(0)], [K(t + 1)], lambda e: e.dma_start(res(K(t + 1)), res(K(0))), "cp%d" % t, 16)
+        ts(v("NM"), K(0), rv, A.is_equal, v("nrv"), A.mult)
         send_rings(t + 1)
+        add_into(K(t + 1), v("NM"), t)
         ts(v("nfb"), v("fa"), -2.0 ** 30, A.mult, 2.0 ** 18, A.add)
 
     send_rings(0)
@@ -895,8 +914,8 @@ def rank_program(g, core, T, topo):
         s[1](*s[2:])
     STEP[0] = ""
     if not SEQ:
-        SEQ.append(order(ops))
-    issue(g, T, ops, SEQ[0])
+        SEQ.extend(order(ops))
+    issue(g, T, ops, SEQ[0], SEQ[1])
 
 
 def hand_on(g, core, T, topo):

@@ -7,15 +7,15 @@ A = AluOpType
 AF = ActivationFunctionType
 RO, SB, CAP = 3, 2048, 96
 BIG = 1.0e9
-R16, R1 = 1.5 * 2 ** 27, 1.5 * 2 ** 23
+R256, R16, R1 = 1.5 * 2 ** 31, 1.5 * 2 ** 27, 1.5 * 2 ** 23
 HALF = 0.5 - 2.0 ** -11
-PS = [[8, 4], [8, 4], [8, 0]]
+PS = [[0, 0, 0, 0], [0, 0, 0, 0], [0, 0, 0, 0]]
 ROWS = {0: [], 4: [(4, 3)], 8: [(2, 1)], 12: [(2, 1), (4, 0)], 16: [(2, 1), (2, 0)]}
 EQ = [[0, 0], [0, 0], [0, 0]]
 KP = [[0, 0], [0, 0], [0, 0]]
-ONV = []
-GW = 64
-OPT = dict(za="s", hz="s", r16="v", mh="v", zx="v", wr="b4")
+SPLIT = {("X", t, q): "ss" for t in range(RO) for q in (1, 3)}
+SPLIT["K", 0, 0] = "sv"
+OPT = dict(za="s", hz="s", r16="vv", dr="s", nf="vv", mh="s", zx="v", wr="b4", xs=1, cap=1, zh=1, ab=0, sm=1, b67=0, split=(0, 0, 0), evn="v")
 REM = 1536
 WS = 17 * SB
 FAIL, DIR = 51 * SB, 290 * SB
@@ -24,12 +24,12 @@ F32 = dict(G8f=8, RN=128, RS=128, RD=128, TH=128, T1=1280, r16=256, sc=256, dr=1
            pr=256, zx=256, za=256, sd=256, cs=256, dl=256, ohd=256, zF=256, row=128, rw=128, pcol=1, p2=1, dcol=1, odd=1, even=1,
            neven=1, nodd=1, c0=1, wcol=1, w25=1, fs=1, fj=16, d04=16, d00=1, d01=1, vmd=16, av=16, hd=16,
            wf=16, hb=16, hc=16, src=16, w2=16, word=16, t1=16, Aq=256, p5=1, fb=1, nR1=1, pR1=1, nfb=1, rb=1, lcol=1, h18=1, sgn=16,
-           r17=256, pR16=1, nR16=1, h10=1, xb=256)
+           r17=256, pR16=1, nR16=1, h10=1, rq=1, drb=1, f0=1, f1=1, f2=1, f3=1, f4=1, nfc=1)
 BF = dict(Ib=128, nIb=128, G16b=128, G8b=8, G8s=8, G8m=8, G8x=8, G8a=8, cK=8, Tri=128, On=128, DM=256, DMB=128, C0=128, C1=128,
-          C2=128, NG0=128, NG4=128, NG8=128, NG12=128, CT=1280, Q=16, LR=256, C256=128, z=256, KN=512, Kw=256, evn=256, mh=512, m0=512, m1=512,
+          C2=128, NG0=128, NG4=128, NG8=128, NG12=128, NG16=128, cM=128, cZ=128, nKI=128, nBI=128, rm=1, CT=1280, Q=16, LR=256, C256=128, z=256, KN=512, Kw=256, evn=256, mh=512, m0=512, m1=512,
           Kvr=256, hz=256, hole=256, fm=256, code=256, cdE=256, cdO=256, oh=256, nf=256, F=16, D=16, act=16, aw=16, aB=16,
           val=256, vm=256, NM=1280, nrv=1, ncome=1)
-H16 = dict(mB=256, BnH=256, Aw=256, Ap=256, Aqh=256, dOh=16)
+H16 = dict(mB=256, BnH=256, Aw=256, Ap=256, Aqh=256, dOh=16, zh=256)
 I32 = dict(PI=1, pi15=1, pb=1, pc=1, D1=256, D15=256, D2=128, D3=128, ic=16, iv=16, kp=256, k2=256, pi=16, pi2=16, Wi=16, wT=16,
            hi=16, h2=16, qi=16, q1=16, q2=16, rvi=1, rva=1, fi=1, fa=1, ci=256, cb=256, nb=256, th=1, tl=1)
 U16 = dict(bl=16, vO=32, nO=32, scO=16, srO=16, dO=32, BnL=256, PL=256)
@@ -75,8 +75,8 @@ CY = 0.00083
 STEP = [""]
 SEQ = []
 INFO = []
-ORD = dict(tail=0.16, hop=7.0, tries=6000, seed=1, slack=0.28, share=0.05, move=3.0, shake=0.15, own=0.25, other=1.0)
-PACE = [(1.2, 1.56, 3.8, 0.25), (1.0, 1.56, 3.8, 0.2), (1.45, 1.3, 3.0, 0.22), (1.1, 2.0, 5.0, 0.2)]
+ORD = dict(tail=0.16, hop=7.0, tries=5500, seed=3, slack=0.25, share=0.05, move=3.0, shake=0.15, swap=0.2, own=0.25, other=1.0)
+PACE = [(1.2, 1.56, 3.8, 0.26), (1.0, 1.56, 3.8, 0.19), (1.45, 1.6, 3.0, 0.3), (1.1, 2.0, 5.0, 0.2)]
 
 
 def rem(t):
@@ -351,6 +351,20 @@ def order(ops):
                 cur = best
         move = (draw(len(names)) < ORD["share"]) * (draw(len(names)) - 0.5) * 2 * ORD["move"]
         key = np.array(cur[1])
+        if r[3] < ORD["swap"]:
+            st, prev, at, held = cur[1], {}, {}, []
+            for i in cur[3]:
+                prev[i], at[q[i]] = at.get(q[i]), i
+            i = max(ends, key=lambda k: st[k] + dur[k] + tail[k])
+            while i is not None:
+                tight = [j for j, lag in fwd[i] if st[j] + lag > st[i] - 1e-6]
+                if not tight and q[i] != "x" and prev[i] is not None:
+                    held.append((prev[i], i))
+                i = tight[0] if tight else prev[i] if q[i] != "x" else None
+            for x in draw(1 + int(3 * r[2])):
+                j, i = held[int(x * len(held))]
+                key[j] = st[i] + dur[i] + (tail[i] if r[1] < 0.5 else 0.0)
+            continue
         if r[1] < 0.7:
             key = -(np.array(place(bwd, -(key + span) + ORD["shake"] * r[2] * draw(n), down)) + np.array(dur))
         key = key + move[step] + ORD["shake"] * r[2] * draw(n)
@@ -469,11 +483,15 @@ def rank_program(g, core, T, topo):
             ops[i][3].add((last[name], False))
         last[name] = i
 
-    def gather(which, out, src):
-        if which in ONV:
-            cp(out, src)
-        else:
-            chain("s", act(out, src))
+    def gather(which, out, table, places, b):
+        how = SPLIT.get(which, "s")
+        w = 64 // len(how)
+        for k, e in enumerate(how):
+            lo = b + w * k
+            if e == "v":
+                cp(v(out, 16 * lo, 16 * (lo + w)), ind(table, v(places, lo, lo + w)))
+            else:
+                chain("s", act(v(out, 16 * lo, 16 * (lo + w)), ind(table, v(places, lo, lo + w))))
 
     def hv(name, c, w=128):
         return v(name, w * c, w * c + w)
@@ -485,6 +503,8 @@ def rank_program(g, core, T, topo):
         return v("b%d" % (2 + c), 128 * k, 128 * k + w)
 
     def SM(c, k):
+        if k < 2 and OPT["sm"]:
+            return v("b%d" % (4 + c), 480 + 8 * k, 488 + 8 * k)
         return v("b%d" % (2 + c), 384 + 8 * k, 392 + 8 * k)
 
     def MI(c, k):
@@ -527,6 +547,8 @@ def rank_program(g, core, T, topo):
     ts(v("RS"), v("RN"), float(SB), A.add)
     ts(v("Ib"), v("D1", 0, 128), 256.0, A.is_equal)
     act(v("nIb"), v("Ib"), scale=-1.0)
+    act(v("nKI"), v("Ib"), scale=-1024.0)
+    act(v("nBI"), v("Ib"), scale=-2.0 ** 19)
     cp(v("bl"), v("ic"))
     ts(v("pb"), v("pcol"), 811.0, A.mult)
     ts(v("pc"), v("pb"), SB - 1, A.bitwise_and)
@@ -535,7 +557,8 @@ def rank_program(g, core, T, topo):
     ts(v("row"), v("Ib"), 512.0, A.mult)
     tt(v("Tri"), v("Tri"), v("row"), A.add)
     for name, x in (("fb", -15.0), ("nR1", -R1), ("pR1", R1), ("nfb", 2.0 ** 18), ("h18", 2.0 ** 18), ("C256", 256.0),
-                    ("pR16", R16), ("nR16", -R16), ("h10", 1024.0)):
+                    ("pR16", R16), ("nR16", -R16), ("h10", 1024.0), ("cM", -128.0), ("cZ", -1024.0), ("nfc", 0.5),
+                    ("drb", -2.0 * (DIR - FAIL + SB)), ("f0", -7.5 / 16), ("f1", 2.0 ** 18 - 7.5 * 2 ** 30)):
         act(v(name), v("On", 0, count(v(name))), scale=x)
     for i in range(2):
         fill(v("KK%d" % i, 1280, REM), 0.0)
@@ -558,8 +581,8 @@ def rank_program(g, core, T, topo):
     for s in sorted(set(x for r in PS for x in r)):
         if s < 16:
             act(v("NG%d" % s), v("G16b"), scale=-float(SB))
-            for x, o in ROWS[s]:
-                fill(v("NG%d" % s, o, 128, x), 0.0)
+        for x, o in ROWS[s]:
+            act(v("NG%d" % s, o, 128, x), v("G16b", o, 128, x), scale=0.0 if OPT["ab"] else float(SB))
     ts(v("th"), v("thI", 0, 1), 6, A.arith_shift_right)
     ts(v("tl"), v("thI", 0, 1), 63, A.bitwise_and)
     ts(v("Q", 0, 1), v("th"), -64.0 * SB, A.mult)
@@ -621,8 +644,8 @@ def rank_program(g, core, T, topo):
 
     def first(t, c):
         u = MI(c, 0)
-        group(u, [(v("Ib"), v("C%d" % t)), (v("G16b"), hv("z", c))])
-        if OPT["r16"] == "v":
+        group(u, [(v("Ib"), v("C%d" % t)), (v("G16b"), hv("zh" if t and OPT["zh"] else "z", c))])
+        if OPT["r16"][c] == "v" or not t:
             ts(hv("r16", c), u, R16, A.add, -R16, A.add)
         else:
             act(hv("r17", c), u, AF.Identity, bias=v("pR16"))
@@ -643,8 +666,8 @@ def rank_program(g, core, T, topo):
         if t < RO - 1:
             mm(MI(c, 1), v("G16b"), hv("mB", c))
 
-    def holes(out, keys):
-        if OPT["mh"] == "v":
+    def holes(out, keys, now=False):
+        if OPT["mh"] == "v" or now:
             ts(out, keys, 0.0, A.is_equal, 1024.0, A.mult)
         else:
             act(out, keys, AF.Relu, scale=-1024.0, bias=v("h10"))
@@ -656,19 +679,27 @@ def rank_program(g, core, T, topo):
         if t:
             act(rawv, ind(old, vo(t, c)))
             holes(hv("mh", c, 256), both)
-            ts(hv("m1", c, 256), both, v("rS%d" % (t - 1), 0, 1), A.is_equal, 1024.0, A.mult)
-            group(KV(c, 0, 256), [(v("Ib"), both), (v("nIb"), hv("mh", c, 256)), (v("nIb"), hv("m1", c, 256))])
+            ts(hv("m1", c, 256), both, -128.0, A.add, v("rm"), A.is_equal)
+            group(KV(c, 0, 256), [(v("Ib"), both), (v("nIb"), hv("mh", c, 256)), (v("nKI"), hv("m1", c, 256))])
         else:
-            holes(v("mh", 256 * c, 256 * c + 128), fifth("KK0", c))
-            holes(v("mh", 256 * c + 128, 256 * c + 256), rawn)
+            holes(v("mh", 256 * c, 256 * c + 128), fifth("KK0", c), True)
+            holes(v("mh", 256 * c + 128, 256 * c + 256), rawn, not c)
             mm(KV(c, 0, 256), v("nIb"), hv("mh", c, 256), True, False)
             mm(KV(c, 0), v("Ib"), fifth("KK0", c), False, False)
             mm(KV(c, 1), v("Ib"), rawn, False, True)
-        for b in range(128 * c, 128 * c + 128, GW):
-            gather(("K", t, b // 64), v("Kc", 16 * b, 16 * (b + GW)), ind(old, v("BnL", b, b + GW)))
-        tt(hv("evn", c), KV(c, 0), rawn, A.is_equal)
+        for b in (128 * c, 128 * c + 64):
+            gather(("K", t, b // 64), "Kc", old, "BnL", b)
+        if OPT["evn"] == "v" or not t:
+            tt(hv("evn", c), KV(c, 0), rawn, A.is_equal)
+        else:
+            group(SC(c, 1), [(v("Ib"), rawv), (v("nIb"), rawn), (v("nIb"), hv("mh", 2 * c)), (v("nKI"), hv("m1", 2 * c))])
+            act(hv("r17", c), SC(c, 1), AF.Abs)
+            act(hv("evn", c), hv("r17", c), AF.Relu, scale=-1.0, bias=v("On", 0, 1))
         mm(SM(c, 1), hv("evn", c), v("G8b"))
-        ts(hv("dr", c, 8), SM(c, 1), 3.0, A.is_ge, float(DIR - FAIL + SB), A.mult)
+        if OPT["dr"] == "v":
+            ts(hv("dr", c, 8), SM(c, 1), 3.0, A.is_ge, float(DIR - FAIL + SB), A.mult)
+        else:
+            act(hv("dr", c, 8), SM(c, 1), AF.Relu, scale=float(DIR - FAIL + SB), bias=v("drb"))
         tt(hv("kn", c, 8), SM(c, 0), hv("dr", c, 8), A.add)
         steps = [(q, e) for q in range(2) for e in range(2)]
         if EQ[t][c]:
@@ -706,7 +737,7 @@ def rank_program(g, core, T, topo):
         else:
             act(hv("hz", c), hv("Kw", c), AF.Relu, scale=-2.0 ** 18, bias=v("h18"))
         tt(hv("pr", c), KV(c, 2), hv("Kw", c), A.mult)
-        if not c:
+        if not c and not OPT["split"][t]:
             mm(WR(0, 8), hv("pr", c), v("G8f"))
 
     def next_nodes(t, c):
@@ -723,36 +754,44 @@ def rank_program(g, core, T, topo):
     def material(t, c):
         for q in range(2):
             lo = 2048 * c + 1024 * q
-            for b in range(lo // 16, lo // 16 + 64, GW):
-                gather(("X", t, b // 64), v("Xc", 16 * b, 16 * (b + GW)), ind(v("X"), v("PL", b, b + GW)))
-            for k, (s, o) in enumerate(ROWS[PS[t][c]]):
+            gather(("X", t, 2 * c + q), "Xc", v("X"), "PL", lo // 16)
+            rows = ROWS[PS[t][2 * c + q]]
+            for s, o in rows:
                 turn[0] += 1
-                m, bank, at = 16 // s, "b%d" % (6 + turn[0] % 2), 2048 * c + 1024 * k
+                m, bank = 16 // s, "b7" if OPT["b67"] else "b%d" % (6 + turn[0] % 2)
                 mm(v(bank, 0, 64 * m), v("Ib"), v("Xc", lo + o, lo + 1024, s), True, False)
                 for i in range(m):
                     mm(v(bank, i, 64 * m, m), v("nIb"), v("z", lo // 16, lo // 16 + 64), False, i == m - 1)
-                act(v("ab", at + 64 * m * q, at + 64 * m * (q + 1)), v(bank, 0, 64 * m), AF.Abs)
+                act(v("mx", lo + o, lo + 1024, s), v(bank, 0, 64 * m), AF.Abs if OPT["ab"] else AF.Relu)
             for p in range(16):
-                if not [s for s, o in ROWS[PS[t][c]] if p % s == o]:
+                if not [s for s, o in rows if p % s == o]:
                     chain("v", tt(v("mx", lo + p, lo + 1024, 16), v("b%d" % c, 256 + 64 * q, 320 + 64 * q),
                                   v("Xc", lo + p, lo + 1024, 16), A.max))
 
     def fourth(t, c):
-        dT, s, lo = SC(c, 2), PS[t][c], 2048 * c
+        dT, lo, bank = SC(c, 2), 2048 * c, "b%d" % (2 + c)
+        s0, s1 = PS[t][2 * c:2 * c + 2]
         mm(dT, v("LR", 128, 256, 1, 0, 4), v("LR", 0, 128, 1, 0, 4), True, False)
-        for p in sorted(range(16), key=lambda r: len([x for x, y in ROWS[s] if r % x == y])):
-            o = v("b%d" % (2 + c), 256 + p, 384, 16)
-            part = [(k, x) for k, (x, y) in enumerate(ROWS[s]) if p % x == y]
-            if part:
-                at, m = lo + 1024 * part[0][0], 16 // part[0][1]
-                mm(o, v("ab", at + p // part[0][1], at + 128 * m, m), v("G8a"), False, p == 15 and s == 16)
-            else:
-                mm(o, v("mx", lo + p, lo + 2048, 16), v("G8m"), False, False)
-                mm(o, v("Xc", lo + p, lo + 2048, 16), v("G8x"), False, False)
-        if s < 16:
-            mm(dT, hv("z", c), v("NG%d" % s), False, True)
+        if OPT["xs"]:
+            for a, b in ((0, 96), (96, 128)):
+                for p in range(16):
+                    mm(v(bank, 256 + p, 384, 16, a, b), v("Xc", lo + 16 * a + p, lo + 16 * b, 16), v("G8x"), False, False)
+        for p in sorted(range(16), key=lambda r: len([x for x, y in ROWS[s0] + ROWS[s1] if r % x == y])):
+            if OPT["ab"] and [x for x, y in ROWS[s1] if p % x == y]:
+                mm(v(bank, 256 + p, 384, 16), v("mx", lo + p, lo + 2048, 16), v("G8a"), False, False)
+                continue
+            if not OPT["xs"]:
+                mm(v(bank, 256 + p, 384, 16), v("Xc", lo + p, lo + 2048, 16), v("G8x"), False, False)
+            mm(v(bank, 256 + p, 384, 16), v("mx", lo + p, lo + 2048, 16), v("G8m"), False, False)
+        if s0 == s1:
+            mm(dT, hv("z", c), v("NG%d" % s0), False, True)
+        else:
+            for q, s in enumerate((s0, s1)):
+                mm(v(bank, 256, 384, 1, 64 * q, 64 * q + 64), hv("z", 2 * c + q, 64), v("NG%d" % s), False, q == 1)
         for step in ((0, 1), (1, 0))[c]:
-            if step:
+            if step and OPT["nf"][c] == "v":
+                ts(hv("nf", c), dT, v("nfc"), A.add, 0.0, A.max)
+            elif step:
                 act(hv("nf", c), dT, AF.Relu, scale=2.0 ** 19, bias=v("nfb"))
             else:
                 scan(hv("sd", c), v("RD"), dT, A.min)
@@ -769,18 +808,24 @@ def rank_program(g, core, T, topo):
             zx = SC(c, 1)
             act(hv("evn", c), ind(v("Xc", lo, lo + 2048), do))
             group(zx, [(v("Ib"), hv("z", c)), (v("Ib"), hv("evn", c))])
-        if OPT["za"] == "v":
+        if OPT["zh"] and t < RO - 1:
+            ts(hv("zh", c), zx, HALF, A.mult, 1024.0, A.add)
+        elif OPT["za"] == "v":
             ts(hv("za", c), zx, HALF, A.mult, R1, A.add)
         else:
             act(hv("za", c), zx, AF.Identity, scale=HALF, bias=v("pR1"))
         if t == RO - 1:
             act(hv("zF", c), hv("za", c), AF.Identity, bias=v("nR1"))
             store("Sy"[c], T.yz[:, 128 * c:128 * c + 128], hv("zF", c), c)
-        else:
+        cap = KV(c, 3) if OPT["cap"] else MI(c, 1)
+        group(cap, [(v("Ib"), v("cM")), (v("Ib"), hv("Kw", c)), (v("nIb"), hv("hz", c)), (hv("nf", c), v("nBI" if OPT["nf"][c] == "v" else "nIb"))])
+        scan(hv("cs", c), v("C256"), cap, A.max, v("cs", 127, 128) if c else -128.0 - 65536)
+        if t < RO - 1 and OPT["zh"]:
+            group(KV(c, 2), [(v("Ib"), v("cZ")), (v("Ib"), hv("zh", c))])
+            act(hv("z", c), KV(c, 2))
+        elif t < RO - 1:
             act(hv("z", c), hv("za", c), AF.Identity, bias=v("nR1"))
             act(KV(c, 2), hv("za", c), AF.Identity, bias=v("nR1"))
-        group(MI(c, 1), [(v("Ib"), hv("Kw", c)), (v("nIb"), hv("hz", c)), (hv("nf", c), v("nIb"))])
-        scan(hv("cs", c), v("C256"), MI(c, 1), A.max, v("cs", 127, 128) if c else -2.0 ** 20)
 
     def active(t, c):
         f, y = hv("F", c, 8), WR(16 + 8 * c, 8)
@@ -793,10 +838,78 @@ def rank_program(g, core, T, topo):
         for gr in range(8):
             e = 384 * gr + 256 * c
             mm(WR(32 + 8 * c + gr, 1), v("E", e, e + 128), v("aw", 8 * c + gr, 8 * c + gr + 1))
-        if not c:
-            mm(WR(24, 8), v("On"), f, True, False)
-            for gr in range(8):
-                mm(WR(24 + gr, 1), v("E", 384 * gr + 128, 384 * gr + 256), v("aB", gr, gr + 1), False, False)
+        if not c and not OPT["split"][t]:
+            across()
+
+    def across():
+        mm(WR(24, 8), v("On"), v("F", 0, 8), True, False)
+        for gr in range(8):
+            mm(WR(24 + gr, 1), v("E", 384 * gr + 128, 384 * gr + 256), v("aB", gr, gr + 1), False, False)
+
+    def writers2(t, c):
+        kk = "KK%d" % min(t, 1)
+
+        def h(name):
+            return hv(name, c, 8)
+        if t:
+            come = v("cI%d" % (t - 1), 0, 1)
+            if not c:
+                ts(v("ncome"), come, -1.0, A.mult)
+                ts(K(0), K(t), come, A.is_equal, v("ncome"), A.mult)
+                add_into(K(0), K(t), 1 + t)
+            active(t, c)
+            ts(h("wf"), WR(32 + 8 * c, 8), v("w25"), A.is_lt)
+            tt(h("av"), h("aB"), h("vmd"), A.mult)
+        else:
+            ts(h("F"), h("Wi"), float(FAIL), A.is_lt)
+            ts(h("D"), h("Wi"), float(DIR), A.is_ge, 1024.0, A.mult)
+            group(WR(16 + 8 * c, 8), [(v("On"), v("F", 0, 8))] * c + [(v("Tri"), h("F")), (v("Ib"), h("D"))])
+            ts(h("act"), WR(16 + 8 * c, 8), 512.0 + CAP, A.is_lt)
+        hs = WR(8 * c, 8)
+        mm(hs, hv("pr", c), v("G8f"))
+        cp(h("hi"), hs)
+        ts(h("h2"), h("hi"), 1023, A.bitwise_and)
+        ts(h("hb"), h("h2"), float(rem(t)), A.add)
+        tt(h("hc"), h("hb"), h("F"), A.mult)
+        tt(h("src"), h("hc"), h("wT"), A.max)
+        so, ro = WR(80 + 8 * c, 8), WR(48 + 8 * c, 8)
+        if t:
+            tt(h("w2"), h("wf"), h("av"), A.mult)
+            tt(hv("Aqh", c), ind(h("w2"), v("bl", 0, 8)), v("DM", 0, 128), A.mult)
+            group(so, [(v("Ib"), h("dOh")), (hv("Aqh", c), v("G8b"))])
+            cp(h("scO"), so)
+            tt(hv("Aq", c), ind(h("src"), v("bl", 0, 8)), v("DM", 0, 128), A.mult)
+            mm(ro, hv("Aq", c), v("G8f"))
+            cp(h("srO"), ro)
+            if not c:
+                across()
+        else:
+            ts(h("hd"), h("src"), -1280.0, A.add)
+            tt(h("word"), h("hd"), h("act"), A.mult)
+            tt(hv("Aqh", c), ind(h("word"), v("bl", 0, 8)), v("DM", 0, 128), A.mult)
+            mm(ro, hv("Aqh", c), v("G8b"))
+            ts(h("srO"), ro, 1280.0, A.add)
+        if t < RO - 1 and c:
+            mm(WR(64), v("On"), v("F"))
+            act(v("fj"), WR(64), AF.Identity, bias=v("f0"), accum_out=v("fs"))
+            act(v("f2"), v("fs"), AF.Identity, bias=v("pR16"))
+            act(v("f3"), v("f2"), AF.Identity, bias=v("nR16"))
+            act(v("f4"), v("f3"), AF.Identity, scale=2.0 ** 30, bias=v("f1"))
+            next_nodes(t, 1)
+        tt(hv("fm", c), ind(v(kk, 0, rem(t) + 1024), h("srO")), hv("hole", c), A.min)
+        if t:
+            tt(hv("val", c), KV(c, 0), hv("fm", c), A.max)
+            ts(hv("vm", c), hv("val", c), come, A.not_equal)
+            tt(ind(v("KK0", 0, REM), h("scO")), hv("val", c), hv("vm", c), A.mult)
+        else:
+            tt(fifth("NBi", c), fifth("NBi", c), KV(c, 3), A.subtract)
+            for x in range(2 * c):
+                tt(fifth(kk, x), KV(x, 0), hv("fm", x), A.max)
+        if t == 1:
+            tt(hv("nb", c), ind(tab, vo(t, c)), hv("ohd", c), A.subtract)
+            cp(ind(v("NBi"), h("scO")), hv("nb", c))
+        if t < RO - 1:
+            ts(h("vmd"), h("wT"), v("d0%d" % c), A.subtract, 2.0 ** -70, A.mult)
 
     def writers(t):
         kk = "KK%d" % min(t, 1)
@@ -842,7 +955,7 @@ def rank_program(g, core, T, topo):
             ts(v("srO"), WR(48), 1280.0, A.add)
         if t < RO - 1:
             mm(WR(64), v("On"), v("F"))
-            act(v("fj"), WR(64), accum_out=v("fs"))
+            act(v("fj"), WR(64), AF.Identity, bias=v("f0"), accum_out=v("fs"))
             next_nodes(t, 1)
         tt(v("fm"), ind(v(kk, 0, rem(t) + 1024), v("srO")), v("hole"), A.min)
         if t:
@@ -858,8 +971,9 @@ def rank_program(g, core, T, topo):
             tt(v("nb"), ind(tab, v("vO", 16, 32)), v("ohd"), A.subtract)
             cp(ind(v("NBi"), v("scO")), v("nb"))
         if t < RO - 1:
-            cp(v("fi"), v("fs"))
-            ts(v("fa"), v("fi"), 15, A.bitwise_and)
+            act(v("f2"), v("fs"), AF.Identity, bias=v("pR16"))
+            act(v("f3"), v("f2"), AF.Identity, bias=v("nR16"))
+            act(v("f4"), v("f3"), AF.Identity, scale=2.0 ** 30, bias=v("f1"))
             for c in range(2):
                 ts(hv("vmd", c, 8), hv("wT", c, 8), v("d0%d" % c), A.subtract, 2.0 ** -70, A.mult)
 
@@ -869,32 +983,35 @@ def rank_program(g, core, T, topo):
         for gr in range(8):
             lo = 32 * (gr // 2)
             m, hi = ("cdO", lo + 32) if gr % 2 else ("code", lo + 16)
-            b = "b%d" % (6 + gr % 2)
+            b = "b6" if OPT["b67"] else "b%d" % (6 + gr % 2)
             mm(v(b, 0, 256), v(m, 0, 128, 1, lo, hi), v(m, 0, 256, 1, lo, hi))
             mm(v(b, 256, 384), v(m, 128, 256, 1, lo, hi), v(m, 128, 256, 1, lo, hi))
             act(v("E", 384 * gr, 384 * gr + 384), v(b, 0, 384), AF.Relu, bias=v("fb"))
 
     def revoke(t):
-        ts(v("rvi"), v("cs", 255, 256), 0.0, A.max)
-        ts(v("rva"), v("rvi"), 255, A.bitwise_and)
+        ts(v("rq"), v("cs", 255, 256), R256, A.add, -R256, A.add)
         if t == RO - 1:
-            ts(v("rb"), v("rva"), -256.0, A.mult)
+            ts(v("f2"), v("cs", 255, 256), 128.0, A.add)
+            ts(v("rb"), v("f2"), v("rq"), A.subtract, -256.0, A.mult)
             for i in range(4):
-                lo, o = 320 * i, v("b%d" % (6 + i % 2), 0, 320)
+                lo, o = 320 * i, v("b%d" % (7 - i), 0, 320)
                 act(o, v("KK0", lo, lo + 320), AF.Abs, scale=256.0, bias=v("rb"))
                 tt(v("Yk", lo, lo + 320), o, v("KK0", lo, lo + 320), A.min)
                 if i % 2:
                     store("yS"[i // 2], T.yk[:, lo - 320:lo + 320], v("Yk", lo - 320, lo + 320), 2 + i)
             return
+        ts(v("rm"), v("cs", 255, 256), v("rq"), A.subtract)
         rv = v("rS%d" % t, 0, 1)
-        cp(rv, v("rva"))
+        ts(rv, v("rm"), 128.0, A.add)
         send_revoked(t)
-        ts(v("nrv"), v("rva"), -1.0, A.mult)
+        ts(v("nrv"), v("rm"), 128.0, A.add, -1.0, A.mult)
         rec("y", 0.05, 3.5, [K(0)], [K(t + 1)], lambda e: e.dma_start(res(K(t + 1)), res(K(0))), "cp%d" % t, 16)
         ts(v("NM"), K(0), rv, A.is_equal, v("nrv"), A.mult)
         send_rings(t + 1)
         add_into(K(t + 1), v("NM"), t)
-        ts(v("nfb"), v("fa"), -2.0 ** 30, A.mult, 2.0 ** 18, A.add)
+        act(v("nfb"), v("fs"), AF.Identity, scale=-2.0 ** 30, bias=v("f4"))
+        if "v" in OPT["nf"]:
+            act(v("nfc"), v("nfb"), scale=2.0 ** -19)
 
     send_rings(0)
     steps = [("first", first, 0, 0), ("first", first, 0, 1)]
@@ -904,8 +1021,11 @@ def rank_program(g, core, T, topo):
         steps += [("same", same_node, t)] * (t > 0)
         steps += [("third", third, t, 1), ("material", material, t, 0)]
         steps += [("next", next_nodes, t, 0)] * more
-        steps += [("active", active, t, 0)] * (t > 0)
-        steps += [("writers", writers, t), ("fourth", fourth, t, 0), ("material", material, t, 1)]
+        if OPT["split"][t]:
+            steps += [("writers", writers2, t, 0), ("writers", writers2, t, 1)]
+        else:
+            steps += [("active", active, t, 0)] * (t > 0) + [("writers", writers, t)]
+        steps += [("fourth", fourth, t, 0), ("material", material, t, 1)]
         steps += [("first", first, t + 1, 0)] * more
         steps += [("fourth", fourth, t, 1), ("revoke", revoke, t)]
         steps += [("first", first, t + 1, 1)] * more

@@ -7,31 +7,24 @@ A = AluOpType
 AF = ActivationFunctionType
 RO, SB, CAP = 3, 2048, 96
 BIG = 1.0e9
-R256, R16, R1 = 1.5 * 2 ** 31, 1.5 * 2 ** 27, 1.5 * 2 ** 23
-HALF = 0.5 - 2.0 ** -11
-PS = [[0, 0, 0, 0], [0, 0, 0, 0], [0, 0, 0, 0]]
-ROWS = {0: [], 4: [(4, 3)], 8: [(2, 1)], 12: [(2, 1), (4, 0)], 16: [(2, 1), (2, 0)]}
-EQ = [[0, 0], [0, 0], [0, 0]]
-KP = [[0, 0], [0, 0], [0, 0]]
+R256, R16 = 1.5 * 2 ** 31, 1.5 * 2 ** 27
 SPLIT = {("X", t, q): "ss" for t in range(RO) for q in (1, 3)}
 SPLIT["K", 0, 0] = "sv"
-OPT = dict(za="s", hz="s", r16="vv", dr="s", nf="vv", mh="s", zx="v", wr="b4", xs=1, cap=1, zh=1, ab=0, sm=1, b67=0, split=(0, 0, 0), evn="v")
 REM = 1536
 WS = 17 * SB
 FAIL, DIR = 51 * SB, 290 * SB
 
-F32 = dict(G8f=8, RN=128, RS=128, RD=128, TH=128, T1=1280, r16=256, sc=256, dr=16, kn=16, cV=256, mn=256, sc2=256, Vn=256, V2=256,
-           pr=256, zx=256, za=256, sd=256, cs=256, dl=256, ohd=256, zF=256, row=128, rw=128, pcol=1, p2=1, dcol=1, odd=1, even=1,
-           neven=1, nodd=1, c0=1, wcol=1, w25=1, fs=1, fj=16, d04=16, d00=1, d01=1, vmd=16, av=16, hd=16,
-           wf=16, hb=16, hc=16, src=16, w2=16, word=16, t1=16, Aq=256, p5=1, fb=1, nR1=1, pR1=1, nfb=1, rb=1, lcol=1, h18=1, sgn=16,
-           r17=256, pR16=1, nR16=1, h10=1, rq=1, drb=1, f0=1, f1=1, f2=1, f3=1, f4=1, nfc=1)
-BF = dict(Ib=128, nIb=128, G16b=128, G8b=8, G8s=8, G8m=8, G8x=8, G8a=8, cK=8, Tri=128, On=128, DM=256, DMB=128, C0=128, C1=128,
-          C2=128, NG0=128, NG4=128, NG8=128, NG12=128, NG16=128, cM=128, cZ=128, nKI=128, nBI=128, rm=1, CT=1280, Q=16, LR=256, C256=128, z=256, KN=512, Kw=256, evn=256, mh=512, m0=512, m1=512,
-          Kvr=256, hz=256, hole=256, fm=256, code=256, cdE=256, cdO=256, oh=256, nf=256, F=16, D=16, act=16, aw=16, aB=16,
-          val=256, vm=256, NM=1280, nrv=1, ncome=1)
+F32 = dict(G8f=8, G8h=8, RN=128, RS=128, RD=128, TH=128, T1=1280, r16=256, sc=256, cV=256, mn=256, sc2=256, Vn=256,
+           V2=256, pr=256, zq=256, sd=256, cs=256, dl=256, ohd=256, zF=256, row=128, rw=128, pcol=1, lcol=1, odd=1, c0=1, wcol=1,
+           w25=1, fj=16, fs=1, f0=1, f1=1, f2=1, f3=1, f4=1, nfc=1, d0m=16, vmd=16, av=16, hd=16, wf=16, hb=16, hc=16, src=16,
+           w2=16, word=16, t1=16, Aq=256, fb=1, h18=1, h10=1, sgn=16, pR16=1, nR16=1, drb=1, q0=1, rq=1, c2=1, rb=1)
+BF = dict(Ib=128, nIb=128, Ih=128, nKI=128, nBI=128, G16b=128, NG=128, G8b=8, G8s=8, G8m=8, G8x=8, cK=8, Tri=128, On=128, DM=256,
+          DMB=128, C0=128, C1=128, C2=128, cM=128, cZ=128, C256=128, CT=1280, Q=16, LR=256, z=256, KN=512, Kw=256, evn=256, mh=512,
+          m1=512, hz=256, hole=256, fm=256, val=256, vm=256, code=256, cdO=256, oh=256, nf=256, F=16, D=16, act=16, aw=16, aB=16,
+          dr=16, NM=1280, nrv=1, ncome=1)
 H16 = dict(mB=256, BnH=256, Aw=256, Ap=256, Aqh=256, dOh=16, zh=256)
-I32 = dict(PI=1, pi15=1, pb=1, pc=1, D1=256, D15=256, D2=128, D3=128, ic=16, iv=16, kp=256, k2=256, pi=16, pi2=16, Wi=16, wT=16,
-           hi=16, h2=16, qi=16, q1=16, q2=16, rvi=1, rva=1, fi=1, fa=1, ci=256, cb=256, nb=256, th=1, tl=1)
+I32 = dict(PI=1, pi15=1, pb=1, pc=1, th=1, tl=1, D1=256, D15=256, D2=128, D3=128, ic=16, kp=256, k2=256, pi=16, pi2=16, Wi=16,
+           wT=16, hi=16, h2=16, nb=256)
 U16 = dict(bl=16, vO=32, nO=32, scO=16, srO=16, dO=32, BnL=256, PL=256)
 
 
@@ -50,9 +43,9 @@ for _d, _n, _t in ((F32, "SF", "float32"), (BF, "SBF", "bfloat16"), (H16, "SH", 
     SCRATCH[_n] = ("sbuf", [128, _w], _t)
     for _k in _d:
         WHERE[_k] = (_n, _p[_k], _d[_k])
-_BIGB = dict(KK0=(REM + 1024, "bfloat16"), KK1=(REM + 2048, "bfloat16"), X=(4096, "bfloat16"),
-             Kc=(4096, "bfloat16"), eqV=(4096, "bfloat16"), eqN=(4096, "bfloat16"), Xc=(4096, "bfloat16"), mx=(4096, "bfloat16"),
-             ab=(4096, "bfloat16"), E=(3072, "bfloat16"), NBi=(REM, "int32"), Yk=(1280, "bfloat16"), thI=(8, "int32"),
+_BIGB = dict(KK0=(REM + 1024, "bfloat16"), KK1=(REM + 2048, "bfloat16"), X=(4096, "bfloat16"), Kc=(4096, "bfloat16"),
+             eqV=(4096, "bfloat16"), eqN=(4096, "bfloat16"), Xc=(4096, "bfloat16"), mx=(4096, "bfloat16"), E=(3072, "bfloat16"),
+             NBi=(REM, "int32"), Yk=(1280, "bfloat16"), thI=(8, "int32"),
              rS0=(8, "bfloat16"), rS1=(8, "bfloat16"), cI0=(8, "bfloat16"), cI1=(8, "bfloat16"))
 for _k in _BIGB:
     SCRATCH[_k] = ("sbuf", [128, _BIGB[_k][0]], _BIGB[_k][1])
@@ -64,10 +57,10 @@ for _k in range(RO):
     SCRATCH["hand%d" % _k] = ("sbuf", [128, 512], "bfloat16")
 for _k in range(RO - 1):
     SCRATCH["hrv%d" % _k] = ("sbuf", [128, 8], "bfloat16")
-SEMAPHORES = ["qv", "qs", "qt", "qg"]
-SEMAPHORES += ["ld%d" % i for i in range(8)] + ["st%d" % i for i in range(6)] + ["ad%d" % i for i in range(4)] + ["cp0", "cp1"]
+SEMAPHORES = ["qv", "qs", "qt", "qg", "cp0", "cp1"]
+SEMAPHORES += ["ld%d" % i for i in range(7)] + ["st%d" % i for i in range(4)] + ["ad%d" % i for i in range(4)]
 for _t in range(RO):
-    SEMAPHORES += ["ks%d0" % _t, "ki%d0" % _t, "ki%d1" % _t, "ha%d" % _t, "hs%d" % _t]
+    SEMAPHORES += ["ks%d" % _t, "ki%d0" % _t, "ki%d1" % _t, "ha%d" % _t, "hs%d" % _t]
 for _t in range(RO - 1):
     SEMAPHORES += ["rs%d" % _t, "ri%d" % _t, "ra%d" % _t, "rl%d" % _t]
 
@@ -75,8 +68,8 @@ CY = 0.00083
 STEP = [""]
 SEQ = []
 INFO = []
-ORD = dict(tail=0.16, hop=7.0, tries=5500, seed=3, slack=0.25, share=0.05, move=3.0, shake=0.15, swap=0.2, own=0.25, other=1.0)
-PACE = [(1.2, 1.56, 3.8, 0.26), (1.0, 1.56, 3.8, 0.19), (1.45, 1.6, 3.0, 0.3), (1.1, 2.0, 5.0, 0.2)]
+ORD = dict(tries=9000, seed=5, slack=0.12, share=0.25, move=3.0, shake=0.4, swap=0.2, near=5.0, back=0.7)
+PACE = [(1.25, 2.0, 4.8, 0.3), (1.0, 1.56, 3.8, 0.23), (1.45, 2.6, 6.5, 0.33), (1.15, 1.3, 3, 0.27)]
 
 
 def rem(t):
@@ -93,16 +86,13 @@ def relays(core, T, topo, dst):
     return out
 
 
-def engines_mask(topo, src, dst, n):
-    m = 0
-    for e in topo.engines(src, dst)[:n]:
-        m |= 1 << e
-    return m
+def engines_mask(topo, src, dst, lo, hi):
+    return sum(1 << e for e in topo.engines(src, dst)[lo:hi])
 
 
-def remote(g, topo, src, dst, out, in_, rsem, lsem, n):
+def remote(g, topo, src, dst, out, in_, rsem, lsem):
     rid, pid = topo.addr(dst, src)
-    return g.remote_dma(out, in_, rsem, lsem, pid, rid, engines_mask(topo, src, dst, n))
+    return g.remote_dma(out, in_, rsem, lsem, pid, rid, engines_mask(topo, src, dst, 0, 8))
 
 
 def view(name, lo=0, hi=None, step=1, plo=0, phi=128):
@@ -161,8 +151,7 @@ def cost(q, m, kw):
     c = 1.0
     if q == "v" and m == "tensor_tensor" and not [i for i in full if psum(i)]:
         c = 2.0
-    if q == "v" and m in ("tensor_copy", "tensor_scalar", "memset", "tensor_tensor_scan") and two(o) and not [
-            i for i in full if not two(i)]:
+    if q == "v" and m != "tensor_tensor" and two(o) and not [i for i in full if not two(i)]:
         c = 0.5
     return (0.0, max(64, n * c), 0, 0)
 
@@ -255,8 +244,8 @@ def noter(T):
             opened[b] = i
         return i
 
-    def land(v, sem, inc, i, late):
-        j = rec("x", 0.0, late, [], [v], None, sem, inc)
+    def land(v, sem, i, late):
+        j = rec("x", 0.0, late, [], [v], None, sem, 8)
         ops[j][3].add((i, True))
 
     return ops, op, rec, land, res
@@ -277,9 +266,8 @@ def order(ops):
         deps.append(keep)
     durs = [[o[1][0] + (o[1][1] * p[0] + o[1][2] * p[1] + o[1][3] * p[2]) * CY for o in ops] for p in PACE]
     tails = [[o[2] or p[3] for o in ops] for p in PACE]
-    tail = tails[0]
     fwds = [[[(j, d[j] + (x[j] if w else 0.0)) for j, w in deps[i]] for i in range(n)] for d, x in zip(durs, tails)]
-    dur, fwd, bwd = durs[0], fwds[0], [[] for _ in range(n)]
+    dur, tail, fwd, bwd = durs[0], tails[0], fwds[0], [[] for _ in range(n)]
     for i in range(n):
         for j, w in deps[i]:
             bwd[j].append((i, dur[i] + (tail[j] if w else 0.0)))
@@ -365,16 +353,17 @@ def order(ops):
                 j, i = held[int(x * len(held))]
                 key[j] = st[i] + dur[i] + (tail[i] if r[1] < 0.5 else 0.0)
             continue
-        if r[1] < 0.7:
-            key = -(np.array(place(bwd, -(key + span) + ORD["shake"] * r[2] * draw(n), down)) + np.array(dur))
-        key = key + move[step] + ORD["shake"] * r[2] * draw(n)
+        near = abs(key - draw(1)[0] * cur[2][0]) < ORD["near"]
+        if r[1] < ORD["back"]:
+            key = -(np.array(place(bwd, -(key + span) + near * ORD["shake"] * r[2] * draw(n), down)) + np.array(dur))
+        key = key + near * (move[step] + ORD["shake"] * r[2] * draw(n))
     INFO[:] = [best[0], best[2], {x: sum(durs[1][i] for i in up if q[i] == x) for x in "vst"}]
-    return best[3], [(best[1][i], best[1][i] + durs[1][i]) for i in up]
+    return best[3]
 
 
-def issue(g, T, ops, seq, when):
+def issue(g, T, ops, seq):
     Q = {"v": g.vector, "s": g.scalar, "t": g.tensor, "g": g, "y": g.sync, "S": g.scalar}
-    total, tok, know, done = {}, {}, {}, {}
+    total, tok, know = {}, {}, {}
     for q in Q:
         know[q] = {}
     know["S"] = know["s"]
@@ -391,14 +380,6 @@ def issue(g, T, ops, seq, when):
                 s, v, sn = tok[j]
                 if k.get(s, 0) < v and (s not in need or need[s][0] < v):
                     need[s] = (v, sn)
-        for s in need:
-            ahead = ORD["own"] if s == sem else ORD["other"]
-            for j in reversed(done.get(s, [])):
-                if tok[j][1] <= need[s][0]:
-                    break
-                if when[j][1] + ahead <= when[i][0]:
-                    need[s] = tok[j][1:]
-                    break
         for s in sorted(need):
             v, sn = need[s]
             if [o for o in need if o != s and need[o][1].get(s, 0) >= v]:
@@ -414,8 +395,6 @@ def issue(g, T, ops, seq, when):
         if r is not None:
             r.then_inc(T.sem[sem], inc)
         tok[i] = (sem, total[sem], dict(k))
-        if inc == 1:
-            done.setdefault(sem, []).append(i)
     for s in sorted(total):
         if know["g"].get(s, 0) < total[s]:
             g.wait_ge(T.sem[s], total[s])
@@ -432,6 +411,7 @@ def rank_program(g, core, T, topo):
     rl = relays(core, T, topo, below)
     rv_relay = relays(core, T, topo, above)[0]
     v = view
+    last = {}
 
     def tt(out, a, b, o):
         return op("v", "tensor_tensor", out=out, in0=a, in1=b, op=o)
@@ -466,32 +446,30 @@ def rank_program(g, core, T, topo):
     def scan(out, a, b, o1, first=0.0, o0=A.add):
         return op("v", "tensor_tensor_scan", out=out, data0=a, data1=b, initial=first, op0=o0, op1=o1)
 
-    def load(q, dst, src, k):
-        chain("load" + q, rec(q, 0.05, (2.7, 2.5, 5.2, 5.3, 5.4, 7.5, 9.6)[k], [], [dst], lambda e: e.dma_start(res(dst), src),
-                              "ld%d" % k, 16))
-
-    def store(q, dst, srcv, k):
-        return rec(q, 0.1, 2.0, [srcv], [], lambda e: e.dma_start(dst, res(srcv)), "st%d" % k, 16)
-
-    def add_into(dst, src, k):
-        return rec("g", 1.0, 4.5, [src], [dst], lambda e: e.dma_start(res(dst), res(src), accum_op=A.add), "ad%d" % k, 16)
-
-    last, turn = {}, [0]
-
     def chain(name, i):
         if name in last:
             ops[i][3].add((last[name], False))
         last[name] = i
 
-    def gather(which, out, table, places, b):
+    def load(q, dst, src, k, late):
+        chain("load" + q, rec(q, 0.05, late, [], [dst], lambda e: e.dma_start(res(dst), src), "ld%d" % k, 16))
+
+    def store(q, dst, src, k):
+        rec(q, 0.1, 2.0, [src], [], lambda e: e.dma_start(dst, res(src)), "st%d" % k, 16)
+
+    def add_into(dst, src, k):
+        rec("g", 1.0, 4.5, [src], [dst], lambda e: e.dma_start(res(dst), res(src), accum_op=A.add), "ad%d" % k, 16)
+
+    def gather(which, out, table, places, b, scale):
         how = SPLIT.get(which, "s")
         w = 64 // len(how)
         for k, e in enumerate(how):
             lo = b + w * k
+            dst, src = v(out, 16 * lo, 16 * (lo + w)), ind(table, v(places, lo, lo + w))
             if e == "v":
-                cp(v(out, 16 * lo, 16 * (lo + w)), ind(table, v(places, lo, lo + w)))
+                ts(dst, src, scale, A.mult)
             else:
-                chain("s", act(v(out, 16 * lo, 16 * (lo + w)), ind(table, v(places, lo, lo + w))))
+                chain("gathers", act(dst, src, scale=scale))
 
     def hv(name, c, w=128):
         return v(name, w * c, w * c + w)
@@ -499,27 +477,27 @@ def rank_program(g, core, T, topo):
     def KV(c, k, w=128):
         return v("b%d" % c, 128 * k, 128 * k + w)
 
-    def SC(c, k, w=128):
-        return v("b%d" % (2 + c), 128 * k, 128 * k + w)
-
-    def SM(c, k):
-        if k < 2 and OPT["sm"]:
-            return v("b%d" % (4 + c), 480 + 8 * k, 488 + 8 * k)
-        return v("b%d" % (2 + c), 384 + 8 * k, 392 + 8 * k)
+    def SC(c, k):
+        return v("b%d" % (2 + c), 128 * k, 128 * k + 128)
 
     def MI(c, k):
         return v("b%d" % (4 + c), 128 * k, 128 * k + 128)
 
-    def WR(k, w=16):
-        return v(OPT["wr"], 384 + k, 384 + k + w)
+    def SM(c, k):
+        if k < 2:
+            return v("b%d" % (4 + c), 480 + 8 * k, 488 + 8 * k)
+        return v("b%d" % (2 + c), 384 + 8 * k, 392 + 8 * k)
 
-    load("y", v("NBi", 0, 640), T.nbr[:, 0:640], 0)
-    load("S", v("z"), T.z0[:], 1)
-    load("S", v("NBi", 640, 1280), T.nbr[:, 640:1280], 2)
-    load("y", v("KK0", 0, 1280), T.ring[:], 3)
-    load("S", v("thI", 0, 1), T.thr[:], 4)
-    load("y", v("X", 0, 2048), T.mat[:], 5)
-    load("y", v("X", 2048, 4096), T.mat[:], 6)
+    def WR(k, w=16):
+        return v("b4", 384 + k, 384 + k + w)
+
+    load("y", v("NBi", 0, 640), T.nbr[:, 0:640], 0, 2.1)
+    load("S", v("z"), T.z0[:], 1, 1.9)
+    load("S", v("NBi", 640, 1280), T.nbr[:, 640:1280], 2, 4.5)
+    load("y", v("KK0", 0, 1280), T.ring[:], 3, 4.6)
+    load("S", v("thI", 0, 1), T.thr[:], 4, 4.7)
+    load("y", v("X", 0, 2048), T.mat[:], 5, 7.0)
+    load("y", v("X", 2048, 4096), T.mat[:], 6, 9.0)
 
     iota(v("PI"), [[1, 1]], 0, 1)
     iota(v("D2"), [[-16, 8], [0, 16]], 128, 1)
@@ -527,6 +505,8 @@ def rank_program(g, core, T, topo):
     iota(v("D3"), [[0, 8], [1, 16]], 0, 0)
     iota(v("ic"), [[1, 16]], 0, 0)
     iota(v("t1"), [[16, 16]], 1280, 0)
+    iota(v("d0m"), [[128, 2], [0, 8]], 1280, 1)
+    iota(v("V2"), [[10, 256]], 1, 0)
     iota(v("T1"), [[1, 1280]], 0, 0)
     ts(v("pi15"), v("PI"), 15, A.bitwise_and)
     cp(v("pcol"), v("pi15"))
@@ -536,39 +516,33 @@ def rank_program(g, core, T, topo):
         ts(v("C%d" % t), v("On"), float(t), A.mult, v("pcol"), A.subtract)
     ts(v("D2"), v("D2"), 4, A.arith_shift_right)
     ts(v("G16b"), v("D2"), 8.0, A.is_equal)
-    g8 = v("G16b", 0, 128, 16)
-    for name, x in (("G8f", 1), ("G8b", 1), ("G8s", WS), ("G8m", 2 * SB), ("G8x", -SB), ("G8a", SB)):
-        act(v(name), g8, scale=float(x))
-    act(v("cK"), v("On", 0, 8), scale=(FAIL - SB) / 128.0)
+    act(v("NG"), v("G16b"), scale=-float(SB))
+    for name, x in (("G8f", 1), ("G8h", 2), ("G8b", 1), ("G8s", WS), ("G8m", 4 * SB), ("G8x", -2 * SB)):
+        act(v(name), v("G16b", 0, 128, 16), scale=float(x))
     ts(v("D15"), v("D1"), 15, A.bitwise_and)
     ts(v("DM"), v("D15"), 0.0, A.is_equal)
     act(v("DMB"), v("DM", 0, 128), scale=4096.0)
     ts(v("RN"), v("D3"), 0.0, A.is_equal, -BIG, A.mult)
     ts(v("RS"), v("RN"), float(SB), A.add)
     ts(v("Ib"), v("D1", 0, 128), 256.0, A.is_equal)
-    act(v("nIb"), v("Ib"), scale=-1.0)
-    act(v("nKI"), v("Ib"), scale=-1024.0)
-    act(v("nBI"), v("Ib"), scale=-2.0 ** 19)
+    for name, x in (("nIb", -1.0), ("nKI", -1024.0), ("nBI", -2.0 ** 19), ("Ih", 0.5), ("row", 512.0)):
+        act(v(name), v("Ib"), scale=x)
     cp(v("bl"), v("ic"))
     ts(v("pb"), v("pcol"), 811.0, A.mult)
     ts(v("pc"), v("pb"), SB - 1, A.bitwise_and)
     cp(v("c0"), v("pc"))
     ts(v("Tri"), v("D1", 0, 128), 256.0, A.is_lt)
-    ts(v("row"), v("Ib"), 512.0, A.mult)
     tt(v("Tri"), v("Tri"), v("row"), A.add)
-    for name, x in (("fb", -15.0), ("nR1", -R1), ("pR1", R1), ("nfb", 2.0 ** 18), ("h18", 2.0 ** 18), ("C256", 256.0),
-                    ("pR16", R16), ("nR16", -R16), ("h10", 1024.0), ("cM", -128.0), ("cZ", -1024.0), ("nfc", 0.5),
-                    ("drb", -2.0 * (DIR - FAIL + SB)), ("f0", -7.5 / 16), ("f1", 2.0 ** 18 - 7.5 * 2 ** 30)):
+    for name, x in (("cK", (FAIL - SB) / 128.0), ("fb", -15.0), ("h18", 2.0 ** 18), ("h10", 1024.0), ("C256", 256.0),
+                    ("pR16", R16), ("nR16", -R16), ("cM", -128.0), ("cZ", -1024.0), ("nfc", 0.5), ("q0", 1023.75),
+                    ("drb", -512.0 * SB), ("f0", -7.5 / 16), ("f1", 0.5 - 7.5 * SB), ("rw", 0.5)):
         act(v(name), v("On", 0, count(v(name))), scale=x)
-    for i in range(2):
-        fill(v("KK%d" % i, 1280, REM), 0.0)
+    for name in ("KK0", "KK1"):
+        act(v(name, 1280, REM), v("DM"), scale=0.0)
     fill(v("NBi", 1280, REM), 0)
     ts(v("dOh"), v("t1"), v("pcol"), A.add)
-    for c in range(2):
-        ts(v("d0%d" % c), v("lcol"), 1280.0 + 128 * c, A.add)
     ts(v("pb"), v("PI"), 4, A.arith_shift_right, 1, A.bitwise_and)
     cp(v("odd"), v("pb"))
-    fill(v("rw"), 0.5)
     scan(v("row"), v("rw"), v("On"), A.mult, 2.0 ** 64, A.mult)
     tt(v("rw"), v("row"), v("Ib"), A.mult)
     op("v", "tensor_reduce", out=v("wcol"), in_=v("rw"), axis=AxisListType.X, op=A.add)
@@ -578,31 +552,24 @@ def rank_program(g, core, T, topo):
     for r in range(11):
         w = min(2 ** r, 1280 - 2 ** r)
         act(v("CT", 2 ** r, 2 ** r + w), v("CT", 0, w), scale=v("sgn", r, r + 1))
-    for s in sorted(set(x for r in PS for x in r)):
-        if s < 16:
-            act(v("NG%d" % s), v("G16b"), scale=-float(SB))
-        for x, o in ROWS[s]:
-            act(v("NG%d" % s, o, 128, x), v("G16b", o, 128, x), scale=0.0 if OPT["ab"] else float(SB))
     ts(v("th"), v("thI", 0, 1), 6, A.arith_shift_right)
     ts(v("tl"), v("thI", 0, 1), 63, A.bitwise_and)
     ts(v("Q", 0, 1), v("th"), -64.0 * SB, A.mult)
     ts(v("Q", 1, 2), v("tl"), -float(SB), A.mult)
-    cp(v("Q", 2, 3), v("pcol"))
-    fill(v("Q", 3, 4), 16.0)
-    fill(v("Q", 4, 7), 1.0)
-    cp(v("Q", 7, 8), v("lcol"))
+    act(v("Q", 2, 3), v("pcol"))
+    act(v("Q", 3, 4), v("On", 0, 1), scale=16.0)
+    act(v("Q", 4, 7), v("On", 0, 3))
+    act(v("Q", 7, 8), v("lcol"))
     mm(v("b6", 0, 128, 1, 0, 4), v("Q", 0, 4), v("Ib"))
     mm(v("b6", 128, 256, 1, 0, 4), v("Q", 4, 8), v("Ib"))
     act(v("LR", 0, 256, 1, 0, 4), v("b6", 0, 256, 1, 0, 4))
     mm(v("b6", 256, 384), v("LR", 128, 256, 1, 0, 2), v("LR", 0, 128, 1, 0, 2))
     act(v("TH"), v("b6", 256, 384))
     tt(v("RD", 1, 128), v("b6", 257, 384), v("TH", 0, 127), A.subtract)
-    fill(v("RD", 0, 128, 16), BIG)
+    act(v("RD", 0, 128, 16), v("On", 0, 8), scale=BIG)
     for c in range(2):
-        iota(hv("V2", c), [[10, 128]], 1 + 1280 * c, 0)
-        if not KP[0][c]:
-            act(MI(c, 2), hv("V2", c))
-        act(KV(c, 2), hv("z", c))
+        act(KV(c, 2), hv("z", c), scale=0.5)
+        act(hv("zq", c), hv("z", c), AF.Identity, scale=0.5, bias=v("q0"))
 
     def send_rings(t):
         names = ("KK0", "NM") if t else ("KK0",)
@@ -611,24 +578,22 @@ def rank_program(g, core, T, topo):
             parts = []
             for h in range(2):
                 rid, pid = topo.addr(rl[h], core)
-                eng = topo.engines(core, rl[h])
-                mask = sum(1 << x for x in eng[8 * h:8 * h + 8])
-                parts.append(RemoteDMATransfer(dst_ids=[DstId(rid=rid, pnc=pid)], dma_engine_mask=mask, remote_sem=T.sem["ha%d" % t],
+                parts.append(RemoteDMATransfer(dst_ids=[DstId(rid=rid, pnc=pid)], remote_sem=T.sem["ha%d" % t],
+                                               dma_engine_mask=engines_mask(topo, core, rl[h], 8 * h, 8 * h + 8),
                                                srcs=[res(v(x, 512 * h, 512 * h + 512)) for x in names],
                                                dsts=[T["hand%d" % t][:]], alu_op=len(names) - 1))
-            g.remote_dma_fused(parts, local_sem=T.sem["ks%d0" % t])
-        i = rec("g", 0.4 if t else 3.0, 4.0, [v(x, 0, 1024) for x in names], [], emit, "ks%d0" % t, 16)
+            g.remote_dma_fused(parts, local_sem=T.sem["ks%d" % t])
+        i = rec("g", 0.4 if t else 3.0, 4.0, [v(x, 0, 1024) for x in names], [], emit, "ks%d" % t, 16)
         for h in range(2):
             lo = rem(t) + 512 * h
-            land(v("KK%d" % min(t, 1), lo, lo + 512), "ki%d%d" % (t, h), 8, i, ORD["hop"] + (0 if t else 3))
+            land(v("KK%d" % min(t, 1), lo, lo + 512), "ki%d%d" % (t, h), i, 7.0 if t else 10.0)
 
     def send_revoked(t):
         src = v("rS%d" % t, 0, 1)
 
         def emit(e):
-            remote(g, topo, core, rv_relay, T["hrv%d" % t][:, 0:1], res(src), T.sem["ra%d" % t], T.sem["rs%d" % t], 8)
-        i = rec("g", 0.3, 4.0, [src], [], emit, "rs%d" % t, 8)
-        land(v("cI%d" % t, 0, 1), "ri%d" % t, 8, i, 5.0)
+            remote(g, topo, core, rv_relay, T["hrv%d" % t][:, 0:1], res(src), T.sem["ra%d" % t], T.sem["rs%d" % t])
+        land(v("cI%d" % t, 0, 1), "ri%d" % t, rec("g", 0.3, 4.0, [src], [], emit, "rs%d" % t, 8), 5.0)
 
     def K(t):
         return v("KK%d" % min(t, 1), 0, 1280)
@@ -640,16 +605,16 @@ def rank_program(g, core, T, topo):
     def fifth(name, c):
         return v(name, 640 * c, 640 * c + 640, 5)
 
+    def to_o(out, copy, x, weights):
+        tt(copy, ind(x, v("bl", 0, 8)), v("DM", 0, 128), A.mult)
+        mm(out, copy, weights)
+
     tab = v("NBi", 0, 1280)
 
     def first(t, c):
         u = MI(c, 0)
-        group(u, [(v("Ib"), v("C%d" % t)), (v("G16b"), hv("zh" if t and OPT["zh"] else "z", c))])
-        if OPT["r16"][c] == "v" or not t:
-            ts(hv("r16", c), u, R16, A.add, -R16, A.add)
-        else:
-            act(hv("r17", c), u, AF.Identity, bias=v("pR16"))
-            act(hv("r16", c), hv("r17", c), AF.Identity, bias=v("nR16"))
+        group(u, [(v("Ib"), v("C%d" % t)), (v("G16b"), hv("zh" if t else "z", c))])
+        ts(hv("r16", c), u, R16, A.add, -R16, A.add)
         if t:
             tt(hv("oh", c), u, hv("r16", c), A.is_equal)
             tt(hv("mB", c), ind(tab, vo(t, c)), hv("oh", c), A.mult)
@@ -662,53 +627,43 @@ def rank_program(g, core, T, topo):
         ts(no, v("sc", 128 * c + 15, 128 * c + 128, 16), -4096.0, A.add)
         cp(hv("BnL", c), ind(tab, no))
         cp(hv("BnH", c), hv("BnL", c))
-        group(SM(c, 0), [(v("On"), v("cK")), (hv("mB", c), v("G8b"))])
         if t < RO - 1:
             mm(MI(c, 1), v("G16b"), hv("mB", c))
-
-    def holes(out, keys, now=False):
-        if OPT["mh"] == "v" or now:
-            ts(out, keys, 0.0, A.is_equal, 1024.0, A.mult)
-        else:
-            act(out, keys, AF.Relu, scale=-1024.0, bias=v("h10"))
+        if not t and not c:
+            act(MI(0, 2), hv("V2", 0))
 
     def second(t, c):
-        old = K(0)
-        both, rawv, rawn = hv("KN", c, 256), v("KN", 256 * c, 256 * c + 128), v("KN", 256 * c + 128, 256 * c + 256)
-        act(rawn, ind(old, v("nO", 16 * c, 16 * c + 8)))
+        both, rawv, rawn = hv("KN", c, 256), hv("KN", 2 * c), hv("KN", 2 * c + 1)
+        act(rawn, ind(K(0), v("nO", 16 * c, 16 * c + 8)))
         if t:
-            act(rawv, ind(old, vo(t, c)))
-            holes(hv("mh", c, 256), both)
-            ts(hv("m1", c, 256), both, -128.0, A.add, v("rm"), A.is_equal)
+            act(rawv, ind(K(0), vo(t, c)))
+            act(hv("mh", c, 256), both, AF.Relu, scale=-1024.0, bias=v("h10"))
+            if c:
+                ts(hv("m1", c, 256), both, v("rS%d" % (t - 1), 0, 1), A.is_equal)
+            else:
+                ts(hv("m1", c, 256), both, v("rq"), A.add, v("c2"), A.is_equal)
             group(KV(c, 0, 256), [(v("Ib"), both), (v("nIb"), hv("mh", c, 256)), (v("nKI"), hv("m1", c, 256))])
         else:
-            holes(v("mh", 256 * c, 256 * c + 128), fifth("KK0", c), True)
-            holes(v("mh", 256 * c + 128, 256 * c + 256), rawn, not c)
+            ts(hv("mh", 2 * c), fifth("KK0", c), 0.0, A.is_equal, 1024.0, A.mult)
+            if c:
+                act(hv("mh", 3), rawn, AF.Relu, scale=-1024.0, bias=v("h10"))
+            else:
+                ts(hv("mh", 1), rawn, 0.0, A.is_equal, 1024.0, A.mult)
             mm(KV(c, 0, 256), v("nIb"), hv("mh", c, 256), True, False)
             mm(KV(c, 0), v("Ib"), fifth("KK0", c), False, False)
             mm(KV(c, 1), v("Ib"), rawn, False, True)
         for b in (128 * c, 128 * c + 64):
-            gather(("K", t, b // 64), "Kc", old, "BnL", b)
-        if OPT["evn"] == "v" or not t:
-            tt(hv("evn", c), KV(c, 0), rawn, A.is_equal)
-        else:
-            group(SC(c, 1), [(v("Ib"), rawv), (v("nIb"), rawn), (v("nIb"), hv("mh", 2 * c)), (v("nKI"), hv("m1", 2 * c))])
-            act(hv("r17", c), SC(c, 1), AF.Abs)
-            act(hv("evn", c), hv("r17", c), AF.Relu, scale=-1.0, bias=v("On", 0, 1))
+            gather(("K", t, b // 64), "Kc", K(0), "BnL", b, 1.0)
+        tt(hv("evn", c), KV(c, 0), rawn, A.is_equal)
         mm(SM(c, 1), hv("evn", c), v("G8b"))
-        if OPT["dr"] == "v":
-            ts(hv("dr", c, 8), SM(c, 1), 3.0, A.is_ge, float(DIR - FAIL + SB), A.mult)
-        else:
-            act(hv("dr", c, 8), SM(c, 1), AF.Relu, scale=float(DIR - FAIL + SB), bias=v("drb"))
-        tt(hv("kn", c, 8), SM(c, 0), hv("dr", c, 8), A.add)
-        steps = [(q, e) for q in range(2) for e in range(2)]
-        if EQ[t][c]:
-            steps = [(q, e) for e in range(2) for q in range(2)]
-        for q, e in steps:
-            for k in range(16):
-                s = (2048 * c + 1024 * q + k, 2048 * c + 1024 * q + 1024, 16)
-                b = 128 * e + 64 * q
-                chain("v", tt(v(("eqV", "eqN")[e], *s), v("b%d" % c, b, b + 64), v("Kc", *s), A.is_equal))
+        act(hv("dr", c, 8), SM(c, 1), AF.Relu, scale=256.0 * SB, bias=v("drb"))
+        group(SM(c, 0), [(v("On"), v("cK")), (hv("mB", c), v("G8b")), (v("Ib"), hv("dr", c, 8))])
+        for q in range(2):
+            for e, eq in enumerate(("eqV", "eqN")):
+                for k in range(16):
+                    s = (2048 * c + 1024 * q + k, 2048 * c + 1024 * q + 1024, 16)
+                    b = 128 * e + 64 * q
+                    chain("eq", tt(v(eq, *s), v("b%d" % c, b, b + 64), v("Kc", *s), A.is_equal))
 
     def third(t, c):
         for o, eq in ((SC(c, 0), "eqV"), (MI(c, 0), "eqN")):
@@ -718,32 +673,27 @@ def rank_program(g, core, T, topo):
         act(hv("cV", c), SC(c, 0))
         tt(hv("mn", c), MI(c, 0), hv("cV", c), A.min)
         scan(hv("sc2", c), v("RS"), hv("mn", c), A.max)
-        tt(hv("Wi", c, 8), v("sc2", 128 * c + 15, 128 * c + 128, 16), hv("kn", c, 8), A.max)
+        tt(hv("Wi", c, 8), v("sc2", 128 * c + 15, 128 * c + 128, 16), SM(c, 0), A.max)
         ts(hv("wT", c, 8), hv("Wi", c, 8), SB - 1, A.bitwise_and)
-        tt(hv("Aw", c), ind(hv("wT", c, 8), v("bl", 0, 8)), v("DM", 0, 128), A.mult)
-        mm(SM(c, 2), hv("Aw", c), v("G8b"))
+        to_o(SM(c, 2), hv("Aw", c), hv("wT", c, 8), v("G8b"))
         w = vo(t + 1, c)
         cp(w, SM(c, 2))
         act(hv("Kw", c), ind(K(t), w))
-        if KP[t][c]:
+        if c:
             tt(hv("kp", c), ind(K(t), w), hv("V2", c), A.mult)
         else:
             tt(hv("kp", c), MI(c, 2), hv("Kw", c), A.mult)
         ts(hv("k2", c), hv("kp", c), 2, A.arith_shift_right, SB - 1, A.bitwise_and)
         ts(hv("PL", c), hv("k2", c), v("c0"), A.add, float(t), A.add)
         act(hv("hole", c), KV(c, 0), AF.Relu, scale=-1.0)
-        if OPT["hz"] == "v":
-            ts(hv("hz", c), hv("Kw", c), 0.0, A.is_equal, 2.0 ** 18, A.mult)
-        else:
-            act(hv("hz", c), hv("Kw", c), AF.Relu, scale=-2.0 ** 18, bias=v("h18"))
+        act(hv("hz", c), hv("Kw", c), AF.Relu, scale=-2.0 ** 18, bias=v("h18"))
         tt(hv("pr", c), KV(c, 2), hv("Kw", c), A.mult)
-        if not c and not OPT["split"][t]:
-            mm(WR(0, 8), hv("pr", c), v("G8f"))
+        mm(SM(c, 4), hv("pr", c), v("G8h"))
+        cp(hv("hi", c, 8), SM(c, 4))
 
     def next_nodes(t, c):
-        w = vo(t + 1, c)
-        act(hv("Vn", c), ind(v("T1"), w))
-        act(hv("V2", c) if KP[t + 1][c] else MI(c, 2), hv("Vn", c), scale=2.0, bias=1.0)
+        act(hv("Vn", c), ind(v("T1"), vo(t + 1, c)))
+        act(hv("V2", c) if c else MI(c, 2), hv("Vn", c), scale=2.0, bias=1.0)
         if t:
             tt(KV(c, 3), MI(c, 1), hv("Vn", c), A.subtract)
             tt(hv("ohd", c), KV(c, 3), hv("oh", c), A.mult)
@@ -754,78 +704,41 @@ def rank_program(g, core, T, topo):
     def material(t, c):
         for q in range(2):
             lo = 2048 * c + 1024 * q
-            gather(("X", t, 2 * c + q), "Xc", v("X"), "PL", lo // 16)
-            rows = ROWS[PS[t][2 * c + q]]
-            for s, o in rows:
-                turn[0] += 1
-                m, bank = 16 // s, "b7" if OPT["b67"] else "b%d" % (6 + turn[0] % 2)
-                mm(v(bank, 0, 64 * m), v("Ib"), v("Xc", lo + o, lo + 1024, s), True, False)
-                for i in range(m):
-                    mm(v(bank, i, 64 * m, m), v("nIb"), v("z", lo // 16, lo // 16 + 64), False, i == m - 1)
-                act(v("mx", lo + o, lo + 1024, s), v(bank, 0, 64 * m), AF.Abs if OPT["ab"] else AF.Relu)
+            gather(("X", t, 2 * c + q), "Xc", v("X"), "PL", lo // 16, 0.5)
             for p in range(16):
-                if not [s for s, o in rows if p % s == o]:
-                    chain("v", tt(v("mx", lo + p, lo + 1024, 16), v("b%d" % c, 256 + 64 * q, 320 + 64 * q),
-                                  v("Xc", lo + p, lo + 1024, 16), A.max))
+                chain("mx", tt(v("mx", lo + p, lo + 1024, 16), v("b%d" % c, 256 + 64 * q, 320 + 64 * q),
+                               v("Xc", lo + p, lo + 1024, 16), A.max))
 
     def fourth(t, c):
         dT, lo, bank = SC(c, 2), 2048 * c, "b%d" % (2 + c)
-        s0, s1 = PS[t][2 * c:2 * c + 2]
         mm(dT, v("LR", 128, 256, 1, 0, 4), v("LR", 0, 128, 1, 0, 4), True, False)
-        if OPT["xs"]:
-            for a, b in ((0, 96), (96, 128)):
-                for p in range(16):
-                    mm(v(bank, 256 + p, 384, 16, a, b), v("Xc", lo + 16 * a + p, lo + 16 * b, 16), v("G8x"), False, False)
-        for p in sorted(range(16), key=lambda r: len([x for x, y in ROWS[s0] + ROWS[s1] if r % x == y])):
-            if OPT["ab"] and [x for x, y in ROWS[s1] if p % x == y]:
-                mm(v(bank, 256 + p, 384, 16), v("mx", lo + p, lo + 2048, 16), v("G8a"), False, False)
-                continue
-            if not OPT["xs"]:
-                mm(v(bank, 256 + p, 384, 16), v("Xc", lo + p, lo + 2048, 16), v("G8x"), False, False)
+        for a, b in ((0, 96), (96, 128)):
+            for p in range(16):
+                mm(v(bank, 256 + p, 384, 16, a, b), v("Xc", lo + 16 * a + p, lo + 16 * b, 16), v("G8x"), False, False)
+        for p in range(16):
             mm(v(bank, 256 + p, 384, 16), v("mx", lo + p, lo + 2048, 16), v("G8m"), False, False)
-        if s0 == s1:
-            mm(dT, hv("z", c), v("NG%d" % s0), False, True)
-        else:
-            for q, s in enumerate((s0, s1)):
-                mm(v(bank, 256, 384, 1, 64 * q, 64 * q + 64), hv("z", 2 * c + q, 64), v("NG%d" % s), False, q == 1)
-        for step in ((0, 1), (1, 0))[c]:
-            if step and OPT["nf"][c] == "v":
-                ts(hv("nf", c), dT, v("nfc"), A.add, 0.0, A.max)
-            elif step:
-                act(hv("nf", c), dT, AF.Relu, scale=2.0 ** 19, bias=v("nfb"))
-            else:
-                scan(hv("sd", c), v("RD"), dT, A.min)
+        mm(dT, hv("z", c), v("NG"), False, True)
+        if c:
+            ts(hv("nf", c), dT, v("nfc"), A.add, 0.0, A.max)
+        scan(hv("sd", c), v("RD"), dT, A.min)
+        if not c:
+            act(hv("nf", c), dT, AF.Relu, bias=v("nfc"))
         cp(hv("pi", c, 8), v("sd", 128 * c + 15, 128 * c + 128, 16))
         ts(hv("pi2", c, 8), hv("pi", c, 8), SB - 1, A.bitwise_and)
-        tt(hv("Ap", c), ind(hv("pi2", c, 8), v("bl", 0, 8)), v("DM", 0, 128), A.mult)
-        mm(SM(c, 3), hv("Ap", c), v("G8b"))
+        to_o(SM(c, 3), hv("Ap", c), hv("pi2", c, 8), v("G8b"))
         do = v("dO", 16 * c, 16 * c + 8)
         cp(do, SM(c, 3))
-        zx = hv("zx", c)
-        if OPT["zx"] == "v":
-            tt(zx, ind(v("Xc", lo, lo + 2048), do), hv("z", c), A.add)
-        else:
-            zx = SC(c, 1)
-            act(hv("evn", c), ind(v("Xc", lo, lo + 2048), do))
-            group(zx, [(v("Ib"), hv("z", c)), (v("Ib"), hv("evn", c))])
-        if OPT["zh"] and t < RO - 1:
-            ts(hv("zh", c), zx, HALF, A.mult, 1024.0, A.add)
-        elif OPT["za"] == "v":
-            ts(hv("za", c), zx, HALF, A.mult, R1, A.add)
-        else:
-            act(hv("za", c), zx, AF.Identity, scale=HALF, bias=v("pR1"))
+        tt(hv("zh", c), ind(v("Xc", lo, lo + 2048), do), hv("zq", c), A.add)
         if t == RO - 1:
-            act(hv("zF", c), hv("za", c), AF.Identity, bias=v("nR1"))
+            ts(hv("zF", c), hv("zh", c), -1024.0, A.add)
             store("Sy"[c], T.yz[:, 128 * c:128 * c + 128], hv("zF", c), c)
-        cap = KV(c, 3) if OPT["cap"] else MI(c, 1)
-        group(cap, [(v("Ib"), v("cM")), (v("Ib"), hv("Kw", c)), (v("nIb"), hv("hz", c)), (hv("nf", c), v("nBI" if OPT["nf"][c] == "v" else "nIb"))])
+        cap = v("b%d" % (6 + c), 128, 256)
+        group(cap, [(v("Ib"), v("cM")), (v("Ib"), hv("Kw", c)), (v("nIb"), hv("hz", c)), (hv("nf", c), v("nBI"))])
         scan(hv("cs", c), v("C256"), cap, A.max, v("cs", 127, 128) if c else -128.0 - 65536)
-        if t < RO - 1 and OPT["zh"]:
-            group(KV(c, 2), [(v("Ib"), v("cZ")), (v("Ib"), hv("zh", c))])
-            act(hv("z", c), KV(c, 2))
-        elif t < RO - 1:
-            act(hv("z", c), hv("za", c), AF.Identity, bias=v("nR1"))
-            act(KV(c, 2), hv("za", c), AF.Identity, bias=v("nR1"))
+        if t < RO - 1:
+            group(KV(c, 2), [(v("Ih"), v("cZ")), (v("Ih"), hv("zh", c))])
+            act(hv("z", c), KV(c, 2), scale=2.0)
+            act(hv("zq", c), KV(c, 2), AF.Identity, bias=v("q0"))
 
     def active(t, c):
         f, y = hv("F", c, 8), WR(16 + 8 * c, 8)
@@ -838,89 +751,19 @@ def rank_program(g, core, T, topo):
         for gr in range(8):
             e = 384 * gr + 256 * c
             mm(WR(32 + 8 * c + gr, 1), v("E", e, e + 128), v("aw", 8 * c + gr, 8 * c + gr + 1))
-        if not c and not OPT["split"][t]:
-            across()
-
-    def across():
-        mm(WR(24, 8), v("On"), v("F", 0, 8), True, False)
-        for gr in range(8):
-            mm(WR(24 + gr, 1), v("E", 384 * gr + 128, 384 * gr + 256), v("aB", gr, gr + 1), False, False)
-
-    def writers2(t, c):
-        kk = "KK%d" % min(t, 1)
-
-        def h(name):
-            return hv(name, c, 8)
-        if t:
-            come = v("cI%d" % (t - 1), 0, 1)
-            if not c:
-                ts(v("ncome"), come, -1.0, A.mult)
-                ts(K(0), K(t), come, A.is_equal, v("ncome"), A.mult)
-                add_into(K(0), K(t), 1 + t)
-            active(t, c)
-            ts(h("wf"), WR(32 + 8 * c, 8), v("w25"), A.is_lt)
-            tt(h("av"), h("aB"), h("vmd"), A.mult)
-        else:
-            ts(h("F"), h("Wi"), float(FAIL), A.is_lt)
-            ts(h("D"), h("Wi"), float(DIR), A.is_ge, 1024.0, A.mult)
-            group(WR(16 + 8 * c, 8), [(v("On"), v("F", 0, 8))] * c + [(v("Tri"), h("F")), (v("Ib"), h("D"))])
-            ts(h("act"), WR(16 + 8 * c, 8), 512.0 + CAP, A.is_lt)
-        hs = WR(8 * c, 8)
-        mm(hs, hv("pr", c), v("G8f"))
-        cp(h("hi"), hs)
-        ts(h("h2"), h("hi"), 1023, A.bitwise_and)
-        ts(h("hb"), h("h2"), float(rem(t)), A.add)
-        tt(h("hc"), h("hb"), h("F"), A.mult)
-        tt(h("src"), h("hc"), h("wT"), A.max)
-        so, ro = WR(80 + 8 * c, 8), WR(48 + 8 * c, 8)
-        if t:
-            tt(h("w2"), h("wf"), h("av"), A.mult)
-            tt(hv("Aqh", c), ind(h("w2"), v("bl", 0, 8)), v("DM", 0, 128), A.mult)
-            group(so, [(v("Ib"), h("dOh")), (hv("Aqh", c), v("G8b"))])
-            cp(h("scO"), so)
-            tt(hv("Aq", c), ind(h("src"), v("bl", 0, 8)), v("DM", 0, 128), A.mult)
-            mm(ro, hv("Aq", c), v("G8f"))
-            cp(h("srO"), ro)
-            if not c:
-                across()
-        else:
-            ts(h("hd"), h("src"), -1280.0, A.add)
-            tt(h("word"), h("hd"), h("act"), A.mult)
-            tt(hv("Aqh", c), ind(h("word"), v("bl", 0, 8)), v("DM", 0, 128), A.mult)
-            mm(ro, hv("Aqh", c), v("G8b"))
-            ts(h("srO"), ro, 1280.0, A.add)
-        if t < RO - 1 and c:
-            mm(WR(64), v("On"), v("F"))
-            act(v("fj"), WR(64), AF.Identity, bias=v("f0"), accum_out=v("fs"))
-            act(v("f2"), v("fs"), AF.Identity, bias=v("pR16"))
-            act(v("f3"), v("f2"), AF.Identity, bias=v("nR16"))
-            act(v("f4"), v("f3"), AF.Identity, scale=2.0 ** 30, bias=v("f1"))
-            next_nodes(t, 1)
-        tt(hv("fm", c), ind(v(kk, 0, rem(t) + 1024), h("srO")), hv("hole", c), A.min)
-        if t:
-            tt(hv("val", c), KV(c, 0), hv("fm", c), A.max)
-            ts(hv("vm", c), hv("val", c), come, A.not_equal)
-            tt(ind(v("KK0", 0, REM), h("scO")), hv("val", c), hv("vm", c), A.mult)
-        else:
-            tt(fifth("NBi", c), fifth("NBi", c), KV(c, 3), A.subtract)
-            for x in range(2 * c):
-                tt(fifth(kk, x), KV(x, 0), hv("fm", x), A.max)
-        if t == 1:
-            tt(hv("nb", c), ind(tab, vo(t, c)), hv("ohd", c), A.subtract)
-            cp(ind(v("NBi"), h("scO")), hv("nb", c))
-        if t < RO - 1:
-            ts(h("vmd"), h("wT"), v("d0%d" % c), A.subtract, 2.0 ** -70, A.mult)
+        if not c:
+            mm(WR(24, 8), v("On"), f, True, False)
+            for gr in range(8):
+                mm(WR(24 + gr, 1), v("E", 384 * gr + 128, 384 * gr + 256), v("aB", gr, gr + 1), False, False)
 
     def writers(t):
-        kk = "KK%d" % min(t, 1)
         if t:
             come = v("cI%d" % (t - 1), 0, 1)
             ts(v("ncome"), come, -1.0, A.mult)
             ts(K(0), K(t), come, A.is_equal, v("ncome"), A.mult)
             add_into(K(0), K(t), 1 + t)
-        if t:
             active(t, 1)
-            ts(v("wf"), WR(32), v("w25"), A.is_lt)
+            ts(v("wf"), WR(32), v("w25"), A.is_lt, 2.0 ** -70, A.mult)
             tt(v("av"), v("aB"), v("vmd"), A.mult)
         else:
             ts(v("F"), v("Wi"), float(FAIL), A.is_lt)
@@ -929,8 +772,6 @@ def rank_program(g, core, T, topo):
             mm(WR(24, 8), v("On"), v("F", 0, 8), False, False)
             mm(WR(16), v("Ib"), v("D"), False, True)
             ts(v("act"), WR(16), 512.0 + CAP, A.is_lt)
-        mm(WR(8, 8), hv("pr", 1), v("G8f"))
-        cp(v("hi"), WR(0))
         ts(v("h2"), v("hi"), 1023, A.bitwise_and)
         ts(v("hb"), v("h2"), float(rem(t)), A.add)
         tt(v("hc"), v("hb"), v("F"), A.mult)
@@ -944,20 +785,20 @@ def rank_program(g, core, T, topo):
             cp(v("scO"), WR(80))
             tt(v("Aq"), ind(v("src"), v("bl")), v("DM"), A.mult)
             for c in range(2):
-                mm(WR(48 + 8 * c, 8), hv("Aq", c), v("G8f"))
-            cp(v("srO"), WR(48))
+                mm(v("b7", 8 * c, 8 * c + 8), hv("Aq", c), v("G8f"))
+            cp(v("srO"), v("b7", 0, 16))
         else:
             ts(v("hd"), v("src"), -1280.0, A.add)
             tt(v("word"), v("hd"), v("act"), A.mult)
             tt(v("Aqh"), ind(v("word"), v("bl")), v("DM"), A.mult)
             for c in range(2):
-                mm(WR(48 + 8 * c, 8), hv("Aqh", c), v("G8b"))
-            ts(v("srO"), WR(48), 1280.0, A.add)
+                mm(v("b7", 8 * c, 8 * c + 8), hv("Aqh", c), v("G8b"))
+            ts(v("srO"), v("b7", 0, 16), 1280.0, A.add)
         if t < RO - 1:
-            mm(WR(64), v("On"), v("F"))
-            act(v("fj"), WR(64), AF.Identity, bias=v("f0"), accum_out=v("fs"))
+            mm(v("b6", 0, 16), v("On"), v("F"))
+            act(v("fj"), v("b6", 0, 16), AF.Identity, bias=v("f0"), accum_out=v("fs"))
             next_nodes(t, 1)
-        tt(v("fm"), ind(v(kk, 0, rem(t) + 1024), v("srO")), v("hole"), A.min)
+        tt(v("fm"), ind(v("KK%d" % min(t, 1), 0, rem(t) + 1024), v("srO")), v("hole"), A.min)
         if t:
             for c in range(2):
                 tt(hv("val", c), KV(c, 0), hv("fm", c), A.max)
@@ -965,7 +806,7 @@ def rank_program(g, core, T, topo):
             tt(ind(v("KK0", 0, REM), v("scO")), v("val"), v("vm"), A.mult)
         else:
             for c in range(2):
-                tt(fifth(kk, c), KV(c, 0), hv("fm", c), A.max)
+                tt(fifth("KK0", c), KV(c, 0), hv("fm", c), A.max)
                 tt(fifth("NBi", c), fifth("NBi", c), KV(c, 3), A.subtract)
         if t == 1:
             tt(v("nb"), ind(tab, v("vO", 16, 32)), v("ohd"), A.subtract)
@@ -973,9 +814,8 @@ def rank_program(g, core, T, topo):
         if t < RO - 1:
             act(v("f2"), v("fs"), AF.Identity, bias=v("pR16"))
             act(v("f3"), v("f2"), AF.Identity, bias=v("nR16"))
-            act(v("f4"), v("f3"), AF.Identity, scale=2.0 ** 30, bias=v("f1"))
-            for c in range(2):
-                ts(hv("vmd", c, 8), hv("wT", c, 8), v("d0%d" % c), A.subtract, 2.0 ** -70, A.mult)
+            act(v("f4"), v("f3"), AF.Identity, scale=float(SB), bias=v("f1"))
+            tt(v("vmd"), v("wT"), v("d0m"), A.subtract)
 
     def same_node(t):
         act(v("code"), ind(v("CT"), v("vO", 16 * (t % 2), 16 * (t % 2) + 16)))
@@ -983,35 +823,32 @@ def rank_program(g, core, T, topo):
         for gr in range(8):
             lo = 32 * (gr // 2)
             m, hi = ("cdO", lo + 32) if gr % 2 else ("code", lo + 16)
-            b = "b6" if OPT["b67"] else "b%d" % (6 + gr % 2)
+            b = "b%d" % (6 + gr % 2)
             mm(v(b, 0, 256), v(m, 0, 128, 1, lo, hi), v(m, 0, 256, 1, lo, hi))
             mm(v(b, 256, 384), v(m, 128, 256, 1, lo, hi), v(m, 128, 256, 1, lo, hi))
             act(v("E", 384 * gr, 384 * gr + 384), v(b, 0, 384), AF.Relu, bias=v("fb"))
 
     def revoke(t):
         ts(v("rq"), v("cs", 255, 256), R256, A.add, -R256, A.add)
+        ts(v("c2"), v("cs", 255, 256), 128.0, A.add)
         if t == RO - 1:
-            ts(v("f2"), v("cs", 255, 256), 128.0, A.add)
-            ts(v("rb"), v("f2"), v("rq"), A.subtract, -256.0, A.mult)
+            ts(v("rb"), v("c2"), v("rq"), A.subtract, -256.0, A.mult)
             for i in range(4):
                 lo, o = 320 * i, v("b%d" % (7 - i), 0, 320)
                 act(o, v("KK0", lo, lo + 320), AF.Abs, scale=256.0, bias=v("rb"))
                 tt(v("Yk", lo, lo + 320), o, v("KK0", lo, lo + 320), A.min)
                 if i % 2:
-                    store("yS"[i // 2], T.yk[:, lo - 320:lo + 320], v("Yk", lo - 320, lo + 320), 2 + i)
+                    store("yS"[i // 2], T.yk[:, lo - 320:lo + 320], v("Yk", lo - 320, lo + 320), 2 + i // 2)
             return
-        ts(v("rm"), v("cs", 255, 256), v("rq"), A.subtract)
         rv = v("rS%d" % t, 0, 1)
-        ts(rv, v("rm"), 128.0, A.add)
+        ts(rv, v("c2"), v("rq"), A.subtract)
         send_revoked(t)
-        ts(v("nrv"), v("rm"), 128.0, A.add, -1.0, A.mult)
-        rec("y", 0.05, 3.5, [K(0)], [K(t + 1)], lambda e: e.dma_start(res(K(t + 1)), res(K(0))), "cp%d" % t, 16)
+        ts(v("nrv"), v("c2"), v("rq"), A.subtract, -1.0, A.mult)
+        rec("y", 0.05, 3.5, [K(0)], [K(1)], lambda e: e.dma_start(res(K(1)), res(K(0))), "cp%d" % t, 16)
         ts(v("NM"), K(0), rv, A.is_equal, v("nrv"), A.mult)
         send_rings(t + 1)
-        add_into(K(t + 1), v("NM"), t)
-        act(v("nfb"), v("fs"), AF.Identity, scale=-2.0 ** 30, bias=v("f4"))
-        if "v" in OPT["nf"]:
-            act(v("nfc"), v("nfb"), scale=2.0 ** -19)
+        add_into(K(1), v("NM"), t)
+        act(v("nfc"), v("fs"), AF.Identity, scale=-float(SB), bias=v("f4"))
 
     send_rings(0)
     steps = [("first", first, 0, 0), ("first", first, 0, 1)]
@@ -1020,12 +857,9 @@ def rank_program(g, core, T, topo):
         steps += [("second", second, t, 0), ("third", third, t, 0), ("second", second, t, 1)]
         steps += [("same", same_node, t)] * (t > 0)
         steps += [("third", third, t, 1), ("material", material, t, 0)]
+        steps += [("active", active, t, 0)] * (t > 0)
         steps += [("next", next_nodes, t, 0)] * more
-        if OPT["split"][t]:
-            steps += [("writers", writers2, t, 0), ("writers", writers2, t, 1)]
-        else:
-            steps += [("active", active, t, 0)] * (t > 0) + [("writers", writers, t)]
-        steps += [("fourth", fourth, t, 0), ("material", material, t, 1)]
+        steps += [("writers", writers, t), ("fourth", fourth, t, 0), ("material", material, t, 1)]
         steps += [("first", first, t + 1, 0)] * more
         steps += [("fourth", fourth, t, 1), ("revoke", revoke, t)]
         steps += [("first", first, t + 1, 1)] * more
@@ -1034,8 +868,8 @@ def rank_program(g, core, T, topo):
         s[1](*s[2:])
     STEP[0] = ""
     if not SEQ:
-        SEQ.extend(order(ops))
-    issue(g, T, ops, SEQ[0], SEQ[1])
+        SEQ.append(order(ops))
+    issue(g, T, ops, SEQ[0])
 
 
 def hand_on(g, core, T, topo):
@@ -1050,13 +884,13 @@ def hand_on(g, core, T, topo):
             if t and core == rv_relay:
                 g.wait_ge(T.sem["ra%d" % (t - 1)], 8)
                 remote(g, topo, core, above, T["cI%d" % (t - 1)][:, 0:1], T["hrv%d" % (t - 1)][:, 0:1],
-                       T.sem["ri%d" % (t - 1)], T.sem["rl%d" % (t - 1)], 8)
+                       T.sem["ri%d" % (t - 1)], T.sem["rl%d" % (t - 1)])
             if core in rl:
                 h = rl.index(core)
                 g.wait_ge(T.sem["ha%d" % t], 8)
                 lo = rem(t) + 512 * h
                 remote(g, topo, core, below, T["KK%d" % min(t, 1)][:, lo:lo + 512], T["hand%d" % t][:],
-                       T.sem["ki%d%d" % (t, h)], T.sem["hs%d" % t], 8)
+                       T.sem["ki%d%d" % (t, h)], T.sem["hs%d" % t])
         for t in range(RO):
             if core in rl:
                 g.wait_ge(T.sem["hs%d" % t], 8)

@@ -10,20 +10,26 @@ BIG = 1.0e9
 R256, R16 = 1.5 * 2 ** 31, 1.5 * 2 ** 27
 SPLIT = {("X", t, q): "ss" for t in range(RO) for q in (1, 3)}
 SPLIT["K", 0, 0] = "sv"
-REM = 1536
+KB = 1040
+SPARE = 1536
 WS = 17 * SB
 FAIL, DIR = 51 * SB, 290 * SB
+RJ = 1.5 * 2 ** 39
+OFF = 15 * 2048 - 120 * 4096
+MID = 2.0 ** 23
+OPT = dict(mxs=[], xs=96, ms=128, fin="v", zb="v", hz="s", cd="s", rs="s")
 
-F32 = dict(G8f=8, G8h=8, RN=128, RS=128, RD=128, TH=128, T1=1280, r16=256, sc=256, cV=256, mn=256, sc2=256, Vn=256,
-           V2=256, pr=256, zq=256, sd=256, cs=256, dl=256, ohd=256, zF=256, row=128, rw=128, pcol=1, lcol=1, odd=1, c0=1, wcol=1,
+F32 = dict(G8h=8, RN=128, RS=136, RD=128, TH=128, T1=1280, sc=256, cV=272, mn=272, Vn=256,
+           V2=256, pr=256, zq=256, cs=256, zF=256, row=128, rw=128, pcol=1, lcol=1, odd=1, c0=1, wcol=1,
            w25=1, fj=16, fs=1, f0=1, f1=1, f2=1, f3=1, f4=1, nfc=1, d0m=16, vmd=16, av=16, hd=16, wf=16, hb=16, hc=16, src=16,
-           w2=16, word=16, t1=16, Aq=256, fb=1, h18=1, h10=1, sgn=16, pR16=1, nR16=1, drb=1, q0=1, rq=1, c2=1, rb=1)
-BF = dict(Ib=128, nIb=128, Ih=128, nKI=128, nBI=128, G16b=128, NG=128, G8b=8, G8s=8, G8m=8, G8x=8, cK=8, Tri=128, On=128, DM=256,
-          DMB=128, C0=128, C1=128, C2=128, cM=128, cZ=128, C256=128, CT=1280, Q=16, LR=256, z=256, KN=512, Kw=256, evn=256, mh=512,
-          m1=512, hz=256, hole=256, fm=256, val=256, vm=256, code=256, cdO=256, oh=256, nf=256, F=16, D=16, act=16, aw=16, aB=16,
+           w2=16, word=16, t1=16, fb=1, h18=1, sgn=16, pR16=1, nR16=1, drb=1, q0=1, rq=1, c2=1, nof=1)
+BF = dict(Ib=128, nIb=128, Ih=128, nKI=128, nBI=128, nHI=128, I17=136, G16b=128, G4=128, nG4=128, NG=128, G8b=8, G8s=8, G8m=8,
+          G8x=8, rb=1, IS=128, Tri=128, On=144, DM=256, C0=128, C1=128, C2=128, E0=128, E1=128, E2=128, pRJ=128, nRJ=128,
+          cM=128, cZ=128, C256=128, CT=1280, Q=16, LR=256, z=256, zb=256, x0=256, KN=512, Kw=256, Kt=256, gv=256, evn=256,
+          m1=512, hz=256, val=256, vm=256, code=256, cdO=256, nf=256, F=16, D=16, act=16, aw=16, aB=16,
           dr=16, NM=1280, nrv=1, ncome=1)
-H16 = dict(mB=256, BnH=256, Aw=256, Ap=256, Aqh=256, dOh=16, zh=256)
-I32 = dict(PI=1, pi15=1, pb=1, pc=1, th=1, tl=1, D1=256, D15=256, D2=128, D3=128, ic=16, kp=256, k2=256, pi=16, pi2=16, Wi=16,
+H16 = dict(mB=256, Bv=256, aH=256, BnH=256, Aw=256, Ap=256, Aqh=256, Aq=256, dOh=16, zh=256)
+I32 = dict(PI=1, pi15=1, pb=1, pc=1, th=1, tl=1, D1=256, D15=256, D2=128, D3=128, ic=16, kp=256, k2=256, pi2=16, sc2=272, sd=256,
            wT=16, hi=16, h2=16, nb=256)
 U16 = dict(bl=16, vO=32, nO=32, scO=16, srO=16, dO=32, BnL=256, PL=256)
 
@@ -43,9 +49,10 @@ for _d, _n, _t in ((F32, "SF", "float32"), (BF, "SBF", "bfloat16"), (H16, "SH", 
     SCRATCH[_n] = ("sbuf", [128, _w], _t)
     for _k in _d:
         WHERE[_k] = (_n, _p[_k], _d[_k])
-_BIGB = dict(KK0=(REM + 1024, "bfloat16"), KK1=(REM + 2048, "bfloat16"), X=(4096, "bfloat16"), Kc=(4096, "bfloat16"),
+_BIGB = dict(KK0=(KB + SPARE, "bfloat16"), KK1=(KB + 1280, "bfloat16"), KK2=(KB + 1280, "bfloat16"), X=(4096, "bfloat16"),
+             Kc=(4096, "bfloat16"), zr=(4096, "bfloat16"),
              eqV=(4096, "bfloat16"), eqN=(4096, "bfloat16"), Xc=(4096, "bfloat16"), mx=(4096, "bfloat16"), E=(3072, "bfloat16"),
-             NBi=(REM, "int32"), Yk=(1280, "bfloat16"), thI=(8, "int32"),
+             NBi=(SPARE, "int32"), Yk=(1280, "bfloat16"), thI=(8, "int32"),
              rS0=(8, "bfloat16"), rS1=(8, "bfloat16"), cI0=(8, "bfloat16"), cI1=(8, "bfloat16"))
 for _k in _BIGB:
     SCRATCH[_k] = ("sbuf", [128, _BIGB[_k][0]], _BIGB[_k][1])
@@ -70,10 +77,6 @@ SEQ = []
 INFO = []
 ORD = dict(tries=9000, seed=5, slack=0.12, share=0.25, move=3.0, shake=0.4, swap=0.2, near=5.0, back=0.7)
 PACE = [(1.25, 2.0, 4.8, 0.3), (1.0, 1.56, 3.8, 0.23), (1.45, 2.6, 6.5, 0.33), (1.15, 1.3, 3, 0.27)]
-
-
-def rem(t):
-    return REM + 1024 * max(t - 1, 0)
 
 
 def relays(core, T, topo, dst):
@@ -139,7 +142,7 @@ def cost(q, m, kw):
         n, mm = count(kw["rhs"]), count(kw["lhsT"])
         return (0.0, max(min(64, mm), n) * (1 if two(kw["lhsT"]) else 4), 0, 0)
     if q == "g":
-        return (0.0, 160 + 2 * count(o), 0, 0)
+        return (0.0, (160 if m == "iota" else 205) + 2 * count(o), 0, 0)
     ins = [kw[k] for k in kw if k not in ("out", "accum_out") and is_view(kw[k])]
     full = [i for i in ins if count(i) > 1]
     n = max([count(o)] + [count(i) for i in full])
@@ -235,6 +238,8 @@ def noter(T):
                 return e.matmul(**a)
             if m == "activation":
                 return e.activation(**a)
+            if m == "affine_select":
+                return e.affine_select(**a)
             return e.iota(**a)
         i = rec(q, cost(q, m, kw), 0.0, reads, writes, emit)
         if m == "matmul":
@@ -477,16 +482,29 @@ def rank_program(g, core, T, topo):
     def KV(c, k, w=128):
         return v("b%d" % c, 128 * k, 128 * k + w)
 
-    def SC(c, k):
-        return v("b%d" % (2 + c), 128 * k, 128 * k + 128)
+    def CV(c, k=0, step=1):
+        return v("b%d" % (2 + c), k, 136, step)
+
+    def CN(c, k=0, step=1):
+        return v("b%d" % (4 + c), 128 + k, 264, step)
 
     def MI(c, k):
-        return v("b%d" % (4 + c), 128 * k, 128 * k + 128)
+        lo = (0, 128, 264)[k]
+        return v("b%d" % (4 + c), lo, lo + 128)
 
     def SM(c, k):
         if k < 2:
             return v("b%d" % (4 + c), 480 + 8 * k, 488 + 8 * k)
         return v("b%d" % (2 + c), 384 + 8 * k, 392 + 8 * k)
+
+    def Wi(c, w=1):
+        return v("sc2", 136 * c + 16, 136 * (c + w), 17)
+
+    def copy_g(out, a):
+        return op("g", "affine_select", out=out, in_=a, pattern=[[0, count(out)]], compare_op=A.is_ge, fill=0.0, base=0,
+                  channel_multiplier=0)
+
+    On = v("On", 0, 128)
 
     def WR(k, w=16):
         return v("b4", 384 + k, 384 + k + w)
@@ -494,7 +512,7 @@ def rank_program(g, core, T, topo):
     load("y", v("NBi", 0, 640), T.nbr[:, 0:640], 0, 2.1)
     load("S", v("z"), T.z0[:], 1, 1.9)
     load("S", v("NBi", 640, 1280), T.nbr[:, 640:1280], 2, 4.5)
-    load("y", v("KK0", 0, 1280), T.ring[:], 3, 4.6)
+    load("y", v("KK0", KB, KB + 1280), T.ring[:], 3, 4.6)
     load("S", v("thI", 0, 1), T.thr[:], 4, 4.7)
     load("y", v("X", 0, 2048), T.mat[:], 5, 7.0)
     load("y", v("X", 2048, 4096), T.mat[:], 6, 9.0)
@@ -502,7 +520,6 @@ def rank_program(g, core, T, topo):
     iota(v("PI"), [[1, 1]], 0, 1)
     iota(v("D2"), [[-16, 8], [0, 16]], 128, 1)
     iota(v("D1"), [[-1, 256]], 256, 1)
-    iota(v("D3"), [[0, 8], [1, 16]], 0, 0)
     iota(v("ic"), [[1, 16]], 0, 0)
     iota(v("t1"), [[16, 16]], 1280, 0)
     iota(v("d0m"), [[128, 2], [0, 8]], 1280, 1)
@@ -513,19 +530,33 @@ def rank_program(g, core, T, topo):
     cp(v("lcol"), v("PI"))
     fill(v("On"), 1.0)
     for t in range(RO):
-        ts(v("C%d" % t), v("On"), float(t), A.mult, v("pcol"), A.subtract)
+        iota(v("C%d" % t, 0, 128, 1, 0, 1), [[0, 8], [-4096, 16]], 4096 * t - 30720, 0)
+        iota(v("E%d" % t, 0, 128, 1, 0, 1), [[0, 8], [4096, 16]], 2048 - 4096 * t, 0)
+    fill(v("pRJ", 0, 128, 1, 0, 1), RJ)
+    fill(v("nRJ", 0, 128, 1, 0, 1), -RJ)
     ts(v("D2"), v("D2"), 4, A.arith_shift_right)
     ts(v("G16b"), v("D2"), 8.0, A.is_equal)
-    act(v("NG"), v("G16b"), scale=-float(SB))
-    for name, x in (("G8f", 1), ("G8h", 2), ("G8b", 1), ("G8s", WS), ("G8m", 4 * SB), ("G8x", -2 * SB)):
+    ts(v("G4"), v("D2"), 8.0, A.is_equal, 4096.0, A.mult)
+    act(v("nG4"), v("G16b"), scale=-4096.0)
+    act(v("NG"), v("G16b"), scale=-2.0 * SB)
+    op("g", "affine_select", out=v("I17"), in_=v("On", 0, 136), pattern=[[-16, 8], [-1, 17]], compare_op=A.is_equal, fill=0.0,
+       base=1, channel_multiplier=1)
+    fill(v("I17", 0, 136, 17), 0.0)
+    for c in OPT["mxs"] and range(2):
+        fill(v("zr", 2048 * c, 2048 * c + 2048, 16), 0.0)
+    for name, x in (("G8h", 2), ("G8b", 1), ("G8s", WS), ("G8m", 4 * SB), ("G8x", -2 * SB)):
         act(v(name), v("G16b", 0, 128, 16), scale=float(x))
     ts(v("D15"), v("D1"), 15, A.bitwise_and)
     ts(v("DM"), v("D15"), 0.0, A.is_equal)
-    act(v("DMB"), v("DM", 0, 128), scale=4096.0)
-    ts(v("RN"), v("D3"), 0.0, A.is_equal, -BIG, A.mult)
-    ts(v("RS"), v("RN"), float(SB), A.add)
+    act(v("sc", 0, 128), v("DM", 15, 143), scale=4096.0)
+    ts(v("sc", 128, 256), v("DM", 0, 128), -BIG, A.mult)
+    tt(v("RN"), v("sc", 0, 128), v("sc", 128, 256), A.add)
+    act(v("nof"), v("DM", 15, 16), scale=4096.0, bias=-4096.0 - OFF)
+    act(v("RS"), v("On", 0, 136), scale=float(SB))
+    act(v("RS", 0, 136, 17), v("On", 0, 8), scale=-BIG)
+    act(v("RS", 1, 136, 17), v("On", 0, 8), scale=float(FAIL - 16 * SB + 128 * SB - OFF))
     ts(v("Ib"), v("D1", 0, 128), 256.0, A.is_equal)
-    for name, x in (("nIb", -1.0), ("nKI", -1024.0), ("nBI", -2.0 ** 19), ("Ih", 0.5), ("row", 512.0)):
+    for name, x in (("IS", 128.0 * SB), ("nIb", -1.0), ("nKI", -1024.0), ("nBI", -2.0 ** 19), ("nHI", -256.0), ("Ih", 0.5), ("row", 512.0)):
         act(v(name), v("Ib"), scale=x)
     cp(v("bl"), v("ic"))
     ts(v("pb"), v("pcol"), 811.0, A.mult)
@@ -533,17 +564,18 @@ def rank_program(g, core, T, topo):
     cp(v("c0"), v("pc"))
     ts(v("Tri"), v("D1", 0, 128), 256.0, A.is_lt)
     tt(v("Tri"), v("Tri"), v("row"), A.add)
-    for name, x in (("cK", (FAIL - SB) / 128.0), ("fb", -15.0), ("h18", 2.0 ** 18), ("h10", 1024.0), ("C256", 256.0),
-                    ("pR16", R16), ("nR16", -R16), ("cM", -128.0), ("cZ", -1024.0), ("nfc", 0.5), ("q0", 1023.75),
-                    ("drb", -512.0 * SB), ("f0", -7.5 / 16), ("f1", 0.5 - 7.5 * SB), ("rw", 0.5)):
+    for name, x in (("fb", -15.0), ("h18", 2.0 ** 18), ("C256", 256.0),
+                    ("pR16", R16), ("nR16", -R16), ("cM", -128.0), ("cZ", -1024.0), ("nfc", 1.0 - MID), ("q0", 1023.75),
+                    ("drb", -2.5), ("f0", -7.5 / 16), ("f1", 1.0 - MID - 7.5 * SB), ("rw", 0.5)):
         act(v(name), v("On", 0, count(v(name))), scale=x)
-    for name in ("KK0", "KK1"):
-        act(v(name, 1280, REM), v("DM"), scale=0.0)
-    fill(v("NBi", 1280, REM), 0)
+    act(v("KK0", KB + 1280, KB + SPARE), v("DM"), scale=0.0)
+    for t in range(RO):
+        act(v("KK%d" % t, 1024, KB), v("On", 0, 16), scale=0.0)
+    fill(v("NBi", 1280, SPARE), 0)
     ts(v("dOh"), v("t1"), v("pcol"), A.add)
     ts(v("pb"), v("PI"), 4, A.arith_shift_right, 1, A.bitwise_and)
     cp(v("odd"), v("pb"))
-    scan(v("row"), v("rw"), v("On"), A.mult, 2.0 ** 64, A.mult)
+    scan(v("row"), v("rw"), On, A.mult, 2.0 ** 64, A.mult)
     tt(v("rw"), v("row"), v("Ib"), A.mult)
     op("v", "tensor_reduce", out=v("wcol"), in_=v("rw"), axis=AxisListType.X, op=A.add)
     act(v("w25"), v("wcol"), scale=2.5)
@@ -554,7 +586,7 @@ def rank_program(g, core, T, topo):
         act(v("CT", 2 ** r, 2 ** r + w), v("CT", 0, w), scale=v("sgn", r, r + 1))
     ts(v("th"), v("thI", 0, 1), 6, A.arith_shift_right)
     ts(v("tl"), v("thI", 0, 1), 63, A.bitwise_and)
-    ts(v("Q", 0, 1), v("th"), -64.0 * SB, A.mult)
+    ts(v("Q", 0, 1), v("th"), -64.0 * SB, A.mult, MID, A.add)
     ts(v("Q", 1, 2), v("tl"), -float(SB), A.mult)
     act(v("Q", 2, 3), v("pcol"))
     act(v("Q", 3, 4), v("On", 0, 1), scale=16.0)
@@ -570,9 +602,10 @@ def rank_program(g, core, T, topo):
     for c in range(2):
         act(KV(c, 2), hv("z", c), scale=0.5)
         act(hv("zq", c), hv("z", c), AF.Identity, scale=0.5, bias=v("q0"))
+        act(hv("zb", c), hv("z", c), scale=0.5)
 
     def send_rings(t):
-        names = ("KK0", "NM") if t else ("KK0",)
+        names = (("KK0", KB), ("NM", 0)) if t else (("KK0", KB),)
 
         def emit(e):
             parts = []
@@ -580,13 +613,12 @@ def rank_program(g, core, T, topo):
                 rid, pid = topo.addr(rl[h], core)
                 parts.append(RemoteDMATransfer(dst_ids=[DstId(rid=rid, pnc=pid)], remote_sem=T.sem["ha%d" % t],
                                                dma_engine_mask=engines_mask(topo, core, rl[h], 8 * h, 8 * h + 8),
-                                               srcs=[res(v(x, 512 * h, 512 * h + 512)) for x in names],
+                                               srcs=[res(v(x, b + 512 * h, b + 512 * h + 512)) for x, b in names],
                                                dsts=[T["hand%d" % t][:]], alu_op=len(names) - 1))
             g.remote_dma_fused(parts, local_sem=T.sem["ks%d" % t])
-        i = rec("g", 0.4 if t else 3.0, 4.0, [v(x, 0, 1024) for x in names], [], emit, "ks%d" % t, 16)
+        i = rec("g", 0.4 if t else 3.0, 4.0, [v(x, b, b + 1024) for x, b in names], [], emit, "ks%d" % t, 16)
         for h in range(2):
-            lo = rem(t) + 512 * h
-            land(v("KK%d" % min(t, 1), lo, lo + 512), "ki%d%d" % (t, h), i, 7.0 if t else 10.0)
+            land(v("KK%d" % t, 512 * h, 512 * h + 512), "ki%d%d" % (t, h), i, 7.0 if t else 10.0)
 
     def send_revoked(t):
         src = v("rS%d" % t, 0, 1)
@@ -596,14 +628,15 @@ def rank_program(g, core, T, topo):
         land(v("cI%d" % t, 0, 1), "ri%d" % t, rec("g", 0.3, 4.0, [src], [], emit, "rs%d" % t, 8), 5.0)
 
     def K(t):
-        return v("KK%d" % min(t, 1), 0, 1280)
+        return v("KK%d" % t, KB, KB + 1280)
 
     def vo(t, c):
         b = 16 * (t % 2)
         return v("vO", b + 8 * c, b + 8 * c + 8)
 
-    def fifth(name, c):
-        return v(name, 640 * c, 640 * c + 640, 5)
+    def fifth(name, c, w=1):
+        b = KB if name == "KK0" else 0
+        return v(name, b + 640 * c, b + 640 * (c + w), 5)
 
     def to_o(out, copy, x, weights):
         tt(copy, ind(x, v("bl", 0, 8)), v("DM", 0, 128), A.mult)
@@ -612,52 +645,39 @@ def rank_program(g, core, T, topo):
     tab = v("NBi", 0, 1280)
 
     def first(t, c):
-        u = MI(c, 0)
-        group(u, [(v("Ib"), v("C%d" % t)), (v("G16b"), hv("zh" if t else "z", c))])
-        ts(hv("r16", c), u, R16, A.add, -R16, A.add)
+        z, one = hv("zh" if t else "z", c), v("On", 0, 128, 1, 0, 1)
+        rows = [v(x, 0, 128, 1, 0, 1) for x in ("C%d" % t, "pRJ", "nRJ", "E%d" % t)]
         if t:
-            tt(hv("oh", c), u, hv("r16", c), A.is_equal)
-            tt(hv("mB", c), ind(tab, vo(t, c)), hv("oh", c), A.mult)
-        else:
-            tt(KV(c, 3), u, hv("r16", c), A.is_equal)
-            tt(hv("mB", c), KV(c, 3), fifth("NBi", c), A.mult)
-        group(u, [(v("Ib"), v("DMB")), (v("G16b"), hv("mB", c))])
-        scan(hv("sc", c), v("RN"), u, A.max)
+            cp(hv("Bv", c), ind(tab, vo(t, c)))
+        group(MI(c, 0), [(rows[0], one), (v("G4"), z), (rows[1], one), (rows[2], one), (v("nG4"), z), (rows[3], one)])
+        tt(hv("mB", c), MI(c, 0), hv("Bv", c) if t else fifth("NBi", c), A.min)
+        mm(MI(c, 1), v("G16b"), hv("mB", c))
+        scan(hv("sc", c), v("RN"), MI(c, 1), A.max)
         no = v("nO", 16 * c, 16 * c + 8)
-        ts(no, v("sc", 128 * c + 15, 128 * c + 128, 16), -4096.0, A.add)
+        ts(no, v("sc", 128 * c + 15, 128 * c + 128, 16), v("nof"), A.add)
         cp(hv("BnL", c), ind(tab, no))
         cp(hv("BnH", c), hv("BnL", c))
-        if t < RO - 1:
-            mm(MI(c, 1), v("G16b"), hv("mB", c))
         if not t and not c:
             act(MI(0, 2), hv("V2", 0))
 
     def second(t, c):
         both, rawv, rawn = hv("KN", c, 256), hv("KN", 2 * c), hv("KN", 2 * c + 1)
-        act(rawn, ind(K(0), v("nO", 16 * c, 16 * c + 8)))
+        act(rawn, ind(K(0), v("nO", 16 * c, 16 * c + 8)), bias=-2.0 ** -11)
         if t:
-            act(rawv, ind(K(0), vo(t, c)))
-            act(hv("mh", c, 256), both, AF.Relu, scale=-1024.0, bias=v("h10"))
+            act(rawv, ind(K(0), vo(t, c)), bias=-2.0 ** -10)
             if c:
                 ts(hv("m1", c, 256), both, v("rS%d" % (t - 1), 0, 1), A.is_equal)
             else:
                 ts(hv("m1", c, 256), both, v("rq"), A.add, v("c2"), A.is_equal)
-            group(KV(c, 0, 256), [(v("Ib"), both), (v("nIb"), hv("mh", c, 256)), (v("nKI"), hv("m1", c, 256))])
+            group(KV(c, 0, 256), [(v("Ib"), both), (v("nKI"), hv("m1", c, 256))])
         else:
-            ts(hv("mh", 2 * c), fifth("KK0", c), 0.0, A.is_equal, 1024.0, A.mult)
-            if c:
-                act(hv("mh", 3), rawn, AF.Relu, scale=-1024.0, bias=v("h10"))
-            else:
-                ts(hv("mh", 1), rawn, 0.0, A.is_equal, 1024.0, A.mult)
-            mm(KV(c, 0, 256), v("nIb"), hv("mh", c, 256), True, False)
-            mm(KV(c, 0), v("Ib"), fifth("KK0", c), False, False)
-            mm(KV(c, 1), v("Ib"), rawn, False, True)
+            act(rawv, fifth("KK0", c), bias=-2.0 ** -10)
+            mm(KV(c, 0, 256), v("Ib"), both)
         for b in (128 * c, 128 * c + 64):
             gather(("K", t, b // 64), "Kc", K(0), "BnL", b, 1.0)
         tt(hv("evn", c), KV(c, 0), rawn, A.is_equal)
         mm(SM(c, 1), hv("evn", c), v("G8b"))
-        act(hv("dr", c, 8), SM(c, 1), AF.Relu, scale=256.0 * SB, bias=v("drb"))
-        group(SM(c, 0), [(v("On"), v("cK")), (hv("mB", c), v("G8b")), (v("Ib"), hv("dr", c, 8))])
+        act(hv("dr", c, 8), SM(c, 1), AF.Sign, bias=v("drb"))
         for q in range(2):
             for e, eq in enumerate(("eqV", "eqN")):
                 for k in range(16):
@@ -666,15 +686,17 @@ def rank_program(g, core, T, topo):
                     chain("eq", tt(v(eq, *s), v("b%d" % c, b, b + 64), v("Kc", *s), A.is_equal))
 
     def third(t, c):
-        for o, eq in ((SC(c, 0), "eqV"), (MI(c, 0), "eqN")):
-            mm(o, hv("BnH", c), v("Ib"), True, False)
+        for o, eq in ((CV, "eqV"), (CN, "eqN")):
+            mm(o(c), hv("BnH", c), v("I17"), True, False)
+            if o is CV:
+                mm(o(c, 0, 17), hv("mB", c), v("G8b"), False, False)
+                mm(o(c, 0, 17), v("IS"), hv("dr", c, 8), False, False)
             for k in range(16):
-                mm(v(o[1], k, 128, 16), v(eq, 2048 * c + k, 2048 * c + 2048, 16), v("G8s"), False, k == 15)
-        act(hv("cV", c), SC(c, 0))
-        tt(hv("mn", c), MI(c, 0), hv("cV", c), A.min)
-        scan(hv("sc2", c), v("RS"), hv("mn", c), A.max)
-        tt(hv("Wi", c, 8), v("sc2", 128 * c + 15, 128 * c + 128, 16), SM(c, 0), A.max)
-        ts(hv("wT", c, 8), hv("Wi", c, 8), SB - 1, A.bitwise_and)
+                mm(o(c, k + 1, 17), v(eq, 2048 * c + k, 2048 * c + 2048, 16), v("G8s"), False, k == 15)
+        act(hv("cV", c, 136), CV(c))
+        tt(hv("mn", c, 136), CN(c), hv("cV", c, 136), A.min)
+        scan(hv("sc2", c, 136), v("RS"), hv("mn", c, 136), A.max)
+        ts(hv("wT", c, 8), Wi(c), SB - 1, A.bitwise_and)
         to_o(SM(c, 2), hv("Aw", c), hv("wT", c, 8), v("G8b"))
         w = vo(t + 1, c)
         cp(w, SM(c, 2))
@@ -685,8 +707,11 @@ def rank_program(g, core, T, topo):
             tt(hv("kp", c), MI(c, 2), hv("Kw", c), A.mult)
         ts(hv("k2", c), hv("kp", c), 2, A.arith_shift_right, SB - 1, A.bitwise_and)
         ts(hv("PL", c), hv("k2", c), v("c0"), A.add, float(t), A.add)
-        act(hv("hole", c), KV(c, 0), AF.Relu, scale=-1.0)
-        act(hv("hz", c), hv("Kw", c), AF.Relu, scale=-2.0 ** 18, bias=v("h18"))
+        act(hv("Kt", c), KV(c, 0), AF.Relu)
+        if OPT["hz"] == "s":
+            act(hv("hz", c), hv("Kw", c), AF.Relu, scale=-2.0 ** 18, bias=v("h18"))
+        else:
+            ts(hv("hz", c), hv("Kw", c), 0.0, A.is_equal, 2.0 ** 18, A.mult)
         tt(hv("pr", c), KV(c, 2), hv("Kw", c), A.mult)
         mm(SM(c, 4), hv("pr", c), v("G8h"))
         cp(hv("hi", c, 8), SM(c, 4))
@@ -694,37 +719,51 @@ def rank_program(g, core, T, topo):
     def next_nodes(t, c):
         act(hv("Vn", c), ind(v("T1"), vo(t + 1, c)))
         act(hv("V2", c) if c else MI(c, 2), hv("Vn", c), scale=2.0, bias=1.0)
-        if t:
-            tt(KV(c, 3), MI(c, 1), hv("Vn", c), A.subtract)
-            tt(hv("ohd", c), KV(c, 3), hv("oh", c), A.mult)
-        else:
-            tt(hv("dl", c), MI(c, 1), hv("Vn", c), A.subtract)
-            tt(KV(c, 3), KV(c, 3), hv("dl", c), A.mult)
+        tt(hv("aH", c), MI(c, 0), hv("Vn", c), A.min)
 
     def material(t, c):
+        run = (t, c) in OPT["mxs"]
+        if run:
+            for p in range(1, 16):
+                copy_g(v("zr", 2048 * c + p, 2048 * c + 2048, 16), hv("zb", c))
         for q in range(2):
             lo = 2048 * c + 1024 * q
             gather(("X", t, 2 * c + q), "Xc", v("X"), "PL", lo // 16, 0.5)
-            for p in range(16):
-                chain("mx", tt(v("mx", lo + p, lo + 1024, 16), v("b%d" % c, 256 + 64 * q, 320 + 64 * q),
-                               v("Xc", lo + p, lo + 1024, 16), A.max))
+            if not run:
+                for p in range(16):
+                    chain("mx", tt(v("mx", lo + p, lo + 1024, 16), v("b%d" % c, 256 + 64 * q, 320 + 64 * q),
+                                   v("Xc", lo + p, lo + 1024, 16), A.max))
+                continue
+            w = 1024 // len(SPLIT.get(("X", t, 2 * c + q), "s"))
+            for a in range(lo, lo + 1024, w):
+                head, keep, zc = v("Xc", a, a + w, 16), v("x0", a // 16, (a + w) // 16), 256 + (a - 2048 * c) // 16
+                (act if OPT["rs"] == "s" else cp)(keep, head)
+                tt(head, v("b%d" % c, zc, zc + w // 16), keep, A.max)
+                chain("mx", scan(v("mx", a, a + w), v("zr", a, a + w), v("Xc", a, a + w), A.max, 0.0, A.min))
+        if run:
+            copy_g(v("Xc", 2048 * c, 2048 * c + 2048, 16), hv("x0", c))
 
     def fourth(t, c):
-        dT, lo, bank = SC(c, 2), 2048 * c, "b%d" % (2 + c)
+        lo, bank = 2048 * c, "b%d" % (2 + c)
+        dT = v(bank, 256, 384)
+        run = (t, c) in OPT["mxs"]
         mm(dT, v("LR", 128, 256, 1, 0, 4), v("LR", 0, 128, 1, 0, 4), True, False)
-        for a, b in ((0, 96), (96, 128)):
+        mm(dT, hv("zb", c), v("NG"), False, False)
+        cuts = [(name, a, b) for name, x in (("Xc", OPT["xs"]), ("mx", OPT["ms"] if run else 128))
+                for a, b in ((0, x), (x, 128)) if b > a]
+        cuts.sort(key=lambda x: x[2])
+        for i, (name, a, b) in enumerate(cuts):
             for p in range(16):
-                mm(v(bank, 256 + p, 384, 16, a, b), v("Xc", lo + 16 * a + p, lo + 16 * b, 16), v("G8x"), False, False)
-        for p in range(16):
-            mm(v(bank, 256 + p, 384, 16), v("mx", lo + p, lo + 2048, 16), v("G8m"), False, False)
-        mm(dT, hv("z", c), v("NG"), False, True)
+                src = v(name, lo + 16 * a + p, lo + 16 * b, 16)
+                if run and name == "Xc" and not p:
+                    src = v("x0", 128 * c + a, 128 * c + b)
+                mm(v(bank, 256 + p, 384, 16, a, b), src, v("G8x" if name == "Xc" else "G8m"), False, i == len(cuts) - 1 and p == 15)
         if c:
-            ts(hv("nf", c), dT, v("nfc"), A.add, 0.0, A.max)
+            ts(hv("nf", c), dT, v("nfc"), A.add, 2.0 ** -12, A.max)
         scan(hv("sd", c), v("RD"), dT, A.min)
         if not c:
             act(hv("nf", c), dT, AF.Relu, bias=v("nfc"))
-        cp(hv("pi", c, 8), v("sd", 128 * c + 15, 128 * c + 128, 16))
-        ts(hv("pi2", c, 8), hv("pi", c, 8), SB - 1, A.bitwise_and)
+        ts(hv("pi2", c, 8), v("sd", 128 * c + 15, 128 * c + 128, 16), SB - 1, A.bitwise_and)
         to_o(SM(c, 3), hv("Ap", c), hv("pi2", c, 8), v("G8b"))
         do = v("dO", 16 * c, 16 * c + 8)
         cp(do, SM(c, 3))
@@ -733,17 +772,22 @@ def rank_program(g, core, T, topo):
             ts(hv("zF", c), hv("zh", c), -1024.0, A.add)
             store("Sy"[c], T.yz[:, 128 * c:128 * c + 128], hv("zF", c), c)
         cap = v("b%d" % (6 + c), 128, 256)
-        group(cap, [(v("Ib"), v("cM")), (v("Ib"), hv("Kw", c)), (v("nIb"), hv("hz", c)), (hv("nf", c), v("nBI"))])
+        group(cap, [(v("Ib"), v("cM"))] * (1 - c) + [(v("Ib"), hv("Kw", c)), (v("nIb"), hv("hz", c)), (hv("nf", c), v("nBI"))])
         scan(hv("cs", c), v("C256"), cap, A.max, v("cs", 127, 128) if c else -128.0 - 65536)
         if t < RO - 1:
-            group(KV(c, 2), [(v("Ih"), v("cZ")), (v("Ih"), hv("zh", c))])
-            act(hv("z", c), KV(c, 2), scale=2.0)
-            act(hv("zq", c), KV(c, 2), AF.Identity, bias=v("q0"))
+            if OPT["zb"] == "t":
+                group(KV(c, 2), [(v("Ih"), v("cZ")), (v("Ih"), hv("zh", c))])
+                act(hv("zb", c), KV(c, 2))
+                act(hv("zq", c), KV(c, 2), AF.Identity, bias=v("q0"))
+            else:
+                ts(hv("zb", c), hv("zh", c), -1024.0, A.add, 0.5, A.mult)
+                mm(KV(c, 2), v("Ib"), hv("zb", c))
+                act(hv("zq", c), hv("zb", c), bias=1023.75)
 
     def active(t, c):
         f, y = hv("F", c, 8), WR(16 + 8 * c, 8)
-        ts(f, hv("Wi", c, 8), float(FAIL), A.is_lt)
-        ts(hv("D", c, 8), hv("Wi", c, 8), float(DIR), A.is_ge, 1024.0, A.mult)
+        ts(f, Wi(c), float(FAIL), A.is_lt)
+        ts(hv("D", c, 8), Wi(c), float(DIR), A.is_ge, 1024.0, A.mult)
         mm(y, v("Tri"), f, not c, False)
         mm(y, v("Ib"), hv("D", c, 8), False, True)
         ts(hv("aw", c, 8), y, 512.0 + CAP, A.is_lt, v("wcol"), A.mult)
@@ -752,7 +796,7 @@ def rank_program(g, core, T, topo):
             e = 384 * gr + 256 * c
             mm(WR(32 + 8 * c + gr, 1), v("E", e, e + 128), v("aw", 8 * c + gr, 8 * c + gr + 1))
         if not c:
-            mm(WR(24, 8), v("On"), f, True, False)
+            mm(WR(24, 8), On, f, True, False)
             for gr in range(8):
                 mm(WR(24 + gr, 1), v("E", 384 * gr + 128, 384 * gr + 256), v("aB", gr, gr + 1), False, False)
 
@@ -766,16 +810,16 @@ def rank_program(g, core, T, topo):
             ts(v("wf"), WR(32), v("w25"), A.is_lt, 2.0 ** -70, A.mult)
             tt(v("av"), v("aB"), v("vmd"), A.mult)
         else:
-            ts(v("F"), v("Wi"), float(FAIL), A.is_lt)
-            ts(v("D"), v("Wi"), float(DIR), A.is_ge, 1024.0, A.mult)
+            ts(v("F"), Wi(0, 2), float(FAIL), A.is_lt)
+            ts(v("D"), Wi(0, 2), float(DIR), A.is_ge, 1024.0, A.mult)
             mm(WR(16), v("Tri"), v("F"), True, False)
-            mm(WR(24, 8), v("On"), v("F", 0, 8), False, False)
+            mm(WR(24, 8), On, v("F", 0, 8), False, False)
             mm(WR(16), v("Ib"), v("D"), False, True)
             ts(v("act"), WR(16), 512.0 + CAP, A.is_lt)
         ts(v("h2"), v("hi"), 1023, A.bitwise_and)
-        ts(v("hb"), v("h2"), float(rem(t)), A.add)
-        tt(v("hc"), v("hb"), v("F"), A.mult)
-        tt(v("src"), v("hc"), v("wT"), A.max)
+        act(v("hb"), v("F"), scale=-2048.0 - KB, bias=2048.0)
+        tt(v("hc"), v("h2"), v("hb"), A.add)
+        tt(v("src"), v("hc"), v("wT"), A.min)
         if t:
             tt(v("w2"), v("wf"), v("av"), A.mult)
             tt(v("Aqh"), ind(v("w2"), v("bl")), v("DM"), A.mult)
@@ -785,32 +829,35 @@ def rank_program(g, core, T, topo):
             cp(v("scO"), WR(80))
             tt(v("Aq"), ind(v("src"), v("bl")), v("DM"), A.mult)
             for c in range(2):
-                mm(v("b7", 8 * c, 8 * c + 8), hv("Aq", c), v("G8f"))
-            cp(v("srO"), v("b7", 0, 16))
+                mm(v("b7", 8 * c, 8 * c + 8), hv("Aq", c), v("G8b"))
+            ts(v("srO"), v("b7", 0, 16), float(KB), A.add)
         else:
-            ts(v("hd"), v("src"), -1280.0, A.add)
+            ts(v("hd"), v("src"), KB - 1024.0, A.add)
             tt(v("word"), v("hd"), v("act"), A.mult)
             tt(v("Aqh"), ind(v("word"), v("bl")), v("DM"), A.mult)
             for c in range(2):
                 mm(v("b7", 8 * c, 8 * c + 8), hv("Aqh", c), v("G8b"))
-            ts(v("srO"), v("b7", 0, 16), 1280.0, A.add)
+            ts(v("srO"), v("b7", 0, 16), 1024.0, A.add)
         if t < RO - 1:
-            mm(v("b6", 0, 16), v("On"), v("F"))
+            mm(v("b6", 0, 16), On, v("F"))
             act(v("fj"), v("b6", 0, 16), AF.Identity, bias=v("f0"), accum_out=v("fs"))
             next_nodes(t, 1)
-        tt(v("fm"), ind(v("KK%d" % min(t, 1), 0, rem(t) + 1024), v("srO")), v("hole"), A.min)
+            dl = v("b6", 256, 512)
+            group(dl, [(v("nIb"), v("mB")), (v("Ib"), v("aH"))])
+            if t:
+                tt(v("nb"), dl, v("Bv"), A.add)
+                cp(ind(v("NBi"), v("scO")), v("nb"))
+            else:
+                tt(fifth("NBi", 0, 2), dl, fifth("NBi", 0, 2), A.add)
+        act(v("gv"), ind(v("KK%d" % t, 0, KB + 1280), v("srO")))
+        laid = v("b7", 256, 512)
+        group(laid, [(v("nHI"), v("Kt")), (v("Ib"), v("gv"))])
         if t:
-            for c in range(2):
-                tt(hv("val", c), KV(c, 0), hv("fm", c), A.max)
+            tt(v("val"), laid, v("Kt"), A.max)
             ts(v("vm"), v("val"), come, A.not_equal)
-            tt(ind(v("KK0", 0, REM), v("scO")), v("val"), v("vm"), A.mult)
+            tt(ind(v("KK0", KB, KB + SPARE), v("scO")), v("val"), v("vm"), A.mult)
         else:
-            for c in range(2):
-                tt(fifth("KK0", c), KV(c, 0), hv("fm", c), A.max)
-                tt(fifth("NBi", c), fifth("NBi", c), KV(c, 3), A.subtract)
-        if t == 1:
-            tt(v("nb"), ind(tab, v("vO", 16, 32)), v("ohd"), A.subtract)
-            cp(ind(v("NBi"), v("scO")), v("nb"))
+            tt(fifth("KK0", 0, 2), laid, v("Kt"), A.max)
         if t < RO - 1:
             act(v("f2"), v("fs"), AF.Identity, bias=v("pR16"))
             act(v("f3"), v("f2"), AF.Identity, bias=v("nR16"))
@@ -819,7 +866,12 @@ def rank_program(g, core, T, topo):
 
     def same_node(t):
         act(v("code"), ind(v("CT"), v("vO", 16 * (t % 2), 16 * (t % 2) + 16)))
-        act(v("cdO"), v("code"), scale=v("odd"))
+        if OPT["cd"] == "s":
+            act(v("cdO"), v("code"), scale=v("odd"))
+        else:
+            for lo in range(0, 128, 32):
+                op("g", "affine_select", out=v("cdO", 0, 256, 1, lo, lo + 32), in_=v("code", 0, 256, 1, lo, lo + 32),
+                   pattern=[[0, 256]], compare_op=A.is_ge, fill=0.0, base=-16, channel_multiplier=1)
         for gr in range(8):
             lo = 32 * (gr // 2)
             m, hi = ("cdO", lo + 32) if gr % 2 else ("code", lo + 16)
@@ -831,23 +883,34 @@ def rank_program(g, core, T, topo):
     def revoke(t):
         ts(v("rq"), v("cs", 255, 256), R256, A.add, -R256, A.add)
         ts(v("c2"), v("cs", 255, 256), 128.0, A.add)
-        if t == RO - 1:
+        if t == RO - 1 and OPT["fin"] == "sv":
             ts(v("rb"), v("c2"), v("rq"), A.subtract, -256.0, A.mult)
             for i in range(4):
                 lo, o = 320 * i, v("b%d" % (7 - i), 0, 320)
-                act(o, v("KK0", lo, lo + 320), AF.Abs, scale=256.0, bias=v("rb"))
-                tt(v("Yk", lo, lo + 320), o, v("KK0", lo, lo + 320), A.min)
+                act(o, v("KK0", KB + lo, KB + lo + 320), AF.Abs, scale=256.0, bias=v("rb"))
+                tt(v("Yk", lo, lo + 320), o, v("KK0", KB + lo, KB + lo + 320), A.min)
                 if i % 2:
                     store("yS"[i // 2], T.yk[:, lo - 320:lo + 320], v("Yk", lo - 320, lo + 320), 2 + i // 2)
+            return
+        if t == RO - 1:
+            ts(v("rb"), v("c2"), v("rq"), A.subtract)
+            ts(v("nrv"), v("c2"), v("rq"), A.subtract, -1.0, A.mult)
+            for i in range(2):
+                lo = 640 * i
+                ts(v("NM", lo, lo + 640), v("KK0", KB + lo, KB + lo + 640), v("rb"), A.is_equal, v("nrv"), A.mult)
+            for i in range(2):
+                lo = 640 * i
+                scan(v("Yk", lo, lo + 640), v("NM", lo, lo + 640), v("KK0", KB + lo, KB + lo + 640), A.add, 0.0, A.min)
+                store("yS"[i], T.yk[:, lo:lo + 640], v("Yk", lo, lo + 640), 2 + i)
             return
         rv = v("rS%d" % t, 0, 1)
         ts(rv, v("c2"), v("rq"), A.subtract)
         send_revoked(t)
         ts(v("nrv"), v("c2"), v("rq"), A.subtract, -1.0, A.mult)
-        rec("y", 0.05, 3.5, [K(0)], [K(1)], lambda e: e.dma_start(res(K(1)), res(K(0))), "cp%d" % t, 16)
+        rec("y", 0.05, 3.5, [K(0)], [K(t + 1)], lambda e: e.dma_start(res(K(t + 1)), res(K(0))), "cp%d" % t, 16)
         ts(v("NM"), K(0), rv, A.is_equal, v("nrv"), A.mult)
         send_rings(t + 1)
-        add_into(K(1), v("NM"), t)
+        add_into(K(t + 1), v("NM"), t)
         act(v("nfc"), v("fs"), AF.Identity, scale=-float(SB), bias=v("f4"))
 
     send_rings(0)
@@ -888,8 +951,7 @@ def hand_on(g, core, T, topo):
             if core in rl:
                 h = rl.index(core)
                 g.wait_ge(T.sem["ha%d" % t], 8)
-                lo = rem(t) + 512 * h
-                remote(g, topo, core, below, T["KK%d" % min(t, 1)][:, lo:lo + 512], T["hand%d" % t][:],
+                remote(g, topo, core, below, T["KK%d" % t][:, 512 * h:512 * h + 512], T["hand%d" % t][:],
                        T.sem["ki%d%d" % (t, h)], T.sem["hs%d" % t])
         for t in range(RO):
             if core in rl:

@@ -7,31 +7,38 @@ A = AluOpType
 AF = ActivationFunctionType
 RO, SB, CAP = 3, 2048, 96
 BIG = 1.0e9
-R256, R16 = 1.5 * 2 ** 31, 1.5 * 2 ** 27
+R256, R16, R1024 = 1.5 * 2 ** 31, 1.5 * 2 ** 27, 1.5 * 2 ** 33
 SPLIT = {("X", t, q): "ss" for t in range(RO) for q in (1, 3)}
-SPLIT["K", 0, 0] = "sv"
+
 KB = 1040
-SPARE = 1536
+SPARE = 1408
 WS = 17 * SB
-FAIL, DIR = 51 * SB, 290 * SB
+FAIL = 51 * SB
 RJ = 1.5 * 2 ** 39
 OFF = 15 * 2048 - 120 * 4096
 MID = 2.0 ** 23
-OPT = dict(mxs=[], xs=96, ms=128, fin="v", zb="v", hz="s", cd="s", rs="s")
+HALF = 0.5 - 2.0 ** -11
+BY = 2
+OPT = dict(run=0, rv="v", xs=(0, 96, 128), drk=14, ms=128, blk=128, split=False, hz="s", piece=256, rs="s", true="dma", come="dma",
+           Bv="s", nO="v", BnL="s", BnH="s", PL="s", nf="s", zb="s", zF="s", nb="s", dO="v", vO="v", scO="v", srO="v", hi="s",
+           hn="s", Kn="post", kp="fused", Hm="s", fill="laid", wipe=False, ct=11, n="v", to="dm", cap=0, same="early")
+OPT.update({("nO", 0, 0): "v", ("BnL", 0, 0): "v", "ct": 7, "hn": "v", "zF": "v"})
+SPLIT.update({(x, t, q): "s....v.." for t in range(RO) for x, q in (("X", 0), ("X", 2), ("K", 0))})
+SPLIT["K", 0, 0] = "sv"
 
-F32 = dict(G8h=8, RN=128, RS=136, RD=128, TH=128, T1=1280, sc=256, cV=272, mn=272, Vn=256,
-           V2=256, pr=256, zq=256, cs=256, zF=256, row=128, rw=128, pcol=1, lcol=1, odd=1, c0=1, wcol=1,
-           w25=1, fj=16, fs=1, f0=1, f1=1, f2=1, f3=1, f4=1, nfc=1, d0m=16, vmd=16, av=16, hd=16, wf=16, hb=16, hc=16, src=16,
-           w2=16, word=16, t1=16, fb=1, h18=1, sgn=16, pR16=1, nR16=1, drb=1, q0=1, rq=1, c2=1, nof=1)
-BF = dict(Ib=128, nIb=128, Ih=128, nKI=128, nBI=128, nHI=128, I17=136, G16b=128, G4=128, nG4=128, NG=128, G8b=8, G8s=8, G8m=8,
-          G8x=8, rb=1, IS=128, Tri=128, On=144, DM=256, C0=128, C1=128, C2=128, E0=128, E1=128, E2=128, pRJ=128, nRJ=128,
-          cM=128, cZ=128, C256=128, CT=1280, Q=16, LR=256, z=256, zb=256, x0=256, KN=512, Kw=256, Kt=256, gv=256, evn=256,
-          m1=512, hz=256, val=256, vm=256, code=256, cdO=256, nf=256, F=16, D=16, act=16, aw=16, aB=16,
-          dr=16, NM=1280, nrv=1, ncome=1)
-H16 = dict(mB=256, Bv=256, aH=256, BnH=256, Aw=256, Ap=256, Aqh=256, Aq=256, dOh=16, zh=256)
-I32 = dict(PI=1, pi15=1, pb=1, pc=1, th=1, tl=1, D1=256, D15=256, D2=128, D3=128, ic=16, kp=256, k2=256, pi2=16, sc2=272, sd=256,
-           wT=16, hi=16, h2=16, nb=256)
-U16 = dict(bl=16, vO=32, nO=32, scO=16, srO=16, dO=32, BnL=256, PL=256)
+F32 = dict(G8h=8, nG8h=8, RN=128, RS=136, RD=128, TH=128, T1=1280, sc=256, cV=272, mn=272,
+           V2=256, pr=256, zq=256, cs=256, zF=256, pcol=1, lcol=1, c0=3, wcol=1, wthr=1, spare=1,
+           fj=16, fs=1, f0=1, f1=1, f2=1, f3=1, f4=1, nfc=1, nw=16, sel=16, hc=16, src=16,
+           slot=16, fb=1, h18=1, sgn=16, pR16=1, nR16=1, drb=1, q0=1, rq=1, c2=1, nof=1)
+BF = dict(Ib=128, nIb=128, I5=128, nKI=128, nBI=128, nHI=128, I44=128, nI44=128, nFI=128, I17=136, G16b=128, G4=128, nG4=128,
+          NG=128, G8b=8, G8s=8, G8m=8, G8x=8, rb=1, IS=128, Tri=128, On=256, DM=256, C0=128, C1=128, C2=128, E0=128, E1=128,
+          E2=128, pRJ=128, nRJ=128, cM=128, cQ=128, c18=128, C256=128, CT=1280, Q=16, LR=256, z=256, zb=256, x0=256, KN=512,
+          Kw=256, Kx=256, Kt=512, gv=256, evn=256, m1=512, m2=512, hz=256, Hm=256, val=256, vm=256, code=256, nf=256, F=16, aw=16, dr=16, NM=1280, NC=1280,
+          nrv=1, Wd=240, Wn=144, M2=128, c12=16, row=128, rw=128)
+H16 = dict(mB=256, Bv=256, aH=256, BnH=256, Aw=256, Ap=256, Aqh=256, Aq=256, zh=256, hn=16)
+I32 = dict(PI=1, pi15=1, pb=1, pc=1, po=1, p8=1, ps=1, th=1, tl=1, D1=16, D15=16, ic=16, kp=256, k2=256, pi2=16, sc2=272,
+           sd=256, wT=32, hi=16, h2=16, nb=256)
+U16 = dict(bl=16, bl2=8, vO=32, nO=32, scO=16, srO=16, hO=16, dO=32, BnL=256, PL=256)
 
 
 def _layout(d):
@@ -49,10 +56,10 @@ for _d, _n, _t in ((F32, "SF", "float32"), (BF, "SBF", "bfloat16"), (H16, "SH", 
     SCRATCH[_n] = ("sbuf", [128, _w], _t)
     for _k in _d:
         WHERE[_k] = (_n, _p[_k], _d[_k])
-_BIGB = dict(KK0=(KB + SPARE, "bfloat16"), KK1=(KB + 1280, "bfloat16"), KK2=(KB + 1280, "bfloat16"), X=(4096, "bfloat16"),
+_BIGB = dict(KK0=(KB + SPARE, "bfloat16"), KK1=(KB + SPARE, "bfloat16"), KK2=(KB + SPARE, "bfloat16"), X=(4096, "bfloat16"),
              Kc=(4096, "bfloat16"), zr=(4096, "bfloat16"),
-             eqV=(4096, "bfloat16"), eqN=(4096, "bfloat16"), Xc=(4096, "bfloat16"), mx=(4096, "bfloat16"), E=(3072, "bfloat16"),
-             NBi=(SPARE, "int32"), Yk=(1280, "bfloat16"), thI=(8, "int32"),
+             eqV=(4096, "bfloat16"), eqN=(4096, "bfloat16"), Xc=(4096, "bfloat16"), mx=(4096, "bfloat16"), E=(2048, "bfloat16"),
+             Y1=(1280, "bfloat16"), W2=(SPARE, "bfloat16"), NBi=(SPARE, "int32"), Yk=(1280, "bfloat16"), thI=(8, "int32"),
              rS0=(8, "bfloat16"), rS1=(8, "bfloat16"), cI0=(8, "bfloat16"), cI1=(8, "bfloat16"))
 for _k in _BIGB:
     SCRATCH[_k] = ("sbuf", [128, _BIGB[_k][0]], _BIGB[_k][1])
@@ -75,8 +82,10 @@ CY = 0.00083
 STEP = [""]
 SEQ = []
 INFO = []
-ORD = dict(tries=9000, seed=5, slack=0.12, share=0.25, move=3.0, shake=0.4, swap=0.2, near=5.0, back=0.7)
-PACE = [(1.25, 2.0, 4.8, 0.3), (1.0, 1.56, 3.8, 0.23), (1.45, 2.6, 6.5, 0.33), (1.15, 1.3, 3, 0.27)]
+ORD = dict(tries=11000, starts=0, heat=700, seed=6, slack=0.12, share=0.25, move=3.0, shake=0.4, swap=0.2, near=5.0, back=0.7, free=True, act=55,
+           moves=16000, lean=0.3, warm=0.006)
+PACE = [(1.25, 1.95, 4.75, 0.3, 1.0, 89.0), (1.0, 1.56, 3.8, 0.1, 0.6, 67.2), (1.0, 1.2, 2.3, 0.15, 1.0, 68.5),
+        (1.25, 1.38, 2.25, 0.16, 0.8, 81.2), (1.25, 2.5, 6.9, 0.16, 0.8, 95.5), (1.45, 2.26, 5.5, 0.25, 1.0, 98.7)]
 
 
 def relays(core, T, topo, dst):
@@ -142,7 +151,7 @@ def cost(q, m, kw):
         n, mm = count(kw["rhs"]), count(kw["lhsT"])
         return (0.0, max(min(64, mm), n) * (1 if two(kw["lhsT"]) else 4), 0, 0)
     if q == "g":
-        return (0.0, (160 if m == "iota" else 205) + 2 * count(o), 0, 0)
+        return (0.0, (220 if m == "iota" else 265) + 2 * count(o), 0, 0)
     ins = [kw[k] for k in kw if k not in ("out", "accum_out") and is_view(kw[k])]
     full = [i for i in ins if count(i) > 1]
     n = max([count(o)] + [count(i) for i in full])
@@ -156,7 +165,7 @@ def cost(q, m, kw):
         c = 2.0
     if q == "v" and m != "tensor_tensor" and two(o) and not [i for i in full if not two(i)]:
         c = 0.5
-    return (0.0, max(64, n * c), 0, 0)
+    return (0.0, max(64, n * c) + ORD["act"] * (q == "s"), 0, 0)
 
 
 def noter(T):
@@ -171,7 +180,7 @@ def noter(T):
             return T[b][x[5]:x[6], lo:range(lo, hi, x[4])[-1] + 1:x[4]]
         return T[b][x[5]:x[6], lo:hi]
 
-    def touch(i, q, v, wr, deps):
+    def touch(i, q, v, wr, deps, turns):
         ps = psum(v)
         keep = []
         for e in hist.setdefault(v[1], []):
@@ -180,7 +189,7 @@ def noter(T):
                 keep.append(e)
                 continue
             if ps and eq != q:
-                deps.add((ei, True))
+                (deps if (wr or ew) and clash(v, ev) else turns).add((ei, True))
                 if wr and covers(v, ev):
                     continue
             elif (wr or ew) and clash(v, ev):
@@ -192,20 +201,26 @@ def noter(T):
         keep.append((v, wr, q, i))
         hist[v[1]] = keep
 
-    def rec(q, c, tail, reads, writes, emit, sem=None, inc=1):
-        i = len(ops)
-        deps = set()
+    def rec(q, c, tail, reads, writes, emit, sem=None, inc=1, join=False):
+        i = len(ops) - join
+        deps, turns, banks = (ops[i][3], ops[i][9], ops[i][10]) if join else (set(), set(), set())
         for v in reads:
-            touch(i, q, v, False, deps)
+            touch(i, q, v, False, deps, turns)
         for v in writes:
-            touch(i, q, v, True, deps)
+            touch(i, q, v, True, deps, turns)
+        banks.update(int(v[1][1:]) for v in reads + writes if psum(v))
         if not isinstance(c, tuple):
             c = (c, 0, 0, 0)
+        if join:
+            ops[i][1] = tuple(a + b for a, b in zip(ops[i][1], c))
+            ops[i][4].append(emit)
+            return i
         name = writes[0][1] if writes else "out"
-        ops.append([q, c, tail, deps, emit, sem or "q" + q, inc, STEP[0] + (name[:2] if q == "v" and name[:2] in ("eq", "mx") else q)])
+        ops.append([q, c, tail, deps, emit and [emit], sem or "q" + q, inc,
+                    STEP[0] + (name[:2] if q == "v" and name[:2] in ("eq", "mx") else q), name, turns, banks])
         return i
 
-    def op(q, m, **kw):
+    def op(q, m, join=False, **kw):
         reads, writes = [], []
         for k in kw:
             x = kw[k]
@@ -230,8 +245,6 @@ def noter(T):
                 return e.tensor_tensor(**a)
             if m == "tensor_scalar":
                 return e.tensor_scalar(**a)
-            if m == "tensor_reduce":
-                return e.tensor_reduce(**a)
             if m == "tensor_tensor_scan":
                 return e.tensor_tensor_scan(**a)
             if m == "matmul":
@@ -241,10 +254,10 @@ def noter(T):
             if m == "affine_select":
                 return e.affine_select(**a)
             return e.iota(**a)
-        i = rec(q, cost(q, m, kw), 0.0, reads, writes, emit)
+        i = rec(q, cost(q, m, kw), 0.0, reads, writes, emit, join=join)
         if m == "matmul":
             b = kw["out"][1]
-            if b in opened:
+            if opened.get(b, i) != i:
                 ops[i][3].add((opened[b], False))
             opened[b] = i
         return i
@@ -262,7 +275,7 @@ def order(ops):
     deps, before = [], [0] * n
     for i in range(n):
         keep, seen = [], 0
-        for j, w in sorted(ops[i][3], reverse=True):
+        for j, w in sorted(ops[i][3] | (set() if ORD["free"] else ops[i][9]), reverse=True):
             if not (w and seen >> j & 1):
                 keep.append((j, w))
             if w:
@@ -270,7 +283,7 @@ def order(ops):
                 before[i] |= before[j] | 1 << j
         deps.append(keep)
     durs = [[o[1][0] + (o[1][1] * p[0] + o[1][2] * p[1] + o[1][3] * p[2]) * CY for o in ops] for p in PACE]
-    tails = [[o[2] or p[3] for o in ops] for p in PACE]
+    tails = [[o[2] * p[4] or p[3] for o in ops] for p in PACE]
     fwds = [[[(j, d[j] + (x[j] if w else 0.0)) for j, w in deps[i]] for i in range(n)] for d, x in zip(durs, tails)]
     dur, tail, fwd, bwd = durs[0], tails[0], fwds[0], [[] for _ in range(n)]
     for i in range(n):
@@ -281,6 +294,9 @@ def order(ops):
     names = sorted(set(o[7] for o in ops))
     step = np.array([names.index(o[7]) for o in ops])
     state = [ORD["seed"]]
+    hop = PACE[0][3]
+    mine = [[3 * b + "vst".index(q[i]) for b in ops[i][10]] for i in range(n)]
+    other = [[3 * b + m for b in ops[i][10] for m in range(3) if "vst"[m] != q[i]] for i in range(n)]
 
     def draw(k):
         state[0] = (state[0] * 6364136223846793005 + 1442695040888963407) % 2 ** 64
@@ -288,54 +304,106 @@ def order(ops):
         return (x * x % 1048573) / 1048573.0
 
     def place(pre, key, turn):
-        key = list(key)
+        key = np.array(key, float).tolist()
         for i in turn:
+            x = key[i]
             for j, _ in pre[i]:
-                if key[j] >= key[i]:
-                    key[i] = key[j] + 1e-7
+                if key[j] >= x:
+                    key[i] = x = key[j] + 1e-7
         st = [0.0] * n
         busy = {x: ([], []) for x in set(q)}
-        for i in sorted(turn, key=lambda k: key[k]):
+        shut = [([], []) for _ in range(24)]
+        for i in np.argsort(key, kind="stable").tolist():
             s = 0.0
             for j, lag in pre[i]:
                 if st[j] + lag > s:
                     s = st[j] + lag
             if q[i] != "x":
                 lo, hi = busy[q[i]]
+                d = dur[i] - 1e-9
                 k = m = len(lo)
                 while k and hi[k - 1] > s:
                     k -= 1
-                while k < m and lo[k] < s + dur[i] - 1e-9:
-                    s = max(s, hi[k])
-                    k += 1
-                lo.insert(k, s)
-                hi.insert(k, s + dur[i])
+                while True:
+                    while k < m and lo[k] < s + d:
+                        if hi[k] > s:
+                            s = hi[k]
+                        k += 1
+                    was = s
+                    for b in mine[i]:
+                        a, z = shut[b]
+                        x = len(a)
+                        while x and z[x - 1] > s:
+                            x -= 1
+                        while x < len(a) and a[x] < s + d:
+                            s = z[x]
+                            x += 1
+                    if s == was:
+                        break
+                e = s + dur[i]
+                if k and hi[k - 1] > s - 0.02:
+                    if k < m and lo[k] < e + 0.02:
+                        hi[k - 1] = hi[k]
+                        del lo[k], hi[k]
+                    else:
+                        hi[k - 1] = e
+                elif k < m and lo[k] < e + 0.02:
+                    lo[k] = s
+                else:
+                    lo.insert(k, s)
+                    hi.insert(k, e)
+                for b in other[i]:
+                    a, z = shut[b]
+                    f, t = s - hop, e + hop
+                    x = len(a)
+                    while x and a[x - 1] > t:
+                        x -= 1
+                    y = x
+                    while y and z[y - 1] >= f:
+                        y -= 1
+                    if y < x:
+                        f, t = min(f, a[y]), max(t, z[x - 1])
+                    a[y:x], z[y:x] = [f], [t]
             st[i] = s
         return st
 
-    def replay(seq, d, pre):
-        free, st = {x: 0.0 for x in set(q)}, [0.0] * n
+    def replay(seq, p):
+        d, pre, tail, hop = durs[p], fwds[p], tails[p], PACE[p][3]
+        free, st, left = {x: 0.0 for x in set(q)}, [0.0] * n, [0.0] * 24
         for i in seq:
             s = free[q[i]]
             for j, lag in pre[i]:
                 if st[j] + lag > s:
                     s = st[j] + lag
+            for b in mine[i]:
+                if left[b] > s:
+                    s = left[b]
             st[i] = s
             if q[i] != "x":
-                free[q[i]] = s + d[i]
+                s += d[i]
+                free[q[i]] = s
+                for b in other[i]:
+                    if s + hop > left[b]:
+                        left[b] = s + hop
         return max(st[i] + d[i] + tail[i] for i in ends)
 
     up, down = list(range(n)), list(range(n - 1, -1, -1))
     key = up
     best = cur = None
-    for _ in range(ORD["tries"]):
+    heats = []
+    for turn in range(ORD["tries"]):
+        if turn and turn % ORD["heat"] == 0 and len(heats) < ORD["starts"]:
+            heats.append(best)
+            best = cur = min(heats) if len(heats) == ORD["starts"] else None
+            key = cur[1] if cur else up
         st = place(fwd, key, up)
         end = max(st[i] + dur[i] + tail[i] for i in ends)
         r = draw(4)
         if cur is None or end <= cur[2][0] * 1.01:
-            seq = sorted(up, key=lambda k: st[k])
-            e = [end] + [replay(seq, durs[k], fwds[k]) for k in range(1, len(PACE))]
-            val = sum(x / p[0] ** 0.85 for x, p in zip(e, PACE)) / len(e)
+            seq = np.argsort(st, kind="stable").tolist()
+            e = [end] + [replay(seq, k) for k in range(1, len(PACE))]
+            rel = [75 * x / p[5] for x, p in zip(e, PACE)]
+            val = (sum(rel) / len(rel) + max(rel)) / 2
             if best is None or val < best[0]:
                 best = (val, st, e, seq)
             if cur is None or val <= cur[0] + ORD["slack"] * r[0]:
@@ -354,7 +422,7 @@ def order(ops):
                 if not tight and q[i] != "x" and prev[i] is not None:
                     held.append((prev[i], i))
                 i = tight[0] if tight else prev[i] if q[i] != "x" else None
-            for x in draw(1 + int(3 * r[2])):
+            for x in draw(1 + int(3 * r[2])) if held else ():
                 j, i = held[int(x * len(held))]
                 key[j] = st[i] + dur[i] + (tail[i] if r[1] < 0.5 else 0.0)
             continue
@@ -362,13 +430,103 @@ def order(ops):
         if r[1] < ORD["back"]:
             key = -(np.array(place(bwd, -(key + span) + near * ORD["shake"] * r[2] * draw(n), down)) + np.array(dur))
         key = key + near * (move[step] + ORD["shake"] * r[2] * draw(n))
-    INFO[:] = [best[0], best[2], {x: sum(durs[1][i] for i in up if q[i] == x) for x in "vst"}]
-    return best[3]
+
+    qi = ["vstgyx".index(x) for x in q]
+    paces = range(len(PACE))
+
+    def rerun(seq, p, st, lo):
+        d, pre, tail, hop = durs[p], fwds[p], tails[p], PACE[p][3]
+        free, left, st = [0.0] * 6, [0.0] * 24, st[:]
+        for i in seq[max(0, lo - 250):lo]:
+            free[qi[i]] = st[i] + d[i]
+            for b in other[i]:
+                left[b] = max(left[b], st[i] + d[i] + hop)
+        free[5] = 0.0
+        for i in seq[lo:]:
+            m = qi[i]
+            s = free[m]
+            for j, lag in pre[i]:
+                if st[j] + lag > s:
+                    s = st[j] + lag
+            for b in mine[i]:
+                if left[b] > s:
+                    s = left[b]
+            st[i] = s
+            if m != 5:
+                s += d[i]
+                free[m] = s
+                for b in other[i]:
+                    if s + hop > left[b]:
+                        left[b] = s + hop
+        return (max(st[i] + d[i] + tail[i] for i in ends) + ORD["lean"] * sum(st) / n) * 75 / PACE[p][5] / len(PACE), st
+
+    seq = best[3]
+    now = [rerun(seq, p, [0.0] * n, 0) for p in paces]
+    keep, runs = (sum(x[0] for x in now), seq), {}
+    for turn in range(ORD["moves"]):
+        r = draw(6).tolist()
+        p = int(r[0] * len(PACE))
+        if p not in runs:
+            pos, prev, at, held, was = [0] * n, [None] * n, [None] * 6, [()] * n, [None] * 24
+            for x, i in enumerate(seq):
+                pos[i], prev[i], at[qi[i]] = x, at[qi[i]], i
+                held[i] = [was[b] for b in other[i] if was[b] is not None]
+                for b in mine[i]:
+                    was[b] = i
+            s, d = now[p][1], durs[p]
+            i = max(ends, key=lambda u: s[u] + d[u] + tails[p][u])
+            found = [[i]]
+            while True:
+                tight = [j for j, lag in fwds[p][i] if s[j] + lag > s[i] - 1e-7]
+                if tight:
+                    found.append([])
+                elif qi[i] != 5 and prev[i] is not None and s[prev[i]] + d[prev[i]] > s[i] - 1e-7:
+                    tight = [prev[i]]
+                else:
+                    tight = [j for j in held[i] if s[j] + d[j] + PACE[p][3] > s[i] - 1e-7]
+                if not tight:
+                    break
+                i = tight[0]
+                found[-1].append(i)
+            runs[p] = ([b for b in found if len(b) > 1], pos)
+        found, pos = runs[p]
+        b = found[int(r[1] * len(found))]
+        x = int(r[2] * (len(b) - 1))
+        i, j = b[x], b[min(len(b) - 1, x + 1 + int(-np.log(r[3] + 1e-9) * 3))]
+        mid = seq[pos[j]:pos[i] + 1]
+        if r[4] < 0.5:
+            mark = {i}
+            for u in reversed(mid[:-1]):
+                if [w for w, _ in bwd[u] if w in mark]:
+                    mark.add(u)
+            new = [u for u in mid if u in mark] + [u for u in mid if u not in mark]
+        else:
+            mark = {j}
+            for u in mid[1:]:
+                if [w for w, _ in fwd[u] if w in mark]:
+                    mark.add(u)
+            new = [u for u in mid if u not in mark] + [u for u in mid if u in mark]
+        if i in mark and j in mark:
+            continue
+        cand = seq[:pos[j]] + new + seq[pos[i] + 1:]
+        one = rerun(cand, p, now[p][1], pos[j])
+        if one[0] > now[p][0] + 0.05:
+            continue
+        then = [one if k == p else rerun(cand, k, now[k][1], pos[j]) for k in paces]
+        val = sum(x[0] for x in then)
+        if val <= sum(x[0] for x in now) - ORD["warm"] * np.log(r[5] + 1e-9):
+            place_of = np.argsort(np.array(then[0][1])[cand], kind="stable")
+            now, seq, runs = then, np.array(cand)[place_of].tolist(), {}
+            if val < keep[0]:
+                keep = (val, seq)
+    e = [replay(keep[1], p) for p in paces]
+    INFO[:] = [sum(75 * x / p[5] for x, p in zip(e, PACE)) / len(e), e, {x: sum(durs[1][i] for i in up if q[i] == x) for x in "vstg"}]
+    return keep[1]
 
 
 def issue(g, T, ops, seq):
     Q = {"v": g.vector, "s": g.scalar, "t": g.tensor, "g": g, "y": g.sync, "S": g.scalar}
-    total, tok, know = {}, {}, {}
+    total, tok, know, inside = {}, {}, {}, [{} for _ in range(8)]
     for q in Q:
         know[q] = {}
     know["S"] = know["s"]
@@ -380,7 +538,10 @@ def issue(g, T, ops, seq):
             continue
         k = know[q]
         need = {}
-        for j, w in deps:
+        turns = [(inside[b][x], True) for b in ops[i][10] for x in inside[b] if x != q]
+        for b in ops[i][10]:
+            inside[b][q] = i
+        for j, w in sorted(deps) + turns:
             if w:
                 s, v, sn = tok[j]
                 if k.get(s, 0) < v and (s not in need or need[s][0] < v):
@@ -395,10 +556,11 @@ def issue(g, T, ops, seq):
             k[s] = max(k.get(s, 0), v)
             for o in sn:
                 k[o] = max(k.get(o, 0), sn[o])
-        total[sem] = total.get(sem, 0) + inc
-        r = emit(Q[q])
-        if r is not None:
-            r.then_inc(T.sem[sem], inc)
+        for one in emit:
+            total[sem] = total.get(sem, 0) + inc
+            r = one(Q[q])
+            if r is not None:
+                r.then_inc(T.sem[sem], inc)
         tok[i] = (sem, total[sem], dict(k))
     for s in sorted(total):
         if know["g"].get(s, 0) < total[s]:
@@ -417,17 +579,28 @@ def rank_program(g, core, T, topo):
     rv_relay = relays(core, T, topo, above)[0]
     v = view
     last = {}
+    BLK = OPT["blk"]
 
-    def tt(out, a, b, o):
-        return op("v", "tensor_tensor", out=out, in0=a, in1=b, op=o)
+    def who(name, t, c=0):
+        return OPT.get((name, t, c), OPT.get((name, t), OPT[name]))
+
+    def tt(out, a, b, o, join=False):
+        return op("v", "tensor_tensor", join, out=out, in0=a, in1=b, op=o)
 
     def ts(out, a, s1, o1, s2=None, o2=None):
         if o2 is None:
             return op("v", "tensor_scalar", out=out, in0=a, scalar1=s1, scalar2=None, op0=o1)
         return op("v", "tensor_scalar", out=out, in0=a, scalar1=s1, scalar2=s2, op0=o1, op1=o2)
 
-    def cp(out, a):
+    def cp(out, a, q="v"):
+        if q == "s":
+            return act(out, a)
         return op("v", "tensor_copy", out=out, in_=a)
+
+    def plus(out, a, x, q):
+        if q == "s":
+            return act(out, a, AF.Identity if is_view(x) else AF.Copy, bias=x)
+        return ts(out, a, x, A.add)
 
     def fill(out, x):
         return op("v", "memset", out=out, constant=x)
@@ -435,12 +608,12 @@ def rank_program(g, core, T, topo):
     def act(out, a, f=AF.Copy, **kw):
         return op("s", "activation", out=out, in_=a, func=f, **kw)
 
-    def mm(out, l, r, start=True, stop=True):
-        return op("t", "matmul", out=out, lhsT=l, rhs=r, start=start, stop=stop)
+    def mm(out, l, r, start=True, stop=True, join=False):
+        return op("t", "matmul", join, out=out, lhsT=l, rhs=r, start=start, stop=stop)
 
-    def group(out, pairs):
+    def group(out, pairs, by=1):
         for i, (l, r) in enumerate(pairs):
-            mm(out, l, r, i == 0, i == len(pairs) - 1)
+            mm(out, l, r, i == 0, i == len(pairs) - 1, i % by > 0)
 
     def iota(out, pattern, base, cm):
         kw = dict(out=out, pattern=pattern, base=base, channel_multiplier=cm)
@@ -448,11 +621,17 @@ def rank_program(g, core, T, topo):
             kw["allow_small_or_imprecise_dtypes"] = True
         return op("g", "iota", **kw)
 
+    def select(out, a, pattern, base, cm, o=A.is_ge, x=0.0):
+        return op("g", "affine_select", out=out, in_=a, pattern=pattern, compare_op=o, fill=x, base=base, channel_multiplier=cm)
+
+    def copy_g(out, a):
+        return select(out, a, [[0, count(out)]], 0, 0)
+
     def scan(out, a, b, o1, first=0.0, o0=A.add):
         return op("v", "tensor_tensor_scan", out=out, data0=a, data1=b, initial=first, op0=o0, op1=o1)
 
     def chain(name, i):
-        if name in last:
+        if last.get(name, i) != i:
             ops[i][3].add((last[name], False))
         last[name] = i
 
@@ -463,13 +642,15 @@ def rank_program(g, core, T, topo):
         rec(q, 0.1, 2.0, [src], [], lambda e: e.dma_start(dst, res(src)), "st%d" % k, 16)
 
     def add_into(dst, src, k):
-        rec("g", 1.0, 4.5, [src], [dst], lambda e: e.dma_start(res(dst), res(src), accum_op=A.add), "ad%d" % k, 16)
+        rec("g", 1.0, 5.3, [src], [dst], lambda e: e.dma_start(res(dst), res(src), accum_op=A.add), "ad%d" % k, 16)
 
     def gather(which, out, table, places, b, scale):
         how = SPLIT.get(which, "s")
-        w = 64 // len(how)
         for k, e in enumerate(how):
-            lo = b + w * k
+            if e == ".":
+                continue
+            more = len(how) - k - len(how[k + 1:].lstrip("."))
+            lo, w = b + 64 // len(how) * k, 64 // len(how) * more
             dst, src = v(out, 16 * lo, 16 * (lo + w)), ind(table, v(places, lo, lo + w))
             if e == "v":
                 ts(dst, src, scale, A.mult)
@@ -478,6 +659,9 @@ def rank_program(g, core, T, topo):
 
     def hv(name, c, w=128):
         return v(name, w * c, w * c + w)
+
+    def top(name, lo=0, hi=None, k=1):
+        return v(name, lo, hi, 1, 0, k)
 
     def KV(c, k, w=128):
         return v("b%d" % c, 128 * k, 128 * k + w)
@@ -489,8 +673,10 @@ def rank_program(g, core, T, topo):
         return v("b%d" % (4 + c), 128 + k, 264, step)
 
     def MI(c, k):
-        lo = (0, 128, 264)[k]
-        return v("b%d" % (4 + c), lo, lo + 128)
+        return v("b%d" % (4 + c), 128 * k, 128 * k + 128)
+
+    def V2p(c):
+        return v("b%d" % (4 + c), 264, 392)
 
     def SM(c, k):
         if k < 2:
@@ -500,112 +686,135 @@ def rank_program(g, core, T, topo):
     def Wi(c, w=1):
         return v("sc2", 136 * c + 16, 136 * (c + w), 17)
 
-    def copy_g(out, a):
-        return op("g", "affine_select", out=out, in_=a, pattern=[[0, count(out)]], compare_op=A.is_ge, fill=0.0, base=0,
-                  channel_multiplier=0)
+    def wT(t, c=0, w=16):
+        b = 16 * (t % 2) + 8 * c
+        return v("wT", b, b + w)
 
     On = v("On", 0, 128)
+    one = top("On", 0, 128)
 
-    def WR(k, w=16):
-        return v("b4", 384 + k, 384 + k + w)
+    def WR(k, w=16, plo=0, phi=128):
+        return v("b4", 384 + k, 384 + k + w, 1, plo, phi)
+
+    def W(t, lo=0, hi=1280):
+        if t > 1 and who("fill", t - 1) == "laid":
+            return v("W2", lo, hi) if t == 2 else v("KK0", KB + lo, KB + hi)
+        return v("KK%d" % max(0, t - 1), KB + lo, KB + hi)
 
     load("y", v("NBi", 0, 640), T.nbr[:, 0:640], 0, 2.1)
     load("S", v("z"), T.z0[:], 1, 1.9)
-    load("S", v("NBi", 640, 1280), T.nbr[:, 640:1280], 2, 4.5)
+    load("y", v("NBi", 640, 1280), T.nbr[:, 640:1280], 2, 3.4)
     load("y", v("KK0", KB, KB + 1280), T.ring[:], 3, 4.6)
-    load("S", v("thI", 0, 1), T.thr[:], 4, 4.7)
+    load("S", v("thI", 0, 1), T.thr[:], 4, 2.5)
     load("y", v("X", 0, 2048), T.mat[:], 5, 7.0)
     load("y", v("X", 2048, 4096), T.mat[:], 6, 9.0)
 
+    fill(v("On"), 1.0)
     iota(v("PI"), [[1, 1]], 0, 1)
-    iota(v("D2"), [[-16, 8], [0, 16]], 128, 1)
-    iota(v("D1"), [[-1, 256]], 256, 1)
-    iota(v("ic"), [[1, 16]], 0, 0)
-    iota(v("t1"), [[16, 16]], 1280, 0)
-    iota(v("d0m"), [[128, 2], [0, 8]], 1280, 1)
+    iota(v("D1"), [[-1, 16]], 256, 1)
+    select(v("G16b"), On, [[-16, 8], [0, 16]], 0, 1)
+    select(v("G16b"), v("G16b"), [[16, 8], [0, 16]], 15, -1)
+    for t in range(RO):
+        iota(top("C%d" % t), [[0, 8], [-4096, 16]], 4096 * t - 30720, 0)
+        iota(top("E%d" % t), [[0, 8], [4096, 16]], 2048 - 4096 * t, 0)
+    select(v("Ib"), On, [[-1, 128]], 0, 1, A.is_equal)
     iota(v("V2"), [[10, 256]], 1, 0)
+    iota(v("ic"), [[1, 16]], 0, 0)
     iota(v("T1"), [[1, 1280]], 0, 0)
     ts(v("pi15"), v("PI"), 15, A.bitwise_and)
-    cp(v("pcol"), v("pi15"))
-    cp(v("lcol"), v("PI"))
-    fill(v("On"), 1.0)
-    for t in range(RO):
-        iota(v("C%d" % t, 0, 128, 1, 0, 1), [[0, 8], [-4096, 16]], 4096 * t - 30720, 0)
-        iota(v("E%d" % t, 0, 128, 1, 0, 1), [[0, 8], [4096, 16]], 2048 - 4096 * t, 0)
-    fill(v("pRJ", 0, 128, 1, 0, 1), RJ)
-    fill(v("nRJ", 0, 128, 1, 0, 1), -RJ)
-    ts(v("D2"), v("D2"), 4, A.arith_shift_right)
-    ts(v("G16b"), v("D2"), 8.0, A.is_equal)
-    ts(v("G4"), v("D2"), 8.0, A.is_equal, 4096.0, A.mult)
-    act(v("nG4"), v("G16b"), scale=-4096.0)
-    act(v("NG"), v("G16b"), scale=-2.0 * SB)
-    op("g", "affine_select", out=v("I17"), in_=v("On", 0, 136), pattern=[[-16, 8], [-1, 17]], compare_op=A.is_equal, fill=0.0,
-       base=1, channel_multiplier=1)
-    fill(v("I17", 0, 136, 17), 0.0)
-    for c in OPT["mxs"] and range(2):
-        fill(v("zr", 2048 * c, 2048 * c + 2048, 16), 0.0)
+    act(v("pcol"), v("pi15"))
+    act(v("lcol"), v("PI"))
+    fill(top("pRJ"), RJ)
+    fill(top("nRJ"), -RJ)
+    for name, x in (("G4", 4096.0), ("nG4", -4096.0)):
+        ts(v(name), v("G16b"), x, A.mult)
+    select(v("I17"), v("On", 0, 136), [[-16, 8], [-1, 17]], 1, 1, A.is_equal)
+    act(v("I17", 0, 136, 17), v("On", 0, 8), scale=0.0)
+    for c in [c for c in range(2) if max(who("run", t, c) for t in range(RO))]:
+        act(v("zr", 2048 * c, 2048 * c + 2048, 16), On, scale=0.0)
     for name, x in (("G8h", 2), ("G8b", 1), ("G8s", WS), ("G8m", 4 * SB), ("G8x", -2 * SB)):
-        act(v(name), v("G16b", 0, 128, 16), scale=float(x))
+        ts(v(name), v("G16b", 0, 128, 16), float(x), A.mult)
     ts(v("D15"), v("D1"), 15, A.bitwise_and)
-    ts(v("DM"), v("D15"), 0.0, A.is_equal)
-    act(v("sc", 0, 128), v("DM", 15, 143), scale=4096.0)
-    ts(v("sc", 128, 256), v("DM", 0, 128), -BIG, A.mult)
-    tt(v("RN"), v("sc", 0, 128), v("sc", 128, 256), A.add)
-    act(v("nof"), v("DM", 15, 16), scale=4096.0, bias=-4096.0 - OFF)
+    ts(v("DM", 0, 16), v("D15"), 0.0, A.is_equal)
+    for w in (16, 32, 64, 128):
+        cp(v("DM", w, 2 * w), v("DM", 0, w))
+    ts(v("RN"), v("DM", 0, 128), -BIG, A.mult, 4096.0, A.add)
+    act(v("nof"), v("pi15"), scale=4096.0, bias=-15 * 4096.0 - OFF)
     act(v("RS"), v("On", 0, 136), scale=float(SB))
     act(v("RS", 0, 136, 17), v("On", 0, 8), scale=-BIG)
     act(v("RS", 1, 136, 17), v("On", 0, 8), scale=float(FAIL - 16 * SB + 128 * SB - OFF))
-    ts(v("Ib"), v("D1", 0, 128), 256.0, A.is_equal)
-    for name, x in (("IS", 128.0 * SB), ("nIb", -1.0), ("nKI", -1024.0), ("nBI", -2.0 ** 19), ("nHI", -256.0), ("Ih", 0.5), ("row", 512.0)):
-        act(v(name), v("Ib"), scale=x)
-    cp(v("bl"), v("ic"))
-    ts(v("pb"), v("pcol"), 811.0, A.mult)
+    for name, x in (("IS", 128.0 * SB), ("nIb", -1.0), ("nKI", -1024.0), ("nBI", -2.0 ** 19), ("nHI", -256.0), ("I5", 512.0),
+                    ("nFI", -4096.0)) + (("I44", 2.0 ** 44), ("nI44", -2.0 ** 44)) * (OPT["hz"] == "t"):
+        ts(v(name), v("Ib"), x, A.mult)
+    act(v("bl"), v("ic"))
+    if OPT["to"] != "dm":
+        ts(v("p8"), v("PI"), 8, A.bitwise_and)
+        act(v("f2"), v("p8"))
+        act(v("bl2"), v("ic", 0, 8), AF.Identity, bias=v("f2"))
+        select(v("M2"), On, [[0, 16], [-16, 8]], 0, 1)
+        select(v("M2"), v("M2"), [[0, 16], [16, 8]], 15, -1)
+        fill(v("Wd"), 0.0)
+        act(v("Wd", 112, 128), v("DM", 0, 16))
+    if OPT["n"] == "t":
+        fill(v("Wn"), 0.0)
+        act(v("Wn", 16, 144, 16), v("G16b", 0, 128, 16))
+    act(v("pb"), v("pi15"), scale=811.0)
     ts(v("pc"), v("pb"), SB - 1, A.bitwise_and)
-    cp(v("c0"), v("pc"))
-    ts(v("Tri"), v("D1", 0, 128), 256.0, A.is_lt)
-    tt(v("Tri"), v("Tri"), v("row"), A.add)
-    for name, x in (("fb", -15.0), ("h18", 2.0 ** 18), ("C256", 256.0),
-                    ("pR16", R16), ("nR16", -R16), ("cM", -128.0), ("cZ", -1024.0), ("nfc", 1.0 - MID), ("q0", 1023.75),
-                    ("drb", -2.5), ("f0", -7.5 / 16), ("f1", 1.0 - MID - 7.5 * SB), ("rw", 0.5)):
-        act(v(name), v("On", 0, count(v(name))), scale=x)
-    act(v("KK0", KB + 1280, KB + SPARE), v("DM"), scale=0.0)
     for t in range(RO):
-        act(v("KK%d" % t, 1024, KB), v("On", 0, 16), scale=0.0)
-    fill(v("NBi", 1280, SPARE), 0)
-    ts(v("dOh"), v("t1"), v("pcol"), A.add)
-    ts(v("pb"), v("PI"), 4, A.arith_shift_right, 1, A.bitwise_and)
-    cp(v("odd"), v("pb"))
-    scan(v("row"), v("rw"), On, A.mult, 2.0 ** 64, A.mult)
-    tt(v("rw"), v("row"), v("Ib"), A.mult)
-    op("v", "tensor_reduce", out=v("wcol"), in_=v("rw"), axis=AxisListType.X, op=A.add)
-    act(v("w25"), v("wcol"), scale=2.5)
+        act(v("c0", t, t + 1), v("pc"), bias=float(t))
+    select(v("Tri"), On, [[1, 128]], 0, -1, A.is_ge)
+    select(v("Tri"), v("Tri"), [[1, 128]], 0, -1, A.not_equal, 512.0)
+    for name, x in (("fb", -3840.0), ("h18", -127 * 2.0 ** 18), ("pR16", R16), ("nR16", -R16), ("nfc", 1.0 - MID),
+                    ("drb", -2.5), ("f0", -7.5 / 16), ("f1", 1.0 - MID - 7.5 * SB)):
+        fill(v(name), x)
+    fill(v("C256"), 256.0)
+    for name, x in (("cQ", -0.25), ("rw", 0.5)) + (("c18", -2.0 ** 18),) * (OPT["hz"] == "t"):
+        fill(top(name), x)
+    act(top("c12"), top("On", 0, 16), scale=4096.0)
+    act(v("KK0", 0, 16), v("On", 0, 16), scale=0.0)
+    for t in (2, 3) if OPT["wipe"] else ():
+        act(W(t, 1280, SPARE), On, scale=0.0)
+    if OPT["wipe"]:
+        act(v("NBi", 1280, SPARE), On, scale=0.0)
+    ts(v("ps"), v("PI"), BLK - 1, A.bitwise_and)
+    act(v("spare"), v("ps"), bias=1280.0)
+    scan(top("row"), top("rw"), one, A.mult, 2.0 ** 64, A.mult)
+    mm(v("b7", 0, 1), top("row"), top("On", 0, 1))
+    act(v("wcol"), v("b7", 0, 1))
+    act(v("wthr"), v("b7", 0, 1), scale=-384.0)
     act(v("sgn"), v("DM", 0, 16), scale=-2.0, bias=1.0)
-    act(v("CT", 0, 1), v("On", 0, 1))
+    ts(v("po"), v("PI"), 4, A.arith_shift_right, 1, A.bitwise_and)
+    act(v("CT", 0, 1), v("po"), scale=15.0, bias=1.0)
     for r in range(11):
         w = min(2 ** r, 1280 - 2 ** r)
-        act(v("CT", 2 ** r, 2 ** r + w), v("CT", 0, w), scale=v("sgn", r, r + 1))
+        if r < OPT["ct"]:
+            act(v("CT", 2 ** r, 2 ** r + w), v("CT", 0, w), scale=v("sgn", r, r + 1))
+        else:
+            ts(v("CT", 2 ** r, 2 ** r + w), v("CT", 0, w), v("sgn", r, r + 1), A.mult)
     ts(v("th"), v("thI", 0, 1), 6, A.arith_shift_right)
     ts(v("tl"), v("thI", 0, 1), 63, A.bitwise_and)
-    ts(v("Q", 0, 1), v("th"), -64.0 * SB, A.mult, MID, A.add)
-    ts(v("Q", 1, 2), v("tl"), -float(SB), A.mult)
+    act(v("Q", 0, 1), v("th"), scale=-64.0 * SB, bias=MID)
+    act(v("Q", 1, 2), v("tl"), scale=-float(SB))
     act(v("Q", 2, 3), v("pcol"))
     act(v("Q", 3, 4), v("On", 0, 1), scale=16.0)
     act(v("Q", 4, 7), v("On", 0, 3))
     act(v("Q", 7, 8), v("lcol"))
-    mm(v("b6", 0, 128, 1, 0, 4), v("Q", 0, 4), v("Ib"))
-    mm(v("b6", 128, 256, 1, 0, 4), v("Q", 4, 8), v("Ib"))
-    act(v("LR", 0, 256, 1, 0, 4), v("b6", 0, 256, 1, 0, 4))
-    mm(v("b6", 256, 384), v("LR", 128, 256, 1, 0, 2), v("LR", 0, 128, 1, 0, 2))
+    mm(top("b6", 0, 128, 4), v("Q", 0, 4), v("Ib"))
+    mm(top("b6", 128, 256, 4), v("Q", 4, 8), v("Ib"))
+    act(top("LR", 0, 256, 4), top("b6", 0, 256, 4))
+    mm(v("b6", 256, 384), top("LR", 128, 256, 2), top("LR", 0, 128, 2))
     act(v("TH"), v("b6", 256, 384))
     tt(v("RD", 1, 128), v("b6", 257, 384), v("TH", 0, 127), A.subtract)
     act(v("RD", 0, 128, 16), v("On", 0, 8), scale=BIG)
     for c in range(2):
         act(KV(c, 2), hv("z", c), scale=0.5)
-        act(hv("zq", c), hv("z", c), AF.Identity, scale=0.5, bias=v("q0"))
-        act(hv("zb", c), hv("z", c), scale=0.5)
+        act(hv("zq", c), hv("z", c), scale=0.5, bias=1023.75)
+        ts(hv("zb", c), hv("z", c), 0.5, A.mult)
+        if who("kp", 0, c) != "fused":
+            act(V2p(c), hv("V2", c))
 
     def send_rings(t):
-        names = (("KK0", KB), ("NM", 0)) if t else (("KK0", KB),)
+        names = [W(t)[1:3]] + [("NM", 0)] * (t > 0) + [("NC", 0)] * (t > 1 and who("fill", 1) != "laid")
 
         def emit(e):
             parts = []
@@ -614,21 +823,21 @@ def rank_program(g, core, T, topo):
                 parts.append(RemoteDMATransfer(dst_ids=[DstId(rid=rid, pnc=pid)], remote_sem=T.sem["ha%d" % t],
                                                dma_engine_mask=engines_mask(topo, core, rl[h], 8 * h, 8 * h + 8),
                                                srcs=[res(v(x, b + 512 * h, b + 512 * h + 512)) for x, b in names],
-                                               dsts=[T["hand%d" % t][:]], alu_op=len(names) - 1))
-            g.remote_dma_fused(parts, local_sem=T.sem["ks%d" % t])
+                                               dsts=[T["hand%d" % t][:]], alu_op=min(1, t)))
+            e.remote_dma_fused(parts, local_sem=T.sem["ks%d" % t])
         i = rec("g", 0.4 if t else 3.0, 4.0, [v(x, b, b + 1024) for x, b in names], [], emit, "ks%d" % t, 16)
         for h in range(2):
-            land(v("KK%d" % t, 512 * h, 512 * h + 512), "ki%d%d" % (t, h), i, 7.0 if t else 10.0)
+            land(v("KK%d" % t, 512 * h + 16, 512 * h + 528), "ki%d%d" % (t, h), i, 7.0 if t else 8.0)
 
     def send_revoked(t):
-        src = v("rS%d" % t, 0, 1)
+        src = v("rS%d" % t, 0, 2)
 
         def emit(e):
-            remote(g, topo, core, rv_relay, T["hrv%d" % t][:, 0:1], res(src), T.sem["ra%d" % t], T.sem["rs%d" % t])
-        land(v("cI%d" % t, 0, 1), "ri%d" % t, rec("g", 0.3, 4.0, [src], [], emit, "rs%d" % t, 8), 5.0)
+            remote(e, topo, core, rv_relay, T["hrv%d" % t][:, 0:2], res(src), T.sem["ra%d" % t], T.sem["rs%d" % t])
+        land(v("cI%d" % t, 0, 2), "ri%d" % t, rec("g", 0.3, 4.0, [src], [], emit, "rs%d" % t, 8), 5.0)
 
-    def K(t):
-        return v("KK%d" % t, KB, KB + 1280)
+    def K(t, lo=0, hi=1280):
+        return v("KK%d" % t, KB + lo, KB + hi)
 
     def vo(t, c):
         b = 16 * (t % 2)
@@ -638,279 +847,355 @@ def rank_program(g, core, T, topo):
         b = KB if name == "KK0" else 0
         return v(name, b + 640 * c, b + 640 * (c + w), 5)
 
-    def to_o(out, copy, x, weights):
+    def to_o(out, copy, x):
         tt(copy, ind(x, v("bl", 0, 8)), v("DM", 0, 128), A.mult)
-        mm(out, copy, weights)
+        mm(out, copy, v("G8b"))
+
+    def both_to_o(out, copy, x):
+        tt(copy, ind(x, v("bl2")), v("M2"), A.mult)
+        group(out, [(v("Wd", 112 - 16 * gr, 240 - 16 * gr), v(copy[1], 16 * gr, 16 * gr + 16)) for gr in range(8)], 4)
+
+    def struck(out, src, keys):
+        for lo in range(0, 1280, OPT["piece"]):
+            hi = min(1280, lo + OPT["piece"])
+            ts(v(out[1], out[2] + lo, out[2] + hi), v(src[1], src[2] + lo, src[2] + hi), keys[0], A.is_equal, keys[1], A.mult)
+
+    def part(x, lo, hi):
+        return v(x[1], x[2] + lo, x[2] + hi)
+
+    def take_off(out, minus, src):
+        for lo in range(0, 1280, OPT["piece"]):
+            a, b, c = [part(x, lo, min(1280, lo + OPT["piece"])) for x in (out, minus, src)]
+            scan(a, b, c, A.add, 0.0, A.min)
+
+    def pre(t):
+        if not t or who("fill", t) == "laid":
+            return W(t + 1)
+        return K(t + 1) if t < RO - 1 and who("true", t) == "dma" else v("Y1")
 
     tab = v("NBi", 0, 1280)
 
     def first(t, c):
-        z, one = hv("zh" if t else "z", c), v("On", 0, 128, 1, 0, 1)
-        rows = [v(x, 0, 128, 1, 0, 1) for x in ("C%d" % t, "pRJ", "nRJ", "E%d" % t)]
+        z = hv("zh" if t else "z", c)
+        rows = [top(x) for x in ("C%d" % t, "pRJ", "nRJ", "E%d" % t)]
         if t:
-            cp(hv("Bv", c), ind(tab, vo(t, c)))
+            cp(hv("Bv", c), ind(tab, vo(t, c)), who("Bv", t, c))
         group(MI(c, 0), [(rows[0], one), (v("G4"), z), (rows[1], one), (rows[2], one), (v("nG4"), z), (rows[3], one)])
         tt(hv("mB", c), MI(c, 0), hv("Bv", c) if t else fifth("NBi", c), A.min)
-        mm(MI(c, 1), v("G16b"), hv("mB", c))
-        scan(hv("sc", c), v("RN"), MI(c, 1), A.max)
         no = v("nO", 16 * c, 16 * c + 8)
-        ts(no, v("sc", 128 * c + 15, 128 * c + 128, 16), v("nof"), A.add)
-        cp(hv("BnL", c), ind(tab, no))
-        cp(hv("BnH", c), hv("BnL", c))
-        if not t and not c:
-            act(MI(0, 2), hv("V2", 0))
+        if who("n", t, c) == "t":
+            out = part(MI(c, 1), 0, 8)
+            group(out, [(v("Wn", 16 - l, 144 - l), v("mB", 128 * c + l, 128 * c + 128, 16)) for l in range(16)], 4)
+            plus(no, out, -float(OFF), who("nO", t, c))
+        else:
+            mm(MI(c, 1), v("G16b"), hv("mB", c))
+            scan(hv("sc", c), v("RN"), MI(c, 1), A.max)
+            plus(no, v("sc", 128 * c + 15, 128 * c + 128, 16), v("nof"), who("nO", t, c))
+        cp(hv("BnL", c), ind(tab, no), who("BnL", t, c))
+        cp(hv("BnH", c), hv("BnL", c), who("BnH", t, c))
+
+    def true_rings(t, c):
+        act(hv("Kt", c, 256), KV(c, 0, 256), AF.Relu)
+        if who("fill", t) == "laid":
+            return
+        if OPT["Hm"] == "s":
+            act(hv("Hm", c), hv("Kt", c), AF.Relu, scale=-1.0, bias=v("On", 0, 1))
+        else:
+            ts(hv("Hm", c), hv("Kt", c), 0.0, A.is_equal)
 
     def second(t, c):
         both, rawv, rawn = hv("KN", c, 256), hv("KN", 2 * c), hv("KN", 2 * c + 1)
-        act(rawn, ind(K(0), v("nO", 16 * c, 16 * c + 8)), bias=-2.0 ** -11)
+        act(rawn, ind(W(t), v("nO", 16 * c, 16 * c + 8)), bias=-2.0 ** -11)
         if t:
-            act(rawv, ind(K(0), vo(t, c)), bias=-2.0 ** -10)
+            act(rawv, ind(W(t), vo(t, c)), bias=-2.0 ** -10)
             if c:
                 ts(hv("m1", c, 256), both, v("rS%d" % (t - 1), 0, 1), A.is_equal)
             else:
                 ts(hv("m1", c, 256), both, v("rq"), A.add, v("c2"), A.is_equal)
-            group(KV(c, 0, 256), [(v("Ib"), both), (v("nKI"), hv("m1", c, 256))])
+            come = []
+            if t > 1 and who("fill", 1) != "laid":
+                ts(hv("m2", c, 256), both, v("cI%d" % (t - 2), 0, 1), A.is_equal)
+                come = [(v("nKI"), hv("m2", c, 256))]
+            group(KV(c, 0, 256), [(v("Ib"), both)] + come + [(v("nKI"), hv("m1", c, 256))])
         else:
-            act(rawv, fifth("KK0", c), bias=-2.0 ** -10)
+            plus(rawv, fifth("KK0", c), -2.0 ** -10, "s" if c else "v")
             mm(KV(c, 0, 256), v("Ib"), both)
         for b in (128 * c, 128 * c + 64):
-            gather(("K", t, b // 64), "Kc", K(0), "BnL", b, 1.0)
+            gather(("K", t, b // 64), "Kc", W(t), "BnL", b, 1.0)
         tt(hv("evn", c), KV(c, 0), rawn, A.is_equal)
         mm(SM(c, 1), hv("evn", c), v("G8b"))
         act(hv("dr", c, 8), SM(c, 1), AF.Sign, bias=v("drb"))
+        if who("Kn", t, c) == "pre":
+            true_rings(t, c)
         for q in range(2):
             for e, eq in enumerate(("eqV", "eqN")):
                 for k in range(16):
                     s = (2048 * c + 1024 * q + k, 2048 * c + 1024 * q + 1024, 16)
                     b = 128 * e + 64 * q
-                    chain("eq", tt(v(eq, *s), v("b%d" % c, b, b + 64), v("Kc", *s), A.is_equal))
+                    chain("eq", tt(v(eq, *s), v("b%d" % c, b, b + 64), v("Kc", *s), A.is_equal, k % BY > 0))
 
     def third(t, c):
         for o, eq in ((CV, "eqV"), (CN, "eqN")):
             mm(o(c), hv("BnH", c), v("I17"), True, False)
             if o is CV:
                 mm(o(c, 0, 17), hv("mB", c), v("G8b"), False, False)
-                mm(o(c, 0, 17), v("IS"), hv("dr", c, 8), False, False)
             for k in range(16):
-                mm(o(c, k + 1, 17), v(eq, 2048 * c + k, 2048 * c + 2048, 16), v("G8s"), False, k == 15)
+                if o is CV and k == OPT["drk"]:
+                    mm(o(c, 0, 17), v("IS"), hv("dr", c, 8), False, False)
+                mm(o(c, k + 1, 17), v(eq, 2048 * c + k, 2048 * c + 2048, 16), v("G8s"), False, k == 15, k % BY > 0)
         act(hv("cV", c, 136), CV(c))
         tt(hv("mn", c, 136), CN(c), hv("cV", c, 136), A.min)
         scan(hv("sc2", c, 136), v("RS"), hv("mn", c, 136), A.max)
-        ts(hv("wT", c, 8), Wi(c), SB - 1, A.bitwise_and)
-        to_o(SM(c, 2), hv("Aw", c), hv("wT", c, 8), v("G8b"))
+        ts(wT(t, c, 8), Wi(c), SB - 1, A.bitwise_and)
+        to_o(SM(c, 2), hv("Aw", c), wT(t, c, 8))
         w = vo(t + 1, c)
-        cp(w, SM(c, 2))
-        act(hv("Kw", c), ind(K(t), w))
-        if c:
+        cp(w, SM(c, 2), who("vO", t, c))
+        act(hv("Kw", c), ind(K(t), w), bias=-128.0)
+        if who("kp", t, c) == "fused":
             tt(hv("kp", c), ind(K(t), w), hv("V2", c), A.mult)
         else:
-            tt(hv("kp", c), MI(c, 2), hv("Kw", c), A.mult)
-        ts(hv("k2", c), hv("kp", c), 2, A.arith_shift_right, SB - 1, A.bitwise_and)
-        ts(hv("PL", c), hv("k2", c), v("c0"), A.add, float(t), A.add)
-        act(hv("Kt", c), KV(c, 0), AF.Relu)
+            act(hv("Kx", c), ind(K(t), w))
+            tt(hv("kp", c), V2p(c), hv("Kx", c), A.mult)
+        ts(hv("k2", c), hv("kp", c), 1 if t else 2, A.arith_shift_right, SB - 1, A.bitwise_and)
+        plus(hv("PL", c), hv("k2", c), v("c0", t, t + 1), who("PL", t, c))
+        if who("Kn", t, c) == "post":
+            true_rings(t, c)
         if OPT["hz"] == "s":
             act(hv("hz", c), hv("Kw", c), AF.Relu, scale=-2.0 ** 18, bias=v("h18"))
-        else:
-            ts(hv("hz", c), hv("Kw", c), 0.0, A.is_equal, 2.0 ** 18, A.mult)
-        tt(hv("pr", c), KV(c, 2), hv("Kw", c), A.mult)
-        mm(SM(c, 4), hv("pr", c), v("G8h"))
-        cp(hv("hi", c, 8), SM(c, 4))
 
     def next_nodes(t, c):
-        act(hv("Vn", c), ind(v("T1"), vo(t + 1, c)))
-        act(hv("V2", c) if c else MI(c, 2), hv("Vn", c), scale=2.0, bias=1.0)
-        tt(hv("aH", c), MI(c, 0), hv("Vn", c), A.min)
+        act(hv("V2", c), ind(v("T1"), vo(t + 1, c)), bias=HALF)
+        tt(hv("aH", c), MI(c, 0), hv("V2", c), A.min)
+        if who("kp", t + 1, c) != "fused":
+            act(V2p(c), hv("V2", c))
 
     def material(t, c):
-        run = (t, c) in OPT["mxs"]
-        if run:
-            for p in range(1, 16):
-                copy_g(v("zr", 2048 * c + p, 2048 * c + 2048, 16), hv("zb", c))
+        run = who("run", t, c)
+        for p in range(1, 16) if run else ():
+            copy_g(v("zr", 2048 * c + p, 2048 * c + 16 * run, 16), v("zb", 128 * c, 128 * c + run))
         for q in range(2):
             lo = 2048 * c + 1024 * q
             gather(("X", t, 2 * c + q), "Xc", v("X"), "PL", lo // 16, 0.5)
-            if not run:
+            if run <= 64 * q:
                 for p in range(16):
                     chain("mx", tt(v("mx", lo + p, lo + 1024, 16), v("b%d" % c, 256 + 64 * q, 320 + 64 * q),
-                                   v("Xc", lo + p, lo + 1024, 16), A.max))
+                                   v("Xc", lo + p, lo + 1024, 16), A.max, p % BY > 0))
                 continue
-            w = 1024 // len(SPLIT.get(("X", t, 2 * c + q), "s"))
+            w = 1024 // len(SPLIT.get(("X", t, 2 * c + q), "s")) if q else 1024
             for a in range(lo, lo + 1024, w):
                 head, keep, zc = v("Xc", a, a + w, 16), v("x0", a // 16, (a + w) // 16), 256 + (a - 2048 * c) // 16
-                (act if OPT["rs"] == "s" else cp)(keep, head)
+                cp(keep, head, OPT["rs"])
                 tt(head, v("b%d" % c, zc, zc + w // 16), keep, A.max)
                 chain("mx", scan(v("mx", a, a + w), v("zr", a, a + w), v("Xc", a, a + w), A.max, 0.0, A.min))
         if run:
-            copy_g(v("Xc", 2048 * c, 2048 * c + 2048, 16), hv("x0", c))
+            copy_g(v("Xc", 2048 * c, 2048 * c + 16 * run, 16), v("x0", 128 * c, 128 * c + run))
 
     def fourth(t, c):
         lo, bank = 2048 * c, "b%d" % (2 + c)
         dT = v(bank, 256, 384)
-        run = (t, c) in OPT["mxs"]
-        mm(dT, v("LR", 128, 256, 1, 0, 4), v("LR", 0, 128, 1, 0, 4), True, False)
-        mm(dT, hv("zb", c), v("NG"), False, False)
-        cuts = [(name, a, b) for name, x in (("Xc", OPT["xs"]), ("mx", OPT["ms"] if run else 128))
-                for a, b in ((0, x), (x, 128)) if b > a]
+        run = who("run", t, c) == 128
+        mm(dT, top("LR", 128, 256, 4), top("LR", 0, 128, 4), True, False)
+        mm(dT, hv("zb", c), v("nG4"), False, False)
+        cuts = [(name, a, b) for name, x in (("Xc", who("xs", t, c)), ("mx", (0, OPT["ms"] if run else 128, 128)))
+                for a, b in zip(x, x[1:]) if b > a]
         cuts.sort(key=lambda x: x[2])
         for i, (name, a, b) in enumerate(cuts):
-            for p in range(16):
+            for k in range(16):
+                p = (k + 1) % 16 if name == "Xc" else k
                 src = v(name, lo + 16 * a + p, lo + 16 * b, 16)
                 if run and name == "Xc" and not p:
                     src = v("x0", 128 * c + a, 128 * c + b)
-                mm(v(bank, 256 + p, 384, 16, a, b), src, v("G8x" if name == "Xc" else "G8m"), False, i == len(cuts) - 1 and p == 15)
-        if c:
-            ts(hv("nf", c), dT, v("nfc"), A.add, 2.0 ** -12, A.max)
+                mm(v(bank, 256 + p, 384, 16, a, b), src, v("G8x" if name == "Xc" else "G8m"), False,
+                   i == len(cuts) - 1 and k == 15, k % BY > 0 and (k < 15 or name == "mx"))
+        nfv = who("nf", t, c) == "v"
+        if nfv and t == RO - 1:
+            ts(hv("nf", c), dT, v("nfc"), A.add, 0.0, A.max)
         scan(hv("sd", c), v("RD"), dT, A.min)
-        if not c:
+        if nfv and t < RO - 1:
+            ts(hv("nf", c), dT, v("nfc"), A.add, 0.0, A.max)
+        if not nfv:
             act(hv("nf", c), dT, AF.Relu, bias=v("nfc"))
         ts(hv("pi2", c, 8), v("sd", 128 * c + 15, 128 * c + 128, 16), SB - 1, A.bitwise_and)
-        to_o(SM(c, 3), hv("Ap", c), hv("pi2", c, 8), v("G8b"))
+        to_o(SM(c, 3), hv("Ap", c), hv("pi2", c, 8))
         do = v("dO", 16 * c, 16 * c + 8)
-        cp(do, SM(c, 3))
+        cp(do, SM(c, 3), who("dO", t, c))
         tt(hv("zh", c), ind(v("Xc", lo, lo + 2048), do), hv("zq", c), A.add)
         if t == RO - 1:
-            ts(hv("zF", c), hv("zh", c), -1024.0, A.add)
+            plus(hv("zF", c), hv("zh", c), -1024.0, who("zF", t, c))
             store("Sy"[c], T.yz[:, 128 * c:128 * c + 128], hv("zF", c), c)
-        cap = v("b%d" % (6 + c), 128, 256)
-        group(cap, [(v("Ib"), v("cM"))] * (1 - c) + [(v("Ib"), hv("Kw", c)), (v("nIb"), hv("hz", c)), (hv("nf", c), v("nBI"))])
+        cap = v("b%d" % (6 + c), 128, 256) if OPT["cap"] == 6 else KV(c, 3)
+        if OPT["hz"] == "t":
+            holes = [(v("I44"), hv("Kw", c)), (top("c18"), one), (v("nI44"), hv("Kw", c))]
+        else:
+            holes = [(v("nIb"), hv("hz", c))]
+        group(cap, holes + [(v("Ib"), hv("Kw", c)), (hv("nf", c), v("nBI"))])
         scan(hv("cs", c), v("C256"), cap, A.max, v("cs", 127, 128) if c else -128.0 - 65536)
         if t < RO - 1:
-            if OPT["zb"] == "t":
-                group(KV(c, 2), [(v("Ih"), v("cZ")), (v("Ih"), hv("zh", c))])
-                act(hv("zb", c), KV(c, 2))
-                act(hv("zq", c), KV(c, 2), AF.Identity, bias=v("q0"))
+            if who("zb", t, c) == "s":
+                act(hv("zb", c), hv("zh", c), scale=0.5, bias=-512.0)
             else:
                 ts(hv("zb", c), hv("zh", c), -1024.0, A.add, 0.5, A.mult)
-                mm(KV(c, 2), v("Ib"), hv("zb", c))
-                act(hv("zq", c), hv("zb", c), bias=1023.75)
+            mm(KV(c, 2), v("Ib"), hv("zb", c))
+            act(hv("zq", c), hv("zh", c), scale=0.5, bias=511.75)
 
-    def active(t, c):
-        f, y = hv("F", c, 8), WR(16 + 8 * c, 8)
-        ts(f, Wi(c), float(FAIL), A.is_lt)
-        ts(hv("D", c, 8), Wi(c), float(DIR), A.is_ge, 1024.0, A.mult)
-        mm(y, v("Tri"), f, not c, False)
-        mm(y, v("Ib"), hv("D", c, 8), False, True)
-        ts(hv("aw", c, 8), y, 512.0 + CAP, A.is_lt, v("wcol"), A.mult)
-        ts(hv("aB", c, 8), y, 512.0 + CAP, A.is_lt, 2.0 ** 70, A.mult)
-        for gr in range(8):
-            e = 384 * gr + 256 * c
-            mm(WR(32 + 8 * c + gr, 1), v("E", e, e + 128), v("aw", 8 * c + gr, 8 * c + gr + 1))
-        if not c:
-            mm(WR(24, 8), On, f, True, False)
-            for gr in range(8):
-                mm(WR(24 + gr, 1), v("E", 384 * gr + 128, 384 * gr + 256), v("aB", gr, gr + 1), False, False)
+    def given(t, halves):
+        a, w = 8 * halves[0], 8 * len(halves)
+        for c in halves:
+            tt(hv("pr", c), KV(c, 2), hv("Kt", 2 * c + 1), A.mult)
+            mm(v("b7", 32 + 8 * c, 40 + 8 * c), hv("pr", c), v("G8h"))
+        cp(v("hi", a, a + w), v("b7", 32 + a, 32 + a + w), who("hi", t))
+        ts(v("h2", a, a + w), v("hi", a, a + w), 1023, A.bitwise_and)
+        plus(v("hn", a, a + w), v("h2", a, a + w), -1024.0, who("hn", t))
+
+    def active(t, halves):
+        a, w = 8 * halves[0], 8 * len(halves)
+        ts(v("F", a, a + w), Wi(halves[0], len(halves)), float(FAIL), A.is_lt)
+        y = WR(16 + a, w)
+        mm(y, v("I5"), v("dr", a, a + w), True, False)
+        if 1 in halves:
+            mm(WR(24, 8), On, v("F", 0, 8), False, False)
+        mm(y, v("Tri"), v("F", a, a + w), False, True)
+
+
+        def into_o(out, copy, x):
+            if w == 8:
+                to_o(out, hv(copy, halves[0]), x)
+            elif OPT["to"] == "dm":
+                tt(v(copy), ind(x, v("bl")), v("DM"), A.mult)
+                for c in range(2):
+                    mm(part(out, 8 * c, 8 * c + 8), hv(copy, c), v("G8b"), True, True, c > 0)
+            else:
+                both_to_o(out, v(copy, 0, 128), x)
+
+        if not t:
+            ts(v("aw", a, a + w), y, float(CAP), A.is_ge, 8.0, A.mult)
+        H = v("b7", 16 + a, 16 + a + w)
+        group(H, [(v("Ib"), v("hn", a, a + w)), (one, top("c12", 0, w)), (v("nFI"), v("F", a, a + w))]
+              + [(v("nKI"), v("aw", a, a + w))] * (not t), 2)
+        tt(v("src", a, a + w), H, wT(t, halves[0], w), A.min)
+        into_o(v("b7", a, a + w), "Aq", v("src", a, a + w))
+        plus(v("srO", a, a + w), v("b7", a, a + w), KB - 16.0 * (t > 0), who("srO", t) if t else "v")
+        if not t:
+            return
+        ts(v("aw", a, a + w), y, float(CAP), A.is_lt, v("wcol"), A.mult)
+        mm(WR(32 + a, w), v("nKI"), v("aw", a, a + w), True, False)
+        todo = [(c, gr, lo) for c in halves for gr in range(8) for lo in range(0, 128, BLK)]
+        for c, gr, lo in todo:
+            e = BLK * (8 * (gr % 2) + 2 * (gr // 2) + c)
+            mm(WR(32 + 8 * c + gr, 1, lo, lo + BLK), v("E", e, e + BLK, 1, lo, lo + BLK),
+               v("aw", 8 * c + gr, 8 * c + gr + 1, 1, lo, lo + BLK), False, (c, gr, lo) == todo[-1], gr % 2 > 0 or lo > 0)
+        ts(v("nw", a, a + w), WR(32 + a, w), v("wthr"), A.is_ge, v("spare"), A.mult)
+        tt(v("sel", a, a + w), v("nw", a, a + w), wT(t - 1, halves[0], w), A.max)
+        into_o(WR(80 + a, w), "Aqh", v("sel", a, a + w))
+        cp(v("scO", a, a + w), WR(80 + a, w), who("scO", t))
 
     def writers(t):
-        if t:
-            come = v("cI%d" % (t - 1), 0, 1)
-            ts(v("ncome"), come, -1.0, A.mult)
-            ts(K(0), K(t), come, A.is_equal, v("ncome"), A.mult)
-            add_into(K(0), K(t), 1 + t)
-            active(t, 1)
-            ts(v("wf"), WR(32), v("w25"), A.is_lt, 2.0 ** -70, A.mult)
-            tt(v("av"), v("aB"), v("vmd"), A.mult)
-        else:
-            ts(v("F"), Wi(0, 2), float(FAIL), A.is_lt)
-            ts(v("D"), Wi(0, 2), float(DIR), A.is_ge, 1024.0, A.mult)
-            mm(WR(16), v("Tri"), v("F"), True, False)
-            mm(WR(24, 8), On, v("F", 0, 8), False, False)
-            mm(WR(16), v("Ib"), v("D"), False, True)
-            ts(v("act"), WR(16), 512.0 + CAP, A.is_lt)
-        ts(v("h2"), v("hi"), 1023, A.bitwise_and)
-        act(v("hb"), v("F"), scale=-2048.0 - KB, bias=2048.0)
-        tt(v("hc"), v("h2"), v("hb"), A.add)
-        tt(v("src"), v("hc"), v("wT"), A.min)
-        if t:
-            tt(v("w2"), v("wf"), v("av"), A.mult)
-            tt(v("Aqh"), ind(v("w2"), v("bl")), v("DM"), A.mult)
-            mm(WR(80), v("Ib"), v("dOh"), True, False)
-            for c in range(2):
-                mm(WR(80 + 8 * c, 8), hv("Aqh", c), v("G8b"), False, c == 1)
-            cp(v("scO"), WR(80))
-            tt(v("Aq"), ind(v("src"), v("bl")), v("DM"), A.mult)
-            for c in range(2):
-                mm(v("b7", 8 * c, 8 * c + 8), hv("Aq", c), v("G8b"))
-            ts(v("srO"), v("b7", 0, 16), float(KB), A.add)
-        else:
-            ts(v("hd"), v("src"), KB - 1024.0, A.add)
-            tt(v("word"), v("hd"), v("act"), A.mult)
-            tt(v("Aqh"), ind(v("word"), v("bl")), v("DM"), A.mult)
-            for c in range(2):
-                mm(v("b7", 8 * c, 8 * c + 8), hv("Aqh", c), v("G8b"))
-            ts(v("srO"), v("b7", 0, 16), 1024.0, A.add)
+        if t and who("fill", t) == "laid":
+            come = [v("cI%d" % (t - 1), k, k + 1) for k in range(2)]
+            if who("come", t) == "dma":
+                struck(W(t + 1), K(t), come)
+                add_into(W(t + 1), K(t), 1 + t)
+            else:
+                struck(v("NC"), K(t), come)
+                take_off(W(t + 1), v("NC"), K(t))
+        active(t, [1] if who("split", t) else [0, 1])
+        skip = 16 if t else 0
+        blocks = range(256 - BLK, -1, -BLK)
         if t < RO - 1:
             mm(v("b6", 0, 16), On, v("F"))
             act(v("fj"), v("b6", 0, 16), AF.Identity, bias=v("f0"), accum_out=v("fs"))
             next_nodes(t, 1)
             dl = v("b6", 256, 512)
-            group(dl, [(v("nIb"), v("mB")), (v("Ib"), v("aH"))])
-            if t:
-                tt(v("nb"), dl, v("Bv"), A.add)
-                cp(ind(v("NBi"), v("scO")), v("nb"))
+            pairs = [(v("nIb"), v("mB")), (v("Ib"), v("aH"))]
+            if t and OPT["nb"] == "s":
+                group(dl, [(v("Ib"), v("Bv"))] + pairs)
+                act(v("nb"), dl, bias=-0.25)
             else:
-                tt(fifth("NBi", 0, 2), dl, fifth("NBi", 0, 2), A.add)
-        act(v("gv"), ind(v("KK%d" % t, 0, KB + 1280), v("srO")))
-        laid = v("b7", 256, 512)
-        group(laid, [(v("nHI"), v("Kt")), (v("Ib"), v("gv"))])
-        if t:
-            tt(v("val"), laid, v("Kt"), A.max)
-            ts(v("vm"), v("val"), come, A.not_equal)
-            tt(ind(v("KK0", KB, KB + SPARE), v("scO")), v("val"), v("vm"), A.mult)
+                group(dl, [(top("cQ"), top("On"))] + pairs)
+                if t:
+                    tt(v("nb"), dl, v("Bv"), A.add)
+                else:
+                    tt(fifth("NBi", 0, 2), dl, fifth("NBi", 0, 2), A.add)
+            for b in blocks if t else ():
+                cp(ind(v("NBi"), v("scO", b // 16, (b + BLK) // 16)), v("nb", b, b + BLK))
+        if who("fill", t) == "laid":
+            act(v("gv"), ind(v("KK%d" % t, skip, KB + 1280), v("srO")))
+            laid = v("b7", 256, 512)
+            mm(laid, v("Ib"), v("gv"), True, False)
+            for c in range(2):
+                mm(part(laid, 128 * c, 128 * c + 128), v("nHI"), hv("Kt", 2 * c), False, c == 1)
+            for c in (1, 0):
+                tt(hv("val", c) if t else fifth("KK0", c), part(laid, 128 * c, 128 * c + 128), hv("Kt", 2 * c), A.max)
+            if t:
+                ts(v("vm"), v("val"), v("cI%d" % (t - 1), 0, 1), A.not_equal)
+                for b in blocks:
+                    tt(ind(W(t + 1, 0, SPARE), v("scO", b // 16, (b + BLK) // 16)), v("val", b, b + BLK), v("vm", b, b + BLK), A.mult)
+        for c in (1, 0) if who("fill", t) != "laid" else ():
+            tt(hv("gv", c), ind(v("KK%d" % t, skip, KB + 1280), v("srO", 8 * c, 8 * c + 8)), hv("Hm", c), A.mult)
+        if who("fill", t) == "laid":
+            pass
+        elif t:
+            for b in blocks:
+                tt(ind(W(t + 1, 0, SPARE), v("scO", b // 16, (b + BLK) // 16)), v("gv", b, b + BLK), v("Kt", b, b + BLK), A.add)
+            come = [v("cI%d" % (t - 1), k, k + 1) for k in range(2)]
+            struck(v("NC"), W(t + 1), come)
+            take_off(pre(t), v("NC"), W(t + 1))
         else:
-            tt(fifth("KK0", 0, 2), laid, v("Kt"), A.max)
+            for c in range(2):
+                tt(fifth("KK0", c), KV(c, 0), hv("gv", c), A.max)
         if t < RO - 1:
             act(v("f2"), v("fs"), AF.Identity, bias=v("pR16"))
             act(v("f3"), v("f2"), AF.Identity, bias=v("nR16"))
             act(v("f4"), v("f3"), AF.Identity, scale=float(SB), bias=v("f1"))
-            tt(v("vmd"), v("wT"), v("d0m"), A.subtract)
 
     def same_node(t):
         act(v("code"), ind(v("CT"), v("vO", 16 * (t % 2), 16 * (t % 2) + 16)))
-        if OPT["cd"] == "s":
-            act(v("cdO"), v("code"), scale=v("odd"))
-        else:
-            for lo in range(0, 128, 32):
-                op("g", "affine_select", out=v("cdO", 0, 256, 1, lo, lo + 32), in_=v("code", 0, 256, 1, lo, lo + 32),
-                   pattern=[[0, 256]], compare_op=A.is_ge, fill=0.0, base=-16, channel_multiplier=1)
-        for gr in range(8):
-            lo = 32 * (gr // 2)
-            m, hi = ("cdO", lo + 32) if gr % 2 else ("code", lo + 16)
-            b = "b%d" % (6 + gr % 2)
-            mm(v(b, 0, 256), v(m, 0, 128, 1, lo, hi), v(m, 0, 256, 1, lo, hi))
-            mm(v(b, 256, 384), v(m, 128, 256, 1, lo, hi), v(m, 128, 256, 1, lo, hi))
-            act(v("E", 384 * gr, 384 * gr + 384), v(b, 0, 384), AF.Relu, bias=v("fb"))
+        per = 256 // BLK
+        done = {}
+        for k in range(4):
+            for odd in range(2):
+                b = "b%d" % (6 + odd)
+                lo = 32 * k
+                hi = lo + 16 + 16 * odd
+                for c in range(2):
+                    for l in range(0, 128, BLK):
+                        at, x = BLK * (2 * (k % per) + c), v("code", 128 * c + l, 128 * c + l + BLK, 1, lo, hi)
+                        i = mm(v(b, at, at + BLK, 1, l, l + BLK), x, x, True, True, l > 0)
+                        if (k - 1, odd) in done:
+                            ops[i][3].add((done[k - 1, odd], True))
+                done[k, odd] = i
+                if k % per == per - 1:
+                    e = BLK * (8 * odd + 2 * (k + 1 - per))
+                    act(v("E", e, e + 512), v(b), AF.Relu, scale=1.0 if odd else 256.0, bias=v("fb"))
 
     def revoke(t):
         ts(v("rq"), v("cs", 255, 256), R256, A.add, -R256, A.add)
         ts(v("c2"), v("cs", 255, 256), 128.0, A.add)
-        if t == RO - 1 and OPT["fin"] == "sv":
-            ts(v("rb"), v("c2"), v("rq"), A.subtract, -256.0, A.mult)
-            for i in range(4):
-                lo, o = 320 * i, v("b%d" % (7 - i), 0, 320)
-                act(o, v("KK0", KB + lo, KB + lo + 320), AF.Abs, scale=256.0, bias=v("rb"))
-                tt(v("Yk", lo, lo + 320), o, v("KK0", KB + lo, KB + lo + 320), A.min)
-                if i % 2:
-                    store("yS"[i // 2], T.yk[:, lo - 320:lo + 320], v("Yk", lo - 320, lo + 320), 2 + i // 2)
-            return
         if t == RO - 1:
             ts(v("rb"), v("c2"), v("rq"), A.subtract)
-            ts(v("nrv"), v("c2"), v("rq"), A.subtract, -1.0, A.mult)
-            for i in range(2):
-                lo = 640 * i
-                ts(v("NM", lo, lo + 640), v("KK0", KB + lo, KB + lo + 640), v("rb"), A.is_equal, v("nrv"), A.mult)
-            for i in range(2):
-                lo = 640 * i
-                scan(v("Yk", lo, lo + 640), v("NM", lo, lo + 640), v("KK0", KB + lo, KB + lo + 640), A.add, 0.0, A.min)
-                store("yS"[i], T.yk[:, lo:lo + 640], v("Yk", lo, lo + 640), 2 + i)
+            ts(v("nrv"), v("rq"), v("c2"), A.subtract)
+            cut = ((0, 800), (800, 1280))
+            for lo, hi in cut:
+                ts(v("NM", lo, hi), part(pre(t), lo, hi), v("rb"), A.is_equal, v("nrv"), A.mult)
+            for i, (lo, hi) in enumerate(cut):
+                scan(v("Yk", lo, hi), v("NM", lo, hi), part(pre(t), lo, hi), A.add, 0.0, A.min)
+                store("Sy"[i], T.yk[:, lo:hi], v("Yk", lo, hi), 2 + i)
             return
-        rv = v("rS%d" % t, 0, 1)
-        ts(rv, v("c2"), v("rq"), A.subtract)
+        rv = [v("rS%d" % t, k, k + 1) for k in range(2)]
+        ts(rv[0], v("c2"), v("rq"), A.subtract)
+        if OPT["rv"] == "s":
+            act(rv[1], v("c2"), AF.Identity, scale=-1.0, bias=v("rq"))
+        else:
+            ts(rv[1], v("rq"), v("c2"), A.subtract)
         send_revoked(t)
-        ts(v("nrv"), v("c2"), v("rq"), A.subtract, -1.0, A.mult)
-        rec("y", 0.05, 3.5, [K(0)], [K(t + 1)], lambda e: e.dma_start(res(K(t + 1)), res(K(0))), "cp%d" % t, 16)
-        ts(v("NM"), K(0), rv, A.is_equal, v("nrv"), A.mult)
+        if who("true", t) == "dma" and pre(t) == W(t + 1):
+            rec("y", 0.05, 4.0, [W(t + 1)], [K(t + 1)], lambda e: e.dma_start(res(K(t + 1)), res(W(t + 1))), "cp%d" % t, 16)
+        struck(v("NM"), pre(t), rv)
         send_rings(t + 1)
-        add_into(K(t + 1), v("NM"), t)
+        if who("true", t) == "dma":
+            add_into(K(t + 1), v("NM"), t)
+        else:
+            take_off(K(t + 1), v("NM"), pre(t))
         act(v("nfc"), v("fs"), AF.Identity, scale=-float(SB), bias=v("f4"))
 
     send_rings(0)
@@ -918,11 +1203,13 @@ def rank_program(g, core, T, topo):
     for t in range(RO):
         more = t < RO - 1
         steps += [("second", second, t, 0), ("third", third, t, 0), ("second", second, t, 1)]
-        steps += [("same", same_node, t)] * (t > 0)
-        steps += [("third", third, t, 1), ("material", material, t, 0)]
-        steps += [("active", active, t, 0)] * (t > 0)
+        steps += [("same", same_node, t)] * (t > 0 and OPT["same"] == "late")
+        steps += [("given", given, t, [0]), ("active", active, t, [0])] * who("split", t)
+        steps += [("third", third, t, 1), ("given", given, t, [1] if who("split", t) else [0, 1]), ("material", material, t, 0)]
         steps += [("next", next_nodes, t, 0)] * more
-        steps += [("writers", writers, t), ("fourth", fourth, t, 0), ("material", material, t, 1)]
+        steps += [("writers", writers, t)]
+        steps += [("same", same_node, t + 1)] * (more and OPT["same"] != "late")
+        steps += [("fourth", fourth, t, 0), ("material", material, t, 1)]
         steps += [("first", first, t + 1, 0)] * more
         steps += [("fourth", fourth, t, 1), ("revoke", revoke, t)]
         steps += [("first", first, t + 1, 1)] * more
@@ -946,12 +1233,12 @@ def hand_on(g, core, T, topo):
         for t in range(RO):
             if t and core == rv_relay:
                 g.wait_ge(T.sem["ra%d" % (t - 1)], 8)
-                remote(g, topo, core, above, T["cI%d" % (t - 1)][:, 0:1], T["hrv%d" % (t - 1)][:, 0:1],
+                remote(g, topo, core, above, T["cI%d" % (t - 1)][:, 0:2], T["hrv%d" % (t - 1)][:, 0:2],
                        T.sem["ri%d" % (t - 1)], T.sem["rl%d" % (t - 1)])
             if core in rl:
                 h = rl.index(core)
                 g.wait_ge(T.sem["ha%d" % t], 8)
-                remote(g, topo, core, below, T["KK%d" % t][:, 512 * h:512 * h + 512], T["hand%d" % t][:],
+                remote(g, topo, core, below, T["KK%d" % t][:, 512 * h + 16:512 * h + 528], T["hand%d" % t][:],
                        T.sem["ki%d%d" % (t, h)], T.sem["hs%d" % t])
         for t in range(RO):
             if core in rl:

import numpy as np
from concourse.bass import DstId, RemoteDMATransfer
from concourse.mybir import dt, AluOpType, AxisListType, ActivationFunctionType
import comms_topo

A = AluOpType
AF = ActivationFunctionType
RO, SB, CAP = 3, 2048, 96
BIG = 1.0e9
R256, R16, R1024 = 1.5 * 2 ** 31, 1.5 * 2 ** 27, 1.5 * 2 ** 33
SPLIT = {("X", t, q): "ss" for t in range(RO) for q in (1, 3)}

KB = 1040
SPARE = 1408
WS = 17 * SB
FAIL = 51 * SB
RJ = 1.5 * 2 ** 39
OFF = 15 * 2048 - 120 * 4096
MID = 2.0 ** 23
HALF = 0.5 - 2.0 ** -11
BY = 2
OPT = dict(run=0, rv="v", xs=(0, 96, 128), drk=14, ms=128, blk=128, split=False, hz="s", piece=256, rs="s", true="dma", come="dma",
           Bv="s", nO="v", BnL="s", BnH="s", PL="s", nf="s", zb="s", zF="s", nb="s", dO="v", vO="v", scO="v", srO="v", hi="s",
           hn="s", Kn="post", kp="fused", Hm="s", fill="laid", wipe=False, ct=11, n="v", to="dm", cap=0, same="early")
OPT.update({("nO", 0, 0): "v", ("BnL", 0, 0): "v", "ct": 7, "hn": "v", "zF": "v"})
SPLIT.update({(x, t, q): "s....v.." for t in range(RO) for x, q in (("X", 0), ("X", 2), ("K", 0))})
SPLIT["K", 0, 0] = "sv"

F32 = dict(G8h=8, nG8h=8, RN=128, RS=136, RD=128, TH=128, T1=1280, sc=256, cV=272, mn=272,
           V2=256, pr=256, zq=256, cs=256, zF=256, pcol=1, lcol=1, c0=3, wcol=1, wthr=1, spare=1,
           fj=16, fs=1, f0=1, f1=1, f2=1, f3=1, f4=1, nfc=1, nw=16, sel=16, hc=16, src=16,
           slot=16, fb=1, h18=1, sgn=16, pR16=1, nR16=1, drb=1, q0=1, rq=1, c2=1, nof=1)
BF = dict(Ib=128, nIb=128, I5=128, nKI=128, nBI=128, nHI=128, I44=128, nI44=128, nFI=128, I17=136, G16b=128, G4=128, nG4=128,
          NG=128, G8b=8, G8s=8, G8m=8, G8x=8, rb=1, IS=128, Tri=128, On=256, DM=256, C0=128, C1=128, C2=128, E0=128, E1=128,
          E2=128, pRJ=128, nRJ=128, cM=128, cQ=128, c18=128, C256=128, CT=1280, Q=16, LR=256, z=256, zb=256, x0=256, KN=512,
          Kw=256, Kx=256, Kt=512, gv=256, evn=256, m1=512, m2=512, hz=256, Hm=256, val=256, vm=256, code=256, nf=256, F=16, aw=16, dr=16, NM=1280, NC=1280,
          nrv=1, Wd=240, Wn=144, M2=128, c12=16, row=128, rw=128)
H16 = dict(mB=256, Bv=256, aH=256, BnH=256, Aw=256, Ap=256, Aqh=256, Aq=256, zh=256, hn=16)
I32 = dict(PI=1, pi15=1, pb=1, pc=1, po=1, p8=1, ps=1, th=1, tl=1, D1=16, D15=16, ic=16, kp=256, k2=256, pi2=16, sc2=272,
           sd=256, wT=32, hi=16, h2=16, nb=256)
U16 = dict(bl=16, bl2=8, vO=32, nO=32, scO=16, srO=16, hO=16, dO=32, BnL=256, PL=256)


def _layout(d):
    pos, at = {}, 0
    for n in d:
        pos[n] = at
        at += (d[n] + 15) // 16 * 16
    return pos, at


WHERE, SCRATCH = {}, {}
for _d, _n, _t in ((F32, "SF", "float32"), (BF, "SBF", "bfloat16"), (H16, "SH", "float16"), (I32, "SI", "int32"),
                   (U16, "SU", "uint16")):
    _p, _w = _layout(_d)
    SCRATCH[_n] = ("sbuf", [128, _w], _t)
    for _k in _d:
        WHERE[_k] = (_n, _p[_k], _d[_k])
_BIGB = dict(KK0=(KB + SPARE, "bfloat16"), KK1=(KB + SPARE, "bfloat16"), KK2=(KB + SPARE, "bfloat16"), X=(4096, "bfloat16"),
             Kc=(4096, "bfloat16"), zr=(4096, "bfloat16"),
             eqV=(4096, "bfloat16"), eqN=(4096, "bfloat16"), Xc=(4096, "bfloat16"), mx=(4096, "bfloat16"), E=(2048, "bfloat16"),
             Y1=(1280, "bfloat16"), W2=(SPARE, "bfloat16"), NBi=(SPARE, "int32"), Yk=(1280, "bfloat16"), thI=(8, "int32"),
             rS0=(8, "bfloat16"), rS1=(8, "bfloat16"), cI0=(8, "bfloat16"), cI1=(8, "bfloat16"))
for _k in _BIGB:
    SCRATCH[_k] = ("sbuf", [128, _BIGB[_k][0]], _BIGB[_k][1])
    WHERE[_k] = (_k, 0, _BIGB[_k][0])
for _k in range(8):
    SCRATCH["b%d" % _k] = ("psum", [128, 512], "float32")
    WHERE["b%d" % _k] = ("b%d" % _k, 0, 512)
for _k in range(RO):
    SCRATCH["hand%d" % _k] = ("sbuf", [128, 512], "bfloat16")
for _k in range(RO - 1):
    SCRATCH["hrv%d" % _k] = ("sbuf", [128, 8], "bfloat16")
SEMAPHORES = ["qv", "qs", "qt", "qg", "cp0", "cp1"]
SEMAPHORES += ["ld%d" % i for i in range(7)] + ["st%d" % i for i in range(4)] + ["ad%d" % i for i in range(4)]
for _t in range(RO):
    SEMAPHORES += ["ks%d" % _t, "ki%d0" % _t, "ki%d1" % _t, "ha%d" % _t, "hs%d" % _t]
for _t in range(RO - 1):
    SEMAPHORES += ["rs%d" % _t, "ri%d" % _t, "ra%d" % _t, "rl%d" % _t]

CY = 0.00083
STEP = [""]
SEQ = []
INFO = []
ORD = dict(tries=11000, starts=0, heat=700, seed=6, slack=0.12, share=0.25, move=3.0, shake=0.4, swap=0.2, near=5.0, back=0.7, free=True, act=55,
           moves=16000, lean=0.3, warm=0.006)
PACE = [(1.25, 1.95, 4.75, 0.3, 1.0, 89.0), (1.0, 1.56, 3.8, 0.1, 0.6, 67.2), (1.0, 1.2, 2.3, 0.15, 1.0, 68.5),
        (1.25, 1.38, 2.25, 0.16, 0.8, 81.2), (1.25, 2.5, 6.9, 0.16, 0.8, 95.5), (1.45, 2.26, 5.5, 0.25, 1.0, 98.7)]


def relays(core, T, topo, dst):
    out = []
    for d in (topo.die(core), 1 - topo.die(core)):
        for c in topo.cores_of(core):
            if c != core and topo.die(c) == d and T.rank_of(c) is None and topo.may_write(c, dst):
                out.append(c)
                break
    return out


def engines_mask(topo, src, dst, lo, hi):
    return sum(1 << e for e in topo.engines(src, dst)[lo:hi])


def remote(g, topo, src, dst, out, in_, rsem, lsem):
    rid, pid = topo.addr(dst, src)
    return g.remote_dma(out, in_, rsem, lsem, pid, rid, engines_mask(topo, src, dst, 0, 8))


def view(name, lo=0, hi=None, step=1, plo=0, phi=128):
    return ("@", name, lo, WHERE[name][2] if hi is None else hi, step, plo, phi)


def ind(win, off):
    return ("#", win, off)


def is_view(x):
    return isinstance(x, tuple) and len(x) > 0 and (x[0] == "@" or x[0] == "#")


def count(x):
    if x[0] == "#":
        return 16 * (x[2][3] - x[2][2])
    return (x[3] - x[2] + x[4] - 1) // x[4]


def psum(x):
    return x[0] == "@" and SCRATCH[WHERE[x[1]][0]][0] == "psum"


def two(x):
    return x[0] == "@" and SCRATCH[WHERE[x[1]][0]][2] in ("bfloat16", "float16", "uint16")


def clash(a, b):
    if a[3] <= b[2] or b[3] <= a[2] or a[6] <= b[5] or b[6] <= a[5]:
        return False
    if a[4] > 1 and a[4] == b[4] and (a[2] - b[2]) % a[4]:
        return False
    return True


def covers(a, b):
    return a[4] == 1 and a[2] <= b[2] and a[3] >= b[3] and a[5] <= b[5] and a[6] >= b[6]


def cost(q, m, kw):
    o = kw.get("out")
    if q == "t":
        n, mm = count(kw["rhs"]), count(kw["lhsT"])
        return (0.0, max(min(64, mm), n) * (1 if two(kw["lhsT"]) else 4), 0, 0)
    if q == "g":
        return (0.0, (220 if m == "iota" else 265) + 2 * count(o), 0, 0)
    ins = [kw[k] for k in kw if k not in ("out", "accum_out") and is_view(kw[k])]
    full = [i for i in ins if count(i) > 1]
    n = max([count(o)] + [count(i) for i in full])
    if o[0] == "#":
        return (0.05, 0, 0, n)
    for i in full:
        if i[0] == "#":
            return (0.065 if q == "s" else 0.05, 0, n, 0)
    c = 1.0
    if q == "v" and m == "tensor_tensor" and not [i for i in full if psum(i)]:
        c = 2.0
    if q == "v" and m != "tensor_tensor" and two(o) and not [i for i in full if not two(i)]:
        c = 0.5
    return (0.0, max(64, n * c) + ORD["act"] * (q == "s"), 0, 0)


def noter(T):
    ops, hist, opened = [], {}, {}

    def res(x):
        if x[0] == "#":
            return res(x[1]).indirect(res(x[2]))
        b, off, _ = WHERE[x[1]]
        lo, hi = off + x[2], off + x[3]
        if x[4] > 1:
            return T[b][x[5]:x[6], lo:range(lo, hi, x[4])[-1] + 1:x[4]]
        return T[b][x[5]:x[6], lo:hi]

    def touch(i, q, v, wr, deps, turns):
        ps = psum(v)
        keep = []
        for e in hist.setdefault(v[1], []):
            ev, ew, eq, ei = e
            if ei == i:
                keep.append(e)
                continue
            if ps and eq != q:
                (deps if (wr or ew) and clash(v, ev) else turns).add((ei, True))
                if wr and covers(v, ev):
                    continue
            elif (wr or ew) and clash(v, ev):
                if not (ps and q == "t"):
                    deps.add((ei, True))
                if wr and covers(v, ev):
                    continue
            keep.append(e)
        keep.append((v, wr, q, i))
        hist[v[1]] = keep

    def rec(q, c, tail, reads, writes, emit, sem=None, inc=1, join=False):
        i = len(ops) - join
        deps, turns, banks = (ops[i][3], ops[i][9], ops[i][10]) if join else (set(), set(), set())
        for v in reads:
            touch(i, q, v, False, deps, turns)
        for v in writes:
            touch(i, q, v, True, deps, turns)
        banks.update(int(v[1][1:]) for v in reads + writes if psum(v))
        if not isinstance(c, tuple):
            c = (c, 0, 0, 0)
        if join:
            ops[i][1] = tuple(a + b for a, b in zip(ops[i][1], c))
            ops[i][4].append(emit)
            return i
        name = writes[0][1] if writes else "out"
        ops.append([q, c, tail, deps, emit and [emit], sem or "q" + q, inc,
                    STEP[0] + (name[:2] if q == "v" and name[:2] in ("eq", "mx") else q), name, turns, banks])
        return i

    def op(q, m, join=False, **kw):
        reads, writes = [], []
        for k in kw:
            x = kw[k]
            if not is_view(x):
                continue
            w = k in ("out", "accum_out")
            if x[0] == "#":
                (writes if w else reads).append(x[1])
                reads.append(x[2])
            else:
                (writes if w else reads).append(x)

        def emit(e):
            a = {}
            for k in kw:
                a[k] = res(kw[k]) if is_view(kw[k]) else kw[k]
            if m == "memset":
                return e.memset(a["out"], a["constant"])
            if m == "tensor_copy":
                return e.tensor_copy(a["out"], a["in_"])
            if m == "tensor_tensor":
                return e.tensor_tensor(**a)
            if m == "tensor_scalar":
                return e.tensor_scalar(**a)
            if m == "tensor_tensor_scan":
                return e.tensor_tensor_scan(**a)
            if m == "matmul":
                return e.matmul(**a)
            if m == "activation":
                return e.activation(**a)
            if m == "affine_select":
                return e.affine_select(**a)
            return e.iota(**a)
        i = rec(q, cost(q, m, kw), 0.0, reads, writes, emit, join=join)
        if m == "matmul":
            b = kw["out"][1]
            if opened.get(b, i) != i:
                ops[i][3].add((opened[b], False))
            opened[b] = i
        return i

    def land(v, sem, i, late):
        j = rec("x", 0.0, late, [], [v], None, sem, 8)
        ops[j][3].add((i, True))

    return ops, op, rec, land, res


def order(ops):
    n = len(ops)
    q = ["s" if o[0] == "S" else o[0] for o in ops]
    deps, before = [], [0] * n
    for i in range(n):
        keep, seen = [], 0
        for j, w in sorted(ops[i][3] | (set() if ORD["free"] else ops[i][9]), reverse=True):
            if not (w and seen >> j & 1):
                keep.append((j, w))
            if w:
                seen |= before[j]
                before[i] |= before[j] | 1 << j
        deps.append(keep)
    durs = [[o[1][0] + (o[1][1] * p[0] + o[1][2] * p[1] + o[1][3] * p[2]) * CY for o in ops] for p in PACE]
    tails = [[o[2] * p[4] or p[3] for o in ops] for p in PACE]
    fwds = [[[(j, d[j] + (x[j] if w else 0.0)) for j, w in deps[i]] for i in range(n)] for d, x in zip(durs, tails)]
    dur, tail, fwd, bwd = durs[0], tails[0], fwds[0], [[] for _ in range(n)]
    for i in range(n):
        for j, w in deps[i]:
            bwd[j].append((i, dur[i] + (tail[j] if w else 0.0)))
    ends = [i for i in range(n) if not bwd[i] and q[i] != "x"]
    span = np.array([dur[i] + (0.0 if bwd[i] else tail[i]) for i in range(n)])
    names = sorted(set(o[7] for o in ops))
    step = np.array([names.index(o[7]) for o in ops])
    state = [ORD["seed"]]
    hop = PACE[0][3]
    mine = [[3 * b + "vst".index(q[i]) for b in ops[i][10]] for i in range(n)]
    other = [[3 * b + m for b in ops[i][10] for m in range(3) if "vst"[m] != q[i]] for i in range(n)]

    def draw(k):
        state[0] = (state[0] * 6364136223846793005 + 1442695040888963407) % 2 ** 64
        x = (np.arange(1, k + 1) * (state[0] >> 44 | 1) + (state[0] >> 20 & 65535)) % 1048573
        return (x * x % 1048573) / 1048573.0

    def place(pre, key, turn):
        key = np.array(key, float).tolist()
        for i in turn:
            x = key[i]
            for j, _ in pre[i]:
                if key[j] >= x:
                    key[i] = x = key[j] + 1e-7
        st = [0.0] * n
        busy = {x: ([], []) for x in set(q)}
        shut = [([], []) for _ in range(24)]
        for i in np.argsort(key, kind="stable").tolist():
            s = 0.0
            for j, lag in pre[i]:
                if st[j] + lag > s:
                    s = st[j] + lag
            if q[i] != "x":
                lo, hi = busy[q[i]]
                d = dur[i] - 1e-9
                k = m = len(lo)
                while k and hi[k - 1] > s:
                    k -= 1
                while True:
                    while k < m and lo[k] < s + d:
                        if hi[k] > s:
                            s = hi[k]
                        k += 1
                    was = s
                    for b in mine[i]:
                        a, z = shut[b]
                        x = len(a)
                        while x and z[x - 1] > s:
                            x -= 1
                        while x < len(a) and a[x] < s + d:
                            s = z[x]
                            x += 1
                    if s == was:
                        break
                e = s + dur[i]
                if k and hi[k - 1] > s - 0.02:
                    if k < m and lo[k] < e + 0.02:
                        hi[k - 1] = hi[k]
                        del lo[k], hi[k]
                    else:
                        hi[k - 1] = e
                elif k < m and lo[k] < e + 0.02:
                    lo[k] = s
                else:
                    lo.insert(k, s)
                    hi.insert(k, e)
                for b in other[i]:
                    a, z = shut[b]
                    f, t = s - hop, e + hop
                    x = len(a)
                    while x and a[x - 1] > t:
                        x -= 1
                    y = x
                    while y and z[y - 1] >= f:
                        y -= 1
                    if y < x:
                        f, t = min(f, a[y]), max(t, z[x - 1])
                    a[y:x], z[y:x] = [f], [t]
            st[i] = s
        return st

    def replay(seq, p):
        d, pre, tail, hop = durs[p], fwds[p], tails[p], PACE[p][3]
        free, st, left = {x: 0.0 for x in set(q)}, [0.0] * n, [0.0] * 24
        for i in seq:
            s = free[q[i]]
            for j, lag in pre[i]:
                if st[j] + lag > s:
                    s = st[j] + lag
            for b in mine[i]:
                if left[b] > s:
                    s = left[b]
            st[i] = s
            if q[i] != "x":
                s += d[i]
                free[q[i]] = s
                for b in other[i]:
                    if s + hop > left[b]:
                        left[b] = s + hop
        return max(st[i] + d[i] + tail[i] for i in ends)

    up, down = list(range(n)), list(range(n - 1, -1, -1))
    key = up
    best = cur = None
    heats = []
    for turn in range(ORD["tries"]):
        if turn and turn % ORD["heat"] == 0 and len(heats) < ORD["starts"]:
            heats.append(best)
            best = cur = min(heats) if len(heats) == ORD["starts"] else None
            key = cur[1] if cur else up
        st = place(fwd, key, up)
        end = max(st[i] + dur[i] + tail[i] for i in ends)
        r = draw(4)
        if cur is None or end <= cur[2][0] * 1.01:
            seq = np.argsort(st, kind="stable").tolist()
            e = [end] + [replay(seq, k) for k in range(1, len(PACE))]
            rel = [75 * x / p[5] for x, p in zip(e, PACE)]
            val = (sum(rel) / len(rel) + max(rel)) / 2
            if best is None or val < best[0]:
                best = (val, st, e, seq)
            if cur is None or val <= cur[0] + ORD["slack"] * r[0]:
                cur = (val, st, e, seq)
            if cur[0] > best[0] + 3 * ORD["slack"]:
                cur = best
        move = (draw(len(names)) < ORD["share"]) * (draw(len(names)) - 0.5) * 2 * ORD["move"]
        key = np.array(cur[1])
        if r[3] < ORD["swap"]:
            st, prev, at, held = cur[1], {}, {}, []
            for i in cur[3]:
                prev[i], at[q[i]] = at.get(q[i]), i
            i = max(ends, key=lambda k: st[k] + dur[k] + tail[k])
            while i is not None:
                tight = [j for j, lag in fwd[i] if st[j] + lag > st[i] - 1e-6]
                if not tight and q[i] != "x" and prev[i] is not None:
                    held.append((prev[i], i))
                i = tight[0] if tight else prev[i] if q[i] != "x" else None
            for x in draw(1 + int(3 * r[2])) if held else ():
                j, i = held[int(x * len(held))]
                key[j] = st[i] + dur[i] + (tail[i] if r[1] < 0.5 else 0.0)
            continue
        near = abs(key - draw(1)[0] * cur[2][0]) < ORD["near"]
        if r[1] < ORD["back"]:
            key = -(np.array(place(bwd, -(key + span) + near * ORD["shake"] * r[2] * draw(n), down)) + np.array(dur))
        key = key + near * (move[step] + ORD["shake"] * r[2] * draw(n))

    qi = ["vstgyx".index(x) for x in q]
    paces = range(len(PACE))

    def rerun(seq, p, st, lo):
        d, pre, tail, hop = durs[p], fwds[p], tails[p], PACE[p][3]
        free, left, st = [0.0] * 6, [0.0] * 24, st[:]
        for i in seq[max(0, lo - 250):lo]:
            free[qi[i]] = st[i] + d[i]
            for b in other[i]:
                left[b] = max(left[b], st[i] + d[i] + hop)
        free[5] = 0.0
        for i in seq[lo:]:
            m = qi[i]
            s = free[m]
            for j, lag in pre[i]:
                if st[j] + lag > s:
                    s = st[j] + lag
            for b in mine[i]:
                if left[b] > s:
                    s = left[b]
            st[i] = s
            if m != 5:
                s += d[i]
                free[m] = s
                for b in other[i]:
                    if s + hop > left[b]:
                        left[b] = s + hop
        return (max(st[i] + d[i] + tail[i] for i in ends) + ORD["lean"] * sum(st) / n) * 75 / PACE[p][5] / len(PACE), st

    seq = best[3]
    now = [rerun(seq, p, [0.0] * n, 0) for p in paces]
    keep, runs = (sum(x[0] for x in now), seq), {}
    for turn in range(ORD["moves"]):
        r = draw(6).tolist()
        p = int(r[0] * len(PACE))
        if p not in runs:
            pos, prev, at, held, was = [0] * n, [None] * n, [None] * 6, [()] * n, [None] * 24
            for x, i in enumerate(seq):
                pos[i], prev[i], at[qi[i]] = x, at[qi[i]], i
                held[i] = [was[b] for b in other[i] if was[b] is not None]
                for b in mine[i]:
                    was[b] = i
            s, d = now[p][1], durs[p]
            i = max(ends, key=lambda u: s[u] + d[u] + tails[p][u])
            found = [[i]]
            while True:
                tight = [j for j, lag in fwds[p][i] if s[j] + lag > s[i] - 1e-7]
                if tight:
                    found.append([])
                elif qi[i] != 5 and prev[i] is not None and s[prev[i]] + d[prev[i]] > s[i] - 1e-7:
                    tight = [prev[i]]
                else:
                    tight = [j for j in held[i] if s[j] + d[j] + PACE[p][3] > s[i] - 1e-7]
                if not tight:
                    break
                i = tight[0]
                found[-1].append(i)
            runs[p] = ([b for b in found if len(b) > 1], pos)
        found, pos = runs[p]
        b = found[int(r[1] * len(found))]
        x = int(r[2] * (len(b) - 1))
        i, j = b[x], b[min(len(b) - 1, x + 1 + int(-np.log(r[3] + 1e-9) * 3))]
        mid = seq[pos[j]:pos[i] + 1]
        if r[4] < 0.5:
            mark = {i}
            for u in reversed(mid[:-1]):
                if [w for w, _ in bwd[u] if w in mark]:
                    mark.add(u)
            new = [u for u in mid if u in mark] + [u for u in mid if u not in mark]
        else:
            mark = {j}
            for u in mid[1:]:
                if [w for w, _ in fwd[u] if w in mark]:
                    mark.add(u)
            new = [u for u in mid if u not in mark] + [u for u in mid if u in mark]
        if i in mark and j in mark:
            continue
        cand = seq[:pos[j]] + new + seq[pos[i] + 1:]
        one = rerun(cand, p, now[p][1], pos[j])
        if one[0] > now[p][0] + 0.05:
            continue
        then = [one if k == p else rerun(cand, k, now[k][1], pos[j]) for k in paces]
        val = sum(x[0] for x in then)
        if val <= sum(x[0] for x in now) - ORD["warm"] * np.log(r[5] + 1e-9):
            place_of = np.argsort(np.array(then[0][1])[cand], kind="stable")
            now, seq, runs = then, np.array(cand)[place_of].tolist(), {}
            if val < keep[0]:
                keep = (val, seq)
    e = [replay(keep[1], p) for p in paces]
    INFO[:] = [sum(75 * x / p[5] for x, p in zip(e, PACE)) / len(e), e, {x: sum(durs[1][i] for i in up if q[i] == x) for x in "vstg"}]
    return keep[1]


def issue(g, T, ops, seq):
    Q = {"v": g.vector, "s": g.scalar, "t": g.tensor, "g": g, "y": g.sync, "S": g.scalar}
    total, tok, know, inside = {}, {}, {}, [{} for _ in range(8)]
    for q in Q:
        know[q] = {}
    know["S"] = know["s"]
    for i in seq:
        q, c, tail, deps, emit, sem, inc = ops[i][:7]
        if emit is None:
            total[sem] = total.get(sem, 0) + inc
            tok[i] = (sem, total[sem], {})
            continue
        k = know[q]
        need = {}
        turns = [(inside[b][x], True) for b in ops[i][10] for x in inside[b] if x != q]
        for b in ops[i][10]:
            inside[b][q] = i
        for j, w in sorted(deps) + turns:
            if w:
                s, v, sn = tok[j]
                if k.get(s, 0) < v and (s not in need or need[s][0] < v):
                    need[s] = (v, sn)
        for s in sorted(need):
            v, sn = need[s]
            if [o for o in need if o != s and need[o][1].get(s, 0) >= v]:
                continue
            Q[q].wait_ge(T.sem[s], v)
        for s in need:
            v, sn = need[s]
            k[s] = max(k.get(s, 0), v)
            for o in sn:
                k[o] = max(k.get(o, 0), sn[o])
        for one in emit:
            total[sem] = total.get(sem, 0) + inc
            r = one(Q[q])
            if r is not None:
                r.then_inc(T.sem[sem], inc)
        tok[i] = (sem, total[sem], dict(k))
    for s in sorted(total):
        if know["g"].get(s, 0) < total[s]:
            g.wait_ge(T.sem[s], total[s])


def rank_program(g, core, T, topo):
    rank = T.rank_of(core)
    n = len(T.cores)
    if rank is None:
        hand_on(g, core, T, topo)
        return
    ops, op, rec, land, res = noter(T)
    below, above = T.cores[(rank - 1) % n], T.cores[(rank + 1) % n]
    rl = relays(core, T, topo, below)
    rv_relay = relays(core, T, topo, above)[0]
    v = view
    last = {}
    BLK = OPT["blk"]

    def who(name, t, c=0):
        return OPT.get((name, t, c), OPT.get((name, t), OPT[name]))

    def tt(out, a, b, o, join=False):
        return op("v", "tensor_tensor", join, out=out, in0=a, in1=b, op=o)

    def ts(out, a, s1, o1, s2=None, o2=None):
        if o2 is None:
            return op("v", "tensor_scalar", out=out, in0=a, scalar1=s1, scalar2=None, op0=o1)
        return op("v", "tensor_scalar", out=out, in0=a, scalar1=s1, scalar2=s2, op0=o1, op1=o2)

    def cp(out, a, q="v"):
        if q == "s":
            return act(out, a)
        return op("v", "tensor_copy", out=out, in_=a)

    def plus(out, a, x, q):
        if q == "s":
            return act(out, a, AF.Identity if is_view(x) else AF.Copy, bias=x)
        return ts(out, a, x, A.add)

    def fill(out, x):
        return op("v", "memset", out=out, constant=x)

    def act(out, a, f=AF.Copy, **kw):
        return op("s", "activation", out=out, in_=a, func=f, **kw)

    def mm(out, l, r, start=True, stop=True, join=False):
        return op("t", "matmul", join, out=out, lhsT=l, rhs=r, start=start, stop=stop)

    def group(out, pairs, by=1):
        for i, (l, r) in enumerate(pairs):
            mm(out, l, r, i == 0, i == len(pairs) - 1, i % by > 0)

    def iota(out, pattern, base, cm):
        kw = dict(out=out, pattern=pattern, base=base, channel_multiplier=cm)
        if WHERE[out[1]][0] != "SI":
            kw["allow_small_or_imprecise_dtypes"] = True
        return op("g", "iota", **kw)

    def select(out, a, pattern, base, cm, o=A.is_ge, x=0.0):
        return op("g", "affine_select", out=out, in_=a, pattern=pattern, compare_op=o, fill=x, base=base, channel_multiplier=cm)

    def copy_g(out, a):
        return select(out, a, [[0, count(out)]], 0, 0)

    def scan(out, a, b, o1, first=0.0, o0=A.add):
        return op("v", "tensor_tensor_scan", out=out, data0=a, data1=b, initial=first, op0=o0, op1=o1)

    def chain(name, i):
        if last.get(name, i) != i:
            ops[i][3].add((last[name], False))
        last[name] = i

    def load(q, dst, src, k, late):
        chain("load" + q, rec(q, 0.05, late, [], [dst], lambda e: e.dma_start(res(dst), src), "ld%d" % k, 16))

    def store(q, dst, src, k):
        rec(q, 0.1, 2.0, [src], [], lambda e: e.dma_start(dst, res(src)), "st%d" % k, 16)

    def add_into(dst, src, k):
        rec("g", 1.0, 5.3, [src], [dst], lambda e: e.dma_start(res(dst), res(src), accum_op=A.add), "ad%d" % k, 16)

    def gather(which, out, table, places, b, scale):
        how = SPLIT.get(which, "s")
        for k, e in enumerate(how):
            if e == ".":
                continue
            more = len(how) - k - len(how[k + 1:].lstrip("."))
            lo, w = b + 64 // len(how) * k, 64 // len(how) * more
            dst, src = v(out, 16 * lo, 16 * (lo + w)), ind(table, v(places, lo, lo + w))
            if e == "v":
                ts(dst, src, scale, A.mult)
            else:
                chain("gathers", act(dst, src, scale=scale))

    def hv(name, c, w=128):
        return v(name, w * c, w * c + w)

    def top(name, lo=0, hi=None, k=1):
        return v(name, lo, hi, 1, 0, k)

    def KV(c, k, w=128):
        return v("b%d" % c, 128 * k, 128 * k + w)

    def CV(c, k=0, step=1):
        return v("b%d" % (2 + c), k, 136, step)

    def CN(c, k=0, step=1):
        return v("b%d" % (4 + c), 128 + k, 264, step)

    def MI(c, k):
        return v("b%d" % (4 + c), 128 * k, 128 * k + 128)

    def V2p(c):
        return v("b%d" % (4 + c), 264, 392)

    def SM(c, k):
        if k < 2:
            return v("b%d" % (4 + c), 480 + 8 * k, 488 + 8 * k)
        return v("b%d" % (2 + c), 384 + 8 * k, 392 + 8 * k)

    def Wi(c, w=1):
        return v("sc2", 136 * c + 16, 136 * (c + w), 17)

    def wT(t, c=0, w=16):
        b = 16 * (t % 2) + 8 * c
        return v("wT", b, b + w)

    On = v("On", 0, 128)
    one = top("On", 0, 128)

    def WR(k, w=16, plo=0, phi=128):
        return v("b4", 384 + k, 384 + k + w, 1, plo, phi)

    def W(t, lo=0, hi=1280):
        if t > 1 and who("fill", t - 1) == "laid":
            return v("W2", lo, hi) if t == 2 else v("KK0", KB + lo, KB + hi)
        return v("KK%d" % max(0, t - 1), KB + lo, KB + hi)

    load("y", v("NBi", 0, 640), T.nbr[:, 0:640], 0, 2.1)
    load("S", v("z"), T.z0[:], 1, 1.9)
    load("y", v("NBi", 640, 1280), T.nbr[:, 640:1280], 2, 3.4)
    load("y", v("KK0", KB, KB + 1280), T.ring[:], 3, 4.6)
    load("S", v("thI", 0, 1), T.thr[:], 4, 2.5)
    load("y", v("X", 0, 2048), T.mat[:], 5, 7.0)
    load("y", v("X", 2048, 4096), T.mat[:], 6, 9.0)

    fill(v("On"), 1.0)
    iota(v("PI"), [[1, 1]], 0, 1)
    iota(v("D1"), [[-1, 16]], 256, 1)
    select(v("G16b"), On, [[-16, 8], [0, 16]], 0, 1)
    select(v("G16b"), v("G16b"), [[16, 8], [0, 16]], 15, -1)
    for t in range(RO):
        iota(top("C%d" % t), [[0, 8], [-4096, 16]], 4096 * t - 30720, 0)
        iota(top("E%d" % t), [[0, 8], [4096, 16]], 2048 - 4096 * t, 0)
    select(v("Ib"), On, [[-1, 128]], 0, 1, A.is_equal)
    iota(v("V2"), [[10, 256]], 1, 0)
    iota(v("ic"), [[1, 16]], 0, 0)
    iota(v("T1"), [[1, 1280]], 0, 0)
    ts(v("pi15"), v("PI"), 15, A.bitwise_and)
    act(v("pcol"), v("pi15"))
    act(v("lcol"), v("PI"))
    fill(top("pRJ"), RJ)
    fill(top("nRJ"), -RJ)
    for name, x in (("G4", 4096.0), ("nG4", -4096.0)):
        ts(v(name), v("G16b"), x, A.mult)
    select(v("I17"), v("On", 0, 136), [[-16, 8], [-1, 17]], 1, 1, A.is_equal)
    act(v("I17", 0, 136, 17), v("On", 0, 8), scale=0.0)
    for c in [c for c in range(2) if max(who("run", t, c) for t in range(RO))]:
        act(v("zr", 2048 * c, 2048 * c + 2048, 16), On, scale=0.0)
    for name, x in (("G8h", 2), ("G8b", 1), ("G8s", WS), ("G8m", 4 * SB), ("G8x", -2 * SB)):
        ts(v(name), v("G16b", 0, 128, 16), float(x), A.mult)
    ts(v("D15"), v("D1"), 15, A.bitwise_and)
    ts(v("DM", 0, 16), v("D15"), 0.0, A.is_equal)
    for w in (16, 32, 64, 128):
        cp(v("DM", w, 2 * w), v("DM", 0, w))
    ts(v("RN"), v("DM", 0, 128), -BIG, A.mult, 4096.0, A.add)
    act(v("nof"), v("pi15"), scale=4096.0, bias=-15 * 4096.0 - OFF)
    act(v("RS"), v("On", 0, 136), scale=float(SB))
    act(v("RS", 0, 136, 17), v("On", 0, 8), scale=-BIG)
    act(v("RS", 1, 136, 17), v("On", 0, 8), scale=float(FAIL - 16 * SB + 128 * SB - OFF))
    for name, x in (("IS", 128.0 * SB), ("nIb", -1.0), ("nKI", -1024.0), ("nBI", -2.0 ** 19), ("nHI", -256.0), ("I5", 512.0),
                    ("nFI", -4096.0)) + (("I44", 2.0 ** 44), ("nI44", -2.0 ** 44)) * (OPT["hz"] == "t"):
        ts(v(name), v("Ib"), x, A.mult)
    act(v("bl"), v("ic"))
    if OPT["to"] != "dm":
        ts(v("p8"), v("PI"), 8, A.bitwise_and)
        act(v("f2"), v("p8"))
        act(v("bl2"), v("ic", 0, 8), AF.Identity, bias=v("f2"))
        select(v("M2"), On, [[0, 16], [-16, 8]], 0, 1)
        select(v("M2"), v("M2"), [[0, 16], [16, 8]], 15, -1)
        fill(v("Wd"), 0.0)
        act(v("Wd", 112, 128), v("DM", 0, 16))
    if OPT["n"] == "t":
        fill(v("Wn"), 0.0)
        act(v("Wn", 16, 144, 16), v("G16b", 0, 128, 16))
    act(v("pb"), v("pi15"), scale=811.0)
    ts(v("pc"), v("pb"), SB - 1, A.bitwise_and)
    for t in range(RO):
        act(v("c0", t, t + 1), v("pc"), bias=float(t))
    select(v("Tri"), On, [[1, 128]], 0, -1, A.is_ge)
    select(v("Tri"), v("Tri"), [[1, 128]], 0, -1, A.not_equal, 512.0)
    for name, x in (("fb", -3840.0), ("h18", -127 * 2.0 ** 18), ("pR16", R16), ("nR16", -R16), ("nfc", 1.0 - MID),
                    ("drb", -2.5), ("f0", -7.5 / 16), ("f1", 1.0 - MID - 7.5 * SB)):
        fill(v(name), x)
    fill(v("C256"), 256.0)
    for name, x in (("cQ", -0.25), ("rw", 0.5)) + (("c18", -2.0 ** 18),) * (OPT["hz"] == "t"):
        fill(top(name), x)
    act(top("c12"), top("On", 0, 16), scale=4096.0)
    act(v("KK0", 0, 16), v("On", 0, 16), scale=0.0)
    for t in (2, 3) if OPT["wipe"] else ():
        act(W(t, 1280, SPARE), On, scale=0.0)
    if OPT["wipe"]:
        act(v("NBi", 1280, SPARE), On, scale=0.0)
    ts(v("ps"), v("PI"), BLK - 1, A.bitwise_and)
    act(v("spare"), v("ps"), bias=1280.0)
    scan(top("row"), top("rw"), one, A.mult, 2.0 ** 64, A.mult)
    mm(v("b7", 0, 1), top("row"), top("On", 0, 1))
    act(v("wcol"), v("b7", 0, 1))
    act(v("wthr"), v("b7", 0, 1), scale=-384.0)
    act(v("sgn"), v("DM", 0, 16), scale=-2.0, bias=1.0)
    ts(v("po"), v("PI"), 4, A.arith_shift_right, 1, A.bitwise_and)
    act(v("CT", 0, 1), v("po"), scale=15.0, bias=1.0)
    for r in range(11):
        w = min(2 ** r, 1280 - 2 ** r)
        if r < OPT["ct"]:
            act(v("CT", 2 ** r, 2 ** r + w), v("CT", 0, w), scale=v("sgn", r, r + 1))
        else:
            ts(v("CT", 2 ** r, 2 ** r + w), v("CT", 0, w), v("sgn", r, r + 1), A.mult)
    ts(v("th"), v("thI", 0, 1), 6, A.arith_shift_right)
    ts(v("tl"), v("thI", 0, 1), 63, A.bitwise_and)
    act(v("Q", 0, 1), v("th"), scale=-64.0 * SB, bias=MID)
    act(v("Q", 1, 2), v("tl"), scale=-float(SB))
    act(v("Q", 2, 3), v("pcol"))
    act(v("Q", 3, 4), v("On", 0, 1), scale=16.0)
    act(v("Q", 4, 7), v("On", 0, 3))
    act(v("Q", 7, 8), v("lcol"))
    mm(top("b6", 0, 128, 4), v("Q", 0, 4), v("Ib"))
    mm(top("b6", 128, 256, 4), v("Q", 4, 8), v("Ib"))
    act(top("LR", 0, 256, 4), top("b6", 0, 256, 4))
    mm(v("b6", 256, 384), top("LR", 128, 256, 2), top("LR", 0, 128, 2))
    act(v("TH"), v("b6", 256, 384))
    tt(v("RD", 1, 128), v("b6", 257, 384), v("TH", 0, 127), A.subtract)
    act(v("RD", 0, 128, 16), v("On", 0, 8), scale=BIG)
    for c in range(2):
        act(KV(c, 2), hv("z", c), scale=0.5)
        act(hv("zq", c), hv("z", c), scale=0.5, bias=1023.75)
        ts(hv("zb", c), hv("z", c), 0.5, A.mult)
        if who("kp", 0, c) != "fused":
            act(V2p(c), hv("V2", c))

    def send_rings(t):
        names = [W(t)[1:3]] + [("NM", 0)] * (t > 0) + [("NC", 0)] * (t > 1 and who("fill", 1) != "laid")

        def emit(e):
            parts = []
            for h in range(2):
                rid, pid = topo.addr(rl[h], core)
                parts.append(RemoteDMATransfer(dst_ids=[DstId(rid=rid, pnc=pid)], remote_sem=T.sem["ha%d" % t],
                                               dma_engine_mask=engines_mask(topo, core, rl[h], 8 * h, 8 * h + 8),
                                               srcs=[res(v(x, b + 512 * h, b + 512 * h + 512)) for x, b in names],
                                               dsts=[T["hand%d" % t][:]], alu_op=min(1, t)))
            e.remote_dma_fused(parts, local_sem=T.sem["ks%d" % t])
        i = rec("g", 0.4 if t else 3.0, 4.0, [v(x, b, b + 1024) for x, b in names], [], emit, "ks%d" % t, 16)
        for h in range(2):
            land(v("KK%d" % t, 512 * h + 16, 512 * h + 528), "ki%d%d" % (t, h), i, 7.0 if t else 8.0)

    def send_revoked(t):
        src = v("rS%d" % t, 0, 2)

        def emit(e):
            remote(e, topo, core, rv_relay, T["hrv%d" % t][:, 0:2], res(src), T.sem["ra%d" % t], T.sem["rs%d" % t])
        land(v("cI%d" % t, 0, 2), "ri%d" % t, rec("g", 0.3, 4.0, [src], [], emit, "rs%d" % t, 8), 5.0)

    def K(t, lo=0, hi=1280):
        return v("KK%d" % t, KB + lo, KB + hi)

    def vo(t, c):
        b = 16 * (t % 2)
        return v("vO", b + 8 * c, b + 8 * c + 8)

    def fifth(name, c, w=1):
        b = KB if name == "KK0" else 0
        return v(name, b + 640 * c, b + 640 * (c + w), 5)

    def to_o(out, copy, x):
        tt(copy, ind(x, v("bl", 0, 8)), v("DM", 0, 128), A.mult)
        mm(out, copy, v("G8b"))

    def both_to_o(out, copy, x):
        tt(copy, ind(x, v("bl2")), v("M2"), A.mult)
        group(out, [(v("Wd", 112 - 16 * gr, 240 - 16 * gr), v(copy[1], 16 * gr, 16 * gr + 16)) for gr in range(8)], 4)

    def struck(out, src, keys):
        for lo in range(0, 1280, OPT["piece"]):
            hi = min(1280, lo + OPT["piece"])
            ts(v(out[1], out[2] + lo, out[2] + hi), v(src[1], src[2] + lo, src[2] + hi), keys[0], A.is_equal, keys[1], A.mult)

    def part(x, lo, hi):
        return v(x[1], x[2] + lo, x[2] + hi)

    def take_off(out, minus, src):
        for lo in range(0, 1280, OPT["piece"]):
            a, b, c = [part(x, lo, min(1280, lo + OPT["piece"])) for x in (out, minus, src)]
            scan(a, b, c, A.add, 0.0, A.min)

    def pre(t):
        if not t or who("fill", t) == "laid":
            return W(t + 1)
        return K(t + 1) if t < RO - 1 and who("true", t) == "dma" else v("Y1")

    tab = v("NBi", 0, 1280)

    def first(t, c):
        z = hv("zh" if t else "z", c)
        rows = [top(x) for x in ("C%d" % t, "pRJ", "nRJ", "E%d" % t)]
        if t:
            cp(hv("Bv", c), ind(tab, vo(t, c)), who("Bv", t, c))
        group(MI(c, 0), [(rows[0], one), (v("G4"), z), (rows[1], one), (rows[2], one), (v("nG4"), z), (rows[3], one)])
        tt(hv("mB", c), MI(c, 0), hv("Bv", c) if t else fifth("NBi", c), A.min)
        no = v("nO", 16 * c, 16 * c + 8)
        if who("n", t, c) == "t":
            out = part(MI(c, 1), 0, 8)
            group(out, [(v("Wn", 16 - l, 144 - l), v("mB", 128 * c + l, 128 * c + 128, 16)) for l in range(16)], 4)
            plus(no, out, -float(OFF), who("nO", t, c))
        else:
            mm(MI(c, 1), v("G16b"), hv("mB", c))
            scan(hv("sc", c), v("RN"), MI(c, 1), A.max)
            plus(no, v("sc", 128 * c + 15, 128 * c + 128, 16), v("nof"), who("nO", t, c))
        cp(hv("BnL", c), ind(tab, no), who("BnL", t, c))
        cp(hv("BnH", c), hv("BnL", c), who("BnH", t, c))

    def true_rings(t, c):
        act(hv("Kt", c, 256), KV(c, 0, 256), AF.Relu)
        if who("fill", t) == "laid":
            return
        if OPT["Hm"] == "s":
            act(hv("Hm", c), hv("Kt", c), AF.Relu, scale=-1.0, bias=v("On", 0, 1))
        else:
            ts(hv("Hm", c), hv("Kt", c), 0.0, A.is_equal)

    def second(t, c):
        both, rawv, rawn = hv("KN", c, 256), hv("KN", 2 * c), hv("KN", 2 * c + 1)
        act(rawn, ind(W(t), v("nO", 16 * c, 16 * c + 8)), bias=-2.0 ** -11)
        if t:
            act(rawv, ind(W(t), vo(t, c)), bias=-2.0 ** -10)
            if c:
                ts(hv("m1", c, 256), both, v("rS%d" % (t - 1), 0, 1), A.is_equal)
            else:
                ts(hv("m1", c, 256), both, v("rq"), A.add, v("c2"), A.is_equal)
            come = []
            if t > 1 and who("fill", 1) != "laid":
                ts(hv("m2", c, 256), both, v("cI%d" % (t - 2), 0, 1), A.is_equal)
                come = [(v("nKI"), hv("m2", c, 256))]
            group(KV(c, 0, 256), [(v("Ib"), both)] + come + [(v("nKI"), hv("m1", c, 256))])
        else:
            plus(rawv, fifth("KK0", c), -2.0 ** -10, "s" if c else "v")
            mm(KV(c, 0, 256), v("Ib"), both)
        for b in (128 * c, 128 * c + 64):
            gather(("K", t, b // 64), "Kc", W(t), "BnL", b, 1.0)
        tt(hv("evn", c), KV(c, 0), rawn, A.is_equal)
        mm(SM(c, 1), hv("evn", c), v("G8b"))
        act(hv("dr", c, 8), SM(c, 1), AF.Sign, bias=v("drb"))
        if who("Kn", t, c) == "pre":
            true_rings(t, c)
        for q in range(2):
            for e, eq in enumerate(("eqV", "eqN")):
                for k in range(16):
                    s = (2048 * c + 1024 * q + k, 2048 * c + 1024 * q + 1024, 16)
                    b = 128 * e + 64 * q
                    chain("eq", tt(v(eq, *s), v("b%d" % c, b, b + 64), v("Kc", *s), A.is_equal, k % BY > 0))

    def third(t, c):
        for o, eq in ((CV, "eqV"), (CN, "eqN")):
            mm(o(c), hv("BnH", c), v("I17"), True, False)
            if o is CV:
                mm(o(c, 0, 17), hv("mB", c), v("G8b"), False, False)
            for k in range(16):
                if o is CV and k == OPT["drk"]:
                    mm(o(c, 0, 17), v("IS"), hv("dr", c, 8), False, False)
                mm(o(c, k + 1, 17), v(eq, 2048 * c + k, 2048 * c + 2048, 16), v("G8s"), False, k == 15, k % BY > 0)
        act(hv("cV", c, 136), CV(c))
        tt(hv("mn", c, 136), CN(c), hv("cV", c, 136), A.min)
        scan(hv("sc2", c, 136), v("RS"), hv("mn", c, 136), A.max)
        ts(wT(t, c, 8), Wi(c), SB - 1, A.bitwise_and)
        to_o(SM(c, 2), hv("Aw", c), wT(t, c, 8))
        w = vo(t + 1, c)
        cp(w, SM(c, 2), who("vO", t, c))
        act(hv("Kw", c), ind(K(t), w), bias=-128.0)
        if who("kp", t, c) == "fused":
            tt(hv("kp", c), ind(K(t), w), hv("V2", c), A.mult)
        else:
            act(hv("Kx", c), ind(K(t), w))
            tt(hv("kp", c), V2p(c), hv("Kx", c), A.mult)
        ts(hv("k2", c), hv("kp", c), 1 if t else 2, A.arith_shift_right, SB - 1, A.bitwise_and)
        plus(hv("PL", c), hv("k2", c), v("c0", t, t + 1), who("PL", t, c))
        if who("Kn", t, c) == "post":
            true_rings(t, c)
        if OPT["hz"] == "s":
            act(hv("hz", c), hv("Kw", c), AF.Relu, scale=-2.0 ** 18, bias=v("h18"))

    def next_nodes(t, c):
        act(hv("V2", c), ind(v("T1"), vo(t + 1, c)), bias=HALF)
        tt(hv("aH", c), MI(c, 0), hv("V2", c), A.min)
        if who("kp", t + 1, c) != "fused":
            act(V2p(c), hv("V2", c))

    def material(t, c):
        run = who("run", t, c)
        for p in range(1, 16) if run else ():
            copy_g(v("zr", 2048 * c + p, 2048 * c + 16 * run, 16), v("zb", 128 * c, 128 * c + run))
        for q in range(2):
            lo = 2048 * c + 1024 * q
            gather(("X", t, 2 * c + q), "Xc", v("X"), "PL", lo // 16, 0.5)
            if run <= 64 * q:
                for p in range(16):
                    chain("mx", tt(v("mx", lo + p, lo + 1024, 16), v("b%d" % c, 256 + 64 * q, 320 + 64 * q),
                                   v("Xc", lo + p, lo + 1024, 16), A.max, p % BY > 0))
                continue
            w = 1024 // len(SPLIT.get(("X", t, 2 * c + q), "s")) if q else 1024
            for a in range(lo, lo + 1024, w):
                head, keep, zc = v("Xc", a, a + w, 16), v("x0", a // 16, (a + w) // 16), 256 + (a - 2048 * c) // 16
                cp(keep, head, OPT["rs"])
                tt(head, v("b%d" % c, zc, zc + w // 16), keep, A.max)
                chain("mx", scan(v("mx", a, a + w), v("zr", a, a + w), v("Xc", a, a + w), A.max, 0.0, A.min))
        if run:
            copy_g(v("Xc", 2048 * c, 2048 * c + 16 * run, 16), v("x0", 128 * c, 128 * c + run))

    def fourth(t, c):
        lo, bank = 2048 * c, "b%d" % (2 + c)
        dT = v(bank, 256, 384)
        run = who("run", t, c) == 128
        mm(dT, top("LR", 128, 256, 4), top("LR", 0, 128, 4), True, False)
        mm(dT, hv("zb", c), v("nG4"), False, False)
        cuts = [(name, a, b) for name, x in (("Xc", who("xs", t, c)), ("mx", (0, OPT["ms"] if run else 128, 128)))
                for a, b in zip(x, x[1:]) if b > a]
        cuts.sort(key=lambda x: x[2])
        for i, (name, a, b) in enumerate(cuts):
            for k in range(16):
                p = (k + 1) % 16 if name == "Xc" else k
                src = v(name, lo + 16 * a + p, lo + 16 * b, 16)
                if run and name == "Xc" and not p:
                    src = v("x0", 128 * c + a, 128 * c + b)
                mm(v(bank, 256 + p, 384, 16, a, b), src, v("G8x" if name == "Xc" else "G8m"), False,
                   i == len(cuts) - 1 and k == 15, k % BY > 0 and (k < 15 or name == "mx"))
        nfv = who("nf", t, c) == "v"
        if nfv and t == RO - 1:
            ts(hv("nf", c), dT, v("nfc"), A.add, 0.0, A.max)
        scan(hv("sd", c), v("RD"), dT, A.min)
        if nfv and t < RO - 1:
            ts(hv("nf", c), dT, v("nfc"), A.add, 0.0, A.max)
        if not nfv:
            act(hv("nf", c), dT, AF.Relu, bias=v("nfc"))
        ts(hv("pi2", c, 8), v("sd", 128 * c + 15, 128 * c + 128, 16), SB - 1, A.bitwise_and)
        to_o(SM(c, 3), hv("Ap", c), hv("pi2", c, 8))
        do = v("dO", 16 * c, 16 * c + 8)
        cp(do, SM(c, 3), who("dO", t, c))
        tt(hv("zh", c), ind(v("Xc", lo, lo + 2048), do), hv("zq", c), A.add)
        if t == RO - 1:
            plus(hv("zF", c), hv("zh", c), -1024.0, who("zF", t, c))
            store("Sy"[c], T.yz[:, 128 * c:128 * c + 128], hv("zF", c), c)
        cap = v("b%d" % (6 + c), 128, 256) if OPT["cap"] == 6 else KV(c, 3)
        if OPT["hz"] == "t":
            holes = [(v("I44"), hv("Kw", c)), (top("c18"), one), (v("nI44"), hv("Kw", c))]
        else:
            holes = [(v("nIb"), hv("hz", c))]
        group(cap, holes + [(v("Ib"), hv("Kw", c)), (hv("nf", c), v("nBI"))])
        scan(hv("cs", c), v("C256"), cap, A.max, v("cs", 127, 128) if c else -128.0 - 65536)
        if t < RO - 1:
            if who("zb", t, c) == "s":
                act(hv("zb", c), hv("zh", c), scale=0.5, bias=-512.0)
            else:
                ts(hv("zb", c), hv("zh", c), -1024.0, A.add, 0.5, A.mult)
            mm(KV(c, 2), v("Ib"), hv("zb", c))
            act(hv("zq", c), hv("zh", c), scale=0.5, bias=511.75)

    def given(t, halves):
        a, w = 8 * halves[0], 8 * len(halves)
        for c in halves:
            tt(hv("pr", c), KV(c, 2), hv("Kt", 2 * c + 1), A.mult)
            mm(v("b7", 32 + 8 * c, 40 + 8 * c), hv("pr", c), v("G8h"))
        cp(v("hi", a, a + w), v("b7", 32 + a, 32 + a + w), who("hi", t))
        ts(v("h2", a, a + w), v("hi", a, a + w), 1023, A.bitwise_and)
        plus(v("hn", a, a + w), v("h2", a, a + w), -1024.0, who("hn", t))

    def active(t, halves):
        a, w = 8 * halves[0], 8 * len(halves)
        ts(v("F", a, a + w), Wi(halves[0], len(halves)), float(FAIL), A.is_lt)
        y = WR(16 + a, w)
        mm(y, v("I5"), v("dr", a, a + w), True, False)
        if 1 in halves:
            mm(WR(24, 8), On, v("F", 0, 8), False, False)
        mm(y, v("Tri"), v("F", a, a + w), False, True)


        def into_o(out, copy, x):
            if w == 8:
                to_o(out, hv(copy, halves[0]), x)
            elif OPT["to"] == "dm":
                tt(v(copy), ind(x, v("bl")), v("DM"), A.mult)
                for c in range(2):
                    mm(part(out, 8 * c, 8 * c + 8), hv(copy, c), v("G8b"), True, True, c > 0)
            else:
                both_to_o(out, v(copy, 0, 128), x)

        if not t:
            ts(v("aw", a, a + w), y, float(CAP), A.is_ge, 8.0, A.mult)
        H = v("b7", 16 + a, 16 + a + w)
        group(H, [(v("Ib"), v("hn", a, a + w)), (one, top("c12", 0, w)), (v("nFI"), v("F", a, a + w))]
              + [(v("nKI"), v("aw", a, a + w))] * (not t), 2)
        tt(v("src", a, a + w), H, wT(t, halves[0], w), A.min)
        into_o(v("b7", a, a + w), "Aq", v("src", a, a + w))
        plus(v("srO", a, a + w), v("b7", a, a + w), KB - 16.0 * (t > 0), who("srO", t) if t else "v")
        if not t:
            return
        ts(v("aw", a, a + w), y, float(CAP), A.is_lt, v("wcol"), A.mult)
        mm(WR(32 + a, w), v("nKI"), v("aw", a, a + w), True, False)
        todo = [(c, gr, lo) for c in halves for gr in range(8) for lo in range(0, 128, BLK)]
        for c, gr, lo in todo:
            e = BLK * (8 * (gr % 2) + 2 * (gr // 2) + c)
            mm(WR(32 + 8 * c + gr, 1, lo, lo + BLK), v("E", e, e + BLK, 1, lo, lo + BLK),
               v("aw", 8 * c + gr, 8 * c + gr + 1, 1, lo, lo + BLK), False, (c, gr, lo) == todo[-1], gr % 2 > 0 or lo > 0)
        ts(v("nw", a, a + w), WR(32 + a, w), v("wthr"), A.is_ge, v("spare"), A.mult)
        tt(v("sel", a, a + w), v("nw", a, a + w), wT(t - 1, halves[0], w), A.max)
        into_o(WR(80 + a, w), "Aqh", v("sel", a, a + w))
        cp(v("scO", a, a + w), WR(80 + a, w), who("scO", t))

    def writers(t):
        if t and who("fill", t) == "laid":
            come = [v("cI%d" % (t - 1), k, k + 1) for k in range(2)]
            if who("come", t) == "dma":
                struck(W(t + 1), K(t), come)
                add_into(W(t + 1), K(t), 1 + t)
            else:
                struck(v("NC"), K(t), come)
                take_off(W(t + 1), v("NC"), K(t))
        active(t, [1] if who("split", t) else [0, 1])
        skip = 16 if t else 0
        blocks = range(256 - BLK, -1, -BLK)
        if t < RO - 1:
            mm(v("b6", 0, 16), On, v("F"))
            act(v("fj"), v("b6", 0, 16), AF.Identity, bias=v("f0"), accum_out=v("fs"))
            next_nodes(t, 1)
            dl = v("b6", 256, 512)
            pairs = [(v("nIb"), v("mB")), (v("Ib"), v("aH"))]
            if t and OPT["nb"] == "s":
                group(dl, [(v("Ib"), v("Bv"))] + pairs)
                act(v("nb"), dl, bias=-0.25)
            else:
                group(dl, [(top("cQ"), top("On"))] + pairs)
                if t:
                    tt(v("nb"), dl, v("Bv"), A.add)
                else:
                    tt(fifth("NBi", 0, 2), dl, fifth("NBi", 0, 2), A.add)
            for b in blocks if t else ():
                cp(ind(v("NBi"), v("scO", b // 16, (b + BLK) // 16)), v("nb", b, b + BLK))
        if who("fill", t) == "laid":
            act(v("gv"), ind(v("KK%d" % t, skip, KB + 1280), v("srO")))
            laid = v("b7", 256, 512)
            mm(laid, v("Ib"), v("gv"), True, False)
            for c in range(2):
                mm(part(laid, 128 * c, 128 * c + 128), v("nHI"), hv("Kt", 2 * c), False, c == 1)
            for c in (1, 0):
                tt(hv("val", c) if t else fifth("KK0", c), part(laid, 128 * c, 128 * c + 128), hv("Kt", 2 * c), A.max)
            if t:
                ts(v("vm"), v("val"), v("cI%d" % (t - 1), 0, 1), A.not_equal)
                for b in blocks:
                    tt(ind(W(t + 1, 0, SPARE), v("scO", b // 16, (b + BLK) // 16)), v("val", b, b + BLK), v("vm", b, b + BLK), A.mult)
        for c in (1, 0) if who("fill", t) != "laid" else ():
            tt(hv("gv", c), ind(v("KK%d" % t, skip, KB + 1280), v("srO", 8 * c, 8 * c + 8)), hv("Hm", c), A.mult)
        if who("fill", t) == "laid":
            pass
        elif t:
            for b in blocks:
                tt(ind(W(t + 1, 0, SPARE), v("scO", b // 16, (b + BLK) // 16)), v("gv", b, b + BLK), v("Kt", b, b + BLK), A.add)
            come = [v("cI%d" % (t - 1), k, k + 1) for k in range(2)]
            struck(v("NC"), W(t + 1), come)
            take_off(pre(t), v("NC"), W(t + 1))
        else:
            for c in range(2):
                tt(fifth("KK0", c), KV(c, 0), hv("gv", c), A.max)
        if t < RO - 1:
            act(v("f2"), v("fs"), AF.Identity, bias=v("pR16"))
            act(v("f3"), v("f2"), AF.Identity, bias=v("nR16"))
            act(v("f4"), v("f3"), AF.Identity, scale=float(SB), bias=v("f1"))

    def same_node(t):
        act(v("code"), ind(v("CT"), v("vO", 16 * (t % 2), 16 * (t % 2) + 16)))
        per = 256 // BLK
        done = {}
        for k in range(4):
            for odd in range(2):
                b = "b%d" % (6 + odd)
                lo = 32 * k
                hi = lo + 16 + 16 * odd
                for c in range(2):
                    for l in range(0, 128, BLK):
                        at, x = BLK * (2 * (k % per) + c), v("code", 128 * c + l, 128 * c + l + BLK, 1, lo, hi)
                        i = mm(v(b, at, at + BLK, 1, l, l + BLK), x, x, True, True, l > 0)
                        if (k - 1, odd) in done:
                            ops[i][3].add((done[k - 1, odd], True))
                done[k, odd] = i
                if k % per == per - 1:
                    e = BLK * (8 * odd + 2 * (k + 1 - per))
                    act(v("E", e, e + 512), v(b), AF.Relu, scale=1.0 if odd else 256.0, bias=v("fb"))

    def revoke(t):
        ts(v("rq"), v("cs", 255, 256), R256, A.add, -R256, A.add)
        ts(v("c2"), v("cs", 255, 256), 128.0, A.add)
        if t == RO - 1:
            ts(v("rb"), v("c2"), v("rq"), A.subtract)
            ts(v("nrv"), v("rq"), v("c2"), A.subtract)
            cut = ((0, 800), (800, 1280))
            for lo, hi in cut:
                ts(v("NM", lo, hi), part(pre(t), lo, hi), v("rb"), A.is_equal, v("nrv"), A.mult)
            for i, (lo, hi) in enumerate(cut):
                scan(v("Yk", lo, hi), v("NM", lo, hi), part(pre(t), lo, hi), A.add, 0.0, A.min)
                store("Sy"[i], T.yk[:, lo:hi], v("Yk", lo, hi), 2 + i)
            return
        rv = [v("rS%d" % t, k, k + 1) for k in range(2)]
        ts(rv[0], v("c2"), v("rq"), A.subtract)
        if OPT["rv"] == "s":
            act(rv[1], v("c2"), AF.Identity, scale=-1.0, bias=v("rq"))
        else:
            ts(rv[1], v("rq"), v("c2"), A.subtract)
        send_revoked(t)
        if who("true", t) == "dma" and pre(t) == W(t + 1):
            rec("y", 0.05, 4.0, [W(t + 1)], [K(t + 1)], lambda e: e.dma_start(res(K(t + 1)), res(W(t + 1))), "cp%d" % t, 16)
        struck(v("NM"), pre(t), rv)
        send_rings(t + 1)
        if who("true", t) == "dma":
            add_into(K(t + 1), v("NM"), t)
        else:
            take_off(K(t + 1), v("NM"), pre(t))
        act(v("nfc"), v("fs"), AF.Identity, scale=-float(SB), bias=v("f4"))

    send_rings(0)
    steps = [("first", first, 0, 0), ("first", first, 0, 1)]
    for t in range(RO):
        more = t < RO - 1
        steps += [("second", second, t, 0), ("third", third, t, 0), ("second", second, t, 1)]
        steps += [("same", same_node, t)] * (t > 0 and OPT["same"] == "late")
        steps += [("given", given, t, [0]), ("active", active, t, [0])] * who("split", t)
        steps += [("third", third, t, 1), ("given", given, t, [1] if who("split", t) else [0, 1]), ("material", material, t, 0)]
        steps += [("next", next_nodes, t, 0)] * more
        steps += [("writers", writers, t)]
        steps += [("same", same_node, t + 1)] * (more and OPT["same"] != "late")
        steps += [("fourth", fourth, t, 0), ("material", material, t, 1)]
        steps += [("first", first, t + 1, 0)] * more
        steps += [("fourth", fourth, t, 1), ("revoke", revoke, t)]
        steps += [("first", first, t + 1, 1)] * more
    for s in steps:
        STEP[0] = "%s%s" % (s[0], s[2:])
        s[1](*s[2:])
    STEP[0] = ""
    if not SEQ:
        SEQ.append(order(ops))
    issue(g, T, ops, SEQ[0])


def hand_on(g, core, T, topo):
    n = len(T.cores)
    for r in range(n):
        src, below, above = T.cores[r], T.cores[(r - 1) % n], T.cores[(r + 1) % n]
        rl = relays(src, T, topo, below)
        rv_relay = relays(src, T, topo, above)[0]
        if core not in rl and core != rv_relay:
            continue
        for t in range(RO):
            if t and core == rv_relay:
                g.wait_ge(T.sem["ra%d" % (t - 1)], 8)
                remote(g, topo, core, above, T["cI%d" % (t - 1)][:, 0:2], T["hrv%d" % (t - 1)][:, 0:2],
                       T.sem["ri%d" % (t - 1)], T.sem["rl%d" % (t - 1)])
            if core in rl:
                h = rl.index(core)
                g.wait_ge(T.sem["ha%d" % t], 8)
                remote(g, topo, core, below, T["KK%d" % t][:, 512 * h + 16:512 * h + 528], T["hand%d" % t][:],
                       T.sem["ki%d%d" % (t, h)], T.sem["hs%d" % t])
        for t in range(RO):
            if core in rl:
                g.wait_ge(T.sem["hs%d" % t], 8)
            if t and core == rv_relay:
                g.wait_ge(T.sem["rl%d" % (t - 1)], 8)
